import numpy as np, ml_dtypes
CORES = [24,25,26,27,28,29,30,31]
N = 8
BF = ml_dtypes.bfloat16
def gentries(a):
    return np.ascontiguousarray(a.reshape(8, 16, -1).transpose(0, 2, 1)).reshape(8, -1)
def gtable(e):
    e = np.asarray(e); return np.ascontiguousarray(e.reshape(8, -1, 16).transpose(0, 2, 1)).reshape(128, -1).astype(np.int32)
B, W, F, R, L, S, ST, RO, CAP = 2048, 3200, 4, 768, 128, 2, 2, 3, 64
def points(rng, n):
    hub = rng.integers(0, B, (N, 8, 24))
    return np.where(rng.random((N, 8, n)) < 0.3, np.take_along_axis(hub, rng.integers(0, 24, (N, 8, n)), 2), rng.integers(0, B, (N, 8, n)))
def starts(rng, sizes):
    pool = np.argsort(rng.random((N, 8, B)), axis=-1)
    return np.take_along_axis(pool, (rng.random((N, 8, R)) * sizes).astype(np.int64), 2)
def backs(rng, v):
    return 4 * v + rng.integers(0, F, v.shape)
def fills(rng):
    share = rng.permutation(np.array([0.1, 0.3, 0.5, 0.7, 0.85, 0.9, 0.97, 1.0]))[:, None, None]
    return np.where(rng.random((N, 8, F, B)) < share, rng.integers(0, 7, (N, 8, F, B)), 7)
def parts(rng):
    x = rng.integers(0, 256, (N, 8, 16, B)); q = rng.integers(0, 256, (N, 8, 16, R))
    pf = points(rng, F * B).reshape(N, 8, F, B); mb = points(rng, F * B).reshape(N, 8, F, B)
    sizes = rng.permutation(np.array([8, 24, 64, 128, 256, 512, B, B]))[:, None]
    return x, q, pf, mb, fills(rng), backs(rng, points(rng, B)), starts(rng, sizes)
def pack(x, q, pf, mb, bd, ip, st):
    return {"xn": x.reshape(N, 128, B).astype(np.float32).astype(BF), "qr": q.reshape(N, 128, R).astype(np.float32).astype(BF),
            "pf": pf.reshape(N, 8 * F, B).astype(np.int32), "mb": mb.reshape(N, 8 * F, B).astype(np.int32), "bd": bd.reshape(N, 8 * F, B).astype(np.int32),
            "ip": ip.astype(np.int32), "st": np.stack([gtable(a) for a in st])}
def setup_inputs(rng):
    return pack(*parts(rng))
def setup_inputs_spread(rng):
    def uneven(shape):
        return np.minimum((B * rng.random(shape) ** 3).astype(np.int64), B - 1)
    x = np.minimum((np.exp2(8 * rng.random((N, 8, 1, B))) * rng.random((N, 8, 16, B))).astype(np.int64), 255)
    q = np.minimum((np.exp2(8 * rng.random((N, 8, 1, R))) * rng.random((N, 8, 16, R))).astype(np.int64), 255)
    return pack(x, q, uneven((N, 8, F, B)), B - 1 - uneven((N, 8, F, B)), fills(rng), backs(rng, uneven((N, 8, B))), uneven((N, 8, R)))
def setup_inputs_ends(rng):
    h = B // 2; lo = np.array([2, B - 3, 4, 0]); hi = np.array([B - 2, 1, B - 4, B - 1])
    def near(shape):
        return np.where(rng.random(shape) < 0.74, (B - 1) * rng.integers(0, 2, shape), rng.integers(3, h, shape))
    def ends(n):
        k = rng.integers(0, 4, (N, 8, 1, n)); m = 255 * rng.integers(0, 2, (N, 8, 16, n))
        return np.where(k == 0, 0, np.where(k == 1, 255, m))
    x = ends(B); q = ends(R); x[..., lo] = 0; x[..., hi] = 255
    pf = near((N, 8, F, B)); pf[..., 0] = lo[:F]; pf[..., B - 1] = hi[:F]; mb = near((N, 8, F, B))
    bd = np.where(rng.random((N, 8, F, B)) < 0.8, 7 * rng.integers(0, 2, (N, 8, F, B)), rng.integers(0, 8, (N, 8, F, B)))
    bd[:, 7, :, 0] = 7; bd[:, 7, :, B - 1] = 7
    v = near((N, 8, B)); ip = 4 * v + np.where(v == 0, 0, np.where(v == B - 1, F - 1, rng.integers(0, F, v.shape)))
    st = near((N, 8, R)); st[..., R - 1] = B - 1; q[..., R - 1] = 0; st[..., R - 2] = 0; q[..., R - 2] = 255
    ids = h + np.arange((S + 2) * 4).reshape(S + 2, 4)
    st[..., L - 4:L] = ids[0]
    for s in range(S):
        pf[..., ids[s]] = ids[s + 1]; bd[..., ids[s]] = 7
    bd[..., ids[S - 1]] = 6; bd[..., ids[S + 1]] = 6; ip[..., ids[S - 1]] = 4 * ids[S + 1] + F - 1
    if ST == 2 and RO >= 3 and S <= 3:
        n0 = h + (S + 2) * 4
        a0, a1, w1, w2, w3, y1, b0, b1, y2, z1, e0, e1 = (n0 + np.arange(12)).tolist()
        x[..., n0:n0 + 12] = 0; x[:, :, :2, n0:n0 + 12] = 4; x[:, :, 1, y2] = 3; x[:, :, 8:, b1] = 255; x[:, :, 8:, y1] = 64
        bd[..., n0:n0 + 12] = 7; bd[..., w2] = 6; bd[..., y2] = 6
        for i, j in ((a0, a1), (a1, w1), (w1, w2), (w2, w3), (b0, b1), (b1, w1), (e0, e1), (e1, y2), (y2, z1)):
            pf[..., i] = j
        pf[:, :, 0, w1] = y1; mb[..., w2] = y2
        ip[..., w2] = 4 * w1 + 2; ip[..., w1] = 4 * z1 + 1; ip[..., y2] = 4 * z1 + F - 1
        q[..., L - 9:L - 4] = 0; q[:, :, :2, L - 9:L - 4] = 4; q[:, :, 8:, L - 8] = 255; q[:, :, 0, L - 6] = 3; q[:, :, 1, L - 5] = 3
        st[..., L - 9:L - 4] = np.array([e0, b0, a0, a1, a1] if S == 3 else [e1, b1, a1, w1, w1])
    return pack(x, q, pf, mb, bd, ip, st)
def setup_inputs_corners(rng):
    x, q, pf, mb, bd, ip, st = parts(rng)
    cnt = rng.choice(np.array([0, 1, CAP - 1, CAP, CAP + 1, L]), (N, 8))
    cnt[0] = (CAP, CAP + 1, L, CAP - 1, 1, 0, CAP, L); cnt[1] = (CAP, L, CAP, CAP + 1, CAP, L, 0, CAP)
    cnt[(0 - (RO - 1) % (N - 1)) % N, 5] = CAP
    c = rng.integers(0, 5, (N, 8, F, B)); own = np.arange(B)
    pf = np.where(c == 0, 0, np.where(c == 1, B - 1, np.where(c == 2, own, pf)))
    st[..., R - 1] = B - 1; st[..., R - 2] = 0
    for r in range(N):
        for g in range(8):
            n = int(cnt[r, g]); od = rng.permutation(B); ids = od[:(S + 2) * L].reshape(S + 2, L)
            hit = np.sort(rng.permutation(L)[:n]); low = np.searchsorted(hit, np.arange(L)) - 1
            kind = rng.integers(0, 4, L)
            if ST == 1:
                kind = np.where(kind == 1, 0, np.where(kind == 3, 2, kind))
            kind[low < 0] = 0; kind[hit] = 4
            above = hit[np.maximum(low, 0)] if n else np.zeros(L, np.int64)
            a = st[r, g]; p = pf[r, g]; b = bd[r, g]
            a[:L] = np.where(kind == 2, ids[0][above], ids[0])
            for s in range(S):
                p[:, ids[s]] = ids[s + 1]; b[:, ids[s]] = 7
            b[:, ids[S - 1][(kind == 1) | (kind >= 3)]] = 6
            b[:, ids[S + 1]] = np.where(kind == 4, 5, 7)
            k = rng.integers(0, F, L)
            e = np.where((kind == 4) & (rng.random(L) < 0.2), 4 * ids[S - 1] + k, 4 * ids[S + 1] + k)
            e = np.where(kind == 3, e[above], e)
            ip[r, g][ids[S - 1]] = e
            if r == 1 and g == 5:
                alt = od[(S + 2) * L:(2 * S + 3) * L].reshape(S + 1, L); both = od[:(2 * S + 3) * L]
                xv = x[r, g]; qv = q[r, g]
                xv[:, both] = 0; xv[0, both] = 3; qv[:, :L] = 0; qv[0, :L] = 4
                mb[r, g][:, ids[0]] = alt[0]; b[:, ids[0]] = rng.integers(1, 4, (F, L))
                for s in range(S - 1):
                    p[:, alt[s]] = alt[s + 1]
                b[:, alt.reshape(-1)] = 7; ip[r, g][alt[S - 2]] = 4 * alt[S] + k
    return pack(x, q, pf, mb, bd, ip, st)
def setup_inputs_ties(rng):
    x, q, pf, mb, bd, ip, st = parts(rng)
    col = rng.choice(np.array([0, 1, 2, 255]), (N, 8, 16, 6))
    x = np.take_along_axis(col, rng.integers(0, 6, (N, 8, 1, B)), 3); q = np.take_along_axis(col, rng.integers(0, 6, (N, 8, 1, R)), 3)
    q[..., ::3] = np.minimum(q[..., ::3] + rng.integers(0, 2, q[..., ::3].shape), 255)
    m = rng.random((N, 8, B)) < 0.5
    pf[:, :, 1] = np.where(m, pf[:, :, 0], pf[:, :, 1]); mb[:, :, 2] = np.where(m, pf[:, :, 1], mb[:, :, 2])
    bd = np.where(bd == 7, 7, rng.integers(0, 4, bd.shape))
    st = starts(rng, rng.permutation(np.array([2, 3, 5, 9, 17, 33, 200, B]))[:, None])
    return pack(x, q, pf, mb, bd, ip, st)
def check_inputs(d):
    bad = []
    for k, lo, hi in (("xn", 0, 255), ("qr", 0, 255), ("pf", 0, B - 1), ("mb", 0, B - 1), ("bd", 0, 7), ("ip", 0, 4 * (B - 1) + F - 1), ("st", 0, B - 1)):
        a = np.asarray(d[k]).astype(np.float64)
        if not (np.min(a) >= lo and np.max(a) <= hi): bad.append("range of " + k)
        elif np.any(a != np.floor(a)): bad.append("whole numbers of " + k)
    if np.any((np.asarray(d["ip"]).astype(np.int64) & 3) >= F): bad.append("field of ip")
    return bad
def reference(xn, qr, pf, mb, bd, ip, st):
    X = np.zeros((N, 8, 16, W), np.int64); P = np.zeros((N, 8, F, W), np.int64); M = np.zeros((N, 8, F, W), np.int64)
    D = np.full((N, 8, F, W), 7, np.int64); I = np.zeros((N, 8, W), np.int64)
    X[..., :B] = xn.astype(np.float32).astype(np.int64).reshape(N, 8, 16, B); q = qr.astype(np.float32).astype(np.int64).reshape(N, 8, 16, R)
    P[..., :B] = pf.reshape(N, 8, F, B); M[..., :B] = mb.reshape(N, 8, F, B); D[..., :B] = bd.reshape(N, 8, F, B); I[..., :B] = ip
    start = np.stack([gentries(a) for a in st]).astype(np.int64)
    for t in range(RO):
        tau = np.add.reduce(q, axis=2) & 3; v = start
        for s in range(S):
            i = v[:, :, None, :]
            to = np.where(np.take_along_axis(D, i, 3) <= tau[:, :, None, :], np.take_along_axis(M, i, 3), np.take_along_axis(P, i, 3))
            xt = np.take_along_axis(X, to.reshape(N, 8, 1, F * R), 3).reshape(N, 8, 16, F, R)
            score = np.add.reduce(np.abs(xt - q[:, :, :, None, :]), axis=2)
            k = np.argmin(score, axis=2)
            u = v; v = np.take_along_axis(to, k[:, :, None, :], 2)[:, :, 0]
            q = (q + np.take_along_axis(X, v[:, :, None, :], 3)) >> 1
        base = B + (1 + ST) * L * t; left = {}
        for r in range(N):
            for g in range(8):
                x_, p_, m_, d_, i_ = X[r, g], P[r, g], M[r, g], D[r, g], I[r, g]
                wu, wk, vv, ql = u[r, g, :L], k[r, g, :L], v[r, g, :L], q[r, g][:, :L]
                lane = np.arange(L); wm = base + lane; e = 4 * wu + wk
                p_[:, wm] = p_[:, vv]; m_[:, wm] = m_[:, vv]; d_[:, wm] = d_[:, vv]; x_[:, wm] = ql; i_[wm] = e
                c, first = np.unique(vv, return_index=True)
                x_[:, c] = (x_[:, c] + ql[:, first]) >> 1; i_[c] = e[first]
                for z in range(1, ST + 1):
                    f = np.sort(np.unique(wu, return_index=True)[1])
                    lane, wu, wk, wm = lane[f], wu[f], wk[f], wm[f]
                    full = d_[wk, wu] != 7; o = ~full
                    m_[wk[o], wu[o]] = wm[o]; d_[wk[o], wu[o]] = t + 1
                    lane, wu, wk, wm = lane[full], wu[full], wk[full], wm[full]
                    c = base + L * z + lane
                    y = np.where(d_[:, wu] != 7, m_[:, wu], p_[:, wu]); y[wk, np.arange(len(wu))] = wm
                    x_[:, c] = x_[:, wu]; p_[:, c] = y; m_[:, c] = 0; d_[:, c] = 7
                    e = i_[wu]; i_[c] = e
                    wu, wk, wm = e >> 2, e & 3, c
                left[r, g] = lane[:CAP]
        old = q.copy()
        for r in range(N):
            s = (r - 1 - t % (N - 1)) % N
            for g in range(8):
                h = min(len(left[r, g]), len(left[s, g]))
                q[r, g][:, left[r, g][:h]] = old[s, g][:, left[s, g][:h]]
    return {"yx": X.reshape(N, 128, W).astype(np.float32).astype(BF), "yq": q.reshape(N, 128, R).astype(np.float32).astype(BF),
            "yp": P.reshape(N, 8 * F, W).astype(np.float32), "ym": M.reshape(N, 8 * F, W).astype(np.float32)}

@@ -1,0 +1,756 @@
+from concourse.bass import DstId, RemoteDMATransfer
+from concourse.mybir import dt, AluOpType, AxisListType, ActivationFunctionType
+
+B, W, R, L, RO = 2048, 3200, 768, 128, 3
+OFF = 768
+ENC = 1600.0
+QO = 1280.0
+
+SN = 2816
+CHUNKS = [(0, 128, "AAAA", "V"), (128, 320, "AADD", "S"), (448, 320, "AAAD", "S")]
+LOW = "SVV"
+ONS = "emx"
+SEED, JIT, LOOK, PASSES = 1, 200.0, 0.4, 6
+PIECE, SPLV, SPLS = 4, 1, 1
+S16 = True
+NENG = 16
+CY, PEC, GAM, SCA = 1.04, 0.55, 1.55, 3.8
+HOP, SELF, SFIX = 110.0, 70.0, 30.0
+
+f32, bf, f16, i32, u16 = "float32", "bfloat16", "float16", "int32", "uint16"
+SCRATCH = {
+    "xt": ("sbuf", [128, OFF + W], bf), "mt": ("sbuf", [128, OFF + W], f32), "it": ("sbuf", [128, OFF + W], i32),
+    "xs": ("sbuf", [128, 3 * SN], bf), "mn": ("sbuf", [128, 3 * SN], f32),
+    "mi": ("sbuf", [128, B], i32), "sti": ("sbuf", [128, 48], i32), "stu": ("sbuf", [128, 48], u16),
+    "qb": ("sbuf", [128, R], bf), "qh": ("sbuf", [128, R], f16), "qo": ("sbuf", [128, R], bf),
+    "snd": ("sbuf", [128, 3 * 256], bf), "rcv": ("sbuf", [128, 3 * 256], bf),
+    "ci": ("sbuf", [128, 144], bf), "c4": ("sbuf", [128, 144], bf), "c16": ("sbuf", [128, 128], bf), "j16": ("sbuf", [128, 128], bf),
+    "pi": ("sbuf", [128, 8], i32), "ei": ("sbuf", [128, 8], i32), "eu": ("sbuf", [128, 8], u16),
+    "col": ("sbuf", [128, 64], f32), "cw": ("sbuf", [128, 128], f32),
+    "mz": ("sbuf", [128, 144], bf), "mz4": ("sbuf", [128, 144], f16), "my": ("sbuf", [128, 5 * 144], f16),
+    "mm": ("sbuf", [128, 12 * 128], f16), "mb16": ("sbuf", [128, 3 * 128], bf),
+    "ee": ("sbuf", [128, 3 * 1024], bf), "dg": ("sbuf", [128, 384], f32), "rs": ("sbuf", [128, 384], f32), "jf": ("sbuf", [128, 128], f16), "cst": ("sbuf", [128, 128], f16),
+    "cv": ("sbuf", [128, 128], f32), "kt16": ("sbuf", [128, 192], bf), "tn": ("sbuf", [128, 6 * 128], f32), "c2": ("sbuf", [128, 6 * 128], f32),
+    "g16": ("sbuf", [128, R], f16), "ti": ("sbuf", [128, 192], i32), "tau": ("sbuf", [128, 192], i32),
+    "cc": ("sbuf", [128, 192], f32), "ff": ("sbuf", [128, 192], f32), "t16": ("sbuf", [128, 192], f16), "ou": ("sbuf", [128, 192], u16),
+    "dd": ("sbuf", [128, 4 * R], f32), "xr": ("sbuf", [128, 4 * R], bf), "ab": ("sbuf", [128, 4 * R], bf),
+    "sks": ("sbuf", [128, 144], f32), "m2": ("sbuf", [128, 144], f32), "m1": ("sbuf", [128, 96], f32), "eq": ("sbuf", [128, 192], f32),
+    "zz": ("sbuf", [128, 192], f32), "a2": ("sbuf", [128, 96], f32), "ve": ("sbuf", [128, 96], f32), "lv": ("sbuf", [128, 96], u16),
+    "xg": ("sbuf", [128, R], bf), "sh": ("sbuf", [128, R], f16),
+    "wi": ("sbuf", [128, 16], i32), "xe": ("sbuf", [128, 3 * 128], f16), "fa": ("sbuf", [128, 3 * 1024], f32),
+    "w8": ("sbuf", [128, 192], f32), "la": ("sbuf", [128, 32], u16),
+    "s32": ("sbuf", [128, 128], f32), "mxi": ("sbuf", [128, 128], i32),
+    "km": ("sbuf", [128, 256], f16), "kq": ("sbuf", [128, 256], f16), "gk": ("sbuf", [128, 256], f16), "gs": ("sbuf", [128, 256], f16),
+    "g32": ("sbuf", [128, 256], f32), "e7": ("sbuf", [128, 256], f32), "ua": ("sbuf", [128, 256], f32), "ub": ("sbuf", [128, 256], f32),
+    "yy": ("sbuf", [128, 256], f32), "md": ("sbuf", [128, 256], f32), "ui": ("sbuf", [128, 256], i32),
+    "b1": ("sbuf", [128, 5 * 128], f32), "b2": ("sbuf", [128, 4 * 128], f32), "q1": ("sbuf", [128, 128], bf),
+    "rr": ("sbuf", [128, 128], bf),
+}
+for _b in range(8):
+    SCRATCH["ps%d" % _b] = ("psum", [128, 512], f32)
+NDMA = 40
+SEMAPHORES = ["cV", "cS", "cP", "cG", "snt0", "snt1", "snt2", "arr0", "arr1", "arr2"] + ["d%d" % _i for _i in range(NDMA)]
+TWO = (bf, f16, u16)
+A = AluOpType
+F = ActivationFunctionType
+
+
+def build(rank_peers):
+    ops = []
+    ndma = [0]
+
+    def ref(name, lo, n, step=1):
+        return (name, lo, lo + (n - 1) * step + 1, step)
+
+    def ind(name, lo, hi, off):
+        return ("*", name, lo, hi, off)
+
+    def regs(r):
+        if r[0] == "*":
+            return [(r[1], r[2], r[3]), r[4][:3]]
+        return [r[:3]]
+
+    def nel(r):
+        if r[0] == "*":
+            return 16 * (r[4][2] - r[4][1])
+        return (r[2] - r[1] + r[3] - 1) // r[3]
+
+    def ap(T, r):
+        if not isinstance(r, tuple):
+            return r
+        if r[0] == "*":
+            return T[r[1]][:, r[2]:r[3]].indirect(ap(T, r[4]))
+        if r[3] == 1:
+            return T[r[0]][:, r[1]:r[2]]
+        return T[r[0]][:, r[1]:r[2]:r[3]]
+
+    def kind(r):
+        return SCRATCH[r[1] if r[0] == "*" else r[0]]
+
+    def add(eng, fn, out, ins, cost, lat=0.0, sem=None, inc=1):
+        rd, wr = [], []
+        for r in ins:
+            if isinstance(r, tuple):
+                rd += regs(r)
+        for r in out:
+            if r[0] == "*":
+                wr.append((r[1], r[2], r[3])); rd.append(r[4][:3])
+            else:
+                wr.append(r[:3])
+        ops.append({"e": eng, "fn": fn, "rd": rd, "wr": wr, "c": cost, "lat": lat, "sem": sem, "inc": inc})
+
+    def vcost(out, ins, rate):
+        n = nel(out)
+        if out[0] == "*":
+            return 50 + SCA * n * CY
+        if ins[0][0] == "*":
+            return 50 + GAM * n * CY
+        return max(64, n * rate) * CY
+
+    def half(*rs):
+        return 0.5 if all(kind(r)[2] in TWO for r in rs) else 1.0
+
+    def tc(out, a):
+        add("V", lambda g, T: g.vector.tensor_copy(ap(T, out), ap(T, a)), [out], [a], vcost(out, [a], half(out, a)))
+
+    def tt(out, a, b, op):
+        rate = 1.0 if "psum" in (kind(a)[0], kind(b)[0]) else 2.0
+        add("V", lambda g, T: g.vector.tensor_tensor(ap(T, out), ap(T, a), ap(T, b), op), [out], [a, b], vcost(out, [a], rate))
+
+    def ts(out, a, s1, op0, s2=None, op1=None):
+        if op1 is None:
+            fn = lambda g, T: g.vector.tensor_scalar(ap(T, out), ap(T, a), ap(T, s1), None, op0)
+        else:
+            fn = lambda g, T: g.vector.tensor_scalar(ap(T, out), ap(T, a), ap(T, s1), ap(T, s2), op0, op1)
+        add("V", fn, [out], [a, s1, s2], vcost(out, [a], half(out, a)))
+
+    def scan(out, d0, d1, init, op0, op1):
+        add("V", lambda g, T: g.vector.tensor_tensor_scan(ap(T, out), ap(T, d0), ap(T, d1), init, op0, op1), [out], [d0, d1],
+            max(64, nel(out)) * CY)
+
+    def rmin(out, a):
+        add("V", lambda g, T: g.vector.tensor_reduce(ap(T, out), ap(T, a), AxisListType.X, A.min), [out], [a], max(64, nel(a)) * CY)
+
+    def act(out, a, func, bias=0.0, scale=1.0, accum=None):
+        c = 65 + GAM * nel(out) * CY if a[0] == "*" else max(64, nel(out)) * CY + SFIX + (20 if accum else 0)
+        add("S", lambda g, T: g.scalar.activation(ap(T, out), ap(T, a), func, bias=ap(T, bias), scale=ap(T, scale), accum_out=ap(T, accum)),
+            [out] + ([accum] if accum else []), [a, bias, scale], c)
+
+    def mm(groups, piece=99):
+        calls = [(out, l, r, i == 0, i == len(terms) - 1) for out, terms in groups for i, (l, r) in enumerate(terms)]
+        first = len(ops)
+        for lo in range(0, len(calls), piece):
+            def fn(g, T, part=calls[lo:lo + piece]):
+                for out, l, r, st, sp in part:
+                    last = g.tensor.matmul(ap(T, out), ap(T, l), ap(T, r), st, sp)
+                return last
+            part = calls[lo:lo + piece]
+            add("P", fn, [x[0] for x in part], [x[1] for x in part] + [x[2] for x in part],
+                sum(max(64, nel(x[2])) for x in part) * PEC + (60 if lo + piece >= len(calls) else 0))
+            ops[-1]["free"] = list(range(first, len(ops) - 1))
+            ops[-1]["after"] = ops[-1]["free"][-1:]
+
+    def iota(out, pattern, base, mult):
+        if kind(out)[2] == i32:
+            fn = lambda g, T: g.iota(ap(T, out), pattern, base, mult)
+        else:
+            fn = lambda g, T: g.iota(ap(T, out), pattern, base, mult, allow_small_or_imprecise_dtypes=True)
+        add("G", fn, [out], [], 130 + 2 * nel(out) * CY)
+
+    def dma(q, pairs, out, ins, nbytes):
+        sem = "d%d" % ndma[0]; ndma[0] += 1
+        n = pairs[1]
+
+        def fn(g, T):
+            e = g.sync if q == "Y" else g.scalar
+            for o, i in pairs[0](T):
+                e.dma_start(o, i).then_inc(T.sem[sem], 16)
+            return None
+        add(q, fn, out, ins, 60.0 * n, lat=1800 + nbytes / 180.0, sem=sem, inc=16 * n)
+
+    col = lambda c: ref("col", c, 1)
+    dma("Y", (lambda T: [(T.sti[:], T.st[:])], 1), [ref("sti", 0, 48)], [], 24576)
+    dma("Y", (lambda T: [(T.mi[0::4, :], T.pf[:]), (T.mi[1::4, :], T.mb[:]), (T.mi[2::4, :], T.bd[:]), (T.mi[3::4, :], T.bd[:])], 4),
+        [ref("mi", 0, B)], [], 1 << 20)
+    dma("S", (lambda T: [(T.qb[:], T.qr[:])], 1), [ref("qb", 0, R)], [], 196608)
+    dma("S", (lambda T: [(T.xt[:, OFF:OFF + B], T.xn[:])], 1), [ref("xt", OFF, B)], [], 1 << 20)
+    dma("S", (lambda T: [(T.xs[:, 0:B], T.xn[:])], 1), [ref("xs", 0, B)], [], 1 << 20)
+    dma("Y", (lambda T: [(T.it[r::16, OFF:OFF + B], T.ip[:]) for r in range(16)], 16), [ref("it", OFF, B)], [], 2 << 20)
+    iota(ref("pi", 0, 1), [[0, 1]], 0, 1)
+    iota(ref("ci", 0, 144), [[1, 144]], 0, 0)
+    iota(ref("c4", 0, 144), [[1, 36], [0, 4]], 0, 0)
+    iota(ref("j16", 0, 128), [[0, 8], [1, 16]], 0, 0)
+    iota(ref("c16", 0, 128), [[1, 8], [0, 16]], 0, 0)
+    iota(ref("ei", 0, 8), [[1, 8]], 0, 0)
+    for c0, n, _, _ in CHUNKS:
+        iota(ref("kt16", c0 // 4, n // 4), [[1, 4], [0, n // 16]], 0, 0)
+    p0 = ref("pi", 0, 1)
+    ts(ref("pi", 1, 1), p0, 3, A.bitwise_and)
+    ts(ref("pi", 2, 1), p0, 2, A.logical_shift_right, 3, A.bitwise_and)
+    ts(ref("pi", 3, 1), p0, 112, A.bitwise_and)
+    ts(ref("pi", 4, 1), p0, 15, A.bitwise_and)
+    ts(ref("pi", 5, 1), p0, 2, A.logical_shift_right)
+    tc(ref("col", 0, 6), ref("pi", 0, 6))
+    CP, CTY, CA, CG16, CS, CP4 = [col(i) for i in range(6)]
+    ts(ref("col", 8, 4), ref("ci", 0, 4), CTY, A.is_equal)
+    T0, T1, T2, T3 = [col(8 + i) for i in range(4)]
+    ts(col(12), CG16, CA, A.add, 12.0, A.add)
+    tt(col(13), T1, T0, A.subtract)
+    ts(col(14), CTY, 1.5, A.is_lt, ENC, A.mult)
+    COFF = col(14)
+    ts(col(15), CG16, 0.25, A.mult, 3.0, A.add)
+    for k in range(4):
+        ts(ref("my", 144 * k, 140), ref("ci", 0, 140), col(12), A.is_equal, col(8 + k), A.mult)
+    ts(ref("my", 144 * 4, 140), ref("ci", 0, 140), col(12), A.is_equal, col(13), A.mult)
+    ts(ref("mz4", 0, 140), ref("c4", 0, 140), col(15), A.is_equal)
+    ts(col(16), CG16, 15.0, A.add)
+    ts(ref("mz", 0, 143), ref("ci", 0, 143), col(16), A.is_equal, 4.0, A.mult)
+    Y = lambda k, sh: ref("my", 144 * k + 12 - 4 * sh, 128)
+    M = lambda i: ref("mm", 128 * i, 128)
+    ci = ref("ci", 0, 128)
+    ts(ref("mb16", 0, 128), ci, CP, A.is_equal)
+    ts(ref("mb16", 128, 128), ci, CP, A.is_equal, 0.5, A.mult)
+    IB, IBH = ref("mb16", 0, 128), ref("mb16", 128, 128)
+    ts(M(0), ci, CP, A.is_equal, -1.0, A.mult)
+    ts(M(1), ci, CP, A.is_equal, 0.5, A.mult)
+    ts(M(2), ci, CP, A.is_equal)
+    INEG, IH, I16 = M(0), M(1), M(2)
+    ts(col(17), CG16, 0.0625, A.mult)
+    ts(M(3), ref("c16", 0, 128), col(17), A.is_equal)
+    ts(M(4), ref("c16", 0, 128), col(17), A.is_equal, 4.0, A.mult)
+    ts(M(5), ref("c16", 0, 128), col(17), A.is_equal, T2, A.mult)
+    BO, BO4, BOD = M(3), M(4), M(5)
+    ts(M(6), ref("c4", 0, 128), CP4, A.is_equal, T2, A.mult)
+    tt(col(18), T1, T2, A.add)
+    ts(col(19), col(18), -1.0, A.mult)
+    ts(col(20), CP, -1.0, A.add)
+    ts(col(21), T1, -1.0, A.mult)
+    ts(M(7), ci, CP, A.is_equal, col(18), A.mult)
+    ts(M(8), ci, CP, A.is_equal, col(19), A.mult)
+    ts(M(9), ci, CP, A.is_equal, T0, A.mult)
+    ts(M(10), ci, col(20), A.is_equal, T1, A.mult)
+    ts(M(11), ci, col(20), A.is_equal, col(21), A.mult)
+    DAL, IMD, IMDN, IP, SH, SHN = M(6), M(7), M(8), M(9), M(10), M(11)
+    DG, RS, JF, CST = ref("dg", 0, 128), ref("rs", 0, 128), ref("jf", 0, 128), ref("cst", 0, 128)
+    ts(DG, ref("j16", 0, 128), CS, A.is_equal)
+    ts(RS, ref("j16", 0, 128), 0.5, A.is_gt)
+    ts(JF, ci, 1.0 / 256, A.mult)
+    ts(col(22), T0, ENC, A.mult)
+    ts(col(23), T2, 7.0, A.mult, col(22), A.add)
+    ts(CST, ci, 0.0, A.mult, col(23), A.add)
+    tc(ref("eu", 0, 8), ref("ei", 0, 8))
+    EU = ref("eu", 0, 8)
+    cw = lambda i: ref("cw", 8 * i, 8)
+    cv = lambda i: ref("cv", 8 * i, 8)
+    aff = lambda o, a, s, b: act(o, a, F.Identity, scale=s, bias=b)
+    PK, PKM, PB, PC = ref("ps7", 0, 128), ref("ps0", 256, 128), ref("ps7", 256, 128), ref("ps7", 384, 128)
+    aff(ref("rs", 128, 128), ci, 0.0, 1.0)
+    ts(ref("b1", 128, 128), ci, -1.0, A.mult, 127.0, A.add)
+    ts(ref("b1", 256, 128), ref("b1", 128, 128), CS, A.subtract)
+    aff(ref("b1", 384, 128), RS, 4096.0, 0.0)
+    tt(ref("rs", 256, 128), ref("b1", 256, 128), ref("b1", 384, 128), A.add)
+    ts(cw(0), ref("ei", 0, 8), 16.0, A.mult, CS, A.add)
+    aff(cw(1), cw(0), -4096.0, ENC + OFF)
+    aff(cw(2), cw(0), 1.0 / 256, 0.0)
+    aff(cv(0), cw(0), 1.0, -ENC - OFF)
+    aff(cv(1), cw(0), 4096.0, 0.0)
+    aff(col(24), COFF, 1.0 / ENC, 0.0)
+    aff(col(25), COFF, -1.0, 0.0)
+    aff(ref("dg", 128, 128), DG, 7.5, -1.0)
+    if "P" in LOW:
+        BOB = ref("mb16", 256, 128)
+        ts(BOB, ref("c16", 0, 128), col(17), A.is_equal)
+        aff(ref("b2", 0, 128), ci, 0.0, 0.5)
+        aff(ref("b2", 128, 128), ci, 0.0, -1.0)
+        scan(ref("b2", 256, 128), ref("b2", 0, 128), ref("b2", 128, 128), 2.0 ** 64, A.mult, A.max)
+        tt(ref("b2", 384, 128), ref("b2", 256, 128), DG, A.mult)
+        aff(ref("dg", 256, 128), ref("b2", 384, 128), 2.5, 0.0)
+        scan(ref("b1", 0, 128), RS, ref("b2", 384, 128), 0.0, A.mult, A.add)
+        aff(cv(10), ref("b1", 15, 8, 16), 1.0, 0.0)
+    for t in range(RO):
+        if LOW[0] != "S":
+            aff(cw(3 + t), cw(0), 1.0, 256.0 * t)
+        else:
+            aff(cv(3 + t), cw(0), 1.0, 256.0 * t - ENC - OFF)
+        if LOW[2] == "V":
+            aff(cw(6 + t), cw(0), 1.0, 256.0 * t + 128 + 262144.0)
+        else:
+            aff(cv(6 + t), cw(0), 1.0, 256.0 * t + 128)
+        aff(ref("c2", 256 * t, 128), ci, 1.0, 256.0 * t + 128 - OFF)
+        aff(ref("c2", 256 * t + 128, 128), ci, 1.0 if LOW[2] == "P" else 257.0 / 256, 256.0 * t + 128)
+        aff(col(28 + t), T2, t + 1.0, 0.0)
+        for z in range(2):
+            aff(col(32 + 2 * t + z), col(24), B + 384.0 * t + 128 * z - ENC, col(28 + t))
+            aff(ref("tn", 128 * (2 * t + z), 128), ci, col(24), col(32 + 2 * t + z))
+    iota(ref("mt", 0, OFF), [[0, OFF]], 7, 0)
+    iota(ref("it", 0, OFF), [[0, OFF]], 0, 0)
+    iota(ref("xt", 0, OFF), [[0, OFF]], 0, 0)
+    iota(ref("snd", 0, 768), [[0, 768]], -1, 0)
+    for c0, n, _, _ in CHUNKS:
+        tc(ref("stu", c0 // 16, n // 16), ref("sti", c0 // 16, n // 16))
+        ts(ref("qh", c0, n), ref("qb", c0, n), QO, A.add)
+    for i in range(4):
+        tc(ref("mt", OFF + 512 * i, 512), ref("mi", 512 * i, 512))
+    if S16:
+        dma("Y", (lambda T: [(T.mn[:, 0:B], T.mt[:, OFF:OFF + B])], 1), [ref("mn", 0, B)], [ref("mt", OFF, B)], 1 << 20)
+    dma("Y", (lambda T: [(T.mn[r::4, SN * t:SN * t + B], T.mt[r::4, OFF:OFF + B]) for r in (0, 3) for t in (1, 2)], 4),
+        [ref("mn", SN, B), ref("mn", 2 * SN, B)], [ref("mt", OFF, B)], 1 << 20)
+    dma("Y", (lambda T: [(T.yp[:, 0:B], T.mt[0::4, OFF:OFF + B])], 1), [], [ref("mt", OFF, B)], 262144)
+
+    def reads(t, ci_, c0, n, routes, qroute):
+        base = B + 384 * t
+        m, r4 = n // 16, n // 4
+        pb = "ps%d" % (0 if ci_ == 0 else 2 + ci_)
+        px = [["ps4", "ps6"], ["ps5", "ps6"]][ci_] if len(CHUNKS) == 2 else [["ps7", "ps7"], ["ps5", "ps5"], ["ps6", "ps6"], []][ci_]
+        q = ref("qh", c0, n)
+        o4 = c0 // 4
+        c4_ = lambda nm, lo=0, cnt=r4: ref(nm, o4 + lo, cnt)
+        pD, pE, pP, pT, pS = [ref(pb, r4 * i, r4) for i in range(5)]
+        pt0, n2 = 3 * r4, n // 2
+        if n > 512:
+            pb, px, pt0 = "ps4", ["ps5", "ps6"], 0
+            pT, pS = ref(pb, 0, r4), ref(pb, r4, r4)
+        elif len(CHUNKS) == 2 and n == 128:
+            px = ["ps7", "ps7"]
+        px0 = 0
+        if len(CHUNKS) == 4 and ci_:
+            px, px0 = [pb, pb], 5 * r4
+        pU = pS if ci_ else ref("ps2", 256, r4)
+        pc, sp, ss = (PIECE, SPLV, SPLS) if ci_ else (99, 1, 1)
+        XW = lambda off: ind("xt", OFF, OFF + base, off) if ci_ == 0 else ind("xs", SN * t, SN * t + base, off)
+        MW = lambda off: ind("mt", OFF, OFF + base, off) if ci_ == 0 else ind("mn", SN * t, SN * t + base, off)
+        mm([(pU, [(ref("mz4", 12 - 4 * s, 128), ref("qh", c0 + s, r4, 4)) for s in range(4)])])
+        tc(c4_("ti"), pU)
+        ts(c4_("tau"), c4_("ti"), 3, A.bitwise_and)
+        lst = ref("stu", c0 // 16, m)
+        for rd in range(2):
+            if n > 512:
+                for h in range(2):
+                    l_ = ref(lst[0], lst[1] + h * m // 2, m // 2)
+                    if t == 0 and rd == 0:
+                        ts(ref("g16", c0 + h * n2, n2), ind("mi", 0, B, l_), COFF, A.subtract)
+                    else:
+                        act(ref("g16", c0 + h * n2, n2), MW(l_), F.Identity, bias=col(25))
+            elif t == 0 and (rd == 0 or not S16 or ci_ == 0):
+                ts(ref("g16", c0, n), ind("mi", 0, B, lst), COFF, A.subtract)
+            elif S16:
+                act(ref("g16", c0, n), MW(lst), F.Identity, bias=col(25))
+            else:
+                ts(ref("g16", c0, n), MW(lst), COFF, A.subtract)
+            gs = lambda s: ref("g16", c0 + s, r4, 4)
+            mm([(pD, [(Y(2, s), gs(s)) for s in range(4)])])
+            mm([(pE, [(Y(4, s), gs(s)) for s in range(4)]), (pP, [(Y(0, s), gs(s)) for s in range(4)])], pc)
+            tt(c4_("cc"), pD, c4_("tau"), A.is_le)
+            tt(c4_("ff"), pE, c4_("cc"), A.mult)
+            tt(c4_("t16"), pP, c4_("ff"), A.add)
+            mm([(ref(pb, pt0 + k * m, m), [(Y(k, cl), ref("t16", o4 + cl, m, 4)) for cl in range(4)]) for k in range(4)], pc)
+            ts(c4_("ou"), pT, ENC, A.add)
+            nd = 0
+            order = [k for k in range(4) if routes[k] != "A"] + [k for k in range(4) if routes[k] == "A"]
+            for k in order:
+                off = c4_("ou", k * m, m)
+                at = 4 * c0 + k * n
+                if n > 512:
+                    for h in range(2):
+                        a_, q_, o_ = at + h * n2, ref("qh", c0 + h * n2, n2), XW(c4_("ou", k * m + h * m // 2, m // 2))
+                        if routes[k] == "A" or (routes[k] == "H" and h):
+                            tt(ref("dd", a_, n2), o_, q_, A.subtract)
+                            act(ref("ab", a_, n2), ref("dd", a_, n2), F.Abs, bias=QO)
+                        else:
+                            act(ref("xr", a_, n2), o_, F.Copy)
+                            pd = ref(px[nd % 2], 0, n2); nd += 1
+                            mm([(pd, [(INEG, q_), (IB, ref("xr", a_, n2))])])
+                            act(ref("ab", a_, n2), pd, F.Abs, bias=QO)
+                elif routes[k] == "A":
+                    for h in range(sp):
+                        tt(ref("dd", at + h * n // sp, n // sp), XW(c4_("ou", k * m + h * m // sp, m // sp)), ref("qh", c0 + h * n // sp, n // sp),
+                           A.subtract)
+                    if n > 128 or "D" in routes or k >= 2:
+                        act(ref("ab", at, n), ref("dd", at, n), F.Abs, bias=QO)
+                    elif k % 2:
+                        act(ref("ab", at - n, 2 * n), ref("dd", at - n, 2 * n), F.Abs, bias=QO)
+                else:
+                    for h in range(ss):
+                        act(ref("xr", at + h * n // ss, n // ss), XW(c4_("ou", k * m + h * m // ss, m // ss)), F.Copy)
+                    pd = ref(px[nd % 2], px0, n); nd += 1
+                    mm([(pd, [(INEG, q), (IB, ref("xr", at, n))])])
+                    act(ref("ab", at, n), pd, F.Abs, bias=QO)
+            mm([(pS, [(IB, c4_("kt16"))] + [(ref("mz", 15 - s, 128), ref("ab", 4 * c0 + s, r4, 16)) for s in range(16)])], pc)
+            o3, o2 = 3 * c0 // 16, 2 * c0 // 16
+            sk = lambda lo, cnt: ref(pb, pt0 + r4 + lo, cnt)
+            if n == 128:
+                tc(ref("sks", o3, 2 * m), sk(2 * m, 2 * m)); tc(ref("sks", o3 + 2 * m, m), sk(0, m))
+            else:
+                act(ref("sks", o3, 2 * m), sk(2 * m, 2 * m), F.Copy); act(ref("sks", o3 + 2 * m, m), sk(0, m), F.Copy)
+            tt(ref("m2", o3, 3 * m), sk(0, 3 * m), ref("sks", o3, 3 * m), A.min)
+            tt(ref("m1", o2, 2 * m), ref("m2", o3, 2 * m), ref("m2", o3 + m, 2 * m), A.min)
+            tt(c4_("eq", 0, 2 * m), sk(0, 2 * m), ref("m1", o2, 2 * m), A.is_equal)
+            tt(c4_("eq", 2 * m, 2 * m), sk(2 * m, 2 * m), ref("m1", o2, 2 * m), A.is_equal)
+            tt(c4_("zz"), pT, c4_("eq"), A.mult)
+            tt(ref("a2", o2, 2 * m), c4_("zz", 0, 2 * m), c4_("zz", 2 * m, 2 * m), A.add)
+            ve = ref("ve", 48 * rd + c0 // 16, m)
+            tt(ve, ref("a2", o2, m), ref("a2", o2 + m, m), A.add)
+            lst = ref("lv", 48 * rd + c0 // 16, m)
+            ts(lst, ve, ENC, A.add)
+            if n > 512:
+                for h in range(2):
+                    c_, l_ = c0 + h * n2, XW(ref("lv", 48 * rd + c0 // 16 + h * m // 2, m // 2))
+                    if qroute == "V" or (qroute == "H" and h):
+                        tt(ref("sh", c_, n2), l_, ref("qh", c_, n2), A.add)
+                        ts(ref("qh", c_, n2), ref("sh", c_, n2), 0.5, A.mult, QO / 2 - 0.25, A.add)
+                    else:
+                        act(ref("xg", c_, n2), l_, F.Copy)
+                        mm([(ref(px[h], 0, n2), [(IH, ref("qh", c_, n2)), (IBH, ref("xg", c_, n2))])])
+                        act(ref("qh", c_, n2), ref(px[h], 0, n2), F.Identity, bias=QO / 2 - 0.25)
+            elif qroute == "V":
+                tt(ref("sh", c0, n), XW(lst), q, A.add)
+                ts(q, ref("sh", c0, n), 0.5, A.mult, QO / 2 - 0.25, A.add)
+            else:
+                act(ref("xg", c0, n), XW(lst), F.Copy)
+                pq = ref(px[0], px0, n)
+                mm([(pq, [(IH, q), (IBH, ref("xg", c0, n))])])
+                if S16:
+                    act(q, pq, F.Identity, bias=QO / 2 - 0.25)
+                else:
+                    ts(q, pq, QO / 2 - 0.25, A.add)
+            if ci_ == 0 and rd == 0:
+                lowest_of(t, 0, ref("ve", 0, 8), 3 + t)
+                step_a(t, 0, LA(0))
+        c1 = max(c0, L)
+        if t == RO - 1 and c1 < c0 + n:
+            ts(ref("qo", c1, c0 + n - c1), ref("qh", c1, c0 + n - c1), -QO, A.add)
+            dma("Y", (lambda T: [(T.yq[:, c1:c0 + n], T.qo[:, c1:c0 + n])], 1), [], [ref("qo", c1, c0 + n - c1)], 256 * n)
+
+    w8 = lambda i: ref("w8", 8 * i, 8)
+    LA = lambda i: ref("la", 8 * i, 8)
+
+    def lowest(i, key, bias, um, dum, sub, thr):
+        for c in range(8):
+            a = ref("fa", 1024 * i + 128 * c, 16 * c + 16)
+            o = ref("w8", 8 * (6 * i + 2) + c, 1)
+            act(a, ref(key[0], key[1], 16 * c + 16), F.Abs, bias=ref(bias[0], bias[1] + c, 1), scale=-1048576.0)
+            if LOW[i] == "V":
+                rmin(o, a)
+            else:
+                act(a, a, F.Relu, bias=thr(c), scale=-1.0, accum=o)
+        if LOW[i] == "V":
+            tt(w8(6 * i + 3), w8(6 * i + 2), um, A.add)
+        else:
+            tt(w8(6 * i + 3), um, w8(6 * i + 2), A.subtract)
+        tt(w8(6 * i + 4), w8(6 * i + 3), dum, A.max)
+        ts(LA(i), w8(6 * i + 4), sub, A.add)
+
+    def lowest_p(i, key, zc, um, dum, sub):
+        for c in range(8):
+            ts(ref("ee", 1024 * i + 128 * c, 128 - 16 * c), ref(key[0], key[1] + 16 * c, 128 - 16 * c), zc(c), A.is_equal,
+               ref("cv", 80 + c, 1), A.mult)
+        pw = ref("ps1", 128 * i, 128) if i == 2 else ref("ps7", 256 + 128 * i, 128)
+
+        def fn(g, T):
+            for c in range(8):
+                last = g.tensor.matmul(ap(T, ref(pw[0], pw[1] + 16 * c, 128 - 16 * c)), ap(T, BOB), ap(T, ref("ee", 1024 * i + 128 * c, 128 - 16 * c)),
+                                       c == 0, c == 7)
+            return last
+        add("P", fn, [pw], [BOB, ref("ee", 1024 * i, 1024)], 672 * PEC + 60)
+        fd, fs = ref("fa", 256 * i, 128), ref("fa", 256 * i + 128, 128)
+        tt(fd, pw, ref("dg", 256, 128), A.is_lt)
+        scan(fs, RS, fd, 0.0, A.mult, A.add)
+        tt(w8(6 * i + 3), ref("fa", 256 * i + 128 + 15, 8, 16), um, A.mult)
+        tt(w8(6 * i + 4), w8(6 * i + 3), dum, A.max if sub is None else A.add)
+        tc(LA(i), w8(6 * i + 4))
+
+    def lowest_of(t, i, ve, dum):
+        xe = ref("xe", 128 * i, 128)
+        tt(xe, ind("ve", ve[1], ve[2], EU), DG, A.mult)
+        key = ref("ps2", 128 * i, 128)
+        if LOW[i] == "P":
+            mm([(key, [(BO, xe)])])
+            act(w8(6 * i + 1), ve, F.Identity, bias=ENC + OFF)
+            lowest_p(i, key, lambda c: ref(ve[0], ve[1] + c, 1), w8(6 * i + 1), cw(dum), None)
+            return
+        mm([(key, [(I16, JF), (BO, xe)])])
+        act(w8(6 * i), ve, F.Copy, scale=1048576.0)
+        if LOW[i] == "V":
+            tt(w8(6 * i + 1), ve, cw(1), A.add)
+            lowest(i, key, w8(6 * i), w8(6 * i + 1), cw(dum), 0.0, None)
+        else:
+            lowest(i, key, w8(6 * i), ve, ref("cv", 8 * dum, 8), ENC + OFF, lambda c: ref("cv", 8 + c, 1))
+
+    pL, pA, pB_, pC = [ref("ps1", 128 * i, 128) for i in range(4)]
+
+    def step_a(t, z, la):
+        h = lambda nm: ref(nm, 128 * z, 128)
+        MW = ind("mt", 0, OFF + B + 384 * t, la)
+        act(h("gs"), MW, F.Identity, bias=col(25))
+        act(h("g32"), MW, F.Copy)
+        mm([(pL, [(DAL, h("gs"))]), (pB_, [(IP, h("gs")), (SHN, h("gs"))])])
+        if "e" in ONS:
+            act(h("e7"), pL, F.Relu, bias=-6.0)
+        else:
+            ts(h("e7"), pL, 7.0, A.is_equal)
+        tt(h("ub"), pB_, h("e7"), A.mult)
+
+    def step(t, z, la):
+        base = B + 384 * t
+        h = lambda nm: ref(nm, 128 * z, 128)
+        MW = ind("mt", 0, OFF + base, la)
+        cc_ = OFF + base + 128 * (z + 1)
+        if z == 1:
+            tt(ref("km", 128, 128), MW, ref("km", 0, 128), A.mult)
+            mm([(PK, [(BO, ref("km", 128, 128))])])
+            ts(h("md"), PK, 7.0, A.not_equal)
+            send(t)
+            step_a(t, z, la)
+        tt(h("gk"), PKM, h("gs"), A.mult)
+        if z == 0:
+            mm([(PK, [(BOD, h("gk"))])])
+        tt(h("kq"), PKM, ref("tn", 128 * (2 * t + z), 128), A.mult)
+        mm([(pA, [(IMD, h("kq")), (IMDN, h("gk"))]), (pC, [(I16, CST), (SH, h("gs")), (SHN, h("gk")), (IP, h("kq"))])])
+        if "m" in ONS and z == 0:
+            act(h("md"), PK, F.Sign, bias=7.0, scale=-1.0)
+        elif z == 0:
+            ts(h("md"), PK, 7.0, A.not_equal)
+        tt(h("ua"), pA, h("e7"), A.mult)
+        tt(MW, h("g32"), h("ua"), A.add)
+        tt(pC, pC, h("ub"), A.add)
+        tt(ref("mt", cc_, 128), pC, h("md"), A.mult)
+        tt(ref("xt", cc_, 128), ind("xt", 0, OFF + base, la), h("md"), A.mult)
+        if t < RO - 1:
+            tc(ref("it", cc_, 128), ind("it", 0, OFF + base, la))
+
+    sent = []
+
+    def send(t):
+        b2 = lambda i: ref("b2", 128 * i, 128)
+        tt(b2(1), PK, ref("dg", 128, 128), A.is_lt)
+        scan(PC, ref("md", 128, 128), ref("rs", 128, 128), -1.0, A.add, A.add)
+        tt(b2(2), PC, b2(1), A.mult)
+        scan(b2(3), ref("rs", 256, 128), b2(2), 128.0, A.min, A.add)
+        tc(LA(3), ref("b2", 384 + 15, 8, 16))
+        tc(ind("snd", 256 * t, 256 * t + 256, LA(3)), ref("xt", OFF + B + 384 * t, 128))
+        rid, pid, mask = rank_peers[t]
+        so, ro = ref("snd", 256 * t + 128, 64), ref("rcv", 64 * t, 64)
+        add("G", lambda g, T: g.remote_dma(ap(T, ro), ap(T, so), T.sem["arr%d" % t], T.sem["snt%d" % t], pid, rid, mask),
+            [], [so], 200.0, lat=2000.0, sem="snt%d" % t, inc=NENG)
+        sent.append(len(ops) - 1)
+        add("G", lambda g, T: None, [ro], [so], 1.0, lat=2700.0, sem="arr%d" % t, inc=NENG)
+
+    def writers(t):
+        base = B + 384 * t
+        q = ref("qh", 0, 128)
+        ve, lv = ref("ve", 48, 8), ref("lv", 48, 8)
+        nn = OFF + base
+        lowest_of(t, 1, ve, 0)
+        tc(ref("wi", 0, 8), ref("m1", 0, 8))
+        ts(ref("wi", 8, 8), ref("wi", 0, 8), 3, A.bitwise_and)
+        xk = ref("xe", 256, 128)
+        tt(xk, ind("wi", 8, 16, EU), DG, A.mult)
+        pI, pk = pL, pB_
+        mm([(pk, [(BO, xk)]), (pI, [(BO4, ref("xe", 0, 128)), (BO, xk)])])
+        ts(PKM, pk, CA, A.is_equal)
+        ts(ref("it", nn, 128), pI, 4 * ENC, A.add)
+        act(ref("mt", nn, 128), ind("mt", OFF, OFF + base, lv), F.Copy)
+        if "x" in ONS:
+            act(ref("xt", nn, 128), q, F.Identity, bias=-QO)
+        else:
+            ts(ref("xt", nn, 128), q, -QO, A.add)
+        if CHUNKS[0][3] == "V":
+            tt(ref("s32", 0, 128), ind("xt", OFF, OFF + base, lv), q, A.add)
+            ts(ref("mxi", 0, 128), ref("s32", 0, 128), 0.5, A.mult, -QO / 2 - 0.25, A.add)
+        else:
+            mm([(PC, [(IH, q), (IBH, ref("xg", 0, 128))])])
+            ts(ref("mxi", 0, 128), PC, -QO / 2 - 0.25, A.add)
+        tc(ind("it", 0, OFF + base, LA(1)), ref("it", nn, 128))
+        tc(ind("xt", 0, OFF + base, LA(1)), ref("mxi", 0, 128))
+        sn = SN * (t + 1)
+        if t < RO - 1:
+            dma("Y", (lambda T: [(T.xs[:, sn:sn + base], T.xt[:, OFF:nn])], 1), [ref("xs", sn, base)], [ref("xt", OFF, base)], 256 * base)
+        step(t, 0, LA(0))
+        ib = ind("it", 0, OFF + base, LA(0))
+        b1 = lambda i: ref("b1", 128 * i, 128)
+        ts(ref("ui", 0, 128), ib, 2, A.logical_shift_right)
+        ts(ref("ui", 128, 128), ib if t == RO - 1 else ref("it", nn + 128, 128), 3, A.bitwise_and)
+        ts(PKM, ref("ui", 128, 128), CA, A.is_equal)
+        ts(ref("km", 0, 128), ref("ui", 128, 128), CA, A.is_equal, T2, A.mult)
+        ts(PB, PK, 7.0, A.not_equal)
+        tt(b1(0), PB, ref("c2", 256 * t, 128), A.mult)
+        tt(b1(1), ref("c2", 256 * t + 128, 128), b1(0), A.subtract)
+        tt(PB, PB, ref("ui", 0, 128), A.mult)
+        tt(PB, PB, b1(1), A.add)
+        tt(b1(3), PB, DG, A.mult)
+        scan(b1(4), RS, b1(3), 0.0, A.mult, A.add)
+        kw = ref("b1", 512 + 15, 8, 16)
+        if LOW[2] == "P":
+            lowest_p(2, PB, lambda c: ref("b1", 512 + 15 + 16 * c, 1), kw, ref("cv", 8 * (6 + t), 8), None)
+        else:
+            act(w8(12), kw, F.Identity, scale=1048576.0, bias=-262144.0)
+            tt(w8(13), kw, cw(2), A.subtract)
+        if LOW[2] == "V":
+            lowest(2, PB, w8(12), w8(13), cw(6 + t), -262144.0, None)
+        elif LOW[2] == "S":
+            lowest(2, PB, w8(12), w8(13), ref("cv", 8 * (6 + t), 8), 0.0, lambda c: 262144.0)
+        step(t, 1, LA(2))
+        SW = ind("snd", 256 * t, 256 * t + 256, LA(3))
+        so, ro = ref("snd", 256 * t + 128, 64), ref("rcv", 64 * t, 64)
+        if t < RO - 1:
+            news = [sn + base] + ([sn + SN + base] if t == 0 else [])
+            dma("Y", (lambda T: [(T.mn[r::4, sn:sn + base], T.mt[r::4, OFF:nn]) for r in (1, 2)]
+                      + [(T.mn[:, x:x + 384], T.mt[:, nn:nn + 384]) for x in news] + [(T.xs[:, sn + base:sn + base + 384], T.xt[:, nn:nn + 384])],
+                      3 + len(news)),
+                [ref("mn", sn, base), ref("xs", sn + base, 384)] + [ref("mn", x, 384) for x in news],
+                [ref("mt", OFF, base + 384), ref("xt", nn, 384)], 256 * base + 300000)
+            ops[-1]["after"] = [sent[t]]
+        ts(ref("rr", 0, 64), ro, -0.5, A.is_lt)
+        tt(ref("rr", 64, 64), ref("rr", 0, 64), so, A.mult)
+        tt(so, ref("rr", 64, 64), ro, A.max)
+        if t < RO - 1:
+            ts(q, SW, QO, A.add)
+        else:
+            act(ref("qo", 0, 128), SW, F.Copy)
+            dma("S", (lambda T: [(T.yq[:, 0:128], T.qo[:, 0:128])], 1), [], [ref("qo", 0, 128)], 32768)
+
+    for t in range(RO):
+        for i, (c0, n, routes, qroute) in enumerate(CHUNKS):
+            reads(t, i, c0, n, routes, qroute)
+        writers(t)
+    e0 = W - 256
+    dma("Y", (lambda T: [(T.yx[:, 0:e0], T.xt[:, OFF:OFF + e0])], 1), [], [ref("xt", OFF, e0)], 256 * e0)
+    dma("Y", (lambda T: [(T.yp[:, B:e0], T.mt[0::4, OFF + B:OFF + e0])], 1), [], [ref("mt", OFF + B, e0 - B)], 128 * (e0 - B))
+    dma("Y", (lambda T: [(T.ym[:], T.mt[1::4, OFF:OFF + W])], 1), [], [ref("mt", OFF, W)], 128 * W)
+    dma("S", (lambda T: [(T.yx[:, e0:W], T.xt[:, OFF + e0:OFF + W]), (T.yp[:, e0:W], T.mt[0::4, OFF + e0:OFF + W])], 2), [],
+        [ref("xt", OFF + e0, 256), ref("mt", OFF + e0, 256)], 98304)
+    return ops
+
+
+def depends(ops):
+    hist = {}
+    for i, o in enumerate(ops):
+        dep = set(o.get("after", ()))
+        for acc, regs in ((0, o["rd"]), (1, o["wr"])):
+            for nm, lo, hi in regs:
+                ps = SCRATCH[nm][0] == "psum"
+                for j, w, l2, h2 in hist.get(nm, ()):
+                    if j == i:
+                        continue
+                    if (l2 < hi and lo < h2 and (w or acc)) or (ps and ops[j]["e"] != o["e"]):
+                        dep.add(j)
+        for acc, regs in ((0, o["rd"]), (1, o["wr"])):
+            for nm, lo, hi in regs:
+                h = hist.setdefault(nm, [])
+                if acc:
+                    h[:] = [x for x in h if not (lo <= x[2] and x[3] <= hi)]
+                h.append((i, acc, lo, hi))
+        o["dep"] = sorted(dep)
+
+
+def schedule(ops):
+    n = len(ops)
+    succ, pred = [[] for _ in ops], [[] for _ in ops]
+    for i, o in enumerate(ops):
+        for j in o["dep"]:
+            p = ops[j]
+            d = p["lat"] + (0.0 if j in o.get("free", ()) else SELF if p["e"] == o["e"] and not p["sem"] else HOP)
+            succ[j].append((i, d)); pred[i].append((j, d))
+    pr = [0.0] * n
+    for i in range(n - 1, -1, -1):
+        pr[i] = ops[i]["c"] + max([pr[j] + d for j, d in succ[i]] + [ops[i]["lat"]])
+    x = SEED
+    best = None
+    for it in range(PASSES):
+        for i in range(n):
+            x = (x * 1103515245 + 12345) % 2147483648
+            pr[i] += JIT * (x / 2147483648.0)
+        order, st = one_pass(ops, succ, pred, pr, [0.0] * n)
+        end = max(st[i] + ops[i]["c"] + ops[i]["lat"] for i in range(n))
+        if best is None or end < best[1]:
+            best = (order, end, st)
+        if it + 1 < PASSES:
+            _, sb = one_pass(ops, pred, succ, [st[i] + ops[i]["c"] for i in range(n)], [o["lat"] for o in ops])
+            pr = [sb[i] + ops[i]["c"] for i in range(n)]
+    for i in range(n):
+        ops[i]["t"] = best[2][i]
+    return best[0], best[1]
+
+
+def one_pass(ops, succ, pred, pr, rdy):
+    n = len(ops)
+    left = [len(p) for p in pred]
+    free = {e: 0.0 for e in "VSPGY"}
+    pool = {e: [] for e in free}
+    for i in range(n):
+        if not left[i]:
+            pool[ops[i]["e"]].append(i)
+    order, start = [], [0.0] * n
+    while len(order) < n:
+        best = None
+        for e in pool:
+            if pool[e]:
+                t0 = max(free[e], min(rdy[i] for i in pool[e]))
+                if best is None or t0 < best[0]:
+                    best = (t0, e)
+        t0, e = best
+        i = max((i for i in pool[e] if rdy[i] <= t0 + 40.0), key=lambda i: pr[i])
+        late = [j for j in pool[e] if t0 + 40.0 < rdy[j] < t0 + LOOK * ops[i]["c"] and pr[j] > pr[i] + ops[i]["c"]]
+        if late:
+            j = max(late, key=lambda j: pr[j])
+            fit = [k for k in pool[e] if rdy[k] <= t0 + 40.0 and t0 + ops[k]["c"] <= rdy[j] + 30.0]
+            i = max(fit, key=lambda k: pr[k]) if fit else j
+        pool[e].remove(i)
+        start[i] = max(t0, rdy[i])
+        free[e] = start[i] + ops[i]["c"]
+        order.append(i)
+        for j, d in succ[i]:
+            rdy[j] = max(rdy[j], free[e] + d)
+            left[j] -= 1
+            if not left[j]:
+                pool[ops[j]["e"]].append(j)
+    return order, start
+
+
+def rank_program(g, core, T, topo):
+    rank = T.rank_of(core)
+    if rank is None:
+        return
+    n = len(T.cores)
+    peers = []
+    for t in range(RO):
+        dst = T.cores[(rank + 1 + t % (n - 1)) % n]
+        rid, pid, _ = topo.addr(dst)
+        peers.append((rid, pid, sum(1 << e for e in topo.engines(core, dst)[:NENG])))
+    ops = build(peers)
+    depends(ops)
+    order, _ = schedule(ops)
+    queue = {"V": g.vector, "S": g.scalar, "P": g.tensor, "G": g, "Y": g.sync}
+    count = {}
+    known = {e: {} for e in queue}
+    for i in order:
+        o = ops[i]
+        e = o["e"]
+        kn = known[e]
+        need = {}
+        for j in o["dep"]:
+            if j in o.get("free", ()):
+                continue
+            s, v = ops[j]["sig"]
+            if kn.get(s, 0) < v and need.get(s, (0, 0))[0] < v:
+                need[s] = (v, j)
+        for s, (v, j) in sorted(need.items(), key=lambda x: -ops[x[1][1]]["t"]):
+            if kn.get(s, 0) < v:
+                queue[e].wait_ge(T.sem[s], v)
+                kn[s] = v
+                for s2, v2 in ops[j]["kn"].items():
+                    if kn.get(s2, 0) < v2:
+                        kn[s2] = v2
+        o["kn"] = dict(kn)
+        ins = o["fn"](g, T)
+        if o["sem"]:
+            o["sig"] = (o["sem"], o["inc"])
+            count[o["sem"]] = o["inc"]
+        else:
+            s = "c" + e
+            count[s] = count.get(s, 0) + 1
+            o["sig"] = (s, count[s])
+            ins.then_inc(T.sem[s], 1)
+    for s in sorted(count):
+        if known["G"].get(s, 0) < count[s]:
+            g.wait_ge(T.sem[s], count[s])

@@ -7,15 +7,15 @@ ENC = 1600.0
 QO = 1280.0
 
 SN = 2816
-CHUNKS = [(0, 128, "AAAA", "V"), (128, 320, "AADD", "S"), (448, 320, "AAAD", "S")]
-LOW = "SVV"
-ONS = "emx"
-SEED, JIT, LOOK, PASSES = 1, 200.0, 0.4, 6
-PIECE, SPLV, SPLS = 4, 1, 1
+CHUNKS = [(0, 128, "AAAD", "V"), (128, 320, "AADD", "T"), (448, 320, "AAAD", "T")]
+LOW = "PVV"
+ONS = ""
+SEED, JIT, LOOK, PASSES = 3, 200.0, 0.4, 5
+PIECE, SPLV, SPLS, INORDER = 4, 1, 1, 0
 S16 = True
 NENG = 16
-CY, PEC, GAM, SCA = 1.04, 0.55, 1.55, 3.8
-HOP, SELF, SFIX = 110.0, 70.0, 30.0
+CY, PEC, GAM, SCA = 0.9, 0.45, 1.55, 3.8
+HOP, SELF, SFIX = 200.0, 170.0, 90.0
 
 f32, bf, f16, i32, u16 = "float32", "bfloat16", "float16", "int32", "uint16"
 SCRATCH = {
@@ -25,17 +25,18 @@ SCRATCH = {
     "qb": ("sbuf", [128, R], bf), "qh": ("sbuf", [128, R], f16), "qo": ("sbuf", [128, R], bf),
     "snd": ("sbuf", [128, 3 * 256], bf), "rcv": ("sbuf", [128, 3 * 256], bf),
     "ci": ("sbuf", [128, 144], bf), "c4": ("sbuf", [128, 144], bf), "c16": ("sbuf", [128, 128], bf), "j16": ("sbuf", [128, 128], bf),
-    "pi": ("sbuf", [128, 8], i32), "ei": ("sbuf", [128, 8], i32), "eu": ("sbuf", [128, 8], u16),
+    "pi": ("sbuf", [128, 8], i32), "ei": ("sbuf", [128, 8], i32), "eu": ("sbuf", [128, 16], u16),
     "col": ("sbuf", [128, 64], f32), "cw": ("sbuf", [128, 128], f32),
-    "mz": ("sbuf", [128, 144], bf), "mz4": ("sbuf", [128, 144], f16), "my": ("sbuf", [128, 5 * 144], f16),
+    "mz": ("sbuf", [128, 144], bf), "mz4": ("sbuf", [128, 144], f16), "my": ("sbuf", [128, 8 * 144], f16),
     "mm": ("sbuf", [128, 12 * 128], f16), "mb16": ("sbuf", [128, 3 * 128], bf),
-    "ee": ("sbuf", [128, 3 * 1024], bf), "dg": ("sbuf", [128, 384], f32), "rs": ("sbuf", [128, 384], f32), "jf": ("sbuf", [128, 128], f16), "cst": ("sbuf", [128, 128], f16),
+    "ee": ("sbuf", [128, 3 * 1024], bf), "dg": ("sbuf", [128, 384], f32), "rs": ("sbuf", [128, 512], f32), "jf": ("sbuf", [128, 128], f16), "cst": ("sbuf", [128, 128], f16),
     "cv": ("sbuf", [128, 128], f32), "kt16": ("sbuf", [128, 192], bf), "tn": ("sbuf", [128, 6 * 128], f32), "c2": ("sbuf", [128, 6 * 128], f32),
     "g16": ("sbuf", [128, R], f16), "ti": ("sbuf", [128, 192], i32), "tau": ("sbuf", [128, 192], i32),
-    "cc": ("sbuf", [128, 192], f32), "ff": ("sbuf", [128, 192], f32), "t16": ("sbuf", [128, 192], f16), "ou": ("sbuf", [128, 192], u16),
-    "dd": ("sbuf", [128, 4 * R], f32), "xr": ("sbuf", [128, 4 * R], bf), "ab": ("sbuf", [128, 4 * R], bf),
-    "sks": ("sbuf", [128, 144], f32), "m2": ("sbuf", [128, 144], f32), "m1": ("sbuf", [128, 96], f32), "eq": ("sbuf", [128, 192], f32),
-    "zz": ("sbuf", [128, 192], f32), "a2": ("sbuf", [128, 96], f32), "ve": ("sbuf", [128, 96], f32), "lv": ("sbuf", [128, 96], u16),
+    "cc": ("sbuf", [128, 384], f32), "t16": ("sbuf", [128, 384], f16), "ou": ("sbuf", [128, 192], u16),
+    "dd": ("sbuf", [128, 4 * R], f32), "xr": ("sbuf", [128, 4 * R], bf),
+    "ab0": ("sbuf", [128, 8, 4, 16], bf), "ab1": ("sbuf", [128, 20, 4, 16], bf), "ab2": ("sbuf", [128, 20, 4, 16], bf),
+    "pm": ("sbuf", [128, 192], f32), "rk": ("sbuf", [128, 80], f32), "eq": ("sbuf", [128, 192], f32),
+    "ve": ("sbuf", [128, 384], f32), "lv": ("sbuf", [128, 96], u16), "l0": ("sbuf", [128, 48], f32), "l1": ("sbuf", [128, 144], f32),
     "xg": ("sbuf", [128, R], bf), "sh": ("sbuf", [128, R], f16),
     "wi": ("sbuf", [128, 16], i32), "xe": ("sbuf", [128, 3 * 128], f16), "fa": ("sbuf", [128, 3 * 1024], f32),
     "w8": ("sbuf", [128, 192], f32), "la": ("sbuf", [128, 32], u16),
@@ -71,6 +72,8 @@ def build(rank_peers):
         return [r[:3]]
 
     def nel(r):
+        if len(r) == 6:
+            return r[4]
         if r[0] == "*":
             return 16 * (r[4][2] - r[4][1])
         return (r[2] - r[1] + r[3] - 1) // r[3]
@@ -78,6 +81,8 @@ def build(rank_peers):
     def ap(T, r):
         if not isinstance(r, tuple):
             return r
+        if len(r) == 6:
+            return T[r[0]][r[5]]
         if r[0] == "*":
             return T[r[1]][:, r[2]:r[3]].indirect(ap(T, r[4]))
         if r[3] == 1:
@@ -174,16 +179,18 @@ def build(rank_peers):
         [ref("mi", 0, B)], [], 1 << 20)
     dma("S", (lambda T: [(T.qb[:], T.qr[:])], 1), [ref("qb", 0, R)], [], 196608)
     dma("S", (lambda T: [(T.xt[:, OFF:OFF + B], T.xn[:])], 1), [ref("xt", OFF, B)], [], 1 << 20)
-    dma("S", (lambda T: [(T.xs[:, 0:B], T.xn[:])], 1), [ref("xs", 0, B)], [], 1 << 20)
-    dma("Y", (lambda T: [(T.it[r::16, OFF:OFF + B], T.ip[:]) for r in range(16)], 16), [ref("it", OFF, B)], [], 2 << 20)
+    dma("Y", (lambda T: [(T.xs[:, 0:B], T.xn[:])], 1), [ref("xs", 0, B)], [], 1 << 19)
+    ops[-1]["after"] = [1]
+    dma("Y", (lambda T: [(T.it[r::16, OFF:OFF + B], T.ip[:]) for r in range(16)], 16), [ref("it", OFF, B)], [], 3 << 19)
+    ops[-1]["after"] = [1, len(ops) - 2]
     iota(ref("pi", 0, 1), [[0, 1]], 0, 1)
     iota(ref("ci", 0, 144), [[1, 144]], 0, 0)
     iota(ref("c4", 0, 144), [[1, 36], [0, 4]], 0, 0)
     iota(ref("j16", 0, 128), [[0, 8], [1, 16]], 0, 0)
     iota(ref("c16", 0, 128), [[1, 8], [0, 16]], 0, 0)
     iota(ref("ei", 0, 8), [[1, 8]], 0, 0)
-    for c0, n, _, _ in CHUNKS:
-        iota(ref("kt16", c0 // 4, n // 4), [[1, 4], [0, n // 16]], 0, 0)
+    iota(ref("kt16", 0, 80), [[0, 20], [1, 4]], 0, 0)
+    iota(ref("cc", 0, 384), [[0, 384]], 0, 0)
     p0 = ref("pi", 0, 1)
     ts(ref("pi", 1, 1), p0, 3, A.bitwise_and)
     ts(ref("pi", 2, 1), p0, 2, A.logical_shift_right, 3, A.bitwise_and)
@@ -202,6 +209,10 @@ def build(rank_peers):
     for k in range(4):
         ts(ref("my", 144 * k, 140), ref("ci", 0, 140), col(12), A.is_equal, col(8 + k), A.mult)
     ts(ref("my", 144 * 4, 140), ref("ci", 0, 140), col(12), A.is_equal, col(13), A.mult)
+    tt(ref("col", 40, 3), ref("col", 8, 3), ref("col", 9, 3), A.subtract)
+    for k in range(3):
+        ts(ref("my", 144 * (5 + k), 140), ref("ci", 0, 140), col(12), A.is_equal, col(40 + k), A.mult)
+    ts(ref("rk", 0, 80), ref("kt16", 0, 80), 0.0, A.is_equal, 1.0e6, A.mult)
     ts(ref("mz4", 0, 140), ref("c4", 0, 140), col(15), A.is_equal)
     ts(col(16), CG16, 15.0, A.add)
     ts(ref("mz", 0, 143), ref("ci", 0, 143), col(16), A.is_equal, 4.0, A.mult)
@@ -239,6 +250,7 @@ def build(rank_peers):
     ts(col(23), T2, 7.0, A.mult, col(22), A.add)
     ts(CST, ci, 0.0, A.mult, col(23), A.add)
     tc(ref("eu", 0, 8), ref("ei", 0, 8))
+    ts(ref("eu", 8, 8), ref("ei", 0, 8), 4.0, A.mult, 3.0, A.add)
     EU = ref("eu", 0, 8)
     cw = lambda i: ref("cw", 8 * i, 8)
     cv = lambda i: ref("cv", 8 * i, 8)
@@ -251,12 +263,13 @@ def build(rank_peers):
     tt(ref("rs", 256, 128), ref("b1", 256, 128), ref("b1", 384, 128), A.add)
     ts(cw(0), ref("ei", 0, 8), 16.0, A.mult, CS, A.add)
     aff(cw(1), cw(0), -4096.0, ENC + OFF)
-    aff(cw(2), cw(0), 1.0 / 256, 0.0)
+    aff(cw(2), cw(0), -1.0 / 256, 0.25)
+    aff(col(26), T2, 6.5, 0.0)
     aff(cv(0), cw(0), 1.0, -ENC - OFF)
     aff(cv(1), cw(0), 4096.0, 0.0)
     aff(col(24), COFF, 1.0 / ENC, 0.0)
     aff(col(25), COFF, -1.0, 0.0)
-    aff(ref("dg", 128, 128), DG, 7.5, -1.0)
+    aff(ref("dg", 128, 128), DG, 1048576.0, 0.0)
     if "P" in LOW:
         BOB = ref("mb16", 256, 128)
         ts(BOB, ref("c16", 0, 128), col(17), A.is_equal)
@@ -268,13 +281,11 @@ def build(rank_peers):
         scan(ref("b1", 0, 128), RS, ref("b2", 384, 128), 0.0, A.mult, A.add)
         aff(cv(10), ref("b1", 15, 8, 16), 1.0, 0.0)
     for t in range(RO):
-        if LOW[0] != "S":
+        if LOW[0] == "P":
             aff(cw(3 + t), cw(0), 1.0, 256.0 * t)
-        else:
+        elif LOW[0] == "S":
             aff(cv(3 + t), cw(0), 1.0, 256.0 * t - ENC - OFF)
-        if LOW[2] == "V":
-            aff(cw(6 + t), cw(0), 1.0, 256.0 * t + 128 + 262144.0)
-        else:
+        if LOW[2] == "P":
             aff(cv(6 + t), cw(0), 1.0, 256.0 * t + 128)
         aff(ref("c2", 256 * t, 128), ci, 1.0, 256.0 * t + 128 - OFF)
         aff(ref("c2", 256 * t + 128, 128), ci, 1.0 if LOW[2] == "P" else 257.0 / 256, 256.0 * t + 128)
@@ -285,13 +296,24 @@ def build(rank_peers):
     iota(ref("mt", 0, OFF), [[0, OFF]], 7, 0)
     iota(ref("it", 0, OFF), [[0, OFF]], 0, 0)
     iota(ref("xt", 0, OFF), [[0, OFF]], 0, 0)
-    iota(ref("snd", 0, 768), [[0, 768]], -1, 0)
+    iota(ref("snd", 0, 768), [[0, 768]], 4096, 0)
+    for t in range(RO):
+        iota(ref("rcv", 256 * t, 128), [[0, 128]], 4096, 0)
+        iota(ref("rcv", 256 * t + 192, 64), [[0, 64]], 4096, 0)
+        aff(ref("l1", 48 * t + 1, 8, 2), cw(0), 1.0, 256.0 * t)
+        aff(ref("l1", 48 * t + 17, 8, 2), cw(0), 1.0, 0.0)
+        aff(ref("l1", 48 * t + 33, 8, 2), cw(0), 1.0, 256.0 * t + 128 + 262144.0)
+    aff(ref("l0", 0, 48), ref("ci", 0, 48), 0.0, -1.0e9)
+    aff(ref("rs", 384, 128), RS, 1.0e10, -262144.0)
     for c0, n, _, _ in CHUNKS:
         tc(ref("stu", c0 // 16, n // 16), ref("sti", c0 // 16, n // 16))
-        ts(ref("qh", c0, n), ref("qb", c0, n), QO, A.add)
+        act(ref("qh", c0, n), ref("qb", c0, n), F.Identity, bias=QO)
     for i in range(4):
-        tc(ref("mt", OFF + 512 * i, 512), ref("mi", 512 * i, 512))
-    if S16:
+        if "i" in ONS:
+            act(ref("mt", OFF + 512 * i, 512), ref("mi", 512 * i, 512), F.Copy)
+        else:
+            tc(ref("mt", OFF + 512 * i, 512), ref("mi", 512 * i, 512))
+    if "i" not in ONS:
         dma("Y", (lambda T: [(T.mn[:, 0:B], T.mt[:, OFF:OFF + B])], 1), [ref("mn", 0, B)], [ref("mt", OFF, B)], 1 << 20)
     dma("Y", (lambda T: [(T.mn[r::4, SN * t:SN * t + B], T.mt[r::4, OFF:OFF + B]) for r in (0, 3) for t in (1, 2)], 4),
         [ref("mn", SN, B), ref("mn", 2 * SN, B)], [ref("mt", OFF, B)], 1 << 20)
@@ -301,20 +323,11 @@ def build(rank_peers):
         base = B + 384 * t
         m, r4 = n // 16, n // 4
         pb = "ps%d" % (0 if ci_ == 0 else 2 + ci_)
-        px = [["ps4", "ps6"], ["ps5", "ps6"]][ci_] if len(CHUNKS) == 2 else [["ps7", "ps7"], ["ps5", "ps5"], ["ps6", "ps6"], []][ci_]
+        px = ["ps7", "ps5", "ps6"][ci_]
         q = ref("qh", c0, n)
         o4 = c0 // 4
         c4_ = lambda nm, lo=0, cnt=r4: ref(nm, o4 + lo, cnt)
-        pD, pE, pP, pT, pS = [ref(pb, r4 * i, r4) for i in range(5)]
-        pt0, n2 = 3 * r4, n // 2
-        if n > 512:
-            pb, px, pt0 = "ps4", ["ps5", "ps6"], 0
-            pT, pS = ref(pb, 0, r4), ref(pb, r4, r4)
-        elif len(CHUNKS) == 2 and n == 128:
-            px = ["ps7", "ps7"]
-        px0 = 0
-        if len(CHUNKS) == 4 and ci_:
-            px, px0 = [pb, pb], 5 * r4
+        pD, pE, pP, pT, pS = ref(pb, 0, r4), ref(pb, r4, r4, 2), ref(pb, r4 + 1, r4, 2), ref(pb, 3 * r4, r4), ref(pb, 4 * r4, r4)
         pU = pS if ci_ else ref("ps2", 256, r4)
         pc, sp, ss = (PIECE, SPLV, SPLS) if ci_ else (99, 1, 1)
         XW = lambda off: ind("xt", OFF, OFF + base, off) if ci_ == 0 else ind("xs", SN * t, SN * t + base, off)
@@ -324,121 +337,86 @@ def build(rank_peers):
         ts(c4_("tau"), c4_("ti"), 3, A.bitwise_and)
         lst = ref("stu", c0 // 16, m)
         for rd in range(2):
-            if n > 512:
-                for h in range(2):
-                    l_ = ref(lst[0], lst[1] + h * m // 2, m // 2)
-                    if t == 0 and rd == 0:
-                        ts(ref("g16", c0 + h * n2, n2), ind("mi", 0, B, l_), COFF, A.subtract)
-                    else:
-                        act(ref("g16", c0 + h * n2, n2), MW(l_), F.Identity, bias=col(25))
-            elif t == 0 and (rd == 0 or not S16 or ci_ == 0):
+            if t == 0 and (rd == 0 or ci_ == 0):
                 ts(ref("g16", c0, n), ind("mi", 0, B, lst), COFF, A.subtract)
-            elif S16:
+            elif ci_ or rd == 0 or "g" in ONS:
                 act(ref("g16", c0, n), MW(lst), F.Identity, bias=col(25))
             else:
                 ts(ref("g16", c0, n), MW(lst), COFF, A.subtract)
             gs = lambda s: ref("g16", c0 + s, r4, 4)
             mm([(pD, [(Y(2, s), gs(s)) for s in range(4)])])
             mm([(pE, [(Y(4, s), gs(s)) for s in range(4)]), (pP, [(Y(0, s), gs(s)) for s in range(4)])], pc)
-            tt(c4_("cc"), pD, c4_("tau"), A.is_le)
-            tt(c4_("ff"), pE, c4_("cc"), A.mult)
-            tt(c4_("t16"), pP, c4_("ff"), A.add)
-            mm([(ref(pb, pt0 + k * m, m), [(Y(k, cl), ref("t16", o4 + cl, m, 4)) for cl in range(4)]) for k in range(4)], pc)
+            tt(ref("cc", 2 * o4 + 1, r4, 2), pD, c4_("tau"), A.is_le)
+            scan(ref("t16", 2 * o4, 2 * r4), ref("cc", 2 * o4, 2 * r4), ref(pb, r4, 2 * r4), 0.0, A.mult, A.add)
+            t16 = lambda cl: ref("t16", 2 * o4 + 2 * cl + 1, m, 8)
+            mm([(ref(pb, 3 * r4 + k * m, m), [(Y(k, cl), t16(cl)) for cl in range(4)]) for k in range(4)], pc)
             ts(c4_("ou"), pT, ENC, A.add)
-            nd = 0
+            mm([(ref(pb, 5 * r4 + k, m, 4), [(Y(5 + k if k < 3 else 3, cl), t16(cl)) for cl in range(4)]) for k in range(4)], pc)
+            qo_ = QO / 2 if ci_ == 0 and t > 0 and rd == 0 else QO
+            al = slice(None)
             order = [k for k in range(4) if routes[k] != "A"] + [k for k in range(4) if routes[k] == "A"]
             for k in order:
-                off = c4_("ou", k * m, m)
                 at = 4 * c0 + k * n
-                if n > 512:
-                    for h in range(2):
-                        a_, q_, o_ = at + h * n2, ref("qh", c0 + h * n2, n2), XW(c4_("ou", k * m + h * m // 2, m // 2))
-                        if routes[k] == "A" or (routes[k] == "H" and h):
-                            tt(ref("dd", a_, n2), o_, q_, A.subtract)
-                            act(ref("ab", a_, n2), ref("dd", a_, n2), F.Abs, bias=QO)
-                        else:
-                            act(ref("xr", a_, n2), o_, F.Copy)
-                            pd = ref(px[nd % 2], 0, n2); nd += 1
-                            mm([(pd, [(INEG, q_), (IB, ref("xr", a_, n2))])])
-                            act(ref("ab", a_, n2), pd, F.Abs, bias=QO)
-                elif routes[k] == "A":
+                ab = ("ab%d" % ci_, k, k + 1, 1, n, (al, al, k, al))
+                if routes[k] == "A":
                     for h in range(sp):
                         tt(ref("dd", at + h * n // sp, n // sp), XW(c4_("ou", k * m + h * m // sp, m // sp)), ref("qh", c0 + h * n // sp, n // sp),
                            A.subtract)
-                    if n > 128 or "D" in routes or k >= 2:
-                        act(ref("ab", at, n), ref("dd", at, n), F.Abs, bias=QO)
-                    elif k % 2:
-                        act(ref("ab", at - n, 2 * n), ref("dd", at - n, 2 * n), F.Abs, bias=QO)
+                    act(ab, ref("dd", at, n), F.Abs, bias=qo_)
                 else:
                     for h in range(ss):
                         act(ref("xr", at + h * n // ss, n // ss), XW(c4_("ou", k * m + h * m // ss, m // ss)), F.Copy)
-                    pd = ref(px[nd % 2], px0, n); nd += 1
+                    pd = ref(px, 0, n)
                     mm([(pd, [(INEG, q), (IB, ref("xr", at, n))])])
-                    act(ref("ab", at, n), pd, F.Abs, bias=QO)
-            mm([(pS, [(IB, c4_("kt16"))] + [(ref("mz", 15 - s, 128), ref("ab", 4 * c0 + s, r4, 16)) for s in range(16)])], pc)
-            o3, o2 = 3 * c0 // 16, 2 * c0 // 16
-            sk = lambda lo, cnt: ref(pb, pt0 + r4 + lo, cnt)
-            if n == 128:
-                tc(ref("sks", o3, 2 * m), sk(2 * m, 2 * m)); tc(ref("sks", o3 + 2 * m, m), sk(0, m))
-            else:
-                act(ref("sks", o3, 2 * m), sk(2 * m, 2 * m), F.Copy); act(ref("sks", o3 + 2 * m, m), sk(0, m), F.Copy)
-            tt(ref("m2", o3, 3 * m), sk(0, 3 * m), ref("sks", o3, 3 * m), A.min)
-            tt(ref("m1", o2, 2 * m), ref("m2", o3, 2 * m), ref("m2", o3 + m, 2 * m), A.min)
-            tt(c4_("eq", 0, 2 * m), sk(0, 2 * m), ref("m1", o2, 2 * m), A.is_equal)
-            tt(c4_("eq", 2 * m, 2 * m), sk(2 * m, 2 * m), ref("m1", o2, 2 * m), A.is_equal)
-            tt(c4_("zz"), pT, c4_("eq"), A.mult)
-            tt(ref("a2", o2, 2 * m), c4_("zz", 0, 2 * m), c4_("zz", 2 * m, 2 * m), A.add)
-            ve = ref("ve", 48 * rd + c0 // 16, m)
-            tt(ve, ref("a2", o2, m), ref("a2", o2 + m, m), A.add)
+                    act(ab, pd, F.Abs, bias=qo_)
+            mm([(pS, [(IB, ref("kt16", 0, r4))] + [(ref("mz", 15 - s, 128), ("ab%d" % ci_, 0, 4, 1, r4, (al, al, al, s))) for s in range(16)])], pc)
+            scan(c4_("pm"), ref("rk", 0, r4), pS, 0.0, A.add, A.min)
+            tt(c4_("eq"), pS, c4_("pm"), A.not_equal)
+            scan(ref("ve", 192 * rd + o4, r4), c4_("eq"), ref(pb, 5 * r4, r4), 0.0, A.mult, A.add)
+            ve = ref("ve", 192 * rd + o4 + 3, m, 4)
             lst = ref("lv", 48 * rd + c0 // 16, m)
             ts(lst, ve, ENC, A.add)
-            if n > 512:
-                for h in range(2):
-                    c_, l_ = c0 + h * n2, XW(ref("lv", 48 * rd + c0 // 16 + h * m // 2, m // 2))
-                    if qroute == "V" or (qroute == "H" and h):
-                        tt(ref("sh", c_, n2), l_, ref("qh", c_, n2), A.add)
-                        ts(ref("qh", c_, n2), ref("sh", c_, n2), 0.5, A.mult, QO / 2 - 0.25, A.add)
-                    else:
-                        act(ref("xg", c_, n2), l_, F.Copy)
-                        mm([(ref(px[h], 0, n2), [(IH, ref("qh", c_, n2)), (IBH, ref("xg", c_, n2))])])
-                        act(ref("qh", c_, n2), ref(px[h], 0, n2), F.Identity, bias=QO / 2 - 0.25)
+            hb = QO - qo_ / 2 - 0.25
+            if qroute == "M":
+                tt(ref("sh", c0, n), XW(lst), q, A.add)
+                act(q, ref("sh", c0, n), F.Identity, scale=0.5, bias=hb)
             elif qroute == "V":
                 tt(ref("sh", c0, n), XW(lst), q, A.add)
-                ts(q, ref("sh", c0, n), 0.5, A.mult, QO / 2 - 0.25, A.add)
+                ts(q, ref("sh", c0, n), 0.5, A.mult, hb, A.add)
             else:
                 act(ref("xg", c0, n), XW(lst), F.Copy)
-                pq = ref(px[0], px0, n)
+                pq = ref(px, 0, n)
                 mm([(pq, [(IH, q), (IBH, ref("xg", c0, n))])])
-                if S16:
-                    act(q, pq, F.Identity, bias=QO / 2 - 0.25)
+                if qroute == "S":
+                    act(q, pq, F.Identity, bias=hb)
                 else:
-                    ts(q, pq, QO / 2 - 0.25, A.add)
+                    ts(q, pq, hb, A.add)
             if ci_ == 0 and rd == 0:
-                lowest_of(t, 0, ref("ve", 0, 8), 3 + t)
+                lowest_of(t, 0, ve, 3 + t)
                 step_a(t, 0, LA(0))
         c1 = max(c0, L)
         if t == RO - 1 and c1 < c0 + n:
-            ts(ref("qo", c1, c0 + n - c1), ref("qh", c1, c0 + n - c1), -QO, A.add)
+            act(ref("qo", c1, c0 + n - c1), ref("qh", c1, c0 + n - c1), F.Identity, bias=-QO)
             dma("Y", (lambda T: [(T.yq[:, c1:c0 + n], T.qo[:, c1:c0 + n])], 1), [], [ref("qo", c1, c0 + n - c1)], 256 * n)
 
     w8 = lambda i: ref("w8", 8 * i, 8)
     LA = lambda i: ref("la", 8 * i, 8)
 
-    def lowest(i, key, bias, um, dum, sub, thr):
+    def lowest(t, i, key, bias, um, dum, sub, thr):
         for c in range(8):
             a = ref("fa", 1024 * i + 128 * c, 16 * c + 16)
-            o = ref("w8", 8 * (6 * i + 2) + c, 1)
-            act(a, ref(key[0], key[1], 16 * c + 16), F.Abs, bias=ref(bias[0], bias[1] + c, 1), scale=-1048576.0)
+            act(a, ref(key[0], key[1], 16 * c + 16), F.Abs, bias=ref(bias[0], bias[1] + c * bias[3], 1), scale=-1048576.0)
             if LOW[i] == "V":
-                rmin(o, a)
+                rmin(ref("l0", 16 * i + 2 * c + 1, 1), a)
             else:
-                act(a, a, F.Relu, bias=thr(c), scale=-1.0, accum=o)
+                act(a, a, F.Relu, bias=thr(c), scale=-1.0, accum=ref("w8", 8 * (6 * i + 2) + c, 1))
         if LOW[i] == "V":
-            tt(w8(6 * i + 3), w8(6 * i + 2), um, A.add)
+            scan(ref("w8", 8 * (6 * i + 3), 16), ref("l0", 16 * i, 16), ref("l1", 48 * t + 16 * i, 16), 0.0, A.add, A.max)
+            ts(LA(i), ref("w8", 8 * (6 * i + 3) + 1, 8, 2), sub, A.add)
         else:
             tt(w8(6 * i + 3), um, w8(6 * i + 2), A.subtract)
-        tt(w8(6 * i + 4), w8(6 * i + 3), dum, A.max)
-        ts(LA(i), w8(6 * i + 4), sub, A.add)
+            tt(w8(6 * i + 4), w8(6 * i + 3), dum, A.max)
+            ts(LA(i), w8(6 * i + 4), sub, A.add)
 
     def lowest_p(i, key, zc, um, dum, sub):
         for c in range(8):
@@ -461,20 +439,20 @@ def build(rank_peers):
 
     def lowest_of(t, i, ve, dum):
         xe = ref("xe", 128 * i, 128)
-        tt(xe, ind("ve", ve[1], ve[2], EU), DG, A.mult)
+        tt(xe, ind("ve", ve[1] - 3, ve[2], ref("eu", 8, 8)), DG, A.mult)
         key = ref("ps2", 128 * i, 128)
         if LOW[i] == "P":
             mm([(key, [(BO, xe)])])
             act(w8(6 * i + 1), ve, F.Identity, bias=ENC + OFF)
-            lowest_p(i, key, lambda c: ref(ve[0], ve[1] + c, 1), w8(6 * i + 1), cw(dum), None)
+            lowest_p(i, key, lambda c: ref(ve[0], ve[1] + 4 * c, 1), w8(6 * i + 1), cw(dum), None)
             return
         mm([(key, [(I16, JF), (BO, xe)])])
         act(w8(6 * i), ve, F.Copy, scale=1048576.0)
         if LOW[i] == "V":
-            tt(w8(6 * i + 1), ve, cw(1), A.add)
-            lowest(i, key, w8(6 * i), w8(6 * i + 1), cw(dum), 0.0, None)
+            tt(ref("l1", 48 * t + 16 * i, 8, 2), ve, cw(1), A.add)
+            lowest(t, i, key, w8(6 * i), None, None, 0.0, None)
         else:
-            lowest(i, key, w8(6 * i), ve, ref("cv", 8 * dum, 8), ENC + OFF, lambda c: ref("cv", 8 + c, 1))
+            lowest(t, i, key, w8(6 * i), ve, ref("cv", 8 * dum, 8), ENC + OFF, lambda c: ref("cv", 8 + c, 1))
 
     pL, pA, pB_, pC = [ref("ps1", 128 * i, 128) for i in range(4)]
 
@@ -496,10 +474,10 @@ def build(rank_peers):
         MW = ind("mt", 0, OFF + base, la)
         cc_ = OFF + base + 128 * (z + 1)
         if z == 1:
-            tt(ref("km", 128, 128), MW, ref("km", 0, 128), A.mult)
+            tt(ref("km", 128, 128), MW, ref("km", 0, 128), A.is_lt)
             mm([(PK, [(BO, ref("km", 128, 128))])])
-            ts(h("md"), PK, 7.0, A.not_equal)
             send(t)
+            act(h("md"), PK, F.Copy)
             step_a(t, z, la)
         tt(h("gk"), PKM, h("gs"), A.mult)
         if z == 0:
@@ -522,14 +500,14 @@ def build(rank_peers):
 
     def send(t):
         b2 = lambda i: ref("b2", 128 * i, 128)
-        tt(b2(1), PK, ref("dg", 128, 128), A.is_lt)
-        scan(PC, ref("md", 128, 128), ref("rs", 128, 128), -1.0, A.add, A.add)
+        scan(PC, PK, ref("rs", 128, 128), -1.0, A.add, A.add)
+        tt(b2(1), PK, DG, A.mult)
         tt(b2(2), PC, b2(1), A.mult)
         scan(b2(3), ref("rs", 256, 128), b2(2), 128.0, A.min, A.add)
         tc(LA(3), ref("b2", 384 + 15, 8, 16))
-        tc(ind("snd", 256 * t, 256 * t + 256, LA(3)), ref("xt", OFF + B + 384 * t, 128))
+        tc(ind("snd", 256 * t, 256 * t + 256, LA(3)), ref("q1", 0, 128))
         rid, pid, mask = rank_peers[t]
-        so, ro = ref("snd", 256 * t + 128, 64), ref("rcv", 64 * t, 64)
+        so, ro = ref("snd", 256 * t + 128, 64), ref("rcv", 256 * t + 128, 64)
         add("G", lambda g, T: g.remote_dma(ap(T, ro), ap(T, so), T.sem["arr%d" % t], T.sem["snt%d" % t], pid, rid, mask),
             [], [so], 200.0, lat=2000.0, sem="snt%d" % t, inc=NENG)
         sent.append(len(ops) - 1)
@@ -538,10 +516,10 @@ def build(rank_peers):
     def writers(t):
         base = B + 384 * t
         q = ref("qh", 0, 128)
-        ve, lv = ref("ve", 48, 8), ref("lv", 48, 8)
+        ve, lv = ref("ve", 192 + 3, 8, 4), ref("lv", 48, 8)
         nn = OFF + base
         lowest_of(t, 1, ve, 0)
-        tc(ref("wi", 0, 8), ref("m1", 0, 8))
+        tc(ref("wi", 0, 8), ref("pm", 3, 8, 4))
         ts(ref("wi", 8, 8), ref("wi", 0, 8), 3, A.bitwise_and)
         xk = ref("xe", 256, 128)
         tt(xk, ind("wi", 8, 16, EU), DG, A.mult)
@@ -554,7 +532,8 @@ def build(rank_peers):
             act(ref("xt", nn, 128), q, F.Identity, bias=-QO)
         else:
             ts(ref("xt", nn, 128), q, -QO, A.add)
-        if CHUNKS[0][3] == "V":
+        act(ref("q1", 0, 128), q, F.Identity, scale=-1.0, bias=QO)
+        if CHUNKS[0][3] in "VM":
             tt(ref("s32", 0, 128), ind("xt", OFF, OFF + base, lv), q, A.add)
             ts(ref("mxi", 0, 128), ref("s32", 0, 128), 0.5, A.mult, -QO / 2 - 0.25, A.add)
         else:
@@ -571,27 +550,24 @@ def build(rank_peers):
         ts(ref("ui", 0, 128), ib, 2, A.logical_shift_right)
         ts(ref("ui", 128, 128), ib if t == RO - 1 else ref("it", nn + 128, 128), 3, A.bitwise_and)
         ts(PKM, ref("ui", 128, 128), CA, A.is_equal)
-        ts(ref("km", 0, 128), ref("ui", 128, 128), CA, A.is_equal, T2, A.mult)
+        ts(ref("km", 0, 128), ref("ui", 128, 128), CA, A.is_equal, col(26), A.mult)
         ts(PB, PK, 7.0, A.not_equal)
         tt(b1(0), PB, ref("c2", 256 * t, 128), A.mult)
         tt(b1(1), ref("c2", 256 * t + 128, 128), b1(0), A.subtract)
         tt(PB, PB, ref("ui", 0, 128), A.mult)
         tt(PB, PB, b1(1), A.add)
-        tt(b1(3), PB, DG, A.mult)
-        scan(b1(4), RS, b1(3), 0.0, A.mult, A.add)
         kw = ref("b1", 512 + 15, 8, 16)
         if LOW[2] == "P":
+            tt(b1(3), PB, DG, A.mult)
+            scan(b1(4), RS, b1(3), 0.0, A.mult, A.add)
             lowest_p(2, PB, lambda c: ref("b1", 512 + 15 + 16 * c, 1), kw, ref("cv", 8 * (6 + t), 8), None)
         else:
-            act(w8(12), kw, F.Identity, scale=1048576.0, bias=-262144.0)
-            tt(w8(13), kw, cw(2), A.subtract)
-        if LOW[2] == "V":
-            lowest(2, PB, w8(12), w8(13), cw(6 + t), -262144.0, None)
-        elif LOW[2] == "S":
-            lowest(2, PB, w8(12), w8(13), ref("cv", 8 * (6 + t), 8), 0.0, lambda c: 262144.0)
+            tt(b1(3), PB, ref("dg", 128, 128), A.mult)
+            scan(b1(4), ref("rs", 384, 128), b1(3), 0.0, A.min, A.add)
+            ts(w8(12), kw, 1.0 / 1048576, A.mult)
+            tt(ref("l1", 48 * t + 32, 8, 2), w8(12), cw(2), A.add)
+            lowest(t, 2, PB, kw, None, None, -262144.0, None)
         step(t, 1, LA(2))
-        SW = ind("snd", 256 * t, 256 * t + 256, LA(3))
-        so, ro = ref("snd", 256 * t + 128, 64), ref("rcv", 64 * t, 64)
         if t < RO - 1:
             news = [sn + base] + ([sn + SN + base] if t == 0 else [])
             dma("Y", (lambda T: [(T.mn[r::4, sn:sn + base], T.mt[r::4, OFF:nn]) for r in (1, 2)]
@@ -600,13 +576,11 @@ def build(rank_peers):
                 [ref("mn", sn, base), ref("xs", sn + base, 384)] + [ref("mn", x, 384) for x in news],
                 [ref("mt", OFF, base + 384), ref("xt", nn, 384)], 256 * base + 300000)
             ops[-1]["after"] = [sent[t]]
-        ts(ref("rr", 0, 64), ro, -0.5, A.is_lt)
-        tt(ref("rr", 64, 64), ref("rr", 0, 64), so, A.mult)
-        tt(so, ref("rr", 64, 64), ro, A.max)
+        tt(ref("sh", 0, 128), ind("rcv", 256 * t, 256 * t + 256, LA(3)), q if t < RO - 1 else ref("xt", nn, 128), A.min)
         if t < RO - 1:
-            ts(q, SW, QO, A.add)
+            act(q, ref("sh", 0, 128), F.Abs, bias=-QO / 2)
         else:
-            act(ref("qo", 0, 128), SW, F.Copy)
+            act(ref("qo", 0, 128), ref("sh", 0, 128), F.Abs)
             dma("S", (lambda T: [(T.yq[:, 0:128], T.qo[:, 0:128])], 1), [], [ref("qo", 0, 128)], 32768)
 
     for t in range(RO):
@@ -626,6 +600,7 @@ def depends(ops):
     hist = {}
     for i, o in enumerate(ops):
         dep = set(o.get("after", ()))
+        raw = set()
         for acc, regs in ((0, o["rd"]), (1, o["wr"])):
             for nm, lo, hi in regs:
                 ps = SCRATCH[nm][0] == "psum"
@@ -634,6 +609,10 @@ def depends(ops):
                         continue
                     if (l2 < hi and lo < h2 and (w or acc)) or (ps and ops[j]["e"] != o["e"]):
                         dep.add(j)
+                        if w and not (acc and INORDER > 1):
+                            raw.add(j)
+        if INORDER and o["e"] in "VSP" and not o["sem"]:
+            o["free"] = list(o.get("free", ())) + [j for j in dep if j not in raw and ops[j]["e"] == o["e"] and not ops[j]["sem"]]
         for acc, regs in ((0, o["rd"]), (1, o["wr"])):
             for nm, lo, hi in regs:
                 h = hist.setdefault(nm, [])

@@ -7,15 +7,15 @@ ENC = 1600.0
 QO = 1280.0
 
 SN = 2816
-CHUNKS = [(0, 128, "AAAD", "V"), (128, 320, "AADD", "T"), (448, 320, "AAAD", "T")]
-LOW = "PVV"
-ONS = ""
-SEED, JIT, LOOK, PASSES = 3, 200.0, 0.4, 5
+CHUNKS = [(0, 128, "AAAD", "S"), (128, 320, "AADD", "S"), (448, 320, "AADD", "T")]
+LOW = "VVV"
+ONS = "ex"
+SEED, JIT, LOOK, PASSES = 3, 200.0, 0.4, 6
 PIECE, SPLV, SPLS, INORDER = 4, 1, 1, 0
 S16 = True
 NENG = 16
-CY, PEC, GAM, SCA = 0.9, 0.45, 1.55, 3.8
-HOP, SELF, SFIX = 200.0, 170.0, 90.0
+CY, PEC, GAM, SCA = 0.92, 0.45, 1.55, 3.8
+HOP, SELF, SFIX = 185.0, 220.0, 45.0
 
 f32, bf, f16, i32, u16 = "float32", "bfloat16", "float16", "int32", "uint16"
 SCRATCH = {
@@ -23,15 +23,15 @@ SCRATCH = {
     "xs": ("sbuf", [128, 3 * SN], bf), "mn": ("sbuf", [128, 3 * SN], f32),
     "mi": ("sbuf", [128, B], i32), "sti": ("sbuf", [128, 48], i32), "stu": ("sbuf", [128, 48], u16),
     "qb": ("sbuf", [128, R], bf), "qh": ("sbuf", [128, R], f16), "qo": ("sbuf", [128, R], bf),
-    "snd": ("sbuf", [128, 3 * 256], bf), "rcv": ("sbuf", [128, 3 * 256], bf),
+    "snd": ("sbuf", [128, 2 * 256], f32), "rcv": ("sbuf", [128, 2 * 256], f32), "snl": ("sbuf", [128, 256], bf), "rcl": ("sbuf", [128, 256], bf),
     "ci": ("sbuf", [128, 144], bf), "c4": ("sbuf", [128, 144], bf), "c16": ("sbuf", [128, 128], bf), "j16": ("sbuf", [128, 128], bf),
     "pi": ("sbuf", [128, 8], i32), "ei": ("sbuf", [128, 8], i32), "eu": ("sbuf", [128, 16], u16),
     "col": ("sbuf", [128, 64], f32), "cw": ("sbuf", [128, 128], f32),
-    "mz": ("sbuf", [128, 144], bf), "mz4": ("sbuf", [128, 144], f16), "my": ("sbuf", [128, 8 * 144], f16),
+    "mz": ("sbuf", [128, 144], bf), "mz4": ("sbuf", [128, 144], f16), "my": ("sbuf", [128, 9 * 144], f16),
     "mm": ("sbuf", [128, 12 * 128], f16), "mb16": ("sbuf", [128, 3 * 128], bf),
     "ee": ("sbuf", [128, 3 * 1024], bf), "dg": ("sbuf", [128, 384], f32), "rs": ("sbuf", [128, 512], f32), "jf": ("sbuf", [128, 128], f16), "cst": ("sbuf", [128, 128], f16),
     "cv": ("sbuf", [128, 128], f32), "kt16": ("sbuf", [128, 192], bf), "tn": ("sbuf", [128, 6 * 128], f32), "c2": ("sbuf", [128, 6 * 128], f32),
-    "g16": ("sbuf", [128, R], f16), "ti": ("sbuf", [128, 192], i32), "tau": ("sbuf", [128, 192], i32),
+    "g16": ("sbuf", [128, R], f16), "ti": ("sbuf", [128, 192], i32), "tau": ("sbuf", [128, 192], f32),
     "cc": ("sbuf", [128, 384], f32), "t16": ("sbuf", [128, 384], f16), "ou": ("sbuf", [128, 192], u16),
     "dd": ("sbuf", [128, 4 * R], f32), "xr": ("sbuf", [128, 4 * R], bf),
     "ab0": ("sbuf", [128, 8, 4, 16], bf), "ab1": ("sbuf", [128, 20, 4, 16], bf), "ab2": ("sbuf", [128, 20, 4, 16], bf),
@@ -44,8 +44,8 @@ SCRATCH = {
     "km": ("sbuf", [128, 256], f16), "kq": ("sbuf", [128, 256], f16), "gk": ("sbuf", [128, 256], f16), "gs": ("sbuf", [128, 256], f16),
     "g32": ("sbuf", [128, 256], f32), "e7": ("sbuf", [128, 256], f32), "ua": ("sbuf", [128, 256], f32), "ub": ("sbuf", [128, 256], f32),
     "yy": ("sbuf", [128, 256], f32), "md": ("sbuf", [128, 256], f32), "ui": ("sbuf", [128, 256], i32),
-    "b1": ("sbuf", [128, 5 * 128], f32), "b2": ("sbuf", [128, 4 * 128], f32), "q1": ("sbuf", [128, 128], bf),
-    "rr": ("sbuf", [128, 128], bf),
+    "b1": ("sbuf", [128, 5 * 128], f32), "b2": ("sbuf", [128, 4 * 128], f32), "q1": ("sbuf", [128, 128], f32),
+    "rr": ("sbuf", [128, 128], f32),
 }
 for _b in range(8):
     SCRATCH["ps%d" % _b] = ("psum", [128, 512], f32)
@@ -174,11 +174,10 @@ def build(rank_peers):
         add(q, fn, out, ins, 60.0 * n, lat=1800 + nbytes / 180.0, sem=sem, inc=16 * n)
 
     col = lambda c: ref("col", c, 1)
-    dma("Y", (lambda T: [(T.sti[:], T.st[:])], 1), [ref("sti", 0, 48)], [], 24576)
-    dma("Y", (lambda T: [(T.mi[0::4, :], T.pf[:]), (T.mi[1::4, :], T.mb[:]), (T.mi[2::4, :], T.bd[:]), (T.mi[3::4, :], T.bd[:])], 4),
-        [ref("mi", 0, B)], [], 1 << 20)
-    dma("S", (lambda T: [(T.qb[:], T.qr[:])], 1), [ref("qb", 0, R)], [], 196608)
-    dma("S", (lambda T: [(T.xt[:, OFF:OFF + B], T.xn[:])], 1), [ref("xt", OFF, B)], [], 1 << 20)
+    dma("S", (lambda T: [(T.mi[2::4, :], T.bd[:]), (T.mi[3::4, :], T.bd[:])], 2), [ref("mi", 0, B // 2)], [], 1 << 20)
+    dma("Y", (lambda T: [(T.mi[0::4, :], T.pf[:]), (T.mi[1::4, :], T.mb[:])], 2), [ref("mi", B // 2, B // 2)], [], 1 << 20)
+    dma("Y", (lambda T: [(T.sti[:], T.st[:]), (T.qb[:], T.qr[:])], 2), [ref("sti", 0, 48), ref("qb", 0, R)], [], 400000)
+    dma("S", (lambda T: [(T.xt[:, OFF:OFF + B], T.xn[:])], 1), [ref("xt", OFF, B)], [], 1100000)
     dma("Y", (lambda T: [(T.xs[:, 0:B], T.xn[:])], 1), [ref("xs", 0, B)], [], 1 << 19)
     ops[-1]["after"] = [1]
     dma("Y", (lambda T: [(T.it[r::16, OFF:OFF + B], T.ip[:]) for r in range(16)], 16), [ref("it", OFF, B)], [], 3 << 19)
@@ -213,7 +212,8 @@ def build(rank_peers):
     for k in range(3):
         ts(ref("my", 144 * (5 + k), 140), ref("ci", 0, 140), col(12), A.is_equal, col(40 + k), A.mult)
     ts(ref("rk", 0, 80), ref("kt16", 0, 80), 0.0, A.is_equal, 1.0e6, A.mult)
-    ts(ref("mz4", 0, 140), ref("c4", 0, 140), col(15), A.is_equal)
+    ts(ref("my", 144 * 8, 140), ref("my", 144 * 2, 140), -0.25, A.mult)
+    ts(ref("mz4", 0, 140), ref("c4", 0, 140), col(15), A.is_equal, 0.25, A.mult)
     ts(col(16), CG16, 15.0, A.add)
     ts(ref("mz", 0, 143), ref("ci", 0, 143), col(16), A.is_equal, 4.0, A.mult)
     Y = lambda k, sh: ref("my", 144 * k + 12 - 4 * sh, 128)
@@ -296,10 +296,11 @@ def build(rank_peers):
     iota(ref("mt", 0, OFF), [[0, OFF]], 7, 0)
     iota(ref("it", 0, OFF), [[0, OFF]], 0, 0)
     iota(ref("xt", 0, OFF), [[0, OFF]], 0, 0)
-    iota(ref("snd", 0, 768), [[0, 768]], 4096, 0)
+    box = [("snd", "rcv", 0), ("snd", "rcv", 256), ("snl", "rcl", 0)]
     for t in range(RO):
-        iota(ref("rcv", 256 * t, 128), [[0, 128]], 4096, 0)
-        iota(ref("rcv", 256 * t + 192, 64), [[0, 64]], 4096, 0)
+        iota(ref(box[t][0], box[t][2], 256), [[0, 256]], 4096, 0)
+        iota(ref(box[t][1], box[t][2], 128), [[0, 128]], 4096, 0)
+        iota(ref(box[t][1], box[t][2] + 192, 64), [[0, 64]], 4096, 0)
         aff(ref("l1", 48 * t + 1, 8, 2), cw(0), 1.0, 256.0 * t)
         aff(ref("l1", 48 * t + 17, 8, 2), cw(0), 1.0, 0.0)
         aff(ref("l1", 48 * t + 33, 8, 2), cw(0), 1.0, 256.0 * t + 128 + 262144.0)
@@ -308,12 +309,10 @@ def build(rank_peers):
     for c0, n, _, _ in CHUNKS:
         tc(ref("stu", c0 // 16, n // 16), ref("sti", c0 // 16, n // 16))
         act(ref("qh", c0, n), ref("qb", c0, n), F.Identity, bias=QO)
-    for i in range(4):
-        if "i" in ONS:
-            act(ref("mt", OFF + 512 * i, 512), ref("mi", 512 * i, 512), F.Copy)
-        else:
-            tc(ref("mt", OFF + 512 * i, 512), ref("mi", 512 * i, 512))
-    if "i" not in ONS:
+    for i in range(8):
+        tc(ref("mt", OFF + 256 * i, 256), ref("mi", 256 * i, 256))
+        ops[-1]["after"] = [0, 1]
+    if "n" not in ONS:
         dma("Y", (lambda T: [(T.mn[:, 0:B], T.mt[:, OFF:OFF + B])], 1), [ref("mn", 0, B)], [ref("mt", OFF, B)], 1 << 20)
     dma("Y", (lambda T: [(T.mn[r::4, SN * t:SN * t + B], T.mt[r::4, OFF:OFF + B]) for r in (0, 3) for t in (1, 2)], 4),
         [ref("mn", SN, B), ref("mn", 2 * SN, B)], [ref("mt", OFF, B)], 1 << 20)
@@ -332,27 +331,36 @@ def build(rank_peers):
         pc, sp, ss = (PIECE, SPLV, SPLS) if ci_ else (99, 1, 1)
         XW = lambda off: ind("xt", OFF, OFF + base, off) if ci_ == 0 else ind("xs", SN * t, SN * t + base, off)
         MW = lambda off: ind("mt", OFF, OFF + base, off) if ci_ == 0 else ind("mn", SN * t, SN * t + base, off)
-        mm([(pU, [(ref("mz4", 12 - 4 * s, 128), ref("qh", c0 + s, r4, 4)) for s in range(4)])])
-        tc(c4_("ti"), pU)
-        ts(c4_("tau"), c4_("ti"), 3, A.bitwise_and)
+        qs = "sh" if ci_ == 0 and t > 0 else "qh"
+        sums = [(ref("mz4", 12 - 4 * s, 128), ref(qs, c0 + s, r4, 4)) for s in range(4)]
+        mm([(pU, sums)])
+        ts(c4_("ti"), pU, -0.375, A.add)
+        tt(c4_("tau"), c4_("ti"), pU, A.subtract)
         lst = ref("stu", c0 // 16, m)
         for rd in range(2):
-            if t == 0 and (rd == 0 or ci_ == 0):
+            if t == 0 and (rd == 0 or ci_ == 0 or "n" in ONS):
                 ts(ref("g16", c0, n), ind("mi", 0, B, lst), COFF, A.subtract)
             elif ci_ or rd == 0 or "g" in ONS:
                 act(ref("g16", c0, n), MW(lst), F.Identity, bias=col(25))
             else:
                 ts(ref("g16", c0, n), MW(lst), COFF, A.subtract)
             gs = lambda s: ref("g16", c0 + s, r4, 4)
-            mm([(pD, [(Y(2, s), gs(s)) for s in range(4)])])
-            mm([(pE, [(Y(4, s), gs(s)) for s in range(4)]), (pP, [(Y(0, s), gs(s)) for s in range(4)])], pc)
-            tt(ref("cc", 2 * o4 + 1, r4, 2), pD, c4_("tau"), A.is_le)
+            if rd == 0 and ci_ == 0:
+                mm([(pE, [(Y(4, s), gs(s)) for s in range(4)]), (pP, [(Y(0, s), gs(s)) for s in range(4)])], pc)
+                mm([(pD, [(Y(8, s), gs(s)) for s in range(4)] + sums)], 4)
+                ops[-2]["after"] = [len(ops) - 3]
+                ops[-2]["free"] = [len(ops) - 3]
+                tt(ref("cc", 2 * o4 + 1, r4, 2), pD, c4_("ti"), A.is_ge)
+            else:
+                mm([(pD, [(Y(8, s), gs(s)) for s in range(4)])])
+                mm([(pE, [(Y(4, s), gs(s)) for s in range(4)]), (pP, [(Y(0, s), gs(s)) for s in range(4)])], pc)
+                tt(ref("cc", 2 * o4 + 1, r4, 2), pD, c4_("tau"), A.is_ge)
             scan(ref("t16", 2 * o4, 2 * r4), ref("cc", 2 * o4, 2 * r4), ref(pb, r4, 2 * r4), 0.0, A.mult, A.add)
             t16 = lambda cl: ref("t16", 2 * o4 + 2 * cl + 1, m, 8)
             mm([(ref(pb, 3 * r4 + k * m, m), [(Y(k, cl), t16(cl)) for cl in range(4)]) for k in range(4)], pc)
             ts(c4_("ou"), pT, ENC, A.add)
             mm([(ref(pb, 5 * r4 + k, m, 4), [(Y(5 + k if k < 3 else 3, cl), t16(cl)) for cl in range(4)]) for k in range(4)], pc)
-            qo_ = QO / 2 if ci_ == 0 and t > 0 and rd == 0 else QO
+            qo_ = QO
             al = slice(None)
             order = [k for k in range(4) if routes[k] != "A"] + [k for k in range(4) if routes[k] == "A"]
             for k in order:
@@ -505,9 +513,10 @@ def build(rank_peers):
         tt(b2(2), PC, b2(1), A.mult)
         scan(b2(3), ref("rs", 256, 128), b2(2), 128.0, A.min, A.add)
         tc(LA(3), ref("b2", 384 + 15, 8, 16))
-        tc(ind("snd", 256 * t, 256 * t + 256, LA(3)), ref("q1", 0, 128))
+        sn_, rc_, lo = box[t]
+        tc(ind(sn_, lo, lo + 256, LA(3)), ref("q1", 0, 128))
         rid, pid, mask = rank_peers[t]
-        so, ro = ref("snd", 256 * t + 128, 64), ref("rcv", 256 * t + 128, 64)
+        so, ro = ref(sn_, lo + 128, 64), ref(rc_, lo + 128, 64)
         add("G", lambda g, T: g.remote_dma(ap(T, ro), ap(T, so), T.sem["arr%d" % t], T.sem["snt%d" % t], pid, rid, mask),
             [], [so], 200.0, lat=2000.0, sem="snt%d" % t, inc=NENG)
         sent.append(len(ops) - 1)
@@ -532,7 +541,10 @@ def build(rank_peers):
             act(ref("xt", nn, 128), q, F.Identity, bias=-QO)
         else:
             ts(ref("xt", nn, 128), q, -QO, A.add)
-        act(ref("q1", 0, 128), q, F.Identity, scale=-1.0, bias=QO)
+        if t < RO - 1:
+            act(ref("q1", 0, 128), q, F.Identity, bias=-QO - 1024.0)
+        else:
+            act(ref("q1", 0, 128), q, F.Identity, scale=-1.0, bias=QO)
         if CHUNKS[0][3] in "VM":
             tt(ref("s32", 0, 128), ind("xt", OFF, OFF + base, lv), q, A.add)
             ts(ref("mxi", 0, 128), ref("s32", 0, 128), 0.5, A.mult, -QO / 2 - 0.25, A.add)
@@ -576,9 +588,10 @@ def build(rank_peers):
                 [ref("mn", sn, base), ref("xs", sn + base, 384)] + [ref("mn", x, 384) for x in news],
                 [ref("mt", OFF, base + 384), ref("xt", nn, 384)], 256 * base + 300000)
             ops[-1]["after"] = [sent[t]]
-        tt(ref("sh", 0, 128), ind("rcv", 256 * t, 256 * t + 256, LA(3)), q if t < RO - 1 else ref("xt", nn, 128), A.min)
+        tt(ref("sh", 0, 128), ind(box[t][1], box[t][2], box[t][2] + 256, LA(3)), q if t < RO - 1 else ref("xt", nn, 128), A.min)
         if t < RO - 1:
-            act(q, ref("sh", 0, 128), F.Abs, bias=-QO / 2)
+            ts(ref("rr", 0, 128), ref("sh", 0, 128), 0.0, A.is_lt, QO + 1024.0, A.mult)
+            tt(q, ref("rr", 0, 128), ref("sh", 0, 128), A.add)
         else:
             act(ref("qo", 0, 128), ref("sh", 0, 128), F.Abs)
             dma("S", (lambda T: [(T.yq[:, 0:128], T.qo[:, 0:128])], 1), [], [ref("qo", 0, 128)], 32768)

@@ -2,17 +2,20 @@ from concourse.bass import DstId, RemoteDMATransfer
 from concourse.mybir import dt, AluOpType, AxisListType, ActivationFunctionType
 
 B, W, R, L, RO = 2048, 3200, 768, 128, 3
-OFF = 768
-ENC = 1600.0
+OFF = 896
+ENC = 1152.0
 QO = 1280.0
+BIG = 4096.0
+LB = 131
+MG = 12582912.0
+BX = 384
 
 SN = 2816
-CHUNKS = [(0, 128, "AAAD", "S"), (128, 320, "AADD", "S"), (448, 320, "AADD", "T")]
-LOW = "VVV"
-ONS = "ex"
+CHUNKS = [(0, 128, "AAAD", "S"), (128, 320, "ADDD", "T"), (448, 320, "AADD", "T")]
+KS = [(0, 4)]
+ONS = "xvr"
 SEED, JIT, LOOK, PASSES = 3, 200.0, 0.4, 6
-PIECE, SPLV, SPLS, INORDER = 4, 1, 1, 0
-S16 = True
+PIECE = 4
 NENG = 16
 CY, PEC, GAM, SCA = 0.92, 0.45, 1.55, 3.8
 HOP, SELF, SFIX = 185.0, 220.0, 45.0
@@ -20,32 +23,32 @@ HOP, SELF, SFIX = 185.0, 220.0, 45.0
 f32, bf, f16, i32, u16 = "float32", "bfloat16", "float16", "int32", "uint16"
 SCRATCH = {
     "xt": ("sbuf", [128, OFF + W], bf), "mt": ("sbuf", [128, OFF + W], f32), "it": ("sbuf", [128, OFF + W], i32),
-    "xs": ("sbuf", [128, 3 * SN], bf), "mn": ("sbuf", [128, 3 * SN], f32),
+    "xs": ("sbuf", [128, 3 * SN], bf), "mn": ("sbuf", [128, 3 * SN], f32), "nt": ("sbuf", [128, SN], f32),
     "mi": ("sbuf", [128, B], i32), "sti": ("sbuf", [128, 48], i32), "stu": ("sbuf", [128, 48], u16),
     "qb": ("sbuf", [128, R], bf), "qh": ("sbuf", [128, R], f16), "qo": ("sbuf", [128, R], bf),
-    "snd": ("sbuf", [128, 2 * 256], f32), "rcv": ("sbuf", [128, 2 * 256], f32), "snl": ("sbuf", [128, 256], bf), "rcl": ("sbuf", [128, 256], bf),
+    "snd": ("sbuf", [128, 3 * BX], bf), "rcv": ("sbuf", [128, 3 * BX], bf),
     "ci": ("sbuf", [128, 144], bf), "c4": ("sbuf", [128, 144], bf), "c16": ("sbuf", [128, 128], bf), "j16": ("sbuf", [128, 128], bf),
-    "pi": ("sbuf", [128, 8], i32), "ei": ("sbuf", [128, 8], i32), "eu": ("sbuf", [128, 16], u16),
-    "col": ("sbuf", [128, 64], f32), "cw": ("sbuf", [128, 128], f32),
-    "mz": ("sbuf", [128, 144], bf), "mz4": ("sbuf", [128, 144], f16), "my": ("sbuf", [128, 9 * 144], f16),
-    "mm": ("sbuf", [128, 12 * 128], f16), "mb16": ("sbuf", [128, 3 * 128], bf),
-    "ee": ("sbuf", [128, 3 * 1024], bf), "dg": ("sbuf", [128, 384], f32), "rs": ("sbuf", [128, 512], f32), "jf": ("sbuf", [128, 128], f16), "cst": ("sbuf", [128, 128], f16),
-    "cv": ("sbuf", [128, 128], f32), "kt16": ("sbuf", [128, 192], bf), "tn": ("sbuf", [128, 6 * 128], f32), "c2": ("sbuf", [128, 6 * 128], f32),
+    "pi": ("sbuf", [128, 8], i32), "ei": ("sbuf", [128, 8], i32), "eu": ("sbuf", [128, 8], u16),
+    "col": ("sbuf", [128, 64], f32), "cw": ("sbuf", [128, 128], f32), "c9": ("sbuf", [128, 64], f16),
+    "mz": ("sbuf", [128, 2 * 144], bf), "mz4": ("sbuf", [128, 144], f16), "my": ("sbuf", [128, 9 * 144], f16),
+    "mm": ("sbuf", [128, 18 * 128], f16), "mb16": ("sbuf", [128, 2 * 128], bf),
+    "dg": ("sbuf", [128, 256], f32), "kt16": ("sbuf", [128, 80], bf), "ktw": ("sbuf", [128, 72], bf), "x9": ("sbuf", [128, 4 * 72], f32),
+    "tn": ("sbuf", [128, 6 * 128], f32), "tc16": ("sbuf", [128, 6 * 128], f16), "jb": ("sbuf", [128, 8 * LB], bf),
+    "dz": ("sbuf", [128, 8 * LB], f16), "ne": ("sbuf", [128, 8 * LB], f16), "lo": ("sbuf", [128, 3 * 8 * LB], f16),
     "g16": ("sbuf", [128, R], f16), "ti": ("sbuf", [128, 192], i32), "tau": ("sbuf", [128, 192], f32),
-    "cc": ("sbuf", [128, 384], f32), "t16": ("sbuf", [128, 384], f16), "ou": ("sbuf", [128, 192], u16),
-    "dd": ("sbuf", [128, 4 * R], f32), "xr": ("sbuf", [128, 4 * R], bf),
-    "ab0": ("sbuf", [128, 8, 4, 16], bf), "ab1": ("sbuf", [128, 20, 4, 16], bf), "ab2": ("sbuf", [128, 20, 4, 16], bf),
-    "pm": ("sbuf", [128, 192], f32), "rk": ("sbuf", [128, 80], f32), "eq": ("sbuf", [128, 192], f32),
-    "ve": ("sbuf", [128, 384], f32), "lv": ("sbuf", [128, 96], u16), "l0": ("sbuf", [128, 48], f32), "l1": ("sbuf", [128, 144], f32),
+    "cc": ("sbuf", [128, 384], f32), "t16": ("sbuf", [128, 448], f16), "ou": ("sbuf", [128, 192], u16),
+    "dd": ("sbuf", [128, 4 * R], f16), "xr": ("sbuf", [128, 4 * R], bf),
+    "ab0": ("sbuf", [128, 8, 9, 8], bf), "ab1": ("sbuf", [128, 20, 4, 16], bf), "ab2": ("sbuf", [128, 20, 4, 16], bf),
+    "pm": ("sbuf", [128, 272], f32), "rk": ("sbuf", [128, 152], f32), "eq": ("sbuf", [128, 192], f32), "eqw": ("sbuf", [128, 72], f32),
+    "ve": ("sbuf", [128, 384], f32), "vw": ("sbuf", [128, 4 * 72], f32), "lv": ("sbuf", [128, 96], u16),
     "xg": ("sbuf", [128, R], bf), "sh": ("sbuf", [128, R], f16),
-    "wi": ("sbuf", [128, 16], i32), "xe": ("sbuf", [128, 3 * 128], f16), "fa": ("sbuf", [128, 3 * 1024], f32),
-    "w8": ("sbuf", [128, 192], f32), "la": ("sbuf", [128, 32], u16),
-    "s32": ("sbuf", [128, 128], f32), "mxi": ("sbuf", [128, 128], i32),
-    "km": ("sbuf", [128, 256], f16), "kq": ("sbuf", [128, 256], f16), "gk": ("sbuf", [128, 256], f16), "gs": ("sbuf", [128, 256], f16),
-    "g32": ("sbuf", [128, 256], f32), "e7": ("sbuf", [128, 256], f32), "ua": ("sbuf", [128, 256], f32), "ub": ("sbuf", [128, 256], f32),
-    "yy": ("sbuf", [128, 256], f32), "md": ("sbuf", [128, 256], f32), "ui": ("sbuf", [128, 256], i32),
-    "b1": ("sbuf", [128, 5 * 128], f32), "b2": ("sbuf", [128, 4 * 128], f32), "q1": ("sbuf", [128, 128], f32),
-    "rr": ("sbuf", [128, 128], f32),
+    "ky": ("sbuf", [128, 256], f16), "k2": ("sbuf", [128, 128], u16), "xk": ("sbuf", [128, 128], f16), "la": ("sbuf", [128, 48], u16),
+    "w8": ("sbuf", [128, 64], f32), "f8": ("sbuf", [128, 16], f16), "mxi": ("sbuf", [128, 128], i32),
+    "dm": ("sbuf", [128, 128], f32), "d1": ("sbuf", [128, 128], f32), "dn": ("sbuf", [128, 128], f32),
+    "km": ("sbuf", [128, 128], f32), "kf": ("sbuf", [128, 128], bf), "kk": ("sbuf", [128, 256], f16), "gs": ("sbuf", [128, 256], f16),
+    "g32": ("sbuf", [128, 256], f32), "yy": ("sbuf", [128, 256], f16), "w1": ("sbuf", [128, 256], f32), "fl": ("sbuf", [128, 256], f16),
+    "t1": ("sbuf", [128, 256], f32), "md": ("sbuf", [128, 128], f32), "ui": ("sbuf", [128, 128], i32),
+    "q1": ("sbuf", [128, 128], bf), "rr": ("sbuf", [128, 128], f16),
 }
 for _b in range(8):
     SCRATCH["ps%d" % _b] = ("psum", [128, 512], f32)
@@ -54,6 +57,13 @@ SEMAPHORES = ["cV", "cS", "cP", "cG", "snt0", "snt1", "snt2", "arr0", "arr1", "a
 TWO = (bf, f16, u16)
 A = AluOpType
 F = ActivationFunctionType
+al = slice(None)
+
+
+def bits(lo, n, step=1):
+    if step == 1:
+        return ((1 << n) - 1) << lo
+    return sum(1 << (lo + i * step) for i in range(n))
 
 
 def build(rank_peers):
@@ -63,13 +73,14 @@ def build(rank_peers):
     def ref(name, lo, n, step=1):
         return (name, lo, lo + (n - 1) * step + 1, step)
 
+    def view(name, *idx):
+        cols = [0]
+        for d, x in zip(SCRATCH[name][1][1:], idx):
+            cols = [c * d + j for c in cols for j in (range(d)[x] if isinstance(x, slice) else [x])]
+        return (name, sum(1 << c for c in cols), None, None, len(cols), (al,) + idx)
+
     def ind(name, lo, hi, off):
         return ("*", name, lo, hi, off)
-
-    def regs(r):
-        if r[0] == "*":
-            return [(r[1], r[2], r[3]), r[4][:3]]
-        return [r[:3]]
 
     def nel(r):
         if len(r) == 6:
@@ -77,6 +88,13 @@ def build(rank_peers):
         if r[0] == "*":
             return 16 * (r[4][2] - r[4][1])
         return (r[2] - r[1] + r[3] - 1) // r[3]
+
+    def reg(r):
+        if len(r) == 6:
+            return r[:2]
+        if r[0] == "*":
+            return (r[1], bits(r[2], r[3] - r[2]))
+        return (r[0], bits(r[1], nel(r), r[3]))
 
     def ap(T, r):
         if not isinstance(r, tuple):
@@ -96,12 +114,13 @@ def build(rank_peers):
         rd, wr = [], []
         for r in ins:
             if isinstance(r, tuple):
-                rd += regs(r)
+                rd.append(reg(r))
+                if r[0] == "*":
+                    rd.append(reg(r[4]))
         for r in out:
+            wr.append(reg(r))
             if r[0] == "*":
-                wr.append((r[1], r[2], r[3])); rd.append(r[4][:3])
-            else:
-                wr.append(r[:3])
+                rd.append(reg(r[4]))
         ops.append({"e": eng, "fn": fn, "rd": rd, "wr": wr, "c": cost, "lat": lat, "sem": sem, "inc": inc})
 
     def vcost(out, ins, rate):
@@ -118,6 +137,9 @@ def build(rank_peers):
     def tc(out, a):
         add("V", lambda g, T: g.vector.tensor_copy(ap(T, out), ap(T, a)), [out], [a], vcost(out, [a], half(out, a)))
 
+    def fill(out, c):
+        add("V", lambda g, T: g.vector.memset(ap(T, out), c), [out], [], max(64, nel(out) * half(out)) * CY)
+
     def tt(out, a, b, op):
         rate = 1.0 if "psum" in (kind(a)[0], kind(b)[0]) else 2.0
         add("V", lambda g, T: g.vector.tensor_tensor(ap(T, out), ap(T, a), ap(T, b), op), [out], [a, b], vcost(out, [a], rate))
@@ -131,18 +153,14 @@ def build(rank_peers):
 
     def scan(out, d0, d1, init, op0, op1):
         add("V", lambda g, T: g.vector.tensor_tensor_scan(ap(T, out), ap(T, d0), ap(T, d1), init, op0, op1), [out], [d0, d1],
-            max(64, nel(out)) * CY)
+            max(64, nel(out) * half(out, d0, d1)) * CY)
 
-    def rmin(out, a):
-        add("V", lambda g, T: g.vector.tensor_reduce(ap(T, out), ap(T, a), AxisListType.X, A.min), [out], [a], max(64, nel(a)) * CY)
-
-    def act(out, a, func, bias=0.0, scale=1.0, accum=None):
-        c = 65 + GAM * nel(out) * CY if a[0] == "*" else max(64, nel(out)) * CY + SFIX + (20 if accum else 0)
-        add("S", lambda g, T: g.scalar.activation(ap(T, out), ap(T, a), func, bias=ap(T, bias), scale=ap(T, scale), accum_out=ap(T, accum)),
-            [out] + ([accum] if accum else []), [a, bias, scale], c)
+    def act(out, a, func, bias=0.0, scale=1.0):
+        c = 65 + GAM * nel(out) * CY if a[0] == "*" else max(64, nel(out)) * CY + SFIX
+        add("S", lambda g, T: g.scalar.activation(ap(T, out), ap(T, a), func, bias=ap(T, bias), scale=ap(T, scale)), [out], [a, bias, scale], c)
 
     def mm(groups, piece=99):
-        calls = [(out, l, r, i == 0, i == len(terms) - 1) for out, terms in groups for i, (l, r) in enumerate(terms)]
+        calls = [(x[2] if len(x) > 2 else out, x[0], x[1], i == 0, i == len(terms) - 1) for out, terms in groups for i, x in enumerate(terms)]
         first = len(ops)
         for lo in range(0, len(calls), piece):
             def fn(g, T, part=calls[lo:lo + piece]):
@@ -174,6 +192,7 @@ def build(rank_peers):
         add(q, fn, out, ins, 60.0 * n, lat=1800 + nbytes / 180.0, sem=sem, inc=16 * n)
 
     col = lambda c: ref("col", c, 1)
+    aff = lambda o, a, s, b: act(o, a, F.Identity, scale=s, bias=b)
     dma("S", (lambda T: [(T.mi[2::4, :], T.bd[:]), (T.mi[3::4, :], T.bd[:])], 2), [ref("mi", 0, B // 2)], [], 1 << 20)
     dma("Y", (lambda T: [(T.mi[0::4, :], T.pf[:]), (T.mi[1::4, :], T.mb[:])], 2), [ref("mi", B // 2, B // 2)], [], 1 << 20)
     dma("Y", (lambda T: [(T.sti[:], T.st[:]), (T.qb[:], T.qr[:])], 2), [ref("sti", 0, 48), ref("qb", 0, R)], [], 400000)
@@ -189,6 +208,11 @@ def build(rank_peers):
     iota(ref("c16", 0, 128), [[1, 8], [0, 16]], 0, 0)
     iota(ref("ei", 0, 8), [[1, 8]], 0, 0)
     iota(ref("kt16", 0, 80), [[0, 20], [1, 4]], 0, 0)
+    iota(ref("x9", 0, 72), [[0, 8], [1, 9]], 0, 0)
+    iota(ref("jb", 0, 8 * LB), [[-16, 8], [1, LB]], -1, 0)
+    iota(ref("nt", 0, B), [[1, B]], -int(ENC), 0)
+    iota(ref("it", 0, 768), [[1024, 3], [0, 2], [4, 128]], 4 * (128 - OFF), 0)
+    iota(ref("nt", B, SN - B), [[1, SN - B]], B - int(ENC), 0)
     iota(ref("cc", 0, 384), [[0, 384]], 0, 0)
     p0 = ref("pi", 0, 1)
     ts(ref("pi", 1, 1), p0, 3, A.bitwise_and)
@@ -196,14 +220,22 @@ def build(rank_peers):
     ts(ref("pi", 3, 1), p0, 112, A.bitwise_and)
     ts(ref("pi", 4, 1), p0, 15, A.bitwise_and)
     ts(ref("pi", 5, 1), p0, 2, A.logical_shift_right)
-    tc(ref("col", 0, 6), ref("pi", 0, 6))
-    CP, CTY, CA, CG16, CS, CP4 = [col(i) for i in range(6)]
+    ts(ref("pi", 6, 1), p0, 3, A.logical_shift_right, 1, A.bitwise_and)
+    tc(ref("col", 0, 7), ref("pi", 0, 7))
+    CP, CTY, CA, CG16, CS, CP4, CH = [col(i) for i in range(7)]
     ts(ref("col", 8, 4), ref("ci", 0, 4), CTY, A.is_equal)
     T0, T1, T2, T3 = [col(8 + i) for i in range(4)]
     ts(col(12), CG16, CA, A.add, 12.0, A.add)
     tt(col(13), T1, T0, A.subtract)
-    ts(col(14), CTY, 1.5, A.is_lt, ENC, A.mult)
-    COFF = col(14)
+    CPM, CGS, CG, CSG, C7, CE0, CAD = [col(14)] + [col(24 + i) for i in range(6)]
+    ts(CPM, CTY, 1.5, A.is_lt)
+    ts(CGS, CTY, 1.5, A.is_lt, -ENC, A.mult)
+    ts(C7, T2, 7.0, A.mult)
+    tt(CG, CGS, C7, A.subtract)
+    tt(CSG, CPM, T2, A.subtract)
+    ts(CE0, T0, ENC, A.mult)
+    ts(col(30), CA, 1.0, A.add, T2, A.mult)
+    ts(CAD, col(30), -1.0, A.add)
     ts(col(15), CG16, 0.25, A.mult, 3.0, A.add)
     for k in range(4):
         ts(ref("my", 144 * k, 140), ref("ci", 0, 140), col(12), A.is_equal, col(8 + k), A.mult)
@@ -212,111 +244,89 @@ def build(rank_peers):
     for k in range(3):
         ts(ref("my", 144 * (5 + k), 140), ref("ci", 0, 140), col(12), A.is_equal, col(40 + k), A.mult)
     ts(ref("rk", 0, 80), ref("kt16", 0, 80), 0.0, A.is_equal, 1.0e6, A.mult)
-    ts(ref("my", 144 * 8, 140), ref("my", 144 * 2, 140), -0.25, A.mult)
+    ts(ref("my", 144 * 8, 140), ref("my", 144 * 2, 140), 0.25, A.mult)
     ts(ref("mz4", 0, 140), ref("c4", 0, 140), col(15), A.is_equal, 0.25, A.mult)
     ts(col(16), CG16, 15.0, A.add)
     ts(ref("mz", 0, 143), ref("ci", 0, 143), col(16), A.is_equal, 4.0, A.mult)
+    tt(ref("mz", 144, 135), ref("mz", 0, 135), ref("mz", 8, 135), A.add)
     Y = lambda k, sh: ref("my", 144 * k + 12 - 4 * sh, 128)
     M = lambda i: ref("mm", 128 * i, 128)
-    ci = ref("ci", 0, 128)
+    ci, c16 = ref("ci", 0, 128), ref("c16", 0, 128)
     ts(ref("mb16", 0, 128), ci, CP, A.is_equal)
     ts(ref("mb16", 128, 128), ci, CP, A.is_equal, 0.5, A.mult)
     IB, IBH = ref("mb16", 0, 128), ref("mb16", 128, 128)
-    ts(M(0), ci, CP, A.is_equal, -1.0, A.mult)
-    ts(M(1), ci, CP, A.is_equal, 0.5, A.mult)
-    ts(M(2), ci, CP, A.is_equal)
-    INEG, IH, I16 = M(0), M(1), M(2)
+    INEG, IH, I16, I4, IBIG, INQ, BO, BOQ, BOD, DAL, DALN, IP, IPB, SH, PMS, BODP, LQ, IS = [M(i) for i in range(18)]
+    for m_, c in ((INEG, -1.0), (IH, 0.5), (I16, 1.0), (I4, 4.0), (IBIG, BIG), (INQ, -0.25), (IP, T0), (IS, -768.0)):
+        ts(m_, ci, CP, A.is_equal, c, A.mult)
     ts(col(17), CG16, 0.0625, A.mult)
-    ts(M(3), ref("c16", 0, 128), col(17), A.is_equal)
-    ts(M(4), ref("c16", 0, 128), col(17), A.is_equal, 4.0, A.mult)
-    ts(M(5), ref("c16", 0, 128), col(17), A.is_equal, T2, A.mult)
-    BO, BO4, BOD = M(3), M(4), M(5)
-    ts(M(6), ref("c4", 0, 128), CP4, A.is_equal, T2, A.mult)
-    tt(col(18), T1, T2, A.add)
-    ts(col(19), col(18), -1.0, A.mult)
+    for m_, c in ((BO, 1.0), (BOQ, 0.25), (BOD, T2)):
+        ts(m_, c16, col(17), A.is_equal, c, A.mult)
+    ts(DAL, ref("c4", 0, 128), CP4, A.is_equal, T2, A.mult)
+    ts(DALN, DAL, -BIG, A.mult)
+    ts(IPB, IP, BIG, A.mult)
     ts(col(20), CP, -1.0, A.add)
-    ts(col(21), T1, -1.0, A.mult)
-    ts(M(7), ci, CP, A.is_equal, col(18), A.mult)
-    ts(M(8), ci, CP, A.is_equal, col(19), A.mult)
-    ts(M(9), ci, CP, A.is_equal, T0, A.mult)
-    ts(M(10), ci, col(20), A.is_equal, T1, A.mult)
-    ts(M(11), ci, col(20), A.is_equal, col(21), A.mult)
-    DAL, IMD, IMDN, IP, SH, SHN = M(6), M(7), M(8), M(9), M(10), M(11)
-    DG, RS, JF, CST = ref("dg", 0, 128), ref("rs", 0, 128), ref("jf", 0, 128), ref("cst", 0, 128)
+    ts(SH, ci, col(20), A.is_equal, T1, A.mult)
+    tt(PMS, IP, SH, A.subtract)
+    fill(ref("km", 0, 128), 0.0)
+    fill(ref("km", 0, 32, 4), -BIG)
+    tt(BODP, BOD, ref("km", 0, 128), A.mult)
+    ts(ref("kf", 0, 128), ci, CP, A.is_gt)
+    tt(LQ, BOQ, ref("kf", 0, 128), A.mult)
+    DG = ref("dg", 0, 128)
     ts(DG, ref("j16", 0, 128), CS, A.is_equal)
-    ts(RS, ref("j16", 0, 128), 0.5, A.is_gt)
-    ts(JF, ci, 1.0 / 256, A.mult)
-    ts(col(22), T0, ENC, A.mult)
-    ts(col(23), T2, 7.0, A.mult, col(22), A.add)
-    ts(CST, ci, 0.0, A.mult, col(23), A.add)
-    tc(ref("eu", 0, 8), ref("ei", 0, 8))
-    ts(ref("eu", 8, 8), ref("ei", 0, 8), 4.0, A.mult, 3.0, A.add)
-    EU = ref("eu", 0, 8)
+    ts(ref("eu", 0, 8), ref("ei", 0, 8), 9.0, A.mult, 7.0, A.add)
     cw = lambda i: ref("cw", 8 * i, 8)
-    cv = lambda i: ref("cv", 8 * i, 8)
-    aff = lambda o, a, s, b: act(o, a, F.Identity, scale=s, bias=b)
-    PK, PKM, PB, PC = ref("ps7", 0, 128), ref("ps0", 256, 128), ref("ps7", 256, 128), ref("ps7", 384, 128)
-    aff(ref("rs", 128, 128), ci, 0.0, 1.0)
-    ts(ref("b1", 128, 128), ci, -1.0, A.mult, 127.0, A.add)
-    ts(ref("b1", 256, 128), ref("b1", 128, 128), CS, A.subtract)
-    aff(ref("b1", 384, 128), RS, 4096.0, 0.0)
-    tt(ref("rs", 256, 128), ref("b1", 256, 128), ref("b1", 384, 128), A.add)
     ts(cw(0), ref("ei", 0, 8), 16.0, A.mult, CS, A.add)
-    aff(cw(1), cw(0), -4096.0, ENC + OFF)
-    aff(cw(2), cw(0), -1.0 / 256, 0.25)
-    aff(col(26), T2, 6.5, 0.0)
-    aff(cv(0), cw(0), 1.0, -ENC - OFF)
-    aff(cv(1), cw(0), 4096.0, 0.0)
-    aff(col(24), COFF, 1.0 / ENC, 0.0)
-    aff(col(25), COFF, -1.0, 0.0)
-    aff(ref("dg", 128, 128), DG, 1048576.0, 0.0)
-    if "P" in LOW:
-        BOB = ref("mb16", 256, 128)
-        ts(BOB, ref("c16", 0, 128), col(17), A.is_equal)
-        aff(ref("b2", 0, 128), ci, 0.0, 0.5)
-        aff(ref("b2", 128, 128), ci, 0.0, -1.0)
-        scan(ref("b2", 256, 128), ref("b2", 0, 128), ref("b2", 128, 128), 2.0 ** 64, A.mult, A.max)
-        tt(ref("b2", 384, 128), ref("b2", 256, 128), DG, A.mult)
-        aff(ref("dg", 256, 128), ref("b2", 384, 128), 2.5, 0.0)
-        scan(ref("b1", 0, 128), RS, ref("b2", 384, 128), 0.0, A.mult, A.add)
-        aff(cv(10), ref("b1", 15, 8, 16), 1.0, 0.0)
+    ts(col(31), CH, 4.0, A.mult)
+    ts(col(32), CH, 4.0, A.mult, 3.0, A.add)
+    x9 = lambda i: ref("x9", 72 * i, 72)
+    ts(ref("rk", 80, 72), x9(0), 0.0, A.is_equal, 1.0e6, A.mult)
+    ts(x9(1), x9(0), col(32), A.is_equal, 4.0, A.mult)
+    ts(x9(2), x9(0), col(31), A.is_ge)
+    ts(x9(3), x9(0), col(32), A.is_gt)
+    tt(x9(2), x9(3), x9(2), A.subtract)
+    tt(x9(1), x9(1), x9(2), A.add)
+    ts(x9(2), x9(2), 1.0, A.add, 32768.0, A.mult)
+    ts(x9(3), x9(0), col(31), A.subtract)
+    tt(ref("ktw", 0, 72), x9(2), x9(3), A.add)
+    fill(view("ab0", al, 8, al), 0.0)
+    blk = lambda nm, i, x: ref(nm, 8 * LB * i + x, 8, LB)
+    ts(ref("dz", 0, 8 * LB), ref("jb", 0, 8 * LB), CS, A.is_equal, -BIG, A.mult)
+    aff(ref("ne", 0, 8 * LB), ref("jb", 0, 8 * LB), 0.0, BIG)
+    aff(blk("dz", 0, 0), cw(0), 0.0, 4 * BIG)
+    aff(blk("dz", 0, LB - 2), cw(0), 0.0, BIG)
+    aff(ref("c9", 48, 8), cw(0), 1.0, 128.0)
+    ts(ref("d1", 0, 128), ref("j16", 0, 128), 0.5, A.is_gt)
     for t in range(RO):
-        if LOW[0] == "P":
-            aff(cw(3 + t), cw(0), 1.0, 256.0 * t)
-        elif LOW[0] == "S":
-            aff(cv(3 + t), cw(0), 1.0, 256.0 * t - ENC - OFF)
-        if LOW[2] == "P":
-            aff(cv(6 + t), cw(0), 1.0, 256.0 * t + 128)
-        aff(ref("c2", 256 * t, 128), ci, 1.0, 256.0 * t + 128 - OFF)
-        aff(ref("c2", 256 * t + 128, 128), ci, 1.0 if LOW[2] == "P" else 257.0 / 256, 256.0 * t + 128)
-        aff(col(28 + t), T2, t + 1.0, 0.0)
+        aff(ref("c9", 16 * t, 8), cw(0), 0.0, 0.0)
+        aff(ref("c9", 16 * t + 8, 8), cw(0), 1.0, 256.0 * t + 128)
+        aff(cw(1 + t), cw(0), -1.0, ENC + OFF - 256.0 * t - 128)
+        aff(cw(4 + t), cw(0), 1.0, 256.0 * t + 128)
+        aff(col(33 + t), T2, 6.0 - t, 0.0)
         for z in range(2):
-            aff(col(32 + 2 * t + z), col(24), B + 384.0 * t + 128 * z - ENC, col(28 + t))
-            aff(ref("tn", 128 * (2 * t + z), 128), ci, col(24), col(32 + 2 * t + z))
-    iota(ref("mt", 0, OFF), [[0, OFF]], 7, 0)
-    iota(ref("it", 0, OFF), [[0, OFF]], 0, 0)
+            m0 = B + 384.0 * t + 128 * z
+            aff(col(44 + 2 * t + z), T1, m0, col(33 + t))
+            aff(ref("tn", 128 * (2 * t + z), 128), ci, T1, col(44 + 2 * t + z))
+            aff(ref("tc16", 128 * (2 * t + z), 128), ci, 1.0, m0 - BIG)
+    iota(ref("mt", 0, OFF), [[0, OFF]], 0, 0)
+    iota(ref("it", 768, 128), [[0, 128]], 0, 0)
     iota(ref("xt", 0, OFF), [[0, OFF]], 0, 0)
-    box = [("snd", "rcv", 0), ("snd", "rcv", 256), ("snl", "rcl", 0)]
     for t in range(RO):
-        iota(ref(box[t][0], box[t][2], 256), [[0, 256]], 4096, 0)
-        iota(ref(box[t][1], box[t][2], 128), [[0, 128]], 4096, 0)
-        iota(ref(box[t][1], box[t][2] + 192, 64), [[0, 64]], 4096, 0)
-        aff(ref("l1", 48 * t + 1, 8, 2), cw(0), 1.0, 256.0 * t)
-        aff(ref("l1", 48 * t + 17, 8, 2), cw(0), 1.0, 0.0)
-        aff(ref("l1", 48 * t + 33, 8, 2), cw(0), 1.0, 256.0 * t + 128 + 262144.0)
-    aff(ref("l0", 0, 48), ref("ci", 0, 48), 0.0, -1.0e9)
-    aff(ref("rs", 384, 128), RS, 1.0e10, -262144.0)
+        iota(ref("snd", BX * t, BX), [[0, BX]], 4096, 0)
+        iota(ref("rcv", BX * t + 64, BX - 64), [[0, BX - 64]], 4096, 0)
     for c0, n, _, _ in CHUNKS:
         tc(ref("stu", c0 // 16, n // 16), ref("sti", c0 // 16, n // 16))
         act(ref("qh", c0, n), ref("qb", c0, n), F.Identity, bias=QO)
     for i in range(8):
-        tc(ref("mt", OFF + 256 * i, 256), ref("mi", 256 * i, 256))
+        ts(ref("mt", OFF + 256 * i, 256), ref("mi", 256 * i, 256), CSG, A.mult, C7, A.add)
         ops[-1]["after"] = [0, 1]
-    if "n" not in ONS:
-        dma("Y", (lambda T: [(T.mn[:, 0:B], T.mt[:, OFF:OFF + B])], 1), [ref("mn", 0, B)], [ref("mt", OFF, B)], 1 << 20)
+    dma("Y", (lambda T: [(T.mn[:, 0:B], T.mt[:, OFF:OFF + B])], 1), [ref("mn", 0, B)], [ref("mt", OFF, B)], 1 << 20)
     dma("Y", (lambda T: [(T.mn[r::4, SN * t:SN * t + B], T.mt[r::4, OFF:OFF + B]) for r in (0, 3) for t in (1, 2)], 4),
         [ref("mn", SN, B), ref("mn", 2 * SN, B)], [ref("mt", OFF, B)], 1 << 20)
     dma("Y", (lambda T: [(T.yp[:, 0:B], T.mt[0::4, OFF:OFF + B])], 1), [], [ref("mt", OFF, B)], 262144)
+
+    LA = lambda i: ref("la", 8 * i, 8)
+    vw = lambda i, x=7: ref("vw", 72 * i + x, 8, 9)
 
     def reads(t, ci_, c0, n, routes, qroute):
         base = B + 384 * t
@@ -326,9 +336,11 @@ def build(rank_peers):
         q = ref("qh", c0, n)
         o4 = c0 // 4
         c4_ = lambda nm, lo=0, cnt=r4: ref(nm, o4 + lo, cnt)
-        pD, pE, pP, pT, pS = ref(pb, 0, r4), ref(pb, r4, r4, 2), ref(pb, r4 + 1, r4, 2), ref(pb, 3 * r4, r4), ref(pb, 4 * r4, r4)
+        pD, pE, pP, pT = ref(pb, 0, r4), ref(pb, r4, r4, 2), ref(pb, r4 + 1, r4, 2), ref(pb, 3 * r4, r4)
+        pS = ref(pb, 4 * r4, r4) if ci_ else ref("ps2", 288, 72)
         pU = pS if ci_ else ref("ps2", 256, r4)
-        pc, sp, ss = (PIECE, SPLV, SPLS) if ci_ else (99, 1, 1)
+        tb = 2 * o4 + (64 if ci_ else 0)
+        pc = PIECE if ci_ else 99
         XW = lambda off: ind("xt", OFF, OFF + base, off) if ci_ == 0 else ind("xs", SN * t, SN * t + base, off)
         MW = lambda off: ind("mt", OFF, OFF + base, off) if ci_ == 0 else ind("mn", SN * t, SN * t + base, off)
         qs = "sh" if ci_ == 0 and t > 0 else "qh"
@@ -338,12 +350,14 @@ def build(rank_peers):
         tt(c4_("tau"), c4_("ti"), pU, A.subtract)
         lst = ref("stu", c0 // 16, m)
         for rd in range(2):
-            if t == 0 and (rd == 0 or ci_ == 0 or "n" in ONS):
-                ts(ref("g16", c0, n), ind("mi", 0, B, lst), COFF, A.subtract)
+            if t == 0 and (rd == 0 or ci_ == 0):
+                ts(ref("g16", c0, n), ind("mi", 0, B, lst), CSG, A.mult, CGS, A.add)
+            elif ci_ and rd == 0:
+                act(ref("g16", c0, n), ind("mt", OFF, OFF + base, lst), F.Identity, bias=CG)
             elif ci_ or rd == 0 or "g" in ONS:
-                act(ref("g16", c0, n), MW(lst), F.Identity, bias=col(25))
+                act(ref("g16", c0, n), MW(lst), F.Identity, bias=CG)
             else:
-                ts(ref("g16", c0, n), MW(lst), COFF, A.subtract)
+                ts(ref("g16", c0, n), MW(lst), CG, A.add)
             gs = lambda s: ref("g16", c0 + s, r4, 4)
             if rd == 0 and ci_ == 0:
                 mm([(pE, [(Y(4, s), gs(s)) for s in range(4)]), (pP, [(Y(0, s), gs(s)) for s in range(4)])], pc)
@@ -355,36 +369,53 @@ def build(rank_peers):
                 mm([(pD, [(Y(8, s), gs(s)) for s in range(4)])])
                 mm([(pE, [(Y(4, s), gs(s)) for s in range(4)]), (pP, [(Y(0, s), gs(s)) for s in range(4)])], pc)
                 tt(ref("cc", 2 * o4 + 1, r4, 2), pD, c4_("tau"), A.is_ge)
-            scan(ref("t16", 2 * o4, 2 * r4), ref("cc", 2 * o4, 2 * r4), ref(pb, r4, 2 * r4), 0.0, A.mult, A.add)
-            t16 = lambda cl: ref("t16", 2 * o4 + 2 * cl + 1, m, 8)
-            mm([(ref(pb, 3 * r4 + k * m, m), [(Y(k, cl), t16(cl)) for cl in range(4)]) for k in range(4)], pc)
-            ts(c4_("ou"), pT, ENC, A.add)
-            mm([(ref(pb, 5 * r4 + k, m, 4), [(Y(5 + k if k < 3 else 3, cl), t16(cl)) for cl in range(4)]) for k in range(4)], pc)
-            qo_ = QO
-            al = slice(None)
+            scan(ref("t16", tb, 2 * r4), ref("cc", 2 * o4, 2 * r4), ref(pb, r4, 2 * r4), 0.0, A.mult, A.add)
+            last = ci_ == 0 and rd == 1
+            if last:
+                ts(ref("t16", 65, r4, 2), pD, -1.7, A.is_gt)
+            t16 = lambda cl, cnt=m: ref("t16", tb + 2 * cl + 1, cnt, 8)
+            for k0, k1 in (KS if ci_ == 0 else [(0, 4)]):
+                mm([(ref(pb, 3 * r4 + k * m, m), [(Y(k, cl), t16(cl)) for cl in range(4)]) for k in range(k0, k1)], pc)
+                ts(c4_("ou", k0 * m, (k1 - k0) * m), ref(pb, 3 * r4 + k0 * m, (k1 - k0) * m), ENC, A.add)
+            YD = lambda k, cl: Y(5 + k if k < 3 else 3, cl)
+            if ci_:
+                mm([(ref(pb, 5 * r4 + k, m, 4), [(YD(k, cl), t16(cl)) for cl in range(4)]) for k in range(4)], pc)
+            else:
+                cnt = 16 if last else 8
+                mm([(ref("ps2", 64 + 4 * h + k, cnt, 9), [(YD(k, cl), t16(cl, cnt)) for cl in (2 * h, 2 * h + 1)]) for h in range(2) for k in range(4)]
+                   + [(ref("ps2", 72, cnt, 9), [(I16, ref("c9", 16 * t, cnt))])])
             order = [k for k in range(4) if routes[k] != "A"] + [k for k in range(4) if routes[k] == "A"]
             for k in order:
                 at = 4 * c0 + k * n
-                ab = ("ab%d" % ci_, k, k + 1, 1, n, (al, al, k, al))
+                ab = view("ab%d" % ci_, al, k if ci_ else slice(k, 8, 4), al)
                 if routes[k] == "A":
-                    for h in range(sp):
-                        tt(ref("dd", at + h * n // sp, n // sp), XW(c4_("ou", k * m + h * m // sp, m // sp)), ref("qh", c0 + h * n // sp, n // sp),
-                           A.subtract)
-                    act(ab, ref("dd", at, n), F.Abs, bias=qo_)
+                    tt(ref("dd", at, n), XW(c4_("ou", k * m, m)), q, A.subtract)
+                    act(ab, ref("dd", at, n), F.Abs, bias=QO)
                 else:
-                    for h in range(ss):
-                        act(ref("xr", at + h * n // ss, n // ss), XW(c4_("ou", k * m + h * m // ss, m // ss)), F.Copy)
+                    act(ref("xr", at, n), XW(c4_("ou", k * m, m)), F.Copy)
                     pd = ref(px, 0, n)
                     mm([(pd, [(INEG, q), (IB, ref("xr", at, n))])])
-                    act(ab, pd, F.Abs, bias=qo_)
-            mm([(pS, [(IB, ref("kt16", 0, r4))] + [(ref("mz", 15 - s, 128), ("ab%d" % ci_, 0, 4, 1, r4, (al, al, al, s))) for s in range(16)])], pc)
-            scan(c4_("pm"), ref("rk", 0, r4), pS, 0.0, A.add, A.min)
-            tt(c4_("eq"), pS, c4_("pm"), A.not_equal)
-            scan(ref("ve", 192 * rd + o4, r4), c4_("eq"), ref(pb, 5 * r4, r4), 0.0, A.mult, A.add)
-            ve = ref("ve", 192 * rd + o4 + 3, m, 4)
+                    act(ab, pd, F.Abs, bias=QO)
             lst = ref("lv", 48 * rd + c0 // 16, m)
-            ts(lst, ve, ENC, A.add)
-            hb = QO - qo_ / 2 - 0.25
+            if ci_:
+                mm([(pS, [(IB, ref("kt16", 0, r4))] + [(ref("mz", 15 - s, 128), view("ab%d" % ci_, al, al, s)) for s in range(16)])], pc)
+                scan(c4_("pm", 48), ref("rk", 0, r4), pS, 0.0, A.add, A.min)
+                tt(c4_("eq"), pS, c4_("pm", 48), A.not_equal)
+                scan(ref("ve", 192 * rd + o4, r4), c4_("eq"), ref(pb, 5 * r4, r4), 0.0, A.mult, A.add)
+                ts(lst, ref("ve", 192 * rd + o4 + 3, m, 4), ENC, A.add)
+            else:
+                mm([(pS, [(IB, ref("ktw", 0, 72))] + [(ref("mz", 144 + 7 - s, 128), view("ab0", al, al, s)) for s in range(8)])])
+                eq = ref("eqw", 0, 72)
+                scan(ref("pm", 0, 72), ref("rk", 80, 72), pS, 0.0, A.add, A.min)
+                tt(eq, pS, ref("pm", 0, 72), A.not_equal)
+                scan(ref("vw", 72 * rd, 72), eq, ref("ps2", 64, 72), 0.0, A.mult, A.add)
+                ts(lst, vw(rd), ENC, A.add)
+                if last:
+                    scan(ref("vw", 144, 72), eq, x9(1), 0.0, A.mult, A.add)
+                    tt(ref("eqw", 8, 8, 9), blk("lo", 0, LB - 1), cw(1 + t), A.add)
+                    scan(ref("vw", 216, 72), eq, ref("ps2", 136, 72), 0.0, A.mult, A.add)
+                    tc(LA(4), vw(3, 8))
+            hb = QO / 2 - 0.25
             if qroute == "M":
                 tt(ref("sh", c0, n), XW(lst), q, A.add)
                 act(q, ref("sh", c0, n), F.Identity, scale=0.5, bias=hb)
@@ -400,201 +431,144 @@ def build(rank_peers):
                 else:
                     ts(q, pq, hb, A.add)
             if ci_ == 0 and rd == 0:
-                lowest_of(t, 0, ve, 3 + t)
+                lowest_of(t, 0, lst)
                 step_a(t, 0, LA(0))
         c1 = max(c0, L)
         if t == RO - 1 and c1 < c0 + n:
             act(ref("qo", c1, c0 + n - c1), ref("qh", c1, c0 + n - c1), F.Identity, bias=-QO)
             dma("Y", (lambda T: [(T.yq[:, c1:c0 + n], T.qo[:, c1:c0 + n])], 1), [], [ref("qo", c1, c0 + n - c1)], 256 * n)
 
-    w8 = lambda i: ref("w8", 8 * i, 8)
-    LA = lambda i: ref("la", 8 * i, 8)
+    def lowest(i, key, own):
+        for c in range(7, -1, -1):
+            ts(ref("ne", LB * c + 1, 16 * c + 16), ref(key[0], key[1], 16 * c + 16), ref(own[0], own[1] + c * own[3], 1), A.not_equal, BIG, A.mult)
+        scan(ref("lo", 8 * LB * i, 8 * LB), ref("dz", 0, 8 * LB), ref("ne", 0, 8 * LB), 0.0, A.add, A.min)
 
-    def lowest(t, i, key, bias, um, dum, sub, thr):
-        for c in range(8):
-            a = ref("fa", 1024 * i + 128 * c, 16 * c + 16)
-            act(a, ref(key[0], key[1], 16 * c + 16), F.Abs, bias=ref(bias[0], bias[1] + c * bias[3], 1), scale=-1048576.0)
-            if LOW[i] == "V":
-                rmin(ref("l0", 16 * i + 2 * c + 1, 1), a)
-            else:
-                act(a, a, F.Relu, bias=thr(c), scale=-1.0, accum=ref("w8", 8 * (6 * i + 2) + c, 1))
-        if LOW[i] == "V":
-            scan(ref("w8", 8 * (6 * i + 3), 16), ref("l0", 16 * i, 16), ref("l1", 48 * t + 16 * i, 16), 0.0, A.add, A.max)
-            ts(LA(i), ref("w8", 8 * (6 * i + 3) + 1, 8, 2), sub, A.add)
+    def lowest_of(t, i, lst):
+        key = ref("ky", 128 * i, 128)
+        act(key, ind("nt", 0, B + 384 * t, lst), F.Copy)
+        aff(blk("dz", 0, LB - 1), cw(0), 1.0, (768.0 if i else 256.0 * t) - OFF - ENC)
+        if "v" in ONS:
+            act(blk("ne", 0, LB - 1), vw(i), F.Copy)
         else:
-            tt(w8(6 * i + 3), um, w8(6 * i + 2), A.subtract)
-            tt(w8(6 * i + 4), w8(6 * i + 3), dum, A.max)
-            ts(LA(i), w8(6 * i + 4), sub, A.add)
+            tc(blk("ne", 0, LB - 1), vw(i))
+        lowest(i, key, vw(i))
+        ts(LA(i), blk("lo", i, LB - 1), OFF + ENC, A.add)
 
-    def lowest_p(i, key, zc, um, dum, sub):
-        for c in range(8):
-            ts(ref("ee", 1024 * i + 128 * c, 128 - 16 * c), ref(key[0], key[1] + 16 * c, 128 - 16 * c), zc(c), A.is_equal,
-               ref("cv", 80 + c, 1), A.mult)
-        pw = ref("ps1", 128 * i, 128) if i == 2 else ref("ps7", 256 + 128 * i, 128)
-
-        def fn(g, T):
-            for c in range(8):
-                last = g.tensor.matmul(ap(T, ref(pw[0], pw[1] + 16 * c, 128 - 16 * c)), ap(T, BOB), ap(T, ref("ee", 1024 * i + 128 * c, 128 - 16 * c)),
-                                       c == 0, c == 7)
-            return last
-        add("P", fn, [pw], [BOB, ref("ee", 1024 * i, 1024)], 672 * PEC + 60)
-        fd, fs = ref("fa", 256 * i, 128), ref("fa", 256 * i + 128, 128)
-        tt(fd, pw, ref("dg", 256, 128), A.is_lt)
-        scan(fs, RS, fd, 0.0, A.mult, A.add)
-        tt(w8(6 * i + 3), ref("fa", 256 * i + 128 + 15, 8, 16), um, A.mult)
-        tt(w8(6 * i + 4), w8(6 * i + 3), dum, A.max if sub is None else A.add)
-        tc(LA(i), w8(6 * i + 4))
-
-    def lowest_of(t, i, ve, dum):
-        xe = ref("xe", 128 * i, 128)
-        tt(xe, ind("ve", ve[1] - 3, ve[2], ref("eu", 8, 8)), DG, A.mult)
-        key = ref("ps2", 128 * i, 128)
-        if LOW[i] == "P":
-            mm([(key, [(BO, xe)])])
-            act(w8(6 * i + 1), ve, F.Identity, bias=ENC + OFF)
-            lowest_p(i, key, lambda c: ref(ve[0], ve[1] + 4 * c, 1), w8(6 * i + 1), cw(dum), None)
-            return
-        mm([(key, [(I16, JF), (BO, xe)])])
-        act(w8(6 * i), ve, F.Copy, scale=1048576.0)
-        if LOW[i] == "V":
-            tt(ref("l1", 48 * t + 16 * i, 8, 2), ve, cw(1), A.add)
-            lowest(t, i, key, w8(6 * i), None, None, 0.0, None)
-        else:
-            lowest(t, i, key, w8(6 * i), ve, ref("cv", 8 * dum, 8), ENC + OFF, lambda c: ref("cv", 8 + c, 1))
-
-    pL, pA, pB_, pC = [ref("ps1", 128 * i, 128) for i in range(4)]
+    pL, pY, pR, pM = [ref("ps1", 128 * i, 128) for i in range(4)]
 
     def step_a(t, z, la):
         h = lambda nm: ref(nm, 128 * z, 128)
         MW = ind("mt", 0, OFF + B + 384 * t, la)
-        act(h("gs"), MW, F.Identity, bias=col(25))
+        act(h("gs"), MW, F.Identity, bias=CGS)
         act(h("g32"), MW, F.Copy)
-        mm([(pL, [(DAL, h("gs"))]), (pB_, [(IP, h("gs")), (SHN, h("gs"))])])
-        if "e" in ONS:
-            act(h("e7"), pL, F.Relu, bias=-6.0)
-        else:
-            ts(h("e7"), pL, 7.0, A.is_equal)
-        tt(h("ub"), pB_, h("e7"), A.mult)
+        mm([(pL, [(DAL, h("gs"))])])
+        act(pL, pL, F.Relu, bias=1.0, scale=-1.0)
+        tt(h("yy"), pL, h("gs"), A.mult)
 
-    def step(t, z, la):
+    def step_b(t, z, la):
         base = B + 384 * t
         h = lambda nm: ref(nm, 128 * z, 128)
-        MW = ind("mt", 0, OFF + base, la)
-        cc_ = OFF + base + 128 * (z + 1)
-        if z == 1:
-            tt(ref("km", 128, 128), MW, ref("km", 0, 128), A.is_lt)
-            mm([(PK, [(BO, ref("km", 128, 128))])])
-            send(t)
-            act(h("md"), PK, F.Copy)
-            step_a(t, z, la)
-        tt(h("gk"), PKM, h("gs"), A.mult)
-        if z == 0:
-            mm([(PK, [(BOD, h("gk"))])])
-        tt(h("kq"), PKM, ref("tn", 128 * (2 * t + z), 128), A.mult)
-        mm([(pA, [(IMD, h("kq")), (IMDN, h("gk"))]), (pC, [(I16, CST), (SH, h("gs")), (SHN, h("gk")), (IP, h("kq"))])])
-        if "m" in ONS and z == 0:
-            act(h("md"), PK, F.Sign, bias=7.0, scale=-1.0)
-        elif z == 0:
-            ts(h("md"), PK, 7.0, A.not_equal)
-        tt(h("ua"), pA, h("e7"), A.mult)
-        tt(MW, h("g32"), h("ua"), A.add)
-        tt(pC, pC, h("ub"), A.add)
-        tt(ref("mt", cc_, 128), pC, h("md"), A.mult)
-        tt(ref("xt", cc_, 128), ind("xt", 0, OFF + base, la), h("md"), A.mult)
-        if t < RO - 1:
-            tc(ref("it", cc_, 128), ind("it", 0, OFF + base, la))
+        mm([(pY, [(DALN, h("gs")), (IBIG, h("kk"))])])
+        tt(h("w1"), pY, ref("tn", 128 * (2 * t + z), 128), A.min)
+        act(h("fl"), pY, F.Relu, scale=1.0 / BIG)
+        tt(ind("mt", 0, OFF + base, la), h("g32"), h("w1"), A.max)
+        mm([(pR, [(SH, h("gs")), (PMS, h("yy")), (BODP, h("fl"))]),
+            (pM, [(IP, ref("tc16", 128 * (2 * t + z), 128)), (IPB, h("kk")), (BODP, h("fl"))])])
+        act(h("t1"), pR, F.Relu, bias=CE0)
+        tt(ref("mt", OFF + base + 128 * (z + 1), 128), pM, h("t1"), A.max)
 
     sent = []
-
-    def send(t):
-        b2 = lambda i: ref("b2", 128 * i, 128)
-        scan(PC, PK, ref("rs", 128, 128), -1.0, A.add, A.add)
-        tt(b2(1), PK, DG, A.mult)
-        tt(b2(2), PC, b2(1), A.mult)
-        scan(b2(3), ref("rs", 256, 128), b2(2), 128.0, A.min, A.add)
-        tc(LA(3), ref("b2", 384 + 15, 8, 16))
-        sn_, rc_, lo = box[t]
-        tc(ind(sn_, lo, lo + 256, LA(3)), ref("q1", 0, 128))
-        rid, pid, mask = rank_peers[t]
-        so, ro = ref(sn_, lo + 128, 64), ref(rc_, lo + 128, 64)
-        add("G", lambda g, T: g.remote_dma(ap(T, ro), ap(T, so), T.sem["arr%d" % t], T.sem["snt%d" % t], pid, rid, mask),
-            [], [so], 200.0, lat=2000.0, sem="snt%d" % t, inc=NENG)
-        sent.append(len(ops) - 1)
-        add("G", lambda g, T: None, [ro], [so], 1.0, lat=2700.0, sem="arr%d" % t, inc=NENG)
 
     def writers(t):
         base = B + 384 * t
         q = ref("qh", 0, 128)
-        ve, lv = ref("ve", 192 + 3, 8, 4), ref("lv", 48, 8)
+        lv = ref("lv", 48, 8)
         nn = OFF + base
-        lowest_of(t, 1, ve, 0)
-        tc(ref("wi", 0, 8), ref("pm", 3, 8, 4))
-        ts(ref("wi", 8, 8), ref("wi", 0, 8), 3, A.bitwise_and)
-        xk = ref("xe", 256, 128)
-        tt(xk, ind("wi", 8, 16, EU), DG, A.mult)
-        pI, pk = pL, pB_
-        mm([(pk, [(BO, xk)]), (pI, [(BO4, ref("xe", 0, 128)), (BO, xk)])])
-        ts(PKM, pk, CA, A.is_equal)
+        lowest_of(t, 1, lv)
+        xk = ref("xk", 0, 128)
+        tt(xk, ind("vw", 144, 216, ref("eu", 0, 8)), DG, A.mult)
+        pk, pI, pmd = [ref("ps0", 128 * i, 128) for i in (1, 2, 3)]
+        mm([(pk, [(BO, xk)]), (pI, [(I4, ref("ky", 0, 128)), (BO, xk)])])
         ts(ref("it", nn, 128), pI, 4 * ENC, A.add)
+        ts(ref("kk", 0, 128), pk, CA, A.is_equal)
         act(ref("mt", nn, 128), ind("mt", OFF, OFF + base, lv), F.Copy)
         if "x" in ONS:
             act(ref("xt", nn, 128), q, F.Identity, bias=-QO)
         else:
             ts(ref("xt", nn, 128), q, -QO, A.add)
         if t < RO - 1:
-            act(ref("q1", 0, 128), q, F.Identity, bias=-QO - 1024.0)
+            act(ref("q1", 0, 128), q, F.Identity, bias=-QO - 256.0)
         else:
             act(ref("q1", 0, 128), q, F.Identity, scale=-1.0, bias=QO)
-        if CHUNKS[0][3] in "VM":
-            tt(ref("s32", 0, 128), ind("xt", OFF, OFF + base, lv), q, A.add)
-            ts(ref("mxi", 0, 128), ref("s32", 0, 128), 0.5, A.mult, -QO / 2 - 0.25, A.add)
-        else:
-            mm([(PC, [(IH, q), (IBH, ref("xg", 0, 128))])])
-            ts(ref("mxi", 0, 128), PC, -QO / 2 - 0.25, A.add)
-        tc(ind("it", 0, OFF + base, LA(1)), ref("it", nn, 128))
-        tc(ind("xt", 0, OFF + base, LA(1)), ref("mxi", 0, 128))
+        PC = ref("ps7", 128, 128)
+        mm([(PC, [(IH, q), (IBH, ref("xg", 0, 128))])])
+        ts(ref("mxi", 0, 128), PC, -QO / 2 - 0.25, A.add)
+        tc(ind("it", 0, nn, LA(1)), ref("it", nn, 128))
+        tc(ind("xt", 0, nn, LA(1)), ref("mxi", 0, 128))
         sn = SN * (t + 1)
         if t < RO - 1:
             dma("Y", (lambda T: [(T.xs[:, sn:sn + base], T.xt[:, OFF:nn])], 1), [ref("xs", sn, base)], [ref("xt", OFF, base)], 256 * base)
-        step(t, 0, LA(0))
-        ib = ind("it", 0, OFF + base, LA(0))
-        b1 = lambda i: ref("b1", 128 * i, 128)
-        ts(ref("ui", 0, 128), ib, 2, A.logical_shift_right)
-        ts(ref("ui", 128, 128), ib if t == RO - 1 else ref("it", nn + 128, 128), 3, A.bitwise_and)
-        ts(PKM, ref("ui", 128, 128), CA, A.is_equal)
-        ts(ref("km", 0, 128), ref("ui", 128, 128), CA, A.is_equal, col(26), A.mult)
-        ts(PB, PK, 7.0, A.not_equal)
-        tt(b1(0), PB, ref("c2", 256 * t, 128), A.mult)
-        tt(b1(1), ref("c2", 256 * t + 128, 128), b1(0), A.subtract)
-        tt(PB, PB, ref("ui", 0, 128), A.mult)
-        tt(PB, PB, b1(1), A.add)
-        kw = ref("b1", 512 + 15, 8, 16)
-        if LOW[2] == "P":
-            tt(b1(3), PB, DG, A.mult)
-            scan(b1(4), RS, b1(3), 0.0, A.mult, A.add)
-            lowest_p(2, PB, lambda c: ref("b1", 512 + 15 + 16 * c, 1), kw, ref("cv", 8 * (6 + t), 8), None)
-        else:
-            tt(b1(3), PB, ref("dg", 128, 128), A.mult)
-            scan(b1(4), ref("rs", 384, 128), b1(3), 0.0, A.min, A.add)
-            ts(w8(12), kw, 1.0 / 1048576, A.mult)
-            tt(ref("l1", 48 * t + 32, 8, 2), w8(12), cw(2), A.add)
-            lowest(t, 2, PB, kw, None, None, -262144.0, None)
-        step(t, 1, LA(2))
+        step_b(t, 0, LA(0))
+        act(ref("xt", nn + 128, 128), ind("xt", 0, nn, LA(4)), F.Copy)
+        ib = ind("it", 0, nn, LA(4))
+        tt(ref("dm", 0, 128), ib, DG, A.mult)
+        ts(ref("k2", 0, 128), ib, 0.25, A.mult, OFF - 0.375, A.add)
+        ts(ref("ui", 0, 128), ib, 3, A.bitwise_and)
+        scan(ref("dn", 0, 128), ref("d1", 0, 128), ref("dm", 0, 128), 0.0, A.mult, A.add)
+        ts(LA(5), ref("dn", 15, 8, 16), 0.25, A.mult, OFF - 0.375, A.add)
+        own = ref("w8", 16, 8)
+        tc(own, LA(5))
+        ts(ref("km", 0, 128), ref("ui", 0, 128), CAD, A.not_equal, 2 * BIG, A.mult)
+        aff(blk("dz", 0, LB - 1), cw(0), 0.0, 0.0)
+        aff(blk("ne", 0, LB - 1), cw(0), 1.0, 128.0)
+        lowest(2, ref("k2", 0, 128), own)
+        tt(ref("kf", 0, 128), ind("mt", 0, nn, LA(5)), ref("km", 0, 128), A.is_gt)
+        pF, pos = ref("ps2", 256, 8), ref("ps2", 272, 8)
+        mm([(pF, [(ref("mz", 15 - s, 128), ref("kf", s, 8, 16)) for s in range(16)])])
+        f, f2 = ref("f8", 0, 8), ref("f8", 8, 8)
+        tt(f, pF, blk("lo", 2, LB - 2), A.min)
+        tt(f2, pF, blk("lo", 2, LB - 1), A.mult)
+        mm([(pos, [(I16, ref("c9", 48, 8)), (LQ, f)] + [(BOQ, ref("f8", 0, 8 - d), ref("ps2", 272 + d, 8 - d)) for d in range(1, 8)] + [(INQ, f2)])])
+        tc(LA(3), pos)
+        tc(ind("snd", BX * t, BX * t + BX, LA(3)), ref("q1", 0, 128))
+        rid, pid, mask = rank_peers[t]
+        so, ro = ref("snd", BX * t, 64), ref("rcv", BX * t, 64)
+        add("G", lambda g, T: g.remote_dma(ap(T, ro), ap(T, so), T.sem["arr%d" % t], T.sem["snt%d" % t], pid, rid, mask),
+            [], [so], 200.0, lat=2000.0, sem="snt%d" % t, inc=NENG)
+        sent.append(len(ops) - 1)
+        add("G", lambda g, T: None, [ro], [so], 1.0, lat=2700.0, sem="arr%d" % t, inc=NENG)
+        w8 = lambda i: ref("w8", 8 * i, 8)
+        tt(w8(0), own, blk("lo", 2, LB - 2), A.min)
+        tt(w8(1), w8(0), cw(4 + t), A.max)
+        tc(LA(2), w8(1))
+        ts(ref("kk", 128, 128), ref("ui", 0, 128), CA, A.is_equal)
         if t < RO - 1:
+            tc(ref("it", nn + 128, 128), ib)
+        step_a(t, 1, LA(2))
+        step_b(t, 1, LA(2))
+        mm([(pmd, [(BOD, ref("fl", 128, 128))])])
+        act(ref("md", 0, 128), pmd, F.Identity, scale=-1.0, bias=1.0)
+        tt(ref("xt", nn + 256, 128), ind("xt", 0, nn, LA(2)), ref("md", 0, 128), A.mult)
+        if t < RO - 1:
+            tc(ref("it", nn + 256, 128), ind("it", 0, nn, LA(2)))
             news = [sn + base] + ([sn + SN + base] if t == 0 else [])
+            dma("Y", (lambda T: [(T.xs[:, sn + base:sn + base + 384], T.xt[:, nn:nn + 384])], 1), [ref("xs", sn + base, 384)], [ref("xt", nn, 384)], 98304)
             dma("Y", (lambda T: [(T.mn[r::4, sn:sn + base], T.mt[r::4, OFF:nn]) for r in (1, 2)]
-                      + [(T.mn[:, x:x + 384], T.mt[:, nn:nn + 384]) for x in news] + [(T.xs[:, sn + base:sn + base + 384], T.xt[:, nn:nn + 384])],
-                      3 + len(news)),
-                [ref("mn", sn, base), ref("xs", sn + base, 384)] + [ref("mn", x, 384) for x in news],
-                [ref("mt", OFF, base + 384), ref("xt", nn, 384)], 256 * base + 300000)
+                      + [(T.mn[:, x:x + 384], T.mt[:, nn:nn + 384]) for x in news], 2 + len(news)),
+                [ref("mn", sn, base)] + [ref("mn", x, 384) for x in news], [ref("mt", OFF, base + 384)], 256 * base + 200000)
             ops[-1]["after"] = [sent[t]]
-        tt(ref("sh", 0, 128), ind(box[t][1], box[t][2], box[t][2] + 256, LA(3)), q if t < RO - 1 else ref("xt", nn, 128), A.min)
-        if t < RO - 1:
-            ts(ref("rr", 0, 128), ref("sh", 0, 128), 0.0, A.is_lt, QO + 1024.0, A.mult)
-            tt(q, ref("rr", 0, 128), ref("sh", 0, 128), A.add)
-        else:
-            act(ref("qo", 0, 128), ref("sh", 0, 128), F.Abs)
+        sh = ref("sh", 0, 128)
+        tt(sh, ind("rcv", BX * t, BX * t + BX, LA(3)), q if t < RO - 1 else ref("xt", nn, 128), A.min)
+        if t == RO - 1:
+            act(ref("qo", 0, 128), sh, F.Abs)
             dma("S", (lambda T: [(T.yq[:, 0:128], T.qo[:, 0:128])], 1), [], [ref("qo", 0, 128)], 32768)
+        elif "r" in ONS:
+            act(ref("rr", 0, 128), sh, F.Sign)
+            mm([(PC, [(I16, sh), (IS, ref("rr", 0, 128))])])
+            act(q, PC, F.Identity, bias=768.0)
+        else:
+            ts(ref("rr", 0, 128), sh, 0.0, A.is_lt, QO + 256.0, A.mult)
+            tt(q, ref("rr", 0, 128), sh, A.add)
 
     for t in range(RO):
         for i, (c0, n, routes, qroute) in enumerate(CHUNKS):
@@ -613,25 +587,18 @@ def depends(ops):
     hist = {}
     for i, o in enumerate(ops):
         dep = set(o.get("after", ()))
-        raw = set()
         for acc, regs in ((0, o["rd"]), (1, o["wr"])):
-            for nm, lo, hi in regs:
+            for nm, cols in regs:
                 ps = SCRATCH[nm][0] == "psum"
-                for j, w, l2, h2 in hist.get(nm, ()):
-                    if j == i:
-                        continue
-                    if (l2 < hi and lo < h2 and (w or acc)) or (ps and ops[j]["e"] != o["e"]):
+                for j, w, c2 in hist.get(nm, ()):
+                    if j != i and ((cols & c2 and (w or acc)) or (ps and ops[j]["e"] != o["e"])):
                         dep.add(j)
-                        if w and not (acc and INORDER > 1):
-                            raw.add(j)
-        if INORDER and o["e"] in "VSP" and not o["sem"]:
-            o["free"] = list(o.get("free", ())) + [j for j in dep if j not in raw and ops[j]["e"] == o["e"] and not ops[j]["sem"]]
         for acc, regs in ((0, o["rd"]), (1, o["wr"])):
-            for nm, lo, hi in regs:
+            for nm, cols in regs:
                 h = hist.setdefault(nm, [])
                 if acc:
-                    h[:] = [x for x in h if not (lo <= x[2] and x[3] <= hi)]
-                h.append((i, acc, lo, hi))
+                    h[:] = [x for x in h if x[2] & ~cols]
+                h.append((i, acc, cols))
         o["dep"] = sorted(dep)
 
 

@@ -6,52 +6,60 @@ OFF = 896
 ENC = 1152.0
 QO = 1280.0
 BIG = 4096.0
-LB = 131
-MG = 12582912.0
+LB = 132
 BX = 384
 
 SN = 2816
-CHUNKS = [(0, 128, "AAAD", "S"), (128, 320, "ADDD", "T"), (448, 320, "AADD", "T")]
+CHUNKS = [(0, 128, ["AAADMS"], ["AAAASS"]), (128, 320, ["ADDDMS"], ["AADDMS"]), (448, 320, ["ADDDMS"], ["ADDDMS"])]
+BANKS = ["07", "35", "46"]
+JOIN = "R"
 KS = [(0, 4)]
-ONS = "xvr"
-SEED, JIT, LOOK, PASSES = 3, 200.0, 0.4, 6
-PIECE = 4
+ONS = "xvro"
+SEED, JIT, LOOK, PASSES = 3, 200.0, 0.3, 6
+PIECE, NV = 4, 4
+AHEAD, WEIGH = 1000.0, {"S": 1.0, "V": 4.0}
+ONV, ONS2 = "cb_ cw_ dz_ kf_ mb16_ mm_ qh00 qh10 qh11 qh20 qo11 xt1".split(), "fl1 g1621 qh21 qh_ qo21".split()
 NENG = 16
-CY, PEC, GAM, SCA = 0.92, 0.45, 1.55, 3.8
+CY, PEC, GAM, SCA, TTG = 1.0, 0.49, 1.55, 3.8, 0.0
 HOP, SELF, SFIX = 185.0, 220.0, 45.0
+DFIX, DRATE, XLAT = 1300.0, 280.0, 1800.0
 
 f32, bf, f16, i32, u16 = "float32", "bfloat16", "float16", "int32", "uint16"
 SCRATCH = {
-    "xt": ("sbuf", [128, OFF + W], bf), "mt": ("sbuf", [128, OFF + W], f32), "it": ("sbuf", [128, OFF + W], i32),
-    "xs": ("sbuf", [128, 3 * SN], bf), "mn": ("sbuf", [128, 3 * SN], f32), "nt": ("sbuf", [128, SN], f32),
+    "xt": ("sbuf", [128, OFF + W], bf), "mt": ("sbuf", [128, OFF + W], f32),
+    "xs": ("sbuf", [128, 3 * SN], bf), "mn": ("sbuf", [128, SN], f32), "nt": ("sbuf", [128, SN], f32),
     "mi": ("sbuf", [128, B], i32), "sti": ("sbuf", [128, 48], i32), "stu": ("sbuf", [128, 48], u16),
     "qb": ("sbuf", [128, R], bf), "qh": ("sbuf", [128, R], f16), "qo": ("sbuf", [128, R], bf),
     "snd": ("sbuf", [128, 3 * BX], bf), "rcv": ("sbuf", [128, 3 * BX], bf),
-    "ci": ("sbuf", [128, 144], bf), "c4": ("sbuf", [128, 144], bf), "c16": ("sbuf", [128, 128], bf), "j16": ("sbuf", [128, 128], bf),
-    "pi": ("sbuf", [128, 8], i32), "ei": ("sbuf", [128, 8], i32), "eu": ("sbuf", [128, 8], u16),
-    "col": ("sbuf", [128, 64], f32), "cw": ("sbuf", [128, 128], f32), "c9": ("sbuf", [128, 64], f16),
-    "mz": ("sbuf", [128, 2 * 144], bf), "mz4": ("sbuf", [128, 144], f16), "my": ("sbuf", [128, 9 * 144], f16),
-    "mm": ("sbuf", [128, 18 * 128], f16), "mb16": ("sbuf", [128, 2 * 128], bf),
-    "dg": ("sbuf", [128, 256], f32), "kt16": ("sbuf", [128, 80], bf), "ktw": ("sbuf", [128, 72], bf), "x9": ("sbuf", [128, 4 * 72], f32),
-    "tn": ("sbuf", [128, 6 * 128], f32), "tc16": ("sbuf", [128, 6 * 128], f16), "jb": ("sbuf", [128, 8 * LB], bf),
+    "ci": ("sbuf", [128, 144], bf), "c4": ("sbuf", [128, 144], bf), "c16": ("sbuf", [128, 128], bf), "j16": ("sbuf", [128, 128], bf), "cp": ("sbuf", [128, 256], bf),
+    "pi": ("sbuf", [128, 8], i32), "ei": ("sbuf", [128, 8], i32), "eu": ("sbuf", [128, 16], u16),
+    "col": ("sbuf", [128, 64], f32), "cw": ("sbuf", [128, 128], f32), "c9": ("sbuf", [128, 48], f16), "cb": ("sbuf", [128, 8], bf),
+    "mz": ("sbuf", [128, 3 * 144], bf), "mz4": ("sbuf", [128, 3 * 144], f16), "my": ("sbuf", [128, 9 * 144], f16),
+    "mm": ("sbuf", [128, 22 * 128], f16), "mb16": ("sbuf", [128, 6 * 128], bf),
+    "dg": ("sbuf", [128, 256], f32), "kt16": ("sbuf", [128, 160], bf), "ktw": ("sbuf", [128, 72], bf), "x9": ("sbuf", [128, 4 * 72], f32),
+    "tc16": ("sbuf", [128, 6 * 128], f16), "jb": ("sbuf", [128, 8 * LB], bf),
     "dz": ("sbuf", [128, 8 * LB], f16), "ne": ("sbuf", [128, 8 * LB], f16), "lo": ("sbuf", [128, 3 * 8 * LB], f16),
     "g16": ("sbuf", [128, R], f16), "ti": ("sbuf", [128, 192], i32), "tau": ("sbuf", [128, 192], f32),
     "cc": ("sbuf", [128, 384], f32), "t16": ("sbuf", [128, 448], f16), "ou": ("sbuf", [128, 192], u16),
-    "dd": ("sbuf", [128, 4 * R], f16), "xr": ("sbuf", [128, 4 * R], bf),
-    "ab0": ("sbuf", [128, 8, 9, 8], bf), "ab1": ("sbuf", [128, 20, 4, 16], bf), "ab2": ("sbuf", [128, 20, 4, 16], bf),
-    "pm": ("sbuf", [128, 272], f32), "rk": ("sbuf", [128, 152], f32), "eq": ("sbuf", [128, 192], f32), "eqw": ("sbuf", [128, 72], f32),
+    "dd": ("sbuf", [128, 4 * L], f16), "xr": ("sbuf", [128, 4 * R], bf), "ab0": ("sbuf", [128, 8, 9, 8], bf),
+    "pm": ("sbuf", [128, 272], f32), "rk": ("sbuf", [128, 240], f32), "eq": ("sbuf", [128, 192], f32), "eqw": ("sbuf", [128, 72], f32),
     "ve": ("sbuf", [128, 384], f32), "vw": ("sbuf", [128, 4 * 72], f32), "lv": ("sbuf", [128, 96], u16),
     "xg": ("sbuf", [128, R], bf), "sh": ("sbuf", [128, R], f16),
-    "ky": ("sbuf", [128, 256], f16), "k2": ("sbuf", [128, 128], u16), "xk": ("sbuf", [128, 128], f16), "la": ("sbuf", [128, 48], u16),
-    "w8": ("sbuf", [128, 64], f32), "f8": ("sbuf", [128, 16], f16), "mxi": ("sbuf", [128, 128], i32),
-    "dm": ("sbuf", [128, 128], f32), "d1": ("sbuf", [128, 128], f32), "dn": ("sbuf", [128, 128], f32),
+    "ky": ("sbuf", [128, 384], f16), "xk": ("sbuf", [128, 128], f16), "la": ("sbuf", [128, 48], u16),
+    "f8": ("sbuf", [128, 16], bf), "xf": ("sbuf", [128, 128], bf), "mxi": ("sbuf", [128, 128], i32), "dm": ("sbuf", [128, 128], f32),
+    "gv": ("sbuf", [128, 128], f16), "gi": ("sbuf", [128, 128], f16),
+    "ic": ("sbuf", [128, 128], i32), "ij": ("sbuf", [128, 256], i32), "iu": ("sbuf", [128, 256], f32),
     "km": ("sbuf", [128, 128], f32), "kf": ("sbuf", [128, 128], bf), "kk": ("sbuf", [128, 256], f16), "gs": ("sbuf", [128, 256], f16),
     "g32": ("sbuf", [128, 256], f32), "yy": ("sbuf", [128, 256], f16), "w1": ("sbuf", [128, 256], f32), "fl": ("sbuf", [128, 256], f16),
-    "t1": ("sbuf", [128, 256], f32), "md": ("sbuf", [128, 128], f32), "ui": ("sbuf", [128, 128], i32),
+    "t1": ("sbuf", [128, 256], f32), "md": ("sbuf", [128, 128], f32),
     "q1": ("sbuf", [128, 128], bf), "rr": ("sbuf", [128, 128], f16),
 }
 for _b in range(8):
     SCRATCH["ps%d" % _b] = ("psum", [128, 512], f32)
+for _b in range(1, len(CHUNKS)):
+    SCRATCH["ab%d" % _b] = ("sbuf", [128, CHUNKS[_b][1], 4], bf)
+    for _r in range(2):
+        SCRATCH["dd%d%d" % (_b, _r)] = ("sbuf", [128, CHUNKS[_b][1], 4], f16)
 NDMA = 40
 SEMAPHORES = ["cV", "cS", "cP", "cG", "snt0", "snt1", "snt2", "arr0", "arr1", "arr2"] + ["d%d" % _i for _i in range(NDMA)]
 TWO = (bf, f16, u16)
@@ -61,23 +69,23 @@ al = slice(None)
 
 
 def bits(lo, n, step=1):
-    if step == 1:
-        return ((1 << n) - 1) << lo
-    return sum(1 << (lo + i * step) for i in range(n))
+    return ((1 << (n * step)) - 1) // ((1 << step) - 1) << lo
 
 
 def build(rank_peers):
     ops = []
-    ndma = [0]
+    ndma, tag = [0], ["_"]
 
     def ref(name, lo, n, step=1):
         return (name, lo, lo + (n - 1) * step + 1, step)
 
     def view(name, *idx):
-        cols = [0]
-        for d, x in zip(SCRATCH[name][1][1:], idx):
-            cols = [c * d + j for c in cols for j in (range(d)[x] if isinstance(x, slice) else [x])]
-        return (name, sum(1 << c for c in cols), None, None, len(cols), (al,) + idx)
+        cols, n, size = 1, 1, 1
+        for d, x in list(zip(SCRATCH[name][1][1:], idx))[::-1]:
+            r = range(d)[x] if isinstance(x, slice) else range(x, x + 1)
+            cols *= bits(r.start * size, len(r), r.step * size)
+            n, size = n * len(r), size * d
+        return (name, cols, None, None, n, (al,) + idx)
 
     def ind(name, lo, hi, off):
         return ("*", name, lo, hi, off)
@@ -128,7 +136,7 @@ def build(rank_peers):
         if out[0] == "*":
             return 50 + SCA * n * CY
         if ins[0][0] == "*":
-            return 50 + GAM * n * CY
+            return 50 + max(GAM, TTG * (rate == 2)) * n * CY
         return max(64, n * rate) * CY
 
     def half(*rs):
@@ -158,6 +166,21 @@ def build(rank_peers):
     def act(out, a, func, bias=0.0, scale=1.0):
         c = 65 + GAM * nel(out) * CY if a[0] == "*" else max(64, nel(out)) * CY + SFIX
         add("S", lambda g, T: g.scalar.activation(ap(T, out), ap(T, a), func, bias=ap(T, bias), scale=ap(T, scale)), [out], [a, bias, scale], c)
+        if func == F.Copy:
+            tc(out, a)
+        elif func == F.Identity:
+            ts(out, a, scale, A.mult, bias, A.add)
+        elif func == F.Relu and scale == 1.0:
+            ts(out, a, bias, A.add, 0.0, A.max)
+        else:
+            return
+        v = ops.pop()
+        name = out[0] + tag[0]
+        ops[-1]["name"] = name
+        if name in ONV:
+            ops[-1].update(e="V", fn=v["fn"], c=v["c"])
+        elif name not in ONS2:
+            ops[-1]["alt"] = {"S": (ops[-1]["fn"], c), "V": (v["fn"], v["c"])}
 
     def mm(groups, piece=99):
         calls = [(x[2] if len(x) > 2 else out, x[0], x[1], i == 0, i == len(terms) - 1) for out, terms in groups for i, x in enumerate(terms)]
@@ -189,7 +212,7 @@ def build(rank_peers):
             for o, i in pairs[0](T):
                 e.dma_start(o, i).then_inc(T.sem[sem], 16)
             return None
-        add(q, fn, out, ins, 60.0 * n, lat=1800 + nbytes / 180.0, sem=sem, inc=16 * n)
+        add(q, fn, out, ins, 60.0 * n, lat=DFIX + nbytes / DRATE, sem=sem, inc=16 * n)
 
     col = lambda c: ref("col", c, 1)
     aff = lambda o, a, s, b: act(o, a, F.Identity, scale=s, bias=b)
@@ -197,21 +220,22 @@ def build(rank_peers):
     dma("Y", (lambda T: [(T.mi[0::4, :], T.pf[:]), (T.mi[1::4, :], T.mb[:])], 2), [ref("mi", B // 2, B // 2)], [], 1 << 20)
     dma("Y", (lambda T: [(T.sti[:], T.st[:]), (T.qb[:], T.qr[:])], 2), [ref("sti", 0, 48), ref("qb", 0, R)], [], 400000)
     dma("S", (lambda T: [(T.xt[:, OFF:OFF + B], T.xn[:])], 1), [ref("xt", OFF, B)], [], 1100000)
-    dma("Y", (lambda T: [(T.xs[:, 0:B], T.xn[:])], 1), [ref("xs", 0, B)], [], 1 << 19)
+    dma("Y", (lambda T: [(T.ic[:], T.ip[:])], 1), [ref("ic", 0, 128)], [], 1100000)
+    dma("Y", (lambda T: [(T.xs[:, 0:B], T.xn[:])], 1), [ref("xs", 0, B)], [], 600000)
     ops[-1]["after"] = [1]
-    dma("Y", (lambda T: [(T.it[r::16, OFF:OFF + B], T.ip[:]) for r in range(16)], 16), [ref("it", OFF, B)], [], 3 << 19)
-    ops[-1]["after"] = [1, len(ops) - 2]
     iota(ref("pi", 0, 1), [[0, 1]], 0, 1)
     iota(ref("ci", 0, 144), [[1, 144]], 0, 0)
     iota(ref("c4", 0, 144), [[1, 36], [0, 4]], 0, 0)
     iota(ref("j16", 0, 128), [[0, 8], [1, 16]], 0, 0)
     iota(ref("c16", 0, 128), [[1, 8], [0, 16]], 0, 0)
+    iota(ref("cp", 0, 128), [[1, 8], [0, 4], [64, 4]], 0, 0)
+    iota(ref("cp", 128, 128), [[1, 8], [16, 16]], -112, 0)
     iota(ref("ei", 0, 8), [[1, 8]], 0, 0)
-    iota(ref("kt16", 0, 80), [[0, 20], [1, 4]], 0, 0)
+    R4 = max(c[1] for c in CHUNKS) // 4
+    iota(ref("kt16", 0, R4), [[0, R4 // 4], [1, 4]], 0, 0)
     iota(ref("x9", 0, 72), [[0, 8], [1, 9]], 0, 0)
     iota(ref("jb", 0, 8 * LB), [[-16, 8], [1, LB]], -1, 0)
     iota(ref("nt", 0, B), [[1, B]], -int(ENC), 0)
-    iota(ref("it", 0, 768), [[1024, 3], [0, 2], [4, 128]], 4 * (128 - OFF), 0)
     iota(ref("nt", B, SN - B), [[1, SN - B]], B - int(ENC), 0)
     iota(ref("cc", 0, 384), [[0, 384]], 0, 0)
     p0 = ref("pi", 0, 1)
@@ -227,13 +251,17 @@ def build(rank_peers):
     T0, T1, T2, T3 = [col(8 + i) for i in range(4)]
     ts(col(12), CG16, CA, A.add, 12.0, A.add)
     tt(col(13), T1, T0, A.subtract)
-    CPM, CGS, CG, CSG, C7, CE0, CAD = [col(14)] + [col(24 + i) for i in range(6)]
+    CPM, CGS, CG, CSG, C7, CGN, CAD = [col(14)] + [col(24 + i) for i in range(6)]
+    CU, CK = col(18), col(19)
     ts(CPM, CTY, 1.5, A.is_lt)
-    ts(CGS, CTY, 1.5, A.is_lt, -ENC, A.mult)
+    ts(CU, CS, 3.0, A.is_equal)
+    ts(CK, CS, 7.0, A.is_equal)
+    ts(col(22), CU, OFF + ENC, A.mult)
+    ts(CGN, CPM, ENC, A.mult, col(22), A.add)
+    ts(CGS, CGN, -1.0, A.mult)
     ts(C7, T2, 7.0, A.mult)
     tt(CG, CGS, C7, A.subtract)
     tt(CSG, CPM, T2, A.subtract)
-    ts(CE0, T0, ENC, A.mult)
     ts(col(30), CA, 1.0, A.add, T2, A.mult)
     ts(CAD, col(30), -1.0, A.add)
     ts(col(15), CG16, 0.25, A.mult, 3.0, A.add)
@@ -243,7 +271,7 @@ def build(rank_peers):
     tt(ref("col", 40, 3), ref("col", 8, 3), ref("col", 9, 3), A.subtract)
     for k in range(3):
         ts(ref("my", 144 * (5 + k), 140), ref("ci", 0, 140), col(12), A.is_equal, col(40 + k), A.mult)
-    ts(ref("rk", 0, 80), ref("kt16", 0, 80), 0.0, A.is_equal, 1.0e6, A.mult)
+    ts(ref("rk", 80, R4), ref("kt16", 0, R4), 0.0, A.is_equal, 1.0e6, A.mult)
     ts(ref("my", 144 * 8, 140), ref("my", 144 * 2, 140), 0.25, A.mult)
     ts(ref("mz4", 0, 140), ref("c4", 0, 140), col(15), A.is_equal, 0.25, A.mult)
     ts(col(16), CG16, 15.0, A.add)
@@ -253,34 +281,54 @@ def build(rank_peers):
     M = lambda i: ref("mm", 128 * i, 128)
     ci, c16 = ref("ci", 0, 128), ref("c16", 0, 128)
     ts(ref("mb16", 0, 128), ci, CP, A.is_equal)
-    ts(ref("mb16", 128, 128), ci, CP, A.is_equal, 0.5, A.mult)
-    IB, IBH = ref("mb16", 0, 128), ref("mb16", 128, 128)
-    INEG, IH, I16, I4, IBIG, INQ, BO, BOQ, BOD, DAL, DALN, IP, IPB, SH, PMS, BODP, LQ, IS = [M(i) for i in range(18)]
-    for m_, c in ((INEG, -1.0), (IH, 0.5), (I16, 1.0), (I4, 4.0), (IBIG, BIG), (INQ, -0.25), (IP, T0), (IS, -768.0)):
-        ts(m_, ci, CP, A.is_equal, c, A.mult)
+    IB, IBH, INQ, BOQ, LQ, BOP = [ref("mb16", 128 * i, 128) for i in range(6)]
+    INEG, IH, I16, BO, DAL, DX, IP, IPB, SH, PMS, BODP, IS, NB, IK3, IT3, IU, IM, IMD, BU, BK, BOK = [M(i) for i in range(21)]
+    iota(NB, [[0, 128]], -int(BIG), 0)
+    if any("R" in x for c in CHUNKS for w in c[2:] for x in w):
+        aff(ref("mz", 288, 143), ref("mz", 0, 143), 2.0, 0.0)
+        aff(ref("mz4", 144, 143), ref("mz", 0, 143), -1.0, 0.0)
     ts(col(17), CG16, 0.0625, A.mult)
-    for m_, c in ((BO, 1.0), (BOQ, 0.25), (BOD, T2)):
-        ts(m_, c16, col(17), A.is_equal, c, A.mult)
+    ts(BO, c16, col(17), A.is_equal)
     ts(DAL, ref("c4", 0, 128), CP4, A.is_equal, T2, A.mult)
-    ts(DALN, DAL, -BIG, A.mult)
-    ts(IPB, IP, BIG, A.mult)
-    ts(col(20), CP, -1.0, A.add)
+    tt(col(20), CP, T1, A.subtract)
     ts(SH, ci, col(20), A.is_equal, T1, A.mult)
-    tt(PMS, IP, SH, A.subtract)
-    fill(ref("km", 0, 128), 0.0)
-    fill(ref("km", 0, 32, 4), -BIG)
-    tt(BODP, BOD, ref("km", 0, 128), A.mult)
-    ts(ref("kf", 0, 128), ci, CP, A.is_gt)
-    tt(LQ, BOQ, ref("kf", 0, 128), A.mult)
+    ts(PMS, ci, col(20), A.is_equal, col(40), A.mult)
+    aff(col(21), T2, -BIG, 0.0)
+    ts(BODP, ref("cp", 0, 128), col(17), A.is_equal, col(21), A.mult)
+    ts(BOP, ref("cp", 0, 128), col(17), A.is_equal, BIG / 4, A.mult)
+    ts(BOK, ref("cp", 128, 128), col(17), A.is_equal)
+    aff(BOQ, BO, 0.25, 0.0)
+    add("G", lambda g, T: g.affine_select(ap(T, LQ), ap(T, BOQ), [[1, 128]], A.is_gt, 0.0, 0, -1), [LQ], [BOQ], 170 + 256 * CY)
     DG = ref("dg", 0, 128)
     ts(DG, ref("j16", 0, 128), CS, A.is_equal)
     ts(ref("eu", 0, 8), ref("ei", 0, 8), 9.0, A.mult, 7.0, A.add)
+    tc(ref("eu", 8, 8), ref("ei", 0, 8))
+    aff(col(36), T0, ENC, col(22))
+    aff(col(37), T0, ENC - BIG, col(22))
+    aff(col(38), T1, -ENC, 0.0)
+    aff(col(39), CU, ENC, 0.0)
+    aff(col(44), T3, -1.0, 1.0)
+    aff(col(45), T1, BIG, 0.0)
+    aff(col(46), T2, BIG, col(45))
+    aff(col(47), T0, BIG, 0.0)
+    rows = [(INEG, -1.0), (IH, 0.5), (IBH, 0.5), (I16, 1.0), (IP, T0), (IM, T1), (IPB, col(47)), (IMD, col(46)), (IK3, col(44)), (IT3, T3), (IU, CU),
+            (INQ, -0.25), (IS, -QO / 2)]
+    for i, (m_, c) in enumerate(rows):
+        if i < NV:
+            ts(m_, ci, CP, A.is_equal, c, A.mult)
+        else:
+            aff(m_, IB, c, 0.0)
+    for m_, c in ((BU, CU), (BK, CK)):
+        aff(m_, BO, c, 0.0)
+    aff(ref("kf", 0, 128), DAL, -BIG, 0.0)
+    tt(DX, ref("kf", 0, 128), IM, A.subtract)
+    ts(ref("mz4", 288, 143), ref("ci", 0, 143), col(16), A.is_equal, CU, A.mult)
     cw = lambda i: ref("cw", 8 * i, 8)
     ts(cw(0), ref("ei", 0, 8), 16.0, A.mult, CS, A.add)
     ts(col(31), CH, 4.0, A.mult)
     ts(col(32), CH, 4.0, A.mult, 3.0, A.add)
     x9 = lambda i: ref("x9", 72 * i, 72)
-    ts(ref("rk", 80, 72), x9(0), 0.0, A.is_equal, 1.0e6, A.mult)
+    ts(ref("rk", 0, 72), x9(0), 0.0, A.is_equal, 1.0e6, A.mult)
     ts(x9(1), x9(0), col(32), A.is_equal, 4.0, A.mult)
     ts(x9(2), x9(0), col(31), A.is_ge)
     ts(x9(3), x9(0), col(32), A.is_gt)
@@ -292,24 +340,28 @@ def build(rank_peers):
     fill(view("ab0", al, 8, al), 0.0)
     blk = lambda nm, i, x: ref(nm, 8 * LB * i + x, 8, LB)
     ts(ref("dz", 0, 8 * LB), ref("jb", 0, 8 * LB), CS, A.is_equal, -BIG, A.mult)
-    aff(ref("ne", 0, 8 * LB), ref("jb", 0, 8 * LB), 0.0, BIG)
+    iota(ref("ne", 0, 8 * LB), [[0, 8 * LB]], int(BIG), 0)
     aff(blk("dz", 0, 0), cw(0), 0.0, 4 * BIG)
-    aff(blk("dz", 0, LB - 2), cw(0), 0.0, BIG)
-    aff(ref("c9", 48, 8), cw(0), 1.0, 128.0)
-    ts(ref("d1", 0, 128), ref("j16", 0, 128), 0.5, A.is_gt)
+    aff(blk("dz", 0, LB - 3), cw(0), 0.0, BIG)
+    aff(blk("ne", 0, LB - 1), cw(0), 1.0, 128.0)
+    aff(ref("cb", 0, 8), cw(0), 1.0, 128.0)
+    for i in range(1, len(CHUNKS)):
+        for rd in range(2):
+            w = CHUNKS[i][2 + rd]
+            nh = CHUNKS[i][1] // len(w)
+            for h in range(len(w)):
+                for k in range(4):
+                    if any("R" in x for x in w) and w[h][k] == "D":
+                        iota(view("dd%d%d" % (i, rd), slice(h * nh, h * nh + nh), k), [[0, nh]], -int(QO), 0)
     for t in range(RO):
         aff(ref("c9", 16 * t, 8), cw(0), 0.0, 0.0)
-        aff(ref("c9", 16 * t + 8, 8), cw(0), 1.0, 256.0 * t + 128)
-        aff(cw(1 + t), cw(0), -1.0, ENC + OFF - 256.0 * t - 128)
-        aff(cw(4 + t), cw(0), 1.0, 256.0 * t + 128)
-        aff(col(33 + t), T2, 6.0 - t, 0.0)
-        for z in range(2):
-            m0 = B + 384.0 * t + 128 * z
-            aff(col(44 + 2 * t + z), T1, m0, col(33 + t))
-            aff(ref("tn", 128 * (2 * t + z), 128), ci, T1, col(44 + 2 * t + z))
-            aff(ref("tc16", 128 * (2 * t + z), 128), ci, 1.0, m0 - BIG)
-    iota(ref("mt", 0, OFF), [[0, OFF]], 0, 0)
-    iota(ref("it", 768, 128), [[0, 128]], 0, 0)
+        aff(ref("c9", 16 * t + 8, 8), cw(0), 1.0, 128.0 * t)
+        aff(cw(1 + t), cw(0), -1.0, ENC + OFF - 128.0 * t)
+        aff(col(33 + t), T2, 6.0 - t - BIG, col(38))
+        iota(ref("tc16", 256 * t, 256), [[1, 256]], B + 384 * t - int(BIG), 0)
+    for z in range(2):
+        aff(ref("mt", 384 * z, 384), ref("nt", 0, 384), CU, col(39))
+    iota(ref("mt", 768, 128), [[0, 128]], 0, 0)
     iota(ref("xt", 0, OFF), [[0, OFF]], 0, 0)
     for t in range(RO):
         iota(ref("snd", BX * t, BX), [[0, BX]], 4096, 0)
@@ -320,44 +372,62 @@ def build(rank_peers):
     for i in range(8):
         ts(ref("mt", OFF + 256 * i, 256), ref("mi", 256 * i, 256), CSG, A.mult, C7, A.add)
         ops[-1]["after"] = [0, 1]
-    dma("Y", (lambda T: [(T.mn[:, 0:B], T.mt[:, OFF:OFF + B])], 1), [ref("mn", 0, B)], [ref("mt", OFF, B)], 1 << 20)
-    dma("Y", (lambda T: [(T.mn[r::4, SN * t:SN * t + B], T.mt[r::4, OFF:OFF + B]) for r in (0, 3) for t in (1, 2)], 4),
-        [ref("mn", SN, B), ref("mn", 2 * SN, B)], [ref("mt", OFF, B)], 1 << 20)
+    conv = list(range(len(ops) - 8, len(ops)))
+    ts(ref("ij", 0, 128), ref("ic", 0, 128), 2, A.logical_shift_right)
+    ts(ref("ij", 128, 128), ref("ic", 0, 128), 3, A.bitwise_and)
+    ts(ref("iu", 0, 128), ref("ij", 0, 128), float(OFF), A.add)
+    tc(ref("iu", 128, 128), ref("ij", 128, 128))
+    dma("Y", (lambda T: [(T.mt[3 + 4 * r::16, OFF:OFF + B], T.iu[:, 128 * r:128 * r + 128]) for r in range(2)], 2), [ref("mt", OFF, B)],
+        [ref("iu", 0, 256)], 1 << 17)
+    back = len(ops) - 1
+    dma("Y", (lambda T: [(T.mn[3::4, 0:B], T.nt[3::4, 0:B])], 1), [ref("mn", 0, B // 2)], [ref("nt", 0, B)], 1 << 18)
+    dma("Y", (lambda T: [(T.mn[r::4, 0:B], T.mt[r::4, OFF:OFF + B]) for r in range(3)], 3), [ref("mn", B // 2, B // 2)], [ref("mt", OFF, B)], 3 << 18)
     dma("Y", (lambda T: [(T.yp[:, 0:B], T.mt[0::4, OFF:OFF + B])], 1), [], [ref("mt", OFF, B)], 262144)
+    for o in ops[-2:]:
+        o["after"], o["skip"] = conv, back
 
     LA = lambda i: ref("la", 8 * i, 8)
     vw = lambda i, x=7: ref("vw", 72 * i + x, 8, 9)
 
-    def reads(t, ci_, c0, n, routes, qroute):
+    def reads(t, ci_, c0, n, ways):
         base = B + 384 * t
         m, r4 = n // 16, n // 4
-        pb = "ps%d" % (0 if ci_ == 0 else 2 + ci_)
-        px = ["ps7", "ps5", "ps6"][ci_]
-        q = ref("qh", c0, n)
+        H = len(ways[0])
+        nh, mh = n // H, m // H
+        pb = pb2 = "ps" + BANKS[ci_][0]
+        at = 0 if pb[2] in BANKS[ci_][1:] else 3 * r4
+        turn = [0]
+
+        def px(h, w):
+            turn[0] += 1
+            b = BANKS[ci_][1 + turn[0] % (len(BANKS[ci_]) - 1)]
+            return ref("ps" + b, 3 * r4 if b == pb[2] else 0, w)
         o4 = c0 // 4
         c4_ = lambda nm, lo=0, cnt=r4: ref(nm, o4 + lo, cnt)
-        pD, pE, pP, pT = ref(pb, 0, r4), ref(pb, r4, r4, 2), ref(pb, r4 + 1, r4, 2), ref(pb, 3 * r4, r4)
-        pS = ref(pb, 4 * r4, r4) if ci_ else ref("ps2", 288, 72)
+        pD, pE, pP = ref(pb, 0, r4), ref(pb, r4, r4, 2), ref(pb, r4 + 1, r4, 2)
+        pS = ref(pb2, at + r4, r4) if ci_ else ref("ps2", 288, 72)
         pU = pS if ci_ else ref("ps2", 256, r4)
         tb = 2 * o4 + (64 if ci_ else 0)
         pc = PIECE if ci_ else 99
-        XW = lambda off: ind("xt", OFF, OFF + base, off) if ci_ == 0 else ind("xs", SN * t, SN * t + base, off)
-        MW = lambda off: ind("mt", OFF, OFF + base, off) if ci_ == 0 else ind("mn", SN * t, SN * t + base, off)
         qs = "sh" if ci_ == 0 and t > 0 else "qh"
         sums = [(ref("mz4", 12 - 4 * s, 128), ref(qs, c0 + s, r4, 4)) for s in range(4)]
         mm([(pU, sums)])
         ts(c4_("ti"), pU, -0.375, A.add)
         tt(c4_("tau"), c4_("ti"), pU, A.subtract)
         lst = ref("stu", c0 // 16, m)
+        part = lambda r, h, w: ref(r[0], r[1] + h * w, w)
         for rd in range(2):
-            if t == 0 and (rd == 0 or ci_ == 0):
-                ts(ref("g16", c0, n), ind("mi", 0, B, lst), CSG, A.mult, CGS, A.add)
-            elif ci_ and rd == 0:
-                act(ref("g16", c0, n), ind("mt", OFF, OFF + base, lst), F.Identity, bias=CG)
-            elif ci_ or rd == 0 or "g" in ONS:
-                act(ref("g16", c0, n), MW(lst), F.Identity, bias=CG)
-            else:
-                ts(ref("g16", c0, n), MW(lst), CG, A.add)
+            tag[0] = "%d%d" % (ci_, rd)
+            XW = lambda off: ind("xt", OFF, OFF + base, off) if ci_ == 0 or t + rd == 0 else ind("xs", SN * t, SN * t + base, off)
+            for h in range(H):
+                groute, lh, go = ways[rd][h][5], part(lst, h, mh), ref("g16", c0 + h * nh, nh)
+                gw = ind("mn", 0, base, lh) if ci_ and rd else ind("mt", OFF, OFF + base, lh)
+                if t == 0 and (rd == 0 or groute == "V"):
+                    ts(go, ind("mi", 0, B, lh), CSG, A.mult, CGS, A.add)
+                elif groute == "S":
+                    act(go, gw, F.Identity, bias=CG)
+                else:
+                    ts(go, gw, CG, A.add)
             gs = lambda s: ref("g16", c0 + s, r4, 4)
             if rd == 0 and ci_ == 0:
                 mm([(pE, [(Y(4, s), gs(s)) for s in range(4)]), (pP, [(Y(0, s), gs(s)) for s in range(4)])], pc)
@@ -366,6 +436,7 @@ def build(rank_peers):
                 ops[-2]["free"] = [len(ops) - 3]
                 tt(ref("cc", 2 * o4 + 1, r4, 2), pD, c4_("ti"), A.is_ge)
             else:
+                pD = ref("ps" + BANKS[ci_][1], n, r4) if ci_ else ref("ps2", 384, r4)
                 mm([(pD, [(Y(8, s), gs(s)) for s in range(4)])])
                 mm([(pE, [(Y(4, s), gs(s)) for s in range(4)]), (pP, [(Y(0, s), gs(s)) for s in range(4)])], pc)
                 tt(ref("cc", 2 * o4 + 1, r4, 2), pD, c4_("tau"), A.is_ge)
@@ -375,68 +446,83 @@ def build(rank_peers):
                 ts(ref("t16", 65, r4, 2), pD, -1.7, A.is_gt)
             t16 = lambda cl, cnt=m: ref("t16", tb + 2 * cl + 1, cnt, 8)
             for k0, k1 in (KS if ci_ == 0 else [(0, 4)]):
-                mm([(ref(pb, 3 * r4 + k * m, m), [(Y(k, cl), t16(cl)) for cl in range(4)]) for k in range(k0, k1)], pc)
-                ts(c4_("ou", k0 * m, (k1 - k0) * m), ref(pb, 3 * r4 + k0 * m, (k1 - k0) * m), ENC, A.add)
+                mm([(ref(pb2, at + k * m, m), [(Y(k, cl), t16(cl)) for cl in range(4)]) for k in range(k0, k1)], pc)
+                ts(c4_("ou", k0 * m, (k1 - k0) * m), ref(pb2, at + k0 * m, (k1 - k0) * m), ENC, A.add)
             YD = lambda k, cl: Y(5 + k if k < 3 else 3, cl)
             if ci_:
-                mm([(ref(pb, 5 * r4 + k, m, 4), [(YD(k, cl), t16(cl)) for cl in range(4)]) for k in range(4)], pc)
+                mm([(ref(pb2, at + 2 * r4 + k, m, 4), [(YD(k, cl), t16(cl)) for cl in range(4)]) for k in range(4)], pc)
             else:
                 cnt = 16 if last else 8
                 mm([(ref("ps2", 64 + 4 * h + k, cnt, 9), [(YD(k, cl), t16(cl, cnt)) for cl in (2 * h, 2 * h + 1)]) for h in range(2) for k in range(4)]
                    + [(ref("ps2", 72, cnt, 9), [(I16, ref("c9", 16 * t, cnt))])])
-            order = [k for k in range(4) if routes[k] != "A"] + [k for k in range(4) if routes[k] == "A"]
-            for k in order:
-                at = 4 * c0 + k * n
-                ab = view("ab%d" % ci_, al, k if ci_ else slice(k, 8, 4), al)
-                if routes[k] == "A":
-                    tt(ref("dd", at, n), XW(c4_("ou", k * m, m)), q, A.subtract)
-                    act(ab, ref("dd", at, n), F.Abs, bias=QO)
-                else:
-                    act(ref("xr", at, n), XW(c4_("ou", k * m, m)), F.Copy)
-                    pd = ref(px, 0, n)
-                    mm([(pd, [(INEG, q), (IB, ref("xr", at, n))])])
-                    act(ab, pd, F.Abs, bias=QO)
+            relu = any("R" in x for x in ways[rd])
+            for h in range(H):
+                routes, q, js = ways[rd][h][:4], ref("qh", c0 + h * nh, nh), slice(h * nh, h * nh + nh)
+                run = lambda x: [(k, k + 1) for k in range(4) if routes[k] == x] if not (ci_ and x in JOIN and (x != "D" or H == 1)) else \
+                    [(routes.index(x), routes.rindex(x) + 1)] if x in routes else []
+                ab = lambda k0, k1: view("ab%d" % ci_, js, slice(k0, k1)) if ci_ else view("ab0", al, slice(k0, 8, 4), al)
+                dd = lambda k0, k1: view("dd%d%d" % (ci_, rd), js, slice(k0, k1) if k1 > k0 + 1 else k0) if ci_ else ref("dd", k0 * n, n)
+                for k0, k1 in run("D"):
+                    act(ref("xr", 4 * c0 + k0 * n + h * nh, (k1 - k0) * nh), XW(c4_("ou", k0 * m + h * mh, (k1 - k0) * mh)), F.Copy)
+                    for k in range(k0, k1):
+                        pd = px(h, nh)
+                        mm([(pd, [(INEG, q), (IB, ref("xr", 4 * c0 + k * n + h * nh, nh))])])
+                        act(ab(k, k + 1), pd, F.Abs, bias=QO / (1 + relu), scale=1.0 / (1 + relu))
+                for x in "AR":
+                    for k0, k1 in run(x):
+                        for k in range(k0, k1):
+                            tt(dd(k, k + 1), XW(c4_("ou", k * m + h * mh, mh)), q, A.subtract)
+                        if x == "A":
+                            act(ab(k0, k1), dd(k0, k1), F.Relu if relu else F.Abs, bias=QO)
+                        else:
+                            ts(ab(k0, k1), dd(k0, k1), QO, A.add, 0.0, A.max)
             lst = ref("lv", 48 * rd + c0 // 16, m)
             if ci_:
-                mm([(pS, [(IB, ref("kt16", 0, r4))] + [(ref("mz", 15 - s, 128), view("ab%d" % ci_, al, al, s)) for s in range(16)])], pc)
-                scan(c4_("pm", 48), ref("rk", 0, r4), pS, 0.0, A.add, A.min)
+                every = lambda nm, s: view(nm % ci_, slice(s, None, 16), al)
+                mm([(pS, [(IB, ref("kt16", 0, r4))] + [(ref("mz4", 144 + 15 - s, 128), every("dd%d" + str(rd), s)) for s in range(16 * relu)]
+                     + [(ref("mz", 288 * relu + 15 - s, 128), every("ab%d", s)) for s in range(16)])], pc)
+                scan(c4_("pm", 48), ref("rk", 80, r4), pS, 0.0, A.add, A.min)
                 tt(c4_("eq"), pS, c4_("pm", 48), A.not_equal)
-                scan(ref("ve", 192 * rd + o4, r4), c4_("eq"), ref(pb, 5 * r4, r4), 0.0, A.mult, A.add)
+                scan(ref("ve", 192 * rd + o4, r4), c4_("eq"), ref(pb2, at + 2 * r4, r4), 0.0, A.mult, A.add)
                 ts(lst, ref("ve", 192 * rd + o4 + 3, m, 4), ENC, A.add)
             else:
                 mm([(pS, [(IB, ref("ktw", 0, 72))] + [(ref("mz", 144 + 7 - s, 128), view("ab0", al, al, s)) for s in range(8)])])
                 eq = ref("eqw", 0, 72)
-                scan(ref("pm", 0, 72), ref("rk", 80, 72), pS, 0.0, A.add, A.min)
+                scan(ref("pm", 0, 72), ref("rk", 0, 72), pS, 0.0, A.add, A.min)
                 tt(eq, pS, ref("pm", 0, 72), A.not_equal)
                 scan(ref("vw", 72 * rd, 72), eq, ref("ps2", 64, 72), 0.0, A.mult, A.add)
                 ts(lst, vw(rd), ENC, A.add)
                 if last:
                     scan(ref("vw", 144, 72), eq, x9(1), 0.0, A.mult, A.add)
-                    tt(ref("eqw", 8, 8, 9), blk("lo", 0, LB - 1), cw(1 + t), A.add)
+                    tt(ref("eqw", 8, 8, 9), blk("lo", 0, LB - 2), cw(1 + t), A.add)
                     scan(ref("vw", 216, 72), eq, ref("ps2", 136, 72), 0.0, A.mult, A.add)
                     tc(LA(4), vw(3, 8))
             hb = QO / 2 - 0.25
-            if qroute == "M":
-                tt(ref("sh", c0, n), XW(lst), q, A.add)
-                act(q, ref("sh", c0, n), F.Identity, scale=0.5, bias=hb)
-            elif qroute == "V":
-                tt(ref("sh", c0, n), XW(lst), q, A.add)
-                ts(q, ref("sh", c0, n), 0.5, A.mult, hb, A.add)
-            else:
-                act(ref("xg", c0, n), XW(lst), F.Copy)
-                pq = ref(px, 0, n)
-                mm([(pq, [(IH, q), (IBH, ref("xg", c0, n))])])
-                if qroute == "S":
-                    act(q, pq, F.Identity, bias=hb)
+            for h in range(H):
+                qroute, c1, xw = ways[rd][h][4], c0 + h * nh, XW(part(lst, h, mh))
+                q, sh, xg, pq = ref("qh", c1, nh), ref("sh", c1, nh), ref("xg", c1, nh), px(h, nh)
+                if qroute == "M":
+                    tt(sh, xw, q, A.add)
+                    act(q, sh, F.Identity, scale=0.5, bias=hb)
+                elif qroute == "V":
+                    tt(sh, xw, q, A.add)
+                    ts(q, sh, 0.5, A.mult, hb, A.add)
                 else:
-                    ts(q, pq, hb, A.add)
+                    act(xg, xw, F.Copy)
+                    mm([(pq, [(IH, q), (IBH, xg)])])
+                    if qroute == "S":
+                        act(q, pq, F.Identity, bias=hb)
+                    else:
+                        ts(q, pq, hb, A.add)
+                if t == RO - 1 and ci_ and rd:
+                    if "o" in ONS:
+                        act(ref("qo", c1, nh), q, F.Identity, bias=-QO)
+                    else:
+                        ts(ref("qo", c1, nh), q, -QO, A.add)
+                    dma("Y", (lambda T, c1=c1: [(T.yq[:, c1:c1 + nh], T.qo[:, c1:c1 + nh])], 1), [], [ref("qo", c1, nh)], 256 * nh)
             if ci_ == 0 and rd == 0:
                 lowest_of(t, 0, lst)
                 step_a(t, 0, LA(0))
-        c1 = max(c0, L)
-        if t == RO - 1 and c1 < c0 + n:
-            act(ref("qo", c1, c0 + n - c1), ref("qh", c1, c0 + n - c1), F.Identity, bias=-QO)
-            dma("Y", (lambda T: [(T.yq[:, c1:c0 + n], T.qo[:, c1:c0 + n])], 1), [], [ref("qo", c1, c0 + n - c1)], 256 * n)
 
     def lowest(i, key, own):
         for c in range(7, -1, -1):
@@ -446,13 +532,13 @@ def build(rank_peers):
     def lowest_of(t, i, lst):
         key = ref("ky", 128 * i, 128)
         act(key, ind("nt", 0, B + 384 * t, lst), F.Copy)
-        aff(blk("dz", 0, LB - 1), cw(0), 1.0, (768.0 if i else 256.0 * t) - OFF - ENC)
+        aff(blk("dz", 0, LB - 2), cw(0), 1.0, (768.0 if i else 384.0 + 128 * t) - OFF - ENC)
         if "v" in ONS:
-            act(blk("ne", 0, LB - 1), vw(i), F.Copy)
+            act(blk("ne", 0, LB - 2), vw(i), F.Copy)
         else:
-            tc(blk("ne", 0, LB - 1), vw(i))
+            tc(blk("ne", 0, LB - 2), vw(i))
         lowest(i, key, vw(i))
-        ts(LA(i), blk("lo", i, LB - 1), OFF + ENC, A.add)
+        ts(LA(i), blk("lo", i, LB - 2), OFF + ENC, A.add)
 
     pL, pY, pR, pM = [ref("ps1", 128 * i, 128) for i in range(4)]
 
@@ -460,21 +546,23 @@ def build(rank_peers):
         h = lambda nm: ref(nm, 128 * z, 128)
         MW = ind("mt", 0, OFF + B + 384 * t, la)
         act(h("gs"), MW, F.Identity, bias=CGS)
-        act(h("g32"), MW, F.Copy)
         mm([(pL, [(DAL, h("gs"))])])
         act(pL, pL, F.Relu, bias=1.0, scale=-1.0)
         tt(h("yy"), pL, h("gs"), A.mult)
 
-    def step_b(t, z, la):
+    def step_b(t, z, lg, la, back):
         base = B + 384 * t
         h = lambda nm: ref(nm, 128 * z, 128)
-        mm([(pY, [(DALN, h("gs")), (IBIG, h("kk"))])])
-        tt(h("w1"), pY, ref("tn", 128 * (2 * t + z), 128), A.min)
-        act(h("fl"), pY, F.Relu, scale=1.0 / BIG)
-        tt(ind("mt", 0, OFF + base, la), h("g32"), h("w1"), A.max)
-        mm([(pR, [(SH, h("gs")), (PMS, h("yy")), (BODP, h("fl"))]),
-            (pM, [(IP, ref("tc16", 128 * (2 * t + z), 128)), (IPB, h("kk")), (BODP, h("fl"))])])
-        act(h("t1"), pR, F.Relu, bias=CE0)
+        name = ref("tc16", 128 * (2 * t + z), 128)
+        act(h("g32"), ind("mt", 0, OFF + base, lg), F.Copy)
+        mm([(pY, [(DX, h("gs")), (IM, name), (IMD, h("kk"))])])
+        act(h("w1"), pY, F.Relu, bias=col(33 + t))
+        if z == 0:
+            act(h("fl"), pY, F.Relu, bias=col(33 + t))
+        tt(ind("mt", 0, OFF + base, la), h("g32"), h("w1"), A.add)
+        off = (BODP, h("fl")) if z == 0 else (BOP, ref("xf", 0, 128))
+        mm([(pR, [(SH, h("gs")), (PMS, h("yy")), (IT3, back), off]), (pM, [(IP, name), (IPB, h("kk"))] + [(IP, NB)] * z + [off])])
+        act(h("t1"), pR, F.Relu, bias=col(37) if z else col(36))
         tt(ref("mt", OFF + base + 128 * (z + 1), 128), pM, h("t1"), A.max)
 
     sent = []
@@ -484,78 +572,73 @@ def build(rank_peers):
         q = ref("qh", 0, 128)
         lv = ref("lv", 48, 8)
         nn = OFF + base
+        tag[0] = "1"
         lowest_of(t, 1, lv)
         xk = ref("xk", 0, 128)
         tt(xk, ind("vw", 144, 216, ref("eu", 0, 8)), DG, A.mult)
-        pk, pI, pmd = [ref("ps0", 128 * i, 128) for i in (1, 2, 3)]
-        mm([(pk, [(BO, xk)]), (pI, [(I4, ref("ky", 0, 128)), (BO, xk)])])
-        ts(ref("it", nn, 128), pI, 4 * ENC, A.add)
+        pk, pN, pmd = ref("ps0", 128, 128), ref("ps0", 256, 128), ref("ps0", 384, 128)
+        act(ref("gv", 0, 128), ind("mt", OFF, OFF + base, lv), F.Identity, bias=CGS)
+        mm([(pN, [(IK3, ref("gv", 0, 128)), (IU, ref("ky", 0, 128)), (BOK, xk)])])
+        act(ref("mt", nn, 128), pN, F.Identity, bias=CGN)
+        mm([(pk, [(BO, xk)])])
         ts(ref("kk", 0, 128), pk, CA, A.is_equal)
-        act(ref("mt", nn, 128), ind("mt", OFF, OFF + base, lv), F.Copy)
         if "x" in ONS:
             act(ref("xt", nn, 128), q, F.Identity, bias=-QO)
         else:
             ts(ref("xt", nn, 128), q, -QO, A.add)
-        if t < RO - 1:
-            act(ref("q1", 0, 128), q, F.Identity, bias=-QO - 256.0)
-        else:
+        if t == RO - 1:
             act(ref("q1", 0, 128), q, F.Identity, scale=-1.0, bias=QO)
         PC = ref("ps7", 128, 128)
         mm([(PC, [(IH, q), (IBH, ref("xg", 0, 128))])])
         ts(ref("mxi", 0, 128), PC, -QO / 2 - 0.25, A.add)
-        tc(ind("it", 0, nn, LA(1)), ref("it", nn, 128))
+        tc(ind("mt", 0, nn, LA(1)), ref("mt", nn, 128))
         tc(ind("xt", 0, nn, LA(1)), ref("mxi", 0, 128))
         sn = SN * (t + 1)
         if t < RO - 1:
             dma("Y", (lambda T: [(T.xs[:, sn:sn + base], T.xt[:, OFF:nn])], 1), [ref("xs", sn, base)], [ref("xt", OFF, base)], 256 * base)
-        step_b(t, 0, LA(0))
+        gi = ref("gi", 0, 128)
+        act(gi, ind("mt", 0, nn, LA(4)), F.Identity, bias=CGS)
+        step_b(t, 0, LA(0), LA(0), gi)
         act(ref("xt", nn + 128, 128), ind("xt", 0, nn, LA(4)), F.Copy)
-        ib = ind("it", 0, nn, LA(4))
-        tt(ref("dm", 0, 128), ib, DG, A.mult)
-        ts(ref("k2", 0, 128), ib, 0.25, A.mult, OFF - 0.375, A.add)
-        ts(ref("ui", 0, 128), ib, 3, A.bitwise_and)
-        scan(ref("dn", 0, 128), ref("d1", 0, 128), ref("dm", 0, 128), 0.0, A.mult, A.add)
-        ts(LA(5), ref("dn", 15, 8, 16), 0.25, A.mult, OFF - 0.375, A.add)
-        own = ref("w8", 16, 8)
-        tc(own, LA(5))
-        ts(ref("km", 0, 128), ref("ui", 0, 128), CAD, A.not_equal, 2 * BIG, A.mult)
-        aff(blk("dz", 0, LB - 1), cw(0), 0.0, 0.0)
-        aff(blk("ne", 0, LB - 1), cw(0), 1.0, 128.0)
-        lowest(2, ref("k2", 0, 128), own)
+        pkey, own, pk2 = ref("ps7", 384, 128), ref("ps2", 0, 8), ref("ps0", 0, 128)
+        mm([(pkey, [(BU, gi)])])
+        mm([(own, [(ref("mz4", 288 + 15 - s, 128), ref("gi", s, 8, 16)) for s in range(16)])])
+        mm([(pk2, [(BK, gi)])])
+        act(ref("ky", 256, 128), pkey, F.Copy)
+        ts(LA(5), own, OFF + ENC, A.add)
+        ts(ref("km", 0, 128), pk2, CAD, A.not_equal, 2 * BIG, A.mult)
+        ts(ref("kk", 128, 128), pk2, CA, A.is_equal)
+        aff(blk("dz", 0, LB - 2), cw(0), 1.0, 128.0 * t - OFF - ENC)
+        aff(blk("dz", 0, LB - 1), cw(0), -1.0, OFF + ENC - 128.0 * t)
+        tc(blk("ne", 0, LB - 2), own)
+        lowest(2, ref("ky", 256, 128), own)
         tt(ref("kf", 0, 128), ind("mt", 0, nn, LA(5)), ref("km", 0, 128), A.is_gt)
         pF, pos = ref("ps2", 256, 8), ref("ps2", 272, 8)
         mm([(pF, [(ref("mz", 15 - s, 128), ref("kf", s, 8, 16)) for s in range(16)])])
         f, f2 = ref("f8", 0, 8), ref("f8", 8, 8)
-        tt(f, pF, blk("lo", 2, LB - 2), A.min)
+        tt(f, pF, blk("lo", 2, LB - 3), A.min)
         tt(f2, pF, blk("lo", 2, LB - 1), A.mult)
-        mm([(pos, [(I16, ref("c9", 48, 8)), (LQ, f)] + [(BOQ, ref("f8", 0, 8 - d), ref("ps2", 272 + d, 8 - d)) for d in range(1, 8)] + [(INQ, f2)])])
+        mm([(pos, [(IB, ref("cb", 0, 8)), (LQ, f)] + [(BOQ, ref("f8", 0, 8 - d), ref("ps2", 272 + d, 8 - d)) for d in range(1, 8)] + [(INQ, f2)])])
         tc(LA(3), pos)
-        tc(ind("snd", BX * t, BX * t + BX, LA(3)), ref("q1", 0, 128))
+        tc(ind("snd", BX * t, BX * t + BX, LA(3)), ref("xt", nn, 128) if t < RO - 1 else ref("q1", 0, 128))
         rid, pid, mask = rank_peers[t]
         so, ro = ref("snd", BX * t, 64), ref("rcv", BX * t, 64)
         add("G", lambda g, T: g.remote_dma(ap(T, ro), ap(T, so), T.sem["arr%d" % t], T.sem["snt%d" % t], pid, rid, mask),
-            [], [so], 200.0, lat=2000.0, sem="snt%d" % t, inc=NENG)
+            [], [so], 200.0, lat=XLAT - 500, sem="snt%d" % t, inc=NENG)
         sent.append(len(ops) - 1)
-        add("G", lambda g, T: None, [ro], [so], 1.0, lat=2700.0, sem="arr%d" % t, inc=NENG)
-        w8 = lambda i: ref("w8", 8 * i, 8)
-        tt(w8(0), own, blk("lo", 2, LB - 2), A.min)
-        tt(w8(1), w8(0), cw(4 + t), A.max)
-        tc(LA(2), w8(1))
-        ts(ref("kk", 128, 128), ref("ui", 0, 128), CA, A.is_equal)
+        add("G", lambda g, T: None, [ro], [so], 1.0, lat=XLAT, sem="arr%d" % t, inc=NENG)
+        ts(LA(2), blk("lo", 2, LB - 2), OFF + ENC, A.add)
+        tt(ref("xf", 0, 128), ind("f8", 0, 8, ref("eu", 8, 8)), DG, A.mult)
+        tag[0] = "2"
+        step_a(t, 1, LA(5))
+        step_b(t, 1, LA(5), LA(2), ref("gs", 128, 128))
+        mm([(pmd, [(BOQ, ref("xf", 0, 128))])])
+        act(ref("md", 0, 128), pmd, F.Copy)
+        tt(ref("xt", nn + 256, 128), ind("xt", 0, nn, LA(5)), ref("md", 0, 128), A.mult)
         if t < RO - 1:
-            tc(ref("it", nn + 128, 128), ib)
-        step_a(t, 1, LA(2))
-        step_b(t, 1, LA(2))
-        mm([(pmd, [(BOD, ref("fl", 128, 128))])])
-        act(ref("md", 0, 128), pmd, F.Identity, scale=-1.0, bias=1.0)
-        tt(ref("xt", nn + 256, 128), ind("xt", 0, nn, LA(2)), ref("md", 0, 128), A.mult)
-        if t < RO - 1:
-            tc(ref("it", nn + 256, 128), ind("it", 0, nn, LA(2)))
-            news = [sn + base] + ([sn + SN + base] if t == 0 else [])
             dma("Y", (lambda T: [(T.xs[:, sn + base:sn + base + 384], T.xt[:, nn:nn + 384])], 1), [ref("xs", sn + base, 384)], [ref("xt", nn, 384)], 98304)
-            dma("Y", (lambda T: [(T.mn[r::4, sn:sn + base], T.mt[r::4, OFF:nn]) for r in (1, 2)]
-                      + [(T.mn[:, x:x + 384], T.mt[:, nn:nn + 384]) for x in news], 2 + len(news)),
-                [ref("mn", sn, base)] + [ref("mn", x, 384) for x in news], [ref("mt", OFF, base + 384)], 256 * base + 200000)
+            dma("Y", (lambda T: [(T.mn[r::4, 0:base], T.mt[r::4, OFF:nn]) for r in (1, 2)] + [(T.mn[:, base:base + 384], T.mt[:, nn:nn + 384])], 3),
+                [ref("mn", 0, base + 384)], [ref("mt", OFF, base + 384)], 256 * base + 200000)
             ops[-1]["after"] = [sent[t]]
         sh = ref("sh", 0, 128)
         tt(sh, ind("rcv", BX * t, BX * t + BX, LA(3)), q if t < RO - 1 else ref("xt", nn, 128), A.min)
@@ -563,16 +646,16 @@ def build(rank_peers):
             act(ref("qo", 0, 128), sh, F.Abs)
             dma("S", (lambda T: [(T.yq[:, 0:128], T.qo[:, 0:128])], 1), [], [ref("qo", 0, 128)], 32768)
         elif "r" in ONS:
-            act(ref("rr", 0, 128), sh, F.Sign)
+            act(ref("rr", 0, 128), sh, F.Sign, bias=-QO / 2)
             mm([(PC, [(I16, sh), (IS, ref("rr", 0, 128))])])
-            act(q, PC, F.Identity, bias=768.0)
+            act(q, PC, F.Identity, bias=QO / 2)
         else:
-            ts(ref("rr", 0, 128), sh, 0.0, A.is_lt, QO + 256.0, A.mult)
+            ts(ref("rr", 0, 128), sh, QO / 2, A.is_lt, QO, A.mult)
             tt(q, ref("rr", 0, 128), sh, A.add)
 
     for t in range(RO):
-        for i, (c0, n, routes, qroute) in enumerate(CHUNKS):
-            reads(t, i, c0, n, routes, qroute)
+        for i, c in enumerate(CHUNKS):
+            reads(t, i, c[0], c[1], c[2:])
         writers(t)
     e0 = W - 256
     dma("Y", (lambda T: [(T.yx[:, 0:e0], T.xt[:, OFF:OFF + e0])], 1), [], [ref("xt", OFF, e0)], 256 * e0)
@@ -584,22 +667,28 @@ def build(rank_peers):
 
 
 def depends(ops):
-    hist = {}
+    hist, bank = {}, {}
     for i, o in enumerate(ops):
         dep = set(o.get("after", ()))
         for acc, regs in ((0, o["rd"]), (1, o["wr"])):
             for nm, cols in regs:
                 ps = SCRATCH[nm][0] == "psum"
                 for j, w, c2 in hist.get(nm, ()):
-                    if j != i and ((cols & c2 and (w or acc)) or (ps and ops[j]["e"] != o["e"])):
+                    if j != i and ((cols & c2 and (w or acc)) or (ps and (ops[j]["e"] != o["e"] or "alt" in o or "alt" in ops[j]))):
                         dep.add(j)
+        if o["e"] == "P":
+            for nm, _ in o["wr"]:
+                j = bank.get(nm, i)
+                if j != i and j not in dep:
+                    dep.add(j); o["free"] = o["free"] + [j]
+                bank[nm] = i
         for acc, regs in ((0, o["rd"]), (1, o["wr"])):
             for nm, cols in regs:
                 h = hist.setdefault(nm, [])
                 if acc:
                     h[:] = [x for x in h if x[2] & ~cols]
                 h.append((i, acc, cols))
-        o["dep"] = sorted(dep)
+        o["dep"] = sorted(dep - {o.get("skip")})
 
 
 def schedule(ops):
@@ -608,7 +697,8 @@ def schedule(ops):
     for i, o in enumerate(ops):
         for j in o["dep"]:
             p = ops[j]
-            d = p["lat"] + (0.0 if j in o.get("free", ()) else SELF if p["e"] == o["e"] and not p["sem"] else HOP)
+            either = "alt" in p or "alt" in o
+            d = p["lat"] + (0.0 if j in o.get("free", ()) else (HOP + SELF) / 2 if either else SELF if p["e"] == o["e"] and not p["sem"] else HOP)
             succ[j].append((i, d)); pred[i].append((j, d))
     pr = [0.0] * n
     for i in range(n - 1, -1, -1):
@@ -619,26 +709,36 @@ def schedule(ops):
         for i in range(n):
             x = (x * 1103515245 + 12345) % 2147483648
             pr[i] += JIT * (x / 2147483648.0)
-        order, st = one_pass(ops, succ, pred, pr, [0.0] * n)
+        order, st = one_pass(ops, succ, pred, pr, [0.0] * n, True)
         end = max(st[i] + ops[i]["c"] + ops[i]["lat"] for i in range(n))
         if best is None or end < best[1]:
-            best = (order, end, st)
+            best = (order, end, st, [o["e"] for o in ops])
         if it + 1 < PASSES:
-            _, sb = one_pass(ops, pred, succ, [st[i] + ops[i]["c"] for i in range(n)], [o["lat"] for o in ops])
+            _, sb = one_pass(ops, pred, succ, [st[i] + ops[i]["c"] for i in range(n)], [o["lat"] for o in ops], False)
             pr = [sb[i] + ops[i]["c"] for i in range(n)]
-    for i in range(n):
-        ops[i]["t"] = best[2][i]
+    for i, o in enumerate(ops):
+        o["t"], o["e"] = best[2][i], best[3][i]
+        if "alt" in o:
+            o["fn"], o["c"] = o["alt"][o["e"]]
     return best[0], best[1]
 
 
-def one_pass(ops, succ, pred, pr, rdy):
+def one_pass(ops, succ, pred, pr, rdy, choose):
     n = len(ops)
     left = [len(p) for p in pred]
     free = {e: 0.0 for e in "VSPGY"}
     pool = {e: [] for e in free}
+
+    def enter(i):
+        o = ops[i]
+        if choose and "alt" in o:
+            end = {e: max(rdy[i], free[e] + sum(ops[j]["c"] for j in pool[e] if pr[j] > pr[i] - AHEAD)) + o["alt"][e][1] * WEIGH[e] for e in "SV"}
+            o["e"] = min("SV", key=lambda e: end[e])
+            o["c"] = o["alt"][o["e"]][1]
+        pool[o["e"]].append(i)
     for i in range(n):
         if not left[i]:
-            pool[ops[i]["e"]].append(i)
+            enter(i)
     order, start = [], [0.0] * n
     while len(order) < n:
         best = None
@@ -662,7 +762,7 @@ def one_pass(ops, succ, pred, pr, rdy):
             rdy[j] = max(rdy[j], free[e] + d)
             left[j] -= 1
             if not left[j]:
-                pool[ops[j]["e"]].append(j)
+                enter(j)
     return order, start
 
 

@@ -1,3 +1,4 @@
+import math
 from concourse.bass import DstId, RemoteDMATransfer
 from concourse.mybir import dt, AluOpType, AxisListType, ActivationFunctionType
 
@@ -10,19 +11,22 @@ LB = 132
 BX = 384
 
 SN = 2816
-CHUNKS = [(0, 128, ["AAADMS"], ["AAAASS"]), (128, 320, ["ADDDMS"], ["AADDMS"]), (448, 320, ["ADDDMS"], ["ADDDMS"])]
+CHUNKS = [(0, 128, ["E2..MS"], ["E2..SS"]), (128, 320, ["AADDMS"], ["AADDMS"]), (448, 320, ["AAADMS"], ["ADDDMS"])]
+PER = {"000": "E1..MS", "210": "AAADMS", "110": "ADDDMS", "100": "AAADSS", "120": "AADDMS", "121": "E...MS"}
+LIVE, LATE = (1, 2), True
 BANKS = ["07", "35", "46"]
 JOIN = "R"
 KS = [(0, 4)]
 ONS = "xvro"
-SEED, JIT, LOOK, PASSES = 3, 200.0, 0.3, 6
+SEED, JIT, LOOK, PASSES = 1, 200.0, 0.3, 6
 PIECE, NV = 4, 4
 AHEAD, WEIGH = 1000.0, {"S": 1.0, "V": 4.0}
-ONV, ONS2 = "cb_ cw_ dz_ kf_ mb16_ mm_ qh00 qh10 qh11 qh20 qo11 xt1".split(), "fl1 g1621 qh21 qh_ qo21".split()
+ONV, ONS2 = "cb_ cw_ dz1 kf_ ky1 mb16_ ne_ qh00 qh10 qh11 qh20 qo11".split(), "dz_ g1600 g1621 md2 ne00 qh21 qh_ qo21 xt1".split()
 NENG = 16
-CY, PEC, GAM, SCA, TTG = 1.0, 0.49, 1.55, 3.8, 0.0
-HOP, SELF, SFIX = 185.0, 220.0, 45.0
-DFIX, DRATE, XLAT = 1300.0, 280.0, 1800.0
+COST = (1.0, 0.49, 1.55, 3.8, 0.0, 45.0, 1300.0, 280.0, 1800.0, 185.0, 220.0)
+OTHER = [(0.84, 0.42, 1.5, 3.6, 0.0, 45.0, 1500.0, 250.0, 2100.0, 205.0, 225.0), (1.05, 0.50, 1.3, 5.0, 0.0, 45.0, 1800.0, 180.0, 2700.0, 150.0, 150.0),
+         (1.05, 0.45, 1.9, 2.5, 2.0, 20.0, 1000.0, 350.0, 1500.0, 250.0, 250.0), (1.22, 0.55, 1.75, 4.5, 0.0, 60.0, 1500.0, 220.0, 2200.0, 200.0, 200.0)]
+MOVES, WARM, FLIP = 24000, 0.0003, 0.3
 
 f32, bf, f16, i32, u16 = "float32", "bfloat16", "float16", "int32", "uint16"
 SCRATCH = {
@@ -33,24 +37,24 @@ SCRATCH = {
     "snd": ("sbuf", [128, 3 * BX], bf), "rcv": ("sbuf", [128, 3 * BX], bf),
     "ci": ("sbuf", [128, 144], bf), "c4": ("sbuf", [128, 144], bf), "c16": ("sbuf", [128, 128], bf), "j16": ("sbuf", [128, 128], bf), "cp": ("sbuf", [128, 256], bf),
     "pi": ("sbuf", [128, 8], i32), "ei": ("sbuf", [128, 8], i32), "eu": ("sbuf", [128, 16], u16),
-    "col": ("sbuf", [128, 64], f32), "cw": ("sbuf", [128, 128], f32), "c9": ("sbuf", [128, 48], f16), "cb": ("sbuf", [128, 8], bf),
-    "mz": ("sbuf", [128, 3 * 144], bf), "mz4": ("sbuf", [128, 3 * 144], f16), "my": ("sbuf", [128, 9 * 144], f16),
+    "col": ("sbuf", [128, 64], f32), "cw": ("sbuf", [128, 128], f32), "c9": ("sbuf", [128, 192], f16), "cb": ("sbuf", [128, 8], bf),
+    "mz": ("sbuf", [128, 4 * 144], bf), "mz4": ("sbuf", [128, 3 * 144], f16), "my": ("sbuf", [128, 9 * 144], f16),
     "mm": ("sbuf", [128, 22 * 128], f16), "mb16": ("sbuf", [128, 6 * 128], bf),
-    "dg": ("sbuf", [128, 256], f32), "kt16": ("sbuf", [128, 160], bf), "ktw": ("sbuf", [128, 72], bf), "x9": ("sbuf", [128, 4 * 72], f32),
+    "dg": ("sbuf", [128, 256], f32), "kt16": ("sbuf", [128, 160], bf), "ktw": ("sbuf", [128, 64], bf), "x9": ("sbuf", [128, 4 * 64], f32),
     "tc16": ("sbuf", [128, 6 * 128], f16), "jb": ("sbuf", [128, 8 * LB], bf),
     "dz": ("sbuf", [128, 8 * LB], f16), "ne": ("sbuf", [128, 8 * LB], f16), "lo": ("sbuf", [128, 3 * 8 * LB], f16),
     "g16": ("sbuf", [128, R], f16), "ti": ("sbuf", [128, 192], i32), "tau": ("sbuf", [128, 192], f32),
     "cc": ("sbuf", [128, 384], f32), "t16": ("sbuf", [128, 448], f16), "ou": ("sbuf", [128, 192], u16),
-    "dd": ("sbuf", [128, 4 * L], f16), "xr": ("sbuf", [128, 4 * R], bf), "ab0": ("sbuf", [128, 8, 9, 8], bf),
-    "pm": ("sbuf", [128, 272], f32), "rk": ("sbuf", [128, 240], f32), "eq": ("sbuf", [128, 192], f32), "eqw": ("sbuf", [128, 72], f32),
-    "ve": ("sbuf", [128, 384], f32), "vw": ("sbuf", [128, 4 * 72], f32), "lv": ("sbuf", [128, 96], u16),
+    "dd": ("sbuf", [128, 4 * L], f16), "xr": ("sbuf", [128, 4 * R], bf), "ab0": ("sbuf", [128, 16, 8, 4], bf),
+    "pm": ("sbuf", [128, 272], f32), "rk": ("sbuf", [128, 240], f32), "eq": ("sbuf", [128, 192], f32), "eqw": ("sbuf", [128, 128], f32),
+    "ve": ("sbuf", [128, 384], f32), "vw": ("sbuf", [128, 5 * 64], f32), "lv": ("sbuf", [128, 96], u16),
     "xg": ("sbuf", [128, R], bf), "sh": ("sbuf", [128, R], f16),
     "ky": ("sbuf", [128, 384], f16), "xk": ("sbuf", [128, 128], f16), "la": ("sbuf", [128, 48], u16),
     "f8": ("sbuf", [128, 16], bf), "xf": ("sbuf", [128, 128], bf), "mxi": ("sbuf", [128, 128], i32), "dm": ("sbuf", [128, 128], f32),
     "gv": ("sbuf", [128, 128], f16), "gi": ("sbuf", [128, 128], f16),
     "ic": ("sbuf", [128, 128], i32), "ij": ("sbuf", [128, 256], i32), "iu": ("sbuf", [128, 256], f32),
-    "km": ("sbuf", [128, 128], f32), "kf": ("sbuf", [128, 128], bf), "kk": ("sbuf", [128, 256], f16), "gs": ("sbuf", [128, 256], f16),
-    "g32": ("sbuf", [128, 256], f32), "yy": ("sbuf", [128, 256], f16), "w1": ("sbuf", [128, 256], f32), "fl": ("sbuf", [128, 256], f16),
+    "kf": ("sbuf", [128, 128], bf), "kk": ("sbuf", [128, 256], f16), "gs": ("sbuf", [128, 256], f16),
+    "g32": ("sbuf", [128, 256], f32), "yy": ("sbuf", [128, 256], f16), "w1": ("sbuf", [128, 256], f32),
     "t1": ("sbuf", [128, 256], f32), "md": ("sbuf", [128, 128], f32),
     "q1": ("sbuf", [128, 128], bf), "rr": ("sbuf", [128, 128], f16),
 }
@@ -72,7 +76,8 @@ def bits(lo, n, step=1):
     return ((1 << (n * step)) - 1) // ((1 << step) - 1) << lo
 
 
-def build(rank_peers):
+def build(rank_peers, cost=None):
+    CY, PEC, GAM, SCA, TTG, SFIX, DFIX, DRATE, XLAT = (cost or COST)[:9]
     ops = []
     ndma, tag = [0], ["_"]
 
@@ -177,10 +182,10 @@ def build(rank_peers):
         v = ops.pop()
         name = out[0] + tag[0]
         ops[-1]["name"] = name
+        ops[-1]["alt"] = {"S": (ops[-1]["fn"], c), "V": (v["fn"], v["c"])}
+        ops[-1]["pin"] = name in ONV or name in ONS2
         if name in ONV:
             ops[-1].update(e="V", fn=v["fn"], c=v["c"])
-        elif name not in ONS2:
-            ops[-1]["alt"] = {"S": (ops[-1]["fn"], c), "V": (v["fn"], v["c"])}
 
     def mm(groups, piece=99):
         calls = [(x[2] if len(x) > 2 else out, x[0], x[1], i == 0, i == len(terms) - 1) for out, terms in groups for i, x in enumerate(terms)]
@@ -233,7 +238,9 @@ def build(rank_peers):
     iota(ref("ei", 0, 8), [[1, 8]], 0, 0)
     R4 = max(c[1] for c in CHUNKS) // 4
     iota(ref("kt16", 0, R4), [[0, R4 // 4], [1, 4]], 0, 0)
-    iota(ref("x9", 0, 72), [[0, 8], [1, 9]], 0, 0)
+    iota(ref("x9", 0, 64), [[0, 8], [1, 8]], 0, 0)
+    iota(ref("eqw", 0, 128), [[0, 128]], 1, 0)
+    iota(ref("c9", 0, 192), [[0, 192]], 0, 0)
     iota(ref("jb", 0, 8 * LB), [[-16, 8], [1, LB]], -1, 0)
     iota(ref("nt", 0, B), [[1, B]], -int(ENC), 0)
     iota(ref("nt", B, SN - B), [[1, SN - B]], B - int(ENC), 0)
@@ -262,8 +269,6 @@ def build(rank_peers):
     ts(C7, T2, 7.0, A.mult)
     tt(CG, CGS, C7, A.subtract)
     tt(CSG, CPM, T2, A.subtract)
-    ts(col(30), CA, 1.0, A.add, T2, A.mult)
-    ts(CAD, col(30), -1.0, A.add)
     ts(col(15), CG16, 0.25, A.mult, 3.0, A.add)
     for k in range(4):
         ts(ref("my", 144 * k, 140), ref("ci", 0, 140), col(12), A.is_equal, col(8 + k), A.mult)
@@ -293,7 +298,7 @@ def build(rank_peers):
     tt(col(20), CP, T1, A.subtract)
     ts(SH, ci, col(20), A.is_equal, T1, A.mult)
     ts(PMS, ci, col(20), A.is_equal, col(40), A.mult)
-    aff(col(21), T2, -BIG, 0.0)
+    ts(col(21), CS, 11.0, A.is_equal, -BIG, A.mult)
     ts(BODP, ref("cp", 0, 128), col(17), A.is_equal, col(21), A.mult)
     ts(BOP, ref("cp", 0, 128), col(17), A.is_equal, BIG / 4, A.mult)
     ts(BOK, ref("cp", 128, 128), col(17), A.is_equal)
@@ -301,12 +306,13 @@ def build(rank_peers):
     add("G", lambda g, T: g.affine_select(ap(T, LQ), ap(T, BOQ), [[1, 128]], A.is_gt, 0.0, 0, -1), [LQ], [BOQ], 170 + 256 * CY)
     DG = ref("dg", 0, 128)
     ts(DG, ref("j16", 0, 128), CS, A.is_equal)
-    ts(ref("eu", 0, 8), ref("ei", 0, 8), 9.0, A.mult, 7.0, A.add)
+    ts(ref("eu", 0, 8), ref("ei", 0, 8), 8.0, A.mult, 7.0, A.add)
     tc(ref("eu", 8, 8), ref("ei", 0, 8))
     aff(col(36), T0, ENC, col(22))
     aff(col(37), T0, ENC - BIG, col(22))
     aff(col(38), T1, -ENC, 0.0)
-    aff(col(39), CU, ENC, 0.0)
+    aff(col(48), col(21), -1.0 / BIG, 0.0)
+    aff(col(39), CU, ENC, col(48))
     aff(col(44), T3, -1.0, 1.0)
     aff(col(45), T1, BIG, 0.0)
     aff(col(46), T2, BIG, col(45))
@@ -323,12 +329,13 @@ def build(rank_peers):
     aff(ref("kf", 0, 128), DAL, -BIG, 0.0)
     tt(DX, ref("kf", 0, 128), IM, A.subtract)
     ts(ref("mz4", 288, 143), ref("ci", 0, 143), col(16), A.is_equal, CU, A.mult)
+    aff(ref("mz", 432, 143), ref("mz", 0, 143), T2, 0.0)
     cw = lambda i: ref("cw", 8 * i, 8)
     ts(cw(0), ref("ei", 0, 8), 16.0, A.mult, CS, A.add)
     ts(col(31), CH, 4.0, A.mult)
     ts(col(32), CH, 4.0, A.mult, 3.0, A.add)
-    x9 = lambda i: ref("x9", 72 * i, 72)
-    ts(ref("rk", 0, 72), x9(0), 0.0, A.is_equal, 1.0e6, A.mult)
+    x9 = lambda i: ref("x9", 64 * i, 64)
+    ts(ref("rk", 0, 64), x9(0), 0.0, A.is_equal, 1.0e6, A.mult)
     ts(x9(1), x9(0), col(32), A.is_equal, 4.0, A.mult)
     ts(x9(2), x9(0), col(31), A.is_ge)
     ts(x9(3), x9(0), col(32), A.is_gt)
@@ -336,8 +343,7 @@ def build(rank_peers):
     tt(x9(1), x9(1), x9(2), A.add)
     ts(x9(2), x9(2), 1.0, A.add, 32768.0, A.mult)
     ts(x9(3), x9(0), col(31), A.subtract)
-    tt(ref("ktw", 0, 72), x9(2), x9(3), A.add)
-    fill(view("ab0", al, 8, al), 0.0)
+    tt(ref("ktw", 0, 64), x9(2), x9(3), A.add)
     blk = lambda nm, i, x: ref(nm, 8 * LB * i + x, 8, LB)
     ts(ref("dz", 0, 8 * LB), ref("jb", 0, 8 * LB), CS, A.is_equal, -BIG, A.mult)
     iota(ref("ne", 0, 8 * LB), [[0, 8 * LB]], int(BIG), 0)
@@ -354,10 +360,10 @@ def build(rank_peers):
                     if any("R" in x for x in w) and w[h][k] == "D":
                         iota(view("dd%d%d" % (i, rd), slice(h * nh, h * nh + nh), k), [[0, nh]], -int(QO), 0)
     for t in range(RO):
-        aff(ref("c9", 16 * t, 8), cw(0), 0.0, 0.0)
-        aff(ref("c9", 16 * t + 8, 8), cw(0), 1.0, 128.0 * t)
+        aff(ref("c9", 64 * t + 7, 8, 8), cw(0), 1.0, 128.0 * t)
         aff(cw(1 + t), cw(0), -1.0, ENC + OFF - 128.0 * t)
         aff(col(33 + t), T2, 6.0 - t - BIG, col(38))
+        aff(col(50 + t), col(33 + t), 1.0, -7 * BIG)
         iota(ref("tc16", 256 * t, 256), [[1, 256]], B + 384 * t - int(BIG), 0)
     for z in range(2):
         aff(ref("mt", 384 * z, 384), ref("nt", 0, 384), CU, col(39))
@@ -370,28 +376,29 @@ def build(rank_peers):
         tc(ref("stu", c0 // 16, n // 16), ref("sti", c0 // 16, n // 16))
         act(ref("qh", c0, n), ref("qb", c0, n), F.Identity, bias=QO)
     for i in range(8):
-        ts(ref("mt", OFF + 256 * i, 256), ref("mi", 256 * i, 256), CSG, A.mult, C7, A.add)
+        aff(ref("mt", OFF + 256 * i, 256), ref("mi", 256 * i, 256), CSG, C7)
         ops[-1]["after"] = [0, 1]
     conv = list(range(len(ops) - 8, len(ops)))
     ts(ref("ij", 0, 128), ref("ic", 0, 128), 2, A.logical_shift_right)
     ts(ref("ij", 128, 128), ref("ic", 0, 128), 3, A.bitwise_and)
-    ts(ref("iu", 0, 128), ref("ij", 0, 128), float(OFF), A.add)
-    tc(ref("iu", 128, 128), ref("ij", 128, 128))
+    aff(ref("iu", 0, 128), ref("ij", 0, 128), 1.0, float(OFF))
+    act(ref("iu", 128, 128), ref("ij", 128, 128), F.Copy)
     dma("Y", (lambda T: [(T.mt[3 + 4 * r::16, OFF:OFF + B], T.iu[:, 128 * r:128 * r + 128]) for r in range(2)], 2), [ref("mt", OFF, B)],
         [ref("iu", 0, 256)], 1 << 17)
     back = len(ops) - 1
     dma("Y", (lambda T: [(T.mn[3::4, 0:B], T.nt[3::4, 0:B])], 1), [ref("mn", 0, B // 2)], [ref("nt", 0, B)], 1 << 18)
-    dma("Y", (lambda T: [(T.mn[r::4, 0:B], T.mt[r::4, OFF:OFF + B]) for r in range(3)], 3), [ref("mn", B // 2, B // 2)], [ref("mt", OFF, B)], 3 << 18)
+    dma("Y", (lambda T: [(T.mn[0::4, 0:B], T.mt[0::4, OFF:OFF + B])], 1), [ref("mn", B // 2, B // 2)], [ref("mt", OFF, B)], 1 << 18)
     dma("Y", (lambda T: [(T.yp[:, 0:B], T.mt[0::4, OFF:OFF + B])], 1), [], [ref("mt", OFF, B)], 262144)
     for o in ops[-2:]:
         o["after"], o["skip"] = conv, back
 
     LA = lambda i: ref("la", 8 * i, 8)
-    vw = lambda i, x=7: ref("vw", 72 * i + x, 8, 9)
+    vw = lambda i: ref("vw", 64 * i + 7, 8, 8)
 
     def reads(t, ci_, c0, n, ways):
         base = B + 384 * t
         m, r4 = n // 16, n // 4
+        ways = [[PER["%d%d%d" % (t, ci_, rd)]] if "%d%d%d" % (t, ci_, rd) in PER else ways[rd] for rd in range(2)]
         H = len(ways[0])
         nh, mh = n // H, m // H
         pb = pb2 = "ps" + BANKS[ci_][0]
@@ -405,8 +412,8 @@ def build(rank_peers):
         o4 = c0 // 4
         c4_ = lambda nm, lo=0, cnt=r4: ref(nm, o4 + lo, cnt)
         pD, pE, pP = ref(pb, 0, r4), ref(pb, r4, r4, 2), ref(pb, r4 + 1, r4, 2)
-        pS = ref(pb2, at + r4, r4) if ci_ else ref("ps2", 288, 72)
-        pU = pS if ci_ else ref("ps2", 256, r4)
+        pS = ref(pb2, at + r4, r4) if ci_ else ref("ps2", 320, 64)
+        pU = pS if ci_ else ref("ps2", 384, r4)
         tb = 2 * o4 + (64 if ci_ else 0)
         pc = PIECE if ci_ else 99
         qs = "sh" if ci_ == 0 and t > 0 else "qh"
@@ -418,12 +425,12 @@ def build(rank_peers):
         part = lambda r, h, w: ref(r[0], r[1] + h * w, w)
         for rd in range(2):
             tag[0] = "%d%d" % (ci_, rd)
-            XW = lambda off: ind("xt", OFF, OFF + base, off) if ci_ == 0 or t + rd == 0 else ind("xs", SN * t, SN * t + base, off)
+            XW = lambda off: ind("xt", OFF, OFF + base, off) if ci_ == 0 or (rd == 0 and (t == 0 or ci_ in LIVE)) else ind("xs", SN * t, SN * t + base, off)
             for h in range(H):
                 groute, lh, go = ways[rd][h][5], part(lst, h, mh), ref("g16", c0 + h * nh, nh)
                 gw = ind("mn", 0, base, lh) if ci_ and rd else ind("mt", OFF, OFF + base, lh)
-                if t == 0 and (rd == 0 or groute == "V"):
-                    ts(go, ind("mi", 0, B, lh), CSG, A.mult, CGS, A.add)
+                if t == 0:
+                    aff(go, ind("mi", 0, B, lh), CSG, CGS)
                 elif groute == "S":
                     act(go, gw, F.Identity, bias=CG)
                 else:
@@ -436,7 +443,7 @@ def build(rank_peers):
                 ops[-2]["free"] = [len(ops) - 3]
                 tt(ref("cc", 2 * o4 + 1, r4, 2), pD, c4_("ti"), A.is_ge)
             else:
-                pD = ref("ps" + BANKS[ci_][1], n, r4) if ci_ else ref("ps2", 384, r4)
+                pD = ref("ps" + BANKS[ci_][1], n, r4) if ci_ else ref("ps2", 416, r4)
                 mm([(pD, [(Y(8, s), gs(s)) for s in range(4)])])
                 mm([(pE, [(Y(4, s), gs(s)) for s in range(4)]), (pP, [(Y(0, s), gs(s)) for s in range(4)])], pc)
                 tt(ref("cc", 2 * o4 + 1, r4, 2), pD, c4_("tau"), A.is_ge)
@@ -445,7 +452,10 @@ def build(rank_peers):
             if last:
                 ts(ref("t16", 65, r4, 2), pD, -1.7, A.is_gt)
             t16 = lambda cl, cnt=m: ref("t16", tb + 2 * cl + 1, cnt, 8)
-            for k0, k1 in (KS if ci_ == 0 else [(0, 4)]):
+            whole = ways[rd][0][0] == "E"
+            if whole:
+                ts(c4_("ou"), ref("t16", tb + 1, r4, 2), ENC, A.add)
+            for k0, k1 in ([] if whole else KS if ci_ == 0 else [(0, 4)]):
                 mm([(ref(pb2, at + k * m, m), [(Y(k, cl), t16(cl)) for cl in range(4)]) for k in range(k0, k1)], pc)
                 ts(c4_("ou", k0 * m, (k1 - k0) * m), ref(pb2, at + k0 * m, (k1 - k0) * m), ENC, A.add)
             YD = lambda k, cl: Y(5 + k if k < 3 else 3, cl)
@@ -453,14 +463,25 @@ def build(rank_peers):
                 mm([(ref(pb2, at + 2 * r4 + k, m, 4), [(YD(k, cl), t16(cl)) for cl in range(4)]) for k in range(4)], pc)
             else:
                 cnt = 16 if last else 8
-                mm([(ref("ps2", 64 + 4 * h + k, cnt, 9), [(YD(k, cl), t16(cl, cnt)) for cl in (2 * h, 2 * h + 1)]) for h in range(2) for k in range(4)]
-                   + [(ref("ps2", 72, cnt, 9), [(I16, ref("c9", 16 * t, cnt))])])
+                mm([(ref("ps2", 64 + 8 * h + 2 * k, cnt, 16), [(YD(k, cl), t16(cl, cnt)) for cl in (2 * h, 2 * h + 1)]) for h in range(2) for k in range(4)]
+                   + [(ref("ps2", 193, 64, 2), [(I16, ref("c9", 64 * t, 64))])] * last)
             relu = any("R" in x for x in ways[rd])
-            for h in range(H):
+            if whole:
+                parts = 4 if ci_ else 1
+                w = n // parts
+                for h in range(parts):
+                    pd, lo = px(0, 4 * w), 4 * (c0 + h * w)
+                    cut = 1 if ci_ else int(ways[rd][0][1])
+                    for x in range(cut):
+                        act(ref("xr", lo + x * 4 * w // cut, 4 * w // cut), XW(c4_("ou", h * w // 4 + x * w // 4 // cut, w // 4 // cut)), F.Copy)
+                    minus = [(INEG, ref("qh", c0 + h * w, w), ref(pd[0], pd[1] + k, w, 4)) for k in range(4)]
+                    mm([(pd, minus + [(IB, ref("xr", lo, 4 * w))])], 4)
+                    act(view("ab%d" % ci_, slice(h * w, h * w + w), al) if ci_ else view("ab0", al, al, al), pd, F.Abs, bias=QO)
+            for h in range(0 if whole else H):
                 routes, q, js = ways[rd][h][:4], ref("qh", c0 + h * nh, nh), slice(h * nh, h * nh + nh)
                 run = lambda x: [(k, k + 1) for k in range(4) if routes[k] == x] if not (ci_ and x in JOIN and (x != "D" or H == 1)) else \
                     [(routes.index(x), routes.rindex(x) + 1)] if x in routes else []
-                ab = lambda k0, k1: view("ab%d" % ci_, js, slice(k0, k1)) if ci_ else view("ab0", al, slice(k0, 8, 4), al)
+                ab = lambda k0, k1: view("ab%d" % ci_, js, slice(k0, k1)) if ci_ else view("ab0", al, al, k0)
                 dd = lambda k0, k1: view("dd%d%d" % (ci_, rd), js, slice(k0, k1) if k1 > k0 + 1 else k0) if ci_ else ref("dd", k0 * n, n)
                 for k0, k1 in run("D"):
                     act(ref("xr", 4 * c0 + k0 * n + h * nh, (k1 - k0) * nh), XW(c4_("ou", k0 * m + h * mh, (k1 - k0) * mh)), F.Copy)
@@ -486,17 +507,17 @@ def build(rank_peers):
                 scan(ref("ve", 192 * rd + o4, r4), c4_("eq"), ref(pb2, at + 2 * r4, r4), 0.0, A.mult, A.add)
                 ts(lst, ref("ve", 192 * rd + o4 + 3, m, 4), ENC, A.add)
             else:
-                mm([(pS, [(IB, ref("ktw", 0, 72))] + [(ref("mz", 144 + 7 - s, 128), view("ab0", al, al, s)) for s in range(8)])])
-                eq = ref("eqw", 0, 72)
-                scan(ref("pm", 0, 72), ref("rk", 0, 72), pS, 0.0, A.add, A.min)
-                tt(eq, pS, ref("pm", 0, 72), A.not_equal)
-                scan(ref("vw", 72 * rd, 72), eq, ref("ps2", 64, 72), 0.0, A.mult, A.add)
+                mm([(pS, [(IB, ref("ktw", 0, 64))] + [(ref("mz", 144 + 7 - s, 128), view("ab0", al, s, al)) for s in range(8)])])
+                eq = ref("eqw", 0, 64, 2)
+                scan(ref("pm", 0, 64), ref("rk", 0, 64), pS, 0.0, A.add, A.min)
+                tt(eq, pS, ref("pm", 0, 64), A.not_equal)
+                scan(ref("vw", 64 * rd, 64), eq, ref("ps2", 64, 64, 2), 0.0, A.mult, A.add)
                 ts(lst, vw(rd), ENC, A.add)
                 if last:
-                    scan(ref("vw", 144, 72), eq, x9(1), 0.0, A.mult, A.add)
-                    tt(ref("eqw", 8, 8, 9), blk("lo", 0, LB - 2), cw(1 + t), A.add)
-                    scan(ref("vw", 216, 72), eq, ref("ps2", 136, 72), 0.0, A.mult, A.add)
-                    tc(LA(4), vw(3, 8))
+                    scan(ref("vw", 128, 64), eq, x9(1), 0.0, A.mult, A.add)
+                    tt(ref("eqw", 15, 8, 16), blk("lo", 0, LB - 2), cw(1 + t), A.add)
+                    scan(ref("vw", 192, 128), ref("eqw", 0, 128), ref("ps2", 192, 128), 0.0, A.mult, A.add)
+                    tc(LA(4), ref("vw", 192 + 15, 8, 16))
             hb = QO / 2 - 0.25
             for h in range(H):
                 qroute, c1, xw = ways[rd][h][4], c0 + h * nh, XW(part(lst, h, mh))
@@ -522,7 +543,8 @@ def build(rank_peers):
                     dma("Y", (lambda T, c1=c1: [(T.yq[:, c1:c1 + nh], T.qo[:, c1:c1 + nh])], 1), [], [ref("qo", c1, nh)], 256 * nh)
             if ci_ == 0 and rd == 0:
                 lowest_of(t, 0, lst)
-                step_a(t, 0, LA(0))
+            elif ci_ == 0:
+                step_a(0)
 
     def lowest(i, key, own):
         for c in range(7, -1, -1):
@@ -542,26 +564,23 @@ def build(rank_peers):
 
     pL, pY, pR, pM = [ref("ps1", 128 * i, 128) for i in range(4)]
 
-    def step_a(t, z, la):
-        h = lambda nm: ref(nm, 128 * z, 128)
-        MW = ind("mt", 0, OFF + B + 384 * t, la)
-        act(h("gs"), MW, F.Identity, bias=CGS)
-        mm([(pL, [(DAL, h("gs"))])])
-        act(pL, pL, F.Relu, bias=1.0, scale=-1.0)
-        tt(h("yy"), pL, h("gs"), A.mult)
+    node = [ref("g16", 0, 128), ref("gs", 0, 128)]
+
+    def step_a(z):
+        mm([(pL, [(DAL, node[z])])])
+        act(pL, pL, F.Relu, bias=1.0 if z else -6.0, scale=-1.0)
+        tt(ref("yy", 128 * z, 128), pL, node[z], A.mult)
 
     def step_b(t, z, lg, la, back):
         base = B + 384 * t
         h = lambda nm: ref(nm, 128 * z, 128)
         name = ref("tc16", 128 * (2 * t + z), 128)
         act(h("g32"), ind("mt", 0, OFF + base, lg), F.Copy)
-        mm([(pY, [(DX, h("gs")), (IM, name), (IMD, h("kk"))])])
-        act(h("w1"), pY, F.Relu, bias=col(33 + t))
-        if z == 0:
-            act(h("fl"), pY, F.Relu, bias=col(33 + t))
+        mm([(pY, [(DX, node[z]), (IM, name), (IMD, h("kk"))])])
+        act(h("w1"), pY, F.Relu, bias=col((33 if z else 50) + t))
         tt(ind("mt", 0, OFF + base, la), h("g32"), h("w1"), A.add)
-        off = (BODP, h("fl")) if z == 0 else (BOP, ref("xf", 0, 128))
-        mm([(pR, [(SH, h("gs")), (PMS, h("yy")), (IT3, back), off]), (pM, [(IP, name), (IPB, h("kk"))] + [(IP, NB)] * z + [off])])
+        off = (BODP, back) if z == 0 else (BOP, ref("xf", 0, 128))
+        mm([(pR, [(SH, node[z]), (PMS, h("yy")), (IT3, back), off]), (pM, [(IP, name), (IPB, h("kk"))] + [(IP, NB)] * z + [off])])
         act(h("t1"), pR, F.Relu, bias=col(37) if z else col(36))
         tt(ref("mt", OFF + base + 128 * (z + 1), 128), pM, h("t1"), A.max)
 
@@ -575,7 +594,7 @@ def build(rank_peers):
         tag[0] = "1"
         lowest_of(t, 1, lv)
         xk = ref("xk", 0, 128)
-        tt(xk, ind("vw", 144, 216, ref("eu", 0, 8)), DG, A.mult)
+        tt(xk, ind("vw", 128, 192, ref("eu", 0, 8)), DG, A.mult)
         pk, pN, pmd = ref("ps0", 128, 128), ref("ps0", 256, 128), ref("ps0", 384, 128)
         act(ref("gv", 0, 128), ind("mt", OFF, OFF + base, lv), F.Identity, bias=CGS)
         mm([(pN, [(IK3, ref("gv", 0, 128)), (IU, ref("ky", 0, 128)), (BOK, xk)])])
@@ -594,7 +613,7 @@ def build(rank_peers):
         tc(ind("mt", 0, nn, LA(1)), ref("mt", nn, 128))
         tc(ind("xt", 0, nn, LA(1)), ref("mxi", 0, 128))
         sn = SN * (t + 1)
-        if t < RO - 1:
+        if t < RO - 1 and not LATE:
             dma("Y", (lambda T: [(T.xs[:, sn:sn + base], T.xt[:, OFF:nn])], 1), [ref("xs", sn, base)], [ref("xt", OFF, base)], 256 * base)
         gi = ref("gi", 0, 128)
         act(gi, ind("mt", 0, nn, LA(4)), F.Identity, bias=CGS)
@@ -606,19 +625,18 @@ def build(rank_peers):
         mm([(pk2, [(BK, gi)])])
         act(ref("ky", 256, 128), pkey, F.Copy)
         ts(LA(5), own, OFF + ENC, A.add)
-        ts(ref("km", 0, 128), pk2, CAD, A.not_equal, 2 * BIG, A.mult)
         ts(ref("kk", 128, 128), pk2, CA, A.is_equal)
         aff(blk("dz", 0, LB - 2), cw(0), 1.0, 128.0 * t - OFF - ENC)
         aff(blk("dz", 0, LB - 1), cw(0), -1.0, OFF + ENC - 128.0 * t)
         tc(blk("ne", 0, LB - 2), own)
         lowest(2, ref("ky", 256, 128), own)
-        tt(ref("kf", 0, 128), ind("mt", 0, nn, LA(5)), ref("km", 0, 128), A.is_gt)
-        pF, pos = ref("ps2", 256, 8), ref("ps2", 272, 8)
-        mm([(pF, [(ref("mz", 15 - s, 128), ref("kf", s, 8, 16)) for s in range(16)])])
+        tt(ref("kf", 0, 128), ind("mt", 0, nn, LA(5)), ref("kk", 128, 128), A.min)
+        pF, pos = ref("ps2", 448, 8), ref("ps2", 464, 8)
+        mm([(pF, [(ref("mz", 432 + 15 - s, 128), ref("kf", s, 8, 16)) for s in range(16)])])
         f, f2 = ref("f8", 0, 8), ref("f8", 8, 8)
         tt(f, pF, blk("lo", 2, LB - 3), A.min)
         tt(f2, pF, blk("lo", 2, LB - 1), A.mult)
-        mm([(pos, [(IB, ref("cb", 0, 8)), (LQ, f)] + [(BOQ, ref("f8", 0, 8 - d), ref("ps2", 272 + d, 8 - d)) for d in range(1, 8)] + [(INQ, f2)])])
+        mm([(pos, [(IB, ref("cb", 0, 8)), (LQ, f)] + [(BOQ, ref("f8", 0, 8 - d), ref("ps2", 464 + d, 8 - d)) for d in range(1, 8)] + [(INQ, f2)])])
         tc(LA(3), pos)
         tc(ind("snd", BX * t, BX * t + BX, LA(3)), ref("xt", nn, 128) if t < RO - 1 else ref("q1", 0, 128))
         rid, pid, mask = rank_peers[t]
@@ -630,13 +648,17 @@ def build(rank_peers):
         ts(LA(2), blk("lo", 2, LB - 2), OFF + ENC, A.add)
         tt(ref("xf", 0, 128), ind("f8", 0, 8, ref("eu", 8, 8)), DG, A.mult)
         tag[0] = "2"
-        step_a(t, 1, LA(5))
-        step_b(t, 1, LA(5), LA(2), ref("gs", 128, 128))
+        act(node[1], ind("mt", 0, nn, LA(5)), F.Identity, bias=CGS)
+        step_a(1)
+        step_b(t, 1, LA(5), LA(2), node[1])
         mm([(pmd, [(BOQ, ref("xf", 0, 128))])])
         act(ref("md", 0, 128), pmd, F.Copy)
         tt(ref("xt", nn + 256, 128), ind("xt", 0, nn, LA(5)), ref("md", 0, 128), A.mult)
         if t < RO - 1:
-            dma("Y", (lambda T: [(T.xs[:, sn + base:sn + base + 384], T.xt[:, nn:nn + 384])], 1), [ref("xs", sn + base, 384)], [ref("xt", nn, 384)], 98304)
+            x0 = 0 if LATE else base
+            dma("Y", (lambda T: [(T.xs[:, sn + x0:sn + base + 384], T.xt[:, OFF + x0:nn + 384])], 1), [ref("xs", sn + x0, base + 384 - x0)],
+                [ref("xt", OFF + x0, base + 384 - x0)], 256 * (base + 384 - x0) * (1 + LATE))
+            ops[-1]["after"] = [sent[t]] * LATE
             dma("Y", (lambda T: [(T.mn[r::4, 0:base], T.mt[r::4, OFF:nn]) for r in (1, 2)] + [(T.mn[:, base:base + 384], T.mt[:, nn:nn + 384])], 3),
                 [ref("mn", 0, base + 384)], [ref("mt", OFF, base + 384)], 256 * base + 200000)
             ops[-1]["after"] = [sent[t]]
@@ -693,6 +715,7 @@ def depends(ops):
 
 def schedule(ops):
     n = len(ops)
+    HOP, SELF = COST[9:]
     succ, pred = [[] for _ in ops], [[] for _ in ops]
     for i, o in enumerate(ops):
         for j in o["dep"]:
@@ -731,7 +754,7 @@ def one_pass(ops, succ, pred, pr, rdy, choose):
 
     def enter(i):
         o = ops[i]
-        if choose and "alt" in o:
+        if choose and "alt" in o and not o["pin"]:
             end = {e: max(rdy[i], free[e] + sum(ops[j]["c"] for j in pool[e] if pr[j] > pr[i] - AHEAD)) + o["alt"][e][1] * WEIGH[e] for e in "SV"}
             o["e"] = min("SV", key=lambda e: end[e])
             o["c"] = o["alt"][o["e"]][1]
@@ -766,6 +789,111 @@ def one_pass(ops, succ, pred, pr, rdy, choose):
     return order, start
 
 
+def replay(s, order, lo, fin):
+    eng, c, pred, ends = s
+    fin, free = fin[:], {}
+    for k in range(lo - 1, -1, -1):
+        if eng[order[k]] not in free:
+            free[eng[order[k]]] = fin[order[k]]
+            if len(free) == 5:
+                break
+    for k in range(lo, len(order)):
+        i = order[k]
+        t = free.get(eng[i], 0.0)
+        for j, d in pred[i]:
+            if fin[j] + d > t:
+                t = fin[j] + d
+        fin[i] = free[eng[i]] = t + c[i]
+    return max(fin[i] + d for i, d in ends), fin
+
+
+def polish(ops, order):
+    n = len(ops)
+    eng = [o["e"] for o in ops]
+    pred = [set(o["dep"]) for o in ops]
+    succ = [set() for _ in ops]
+    for i in range(n):
+        for j in pred[i]:
+            succ[j].add(i)
+    alts = [build([(0, 0, 0)] * RO, cost) for cost in OTHER]
+    sets = [(eng, [0.0] * n, [0] * n, [(i, alt[i]["lat"]) for i in range(n) if not succ[i]]) for alt in alts]
+
+    def price(calls):
+        for s, alt, cost in zip(sets, alts, OTHER):
+            for i in calls:
+                s[1][i] = alt[i]["alt"][eng[i]][1] if "alt" in alt[i] else alt[i]["c"]
+                s[2][i] = [(j, alt[j]["lat"] + (0.0 if j in ops[i].get("free", ()) else cost[10] if eng[i] == eng[j] and not ops[j]["sem"] else cost[9]))
+                           for j in ops[i]["dep"]]
+
+    def flip(i):
+        eng[i] = "S" if eng[i] == "V" else "V"
+        price([i] + sorted(succ[i]))
+    price(range(n))
+    now = [replay(s, order, 0, [0.0] * n) for s in sets]
+    unit = [len(sets) * x[0] for x in now]
+    seed, val, best, held = [SEED], 1.0, (1.0, order, eng[:]), None
+
+    def rnd():
+        seed[0] = (seed[0] * 1103515245 + 12345) % 2147483648
+        return (seed[0] + 1) / 2147483650.0
+    for it in range(MOVES):
+        if held is None:
+            held, last, prev = [], {}, {}
+            for i in order:
+                prev[i], last[eng[i]] = last.get(eng[i], -1), i
+            for s, (_, fin) in zip(sets, now):
+                i = max(s[3], key=lambda x: fin[x[0]] + x[1])[0]
+                while i >= 0:
+                    st, p = fin[i] - s[1][i], prev[i]
+                    if p >= 0 and abs(fin[p] - st) < 1e-6:
+                        if p not in pred[i]:
+                            held.append((p, i))
+                        i = p
+                    else:
+                        i = max([j for j, d in s[2][i] if abs(fin[j] + d - st) < 1e-6] + [-1])
+            place = {x: k for k, x in enumerate(order)}
+        j, i = held[int(rnd() * len(held))]
+        a, b, k, up = place[j], place[i], (0, 0, 1, 2, 3, 5)[int(rnd() * 6)], rnd() < 0.5
+        other = (i if up else j) if "alt" in ops[i if up else j] and rnd() < FLIP else -1
+        if other >= 0:
+            flip(other)
+            a, new = place[other], order
+        else:
+            while k and 0 < a and b < n - 1:
+                a, b = (a - 1, b) if up else (a, b + 1)
+                k -= eng[order[a if up else b]] == eng[i]
+            seg = order[a:b + 1]
+            move = {i if up else j}
+            for x in (seg[::-1] if up else seg):
+                if (succ if up else pred)[x] & move:
+                    move.add(x)
+            if seg[0 if up else -1] in move:
+                continue
+            new = order[:a] + [x for x in seg if (x in move) == up] + [x for x in seg if (x in move) != up] + order[b + 1:]
+        room, got = -WARM * (1 - it / MOVES) * math.log(rnd()), []
+        lost = 0.0
+        for s, x, u in zip(sets, now, unit):
+            got.append(replay(s, new, a, x[1]))
+            lost += (got[-1][0] - x[0]) / u
+            if lost > room + 0.001:
+                break
+        if lost < room:
+            order, val, now, held = new, val + lost, got, None
+            if val < best[0]:
+                best = (val, new, eng[:])
+        elif other >= 0:
+            flip(other)
+    eng[:] = best[2]
+    price(range(n))
+    fin = replay(sets[0], best[1], 0, [0.0] * n)[1]
+    for i, o in enumerate(ops):
+        o["t"], o["e"] = fin[i] - sets[0][1][i], eng[i]
+    return best[1]
+
+
+PLAN = []
+
+
 def rank_program(g, core, T, topo):
     rank = T.rank_of(core)
     if rank is None:
@@ -777,8 +905,14 @@ def rank_program(g, core, T, topo):
         rid, pid, _ = topo.addr(dst)
         peers.append((rid, pid, sum(1 << e for e in topo.engines(core, dst)[:NENG])))
     ops = build(peers)
-    depends(ops)
-    order, _ = schedule(ops)
+    if not PLAN:
+        depends(ops)
+        PLAN.extend([polish(ops, schedule(ops)[0]), ops])
+    order = PLAN[0]
+    for o, p in zip(ops, PLAN[1]):
+        o.update(e=p["e"], dep=p["dep"], free=p.get("free", ()), t=p["t"])
+        if "alt" in o:
+            o["fn"] = o["alt"][o["e"]][0]
     queue = {"V": g.vector, "S": g.scalar, "P": g.tensor, "G": g, "Y": g.sync}
     count = {}
     known = {e: {} for e in queue}

@@ -41,8 +41,8 @@ SCRATCH = {
     "mz": ("sbuf", [128, 4 * 144], bf), "mz4": ("sbuf", [128, 3 * 144], f16), "my": ("sbuf", [128, 9 * 144], f16),
     "mm": ("sbuf", [128, 22 * 128], f16), "mb16": ("sbuf", [128, 6 * 128], bf),
     "dg": ("sbuf", [128, 256], f32), "kt16": ("sbuf", [128, 160], bf), "ktw": ("sbuf", [128, 64], bf), "x9": ("sbuf", [128, 4 * 64], f32),
-    "tc16": ("sbuf", [128, 6 * 128], f16), "jb": ("sbuf", [128, 8 * LB], bf),
-    "dz": ("sbuf", [128, 8 * LB], f16), "ne": ("sbuf", [128, 8 * LB], f16), "lo": ("sbuf", [128, 3 * 8 * LB], f16),
+    "tc16": ("sbuf", [128, 6 * 128], f16), "jb": ("sbuf", [128, 2 * LB], bf),
+    "dz": ("sbuf", [128, 8 * LB], f16), "ne": ("sbuf", [128, 8 * LB], f16), "lo": ("sbuf", [128, 3 * 8 * LB], f16), "ch": ("sbuf", [128, 48], f16),
     "g16": ("sbuf", [128, R], f16), "ti": ("sbuf", [128, 192], i32), "tau": ("sbuf", [128, 192], f32),
     "cc": ("sbuf", [128, 384], f32), "t16": ("sbuf", [128, 448], f16), "ou": ("sbuf", [128, 192], u16),
     "dd": ("sbuf", [128, 4 * L], f16), "xr": ("sbuf", [128, 4 * R], bf), "ab0": ("sbuf", [128, 16, 8, 4], bf),
@@ -67,6 +67,7 @@ for _b in range(1, len(CHUNKS)):
 NDMA = 40
 SEMAPHORES = ["cV", "cS", "cP", "cG", "snt0", "snt1", "snt2", "arr0", "arr1", "arr2"] + ["d%d" % _i for _i in range(NDMA)]
 TWO = (bf, f16, u16)
+HC = set(range(22)) | set(range(40, 48))
 A = AluOpType
 F = ActivationFunctionType
 al = slice(None)
@@ -145,7 +146,7 @@ def build(rank_peers, cost=None):
         return max(64, n * rate) * CY
 
     def half(*rs):
-        return 0.5 if all(kind(r)[2] in TWO for r in rs) else 1.0
+        return 0.5 if all(kind(r)[2] in TWO for r in rs if isinstance(r, tuple)) else 1.0
 
     def tc(out, a):
         add("V", lambda g, T: g.vector.tensor_copy(ap(T, out), ap(T, a)), [out], [a], vcost(out, [a], half(out, a)))
@@ -158,11 +159,13 @@ def build(rank_peers, cost=None):
         add("V", lambda g, T: g.vector.tensor_tensor(ap(T, out), ap(T, a), ap(T, b), op), [out], [a, b], vcost(out, [a], rate))
 
     def ts(out, a, s1, op0, s2=None, op1=None):
+        if nel(out) > 64 and half(out, a) < 1 and a[0] != "*":
+            s1, s2 = [("ch",) + x[1:] if isinstance(x, tuple) and x[0] == "col" and x[1] in HC else x for x in (s1, s2)]
         if op1 is None:
             fn = lambda g, T: g.vector.tensor_scalar(ap(T, out), ap(T, a), ap(T, s1), None, op0)
         else:
             fn = lambda g, T: g.vector.tensor_scalar(ap(T, out), ap(T, a), ap(T, s1), ap(T, s2), op0, op1)
-        add("V", fn, [out], [a, s1, s2], vcost(out, [a], half(out, a)))
+        add("V", fn, [out], [a, s1, s2], vcost(out, [a], half(out, a, s1, s2)))
 
     def scan(out, d0, d1, init, op0, op1):
         add("V", lambda g, T: g.vector.tensor_tensor_scan(ap(T, out), ap(T, d0), ap(T, d1), init, op0, op1), [out], [d0, d1],
@@ -180,6 +183,7 @@ def build(rank_peers, cost=None):
         else:
             return
         v = ops.pop()
+        ops[-1]["rd"] += [x for x in v["rd"] if x not in ops[-1]["rd"]]
         name = out[0] + tag[0]
         ops[-1]["name"] = name
         ops[-1]["alt"] = {"S": (ops[-1]["fn"], c), "V": (v["fn"], v["c"])}
@@ -221,13 +225,18 @@ def build(rank_peers, cost=None):
 
     col = lambda c: ref("col", c, 1)
     aff = lambda o, a, s, b: act(o, a, F.Identity, scale=s, bias=b)
-    dma("S", (lambda T: [(T.mi[2::4, :], T.bd[:]), (T.mi[3::4, :], T.bd[:])], 2), [ref("mi", 0, B // 2)], [], 1 << 20)
-    dma("Y", (lambda T: [(T.mi[0::4, :], T.pf[:]), (T.mi[1::4, :], T.mb[:])], 2), [ref("mi", B // 2, B // 2)], [], 1 << 20)
-    dma("Y", (lambda T: [(T.sti[:], T.st[:]), (T.qb[:], T.qr[:])], 2), [ref("sti", 0, 48), ref("qb", 0, R)], [], 400000)
-    dma("S", (lambda T: [(T.xt[:, OFF:OFF + B], T.xn[:])], 1), [ref("xt", OFF, B)], [], 1100000)
-    dma("Y", (lambda T: [(T.ic[:], T.ip[:])], 1), [ref("ic", 0, 128)], [], 1100000)
+    dma("Y", (lambda T: [(T.sti[:], T.st[:])], 1), [ref("sti", 0, 48)], [], 60000)
+    dma("S", (lambda T: [(T.qb[:], T.qr[:])], 1), [ref("qb", 0, R)], [], 250000)
+    dma("S", (lambda T: [(T.mi[2::4, :], T.bd[:]), (T.mi[3::4, :], T.bd[:])], 2), [ref("mi", 0, B // 2)], [], 1250000)
+    ops[-1].update(after=[1], free=[1])
+    dma("Y", (lambda T: [(T.mi[0::4, :], T.pf[:]), (T.mi[1::4, :], T.mb[:])], 2), [ref("mi", B // 2, B // 2)], [], 1250000)
+    ops[-1].update(after=[0], free=[0])
+    dma("S", (lambda T: [(T.xt[:, OFF:OFF + B], T.xn[:])], 1), [ref("xt", OFF, B)], [], 1750000)
+    ops[-1].update(after=[2], free=[2])
+    dma("Y", (lambda T: [(T.ic[:], T.ip[:])], 1), [ref("ic", 0, 128)], [], 250000)
+    ops[-1]["after"] = [2, 3]
     dma("Y", (lambda T: [(T.xs[:, 0:B], T.xn[:])], 1), [ref("xs", 0, B)], [], 600000)
-    ops[-1]["after"] = [1]
+    ops[-1]["after"] = [4]
     iota(ref("pi", 0, 1), [[0, 1]], 0, 1)
     iota(ref("ci", 0, 144), [[1, 144]], 0, 0)
     iota(ref("c4", 0, 144), [[1, 36], [0, 4]], 0, 0)
@@ -241,7 +250,7 @@ def build(rank_peers, cost=None):
     iota(ref("x9", 0, 64), [[0, 8], [1, 8]], 0, 0)
     iota(ref("eqw", 0, 128), [[0, 128]], 1, 0)
     iota(ref("c9", 0, 192), [[0, 192]], 0, 0)
-    iota(ref("jb", 0, 8 * LB), [[-16, 8], [1, LB]], -1, 0)
+    iota(ref("jb", 0, 2 * LB), [[0, 2], [1, LB]], 19 - LB, 0)
     iota(ref("nt", 0, B), [[1, B]], -int(ENC), 0)
     iota(ref("nt", B, SN - B), [[1, SN - B]], B - int(ENC), 0)
     iota(ref("cc", 0, 384), [[0, 384]], 0, 0)
@@ -270,16 +279,22 @@ def build(rank_peers, cost=None):
     tt(CG, CGS, C7, A.subtract)
     tt(CSG, CPM, T2, A.subtract)
     ts(col(15), CG16, 0.25, A.mult, 3.0, A.add)
+    ts(col(16), CG16, 15.0, A.add)
+    ts(col(17), CG16, 0.0625, A.mult)
+    tt(col(20), CP, T1, A.subtract)
+    ts(col(21), CS, 11.0, A.is_equal, -BIG, A.mult)
+    tc(ref("ch", 0, 7), ref("pi", 0, 7))
+    tc(ref("ch", 8, 6), ref("col", 8, 6))
+    tc(ref("ch", 14, 8), ref("col", 14, 8))
     for k in range(4):
         ts(ref("my", 144 * k, 140), ref("ci", 0, 140), col(12), A.is_equal, col(8 + k), A.mult)
     ts(ref("my", 144 * 4, 140), ref("ci", 0, 140), col(12), A.is_equal, col(13), A.mult)
-    tt(ref("col", 40, 3), ref("col", 8, 3), ref("col", 9, 3), A.subtract)
+    tt(ref("ch", 40, 3), ref("col", 8, 3), ref("col", 9, 3), A.subtract)
     for k in range(3):
         ts(ref("my", 144 * (5 + k), 140), ref("ci", 0, 140), col(12), A.is_equal, col(40 + k), A.mult)
     ts(ref("rk", 80, R4), ref("kt16", 0, R4), 0.0, A.is_equal, 1.0e6, A.mult)
     ts(ref("my", 144 * 8, 140), ref("my", 144 * 2, 140), 0.25, A.mult)
     ts(ref("mz4", 0, 140), ref("c4", 0, 140), col(15), A.is_equal, 0.25, A.mult)
-    ts(col(16), CG16, 15.0, A.add)
     ts(ref("mz", 0, 143), ref("ci", 0, 143), col(16), A.is_equal, 4.0, A.mult)
     tt(ref("mz", 144, 135), ref("mz", 0, 135), ref("mz", 8, 135), A.add)
     Y = lambda k, sh: ref("my", 144 * k + 12 - 4 * sh, 128)
@@ -292,13 +307,10 @@ def build(rank_peers, cost=None):
     if any("R" in x for c in CHUNKS for w in c[2:] for x in w):
         aff(ref("mz", 288, 143), ref("mz", 0, 143), 2.0, 0.0)
         aff(ref("mz4", 144, 143), ref("mz", 0, 143), -1.0, 0.0)
-    ts(col(17), CG16, 0.0625, A.mult)
     ts(BO, c16, col(17), A.is_equal)
     ts(DAL, ref("c4", 0, 128), CP4, A.is_equal, T2, A.mult)
-    tt(col(20), CP, T1, A.subtract)
     ts(SH, ci, col(20), A.is_equal, T1, A.mult)
     ts(PMS, ci, col(20), A.is_equal, col(40), A.mult)
-    ts(col(21), CS, 11.0, A.is_equal, -BIG, A.mult)
     ts(BODP, ref("cp", 0, 128), col(17), A.is_equal, col(21), A.mult)
     ts(BOP, ref("cp", 0, 128), col(17), A.is_equal, BIG / 4, A.mult)
     ts(BOK, ref("cp", 128, 128), col(17), A.is_equal)
@@ -317,6 +329,7 @@ def build(rank_peers, cost=None):
     aff(col(45), T1, BIG, 0.0)
     aff(col(46), T2, BIG, col(45))
     aff(col(47), T0, BIG, 0.0)
+    tc(ref("ch", 44, 4), ref("col", 44, 4))
     rows = [(INEG, -1.0), (IH, 0.5), (IBH, 0.5), (I16, 1.0), (IP, T0), (IM, T1), (IPB, col(47)), (IMD, col(46)), (IK3, col(44)), (IT3, T3), (IU, CU),
             (INQ, -0.25), (IS, -QO / 2)]
     for i, (m_, c) in enumerate(rows):
@@ -345,10 +358,14 @@ def build(rank_peers, cost=None):
     ts(x9(3), x9(0), col(31), A.subtract)
     tt(ref("ktw", 0, 64), x9(2), x9(3), A.add)
     blk = lambda nm, i, x: ref(nm, 8 * LB * i + x, 8, LB)
-    ts(ref("dz", 0, 8 * LB), ref("jb", 0, 8 * LB), CS, A.is_equal, -BIG, A.mult)
-    iota(ref("ne", 0, 8 * LB), [[0, 8 * LB]], int(BIG), 0)
-    aff(blk("dz", 0, 0), cw(0), 0.0, 4 * BIG)
-    aff(blk("dz", 0, LB - 3), cw(0), 0.0, BIG)
+    pair = lambda nm, i, a: ref(nm, 8 * LB * i + 2 * a * (LB - 16) + LB - 20, LB + 20 + 32 * a)
+    for a in range(4):
+        ts(pair("dz", 0, a), ref("jb", LB - 20 - 32 * a, LB + 20 + 32 * a), CS, A.is_equal, -BIG, A.mult)
+        iota(ref("ne", LB * (2 * a + 1), LB - 35 - 32 * a), [[0, LB - 35 - 32 * a]], int(BIG), 0)
+    iota(ref("ne", LB - 20, 4, 2 * LB - 32), [[0, 4]], int(BIG), 0)
+    iota(blk("ne", 0, LB - 3), [[0, 8]], int(BIG), 0)
+    iota(ref("dz", LB - 20, 8, LB - 16), [[0, 8]], 4 * int(BIG), 0)
+    iota(blk("dz", 0, LB - 3), [[0, 8]], int(BIG), 0)
     aff(blk("ne", 0, LB - 1), cw(0), 1.0, 128.0)
     aff(ref("cb", 0, 8), cw(0), 1.0, 128.0)
     for i in range(1, len(CHUNKS)):
@@ -377,7 +394,7 @@ def build(rank_peers, cost=None):
         act(ref("qh", c0, n), ref("qb", c0, n), F.Identity, bias=QO)
     for i in range(8):
         aff(ref("mt", OFF + 256 * i, 256), ref("mi", 256 * i, 256), CSG, C7)
-        ops[-1]["after"] = [0, 1]
+        ops[-1]["after"] = [2, 3]
     conv = list(range(len(ops) - 8, len(ops)))
     ts(ref("ij", 0, 128), ref("ic", 0, 128), 2, A.logical_shift_right)
     ts(ref("ij", 128, 128), ref("ic", 0, 128), 3, A.bitwise_and)
@@ -548,8 +565,9 @@ def build(rank_peers, cost=None):
 
     def lowest(i, key, own):
         for c in range(7, -1, -1):
-            ts(ref("ne", LB * c + 1, 16 * c + 16), ref(key[0], key[1], 16 * c + 16), ref(own[0], own[1] + c * own[3], 1), A.not_equal, BIG, A.mult)
-        scan(ref("lo", 8 * LB * i, 8 * LB), ref("dz", 0, 8 * LB), ref("ne", 0, 8 * LB), 0.0, A.add, A.min)
+            ts(ref("ne", (LB - 16) * c + LB - 19, 16 * c + 16), ref(key[0], key[1], 16 * c + 16), ref("ne", LB * c + LB - 2, 1), A.not_equal, BIG, A.mult)
+        for a in range(3, -1, -1):
+            scan(pair("lo", i, a), pair("dz", 0, a), pair("ne", 0, a), 0.0, A.add, A.min)
 
     def lowest_of(t, i, lst):
         key = ref("ky", 128 * i, 128)
@@ -721,7 +739,7 @@ def schedule(ops):
         for j in o["dep"]:
             p = ops[j]
             either = "alt" in p or "alt" in o
-            d = p["lat"] + (0.0 if j in o.get("free", ()) else (HOP + SELF) / 2 if either else SELF if p["e"] == o["e"] and not p["sem"] else HOP)
+            d = 0.0 if j in o.get("free", ()) else p["lat"] + ((HOP + SELF) / 2 if either else SELF if p["e"] == o["e"] and not p["sem"] else HOP)
             succ[j].append((i, d)); pred[i].append((j, d))
     pr = [0.0] * n
     for i in range(n - 1, -1, -1):
@@ -822,7 +840,7 @@ def polish(ops, order):
         for s, alt, cost in zip(sets, alts, OTHER):
             for i in calls:
                 s[1][i] = alt[i]["alt"][eng[i]][1] if "alt" in alt[i] else alt[i]["c"]
-                s[2][i] = [(j, alt[j]["lat"] + (0.0 if j in ops[i].get("free", ()) else cost[10] if eng[i] == eng[j] and not ops[j]["sem"] else cost[9]))
+                s[2][i] = [(j, 0.0 if j in ops[i].get("free", ()) else alt[j]["lat"] + (cost[10] if eng[i] == eng[j] and not ops[j]["sem"] else cost[9]))
                            for j in ops[i]["dep"]]
 
     def flip(i):

@@ -11,36 +11,40 @@ LB = 132
 BX = 384
 
 SN = 2816
-CHUNKS = [(0, 128, ["E2..MS"], ["E2..SS"]), (128, 320, ["AADDMS"], ["AADDMS"]), (448, 320, ["AAADMS"], ["ADDDMS"])]
-PER = {"000": "E1..MS", "210": "AAADMS", "110": "ADDDMS", "100": "AAADSS", "120": "AADDMS", "121": "E...MS"}
+CHUNKS = [(0, 128, ["F064MS"], ["F064SS"]), (128, 320, ["F192MS"], ["F096MS"]), (448, 320, ["F096MS"], ["F096MS"])]
+PER = {}
 LIVE, LATE = (1, 2), True
 BANKS = ["07", "35", "46"]
 JOIN = "R"
 KS = [(0, 4)]
-ONS = "xvro"
+ONS = "xvo"
 SEED, JIT, LOOK, PASSES = 1, 200.0, 0.3, 6
-PIECE, NV = 4, 4
+PIECE, NV = 4, 13
+Q0 = 768
+GQ, GK = 1, 3
+AW, AWW, DW = 96, 128, 128
 AHEAD, WEIGH = 1000.0, {"S": 1.0, "V": 4.0}
-ONV, ONS2 = "cb_ cw_ dz1 kf_ ky1 mb16_ ne_ qh00 qh10 qh11 qh20 qo11".split(), "dz_ g1600 g1621 md2 ne00 qh21 qh_ qo21 xt1".split()
+ONV, ONS2 = "cb_ cw_ dz1 kf_ ky1 mb16_ ne_ q400 q410 q411 q420 qo11 ab000 ab001".split(), "dz_ g1600 g1621 md2 ne00 q421 q4_ qo21 xt1".split()
 NENG = 16
 COST = (1.0, 0.49, 1.55, 3.8, 0.0, 45.0, 1300.0, 280.0, 1800.0, 185.0, 220.0)
-OTHER = [(0.84, 0.42, 1.5, 3.6, 0.0, 45.0, 1500.0, 250.0, 2100.0, 205.0, 225.0), (1.05, 0.50, 1.3, 5.0, 0.0, 45.0, 1800.0, 180.0, 2700.0, 150.0, 150.0),
-         (1.05, 0.45, 1.9, 2.5, 2.0, 20.0, 1000.0, 350.0, 1500.0, 250.0, 250.0), (1.22, 0.55, 1.75, 4.5, 0.0, 60.0, 1500.0, 220.0, 2200.0, 200.0, 200.0)]
-MOVES, WARM, FLIP = 24000, 0.0003, 0.3
+OTHER = [(0.84, 0.42, 1.55, 3.8, 0.0, 45.0, 1400.0, 300.0, 1700.0, 215.0, 225.0), (1.05, 0.50, 1.3, 5.0, 0.0, 45.0, 1800.0, 200.0, 2500.0, 150.0, 150.0),
+         (1.0, 0.45, 1.9, 2.5, 2.0, 20.0, 1000.0, 350.0, 1500.0, 250.0, 250.0), (1.22, 0.55, 1.75, 4.5, 0.0, 60.0, 1500.0, 250.0, 2200.0, 200.0, 200.0)]
+MOVES, WARM, FLIP = 40000, 0.0003, 0.3
 
 f32, bf, f16, i32, u16 = "float32", "bfloat16", "float16", "int32", "uint16"
 SCRATCH = {
     "xt": ("sbuf", [128, OFF + W], bf), "mt": ("sbuf", [128, OFF + W], f32),
     "xs": ("sbuf", [128, 3 * SN], bf), "mn": ("sbuf", [128, SN], f32), "nt": ("sbuf", [128, SN], f32),
     "mi": ("sbuf", [128, B], i32), "sti": ("sbuf", [128, 48], i32), "stu": ("sbuf", [128, 48], u16),
-    "qb": ("sbuf", [128, R], bf), "qh": ("sbuf", [128, R], f16), "qo": ("sbuf", [128, R], bf),
+    "qb": ("sbuf", [128, R], bf), "qo": ("sbuf", [128, R], bf),
+    "q4": ("sbuf", [128, 4 * R], f16),
     "snd": ("sbuf", [128, 3 * BX], bf), "rcv": ("sbuf", [128, 3 * BX], bf),
     "ci": ("sbuf", [128, 144], bf), "c4": ("sbuf", [128, 144], bf), "c16": ("sbuf", [128, 128], bf), "j16": ("sbuf", [128, 128], bf), "cp": ("sbuf", [128, 256], bf),
     "pi": ("sbuf", [128, 8], i32), "ei": ("sbuf", [128, 8], i32), "eu": ("sbuf", [128, 16], u16),
     "col": ("sbuf", [128, 64], f32), "cw": ("sbuf", [128, 128], f32), "c9": ("sbuf", [128, 192], f16), "cb": ("sbuf", [128, 8], bf),
-    "mz": ("sbuf", [128, 4 * 144], bf), "mz4": ("sbuf", [128, 3 * 144], f16), "my": ("sbuf", [128, 9 * 144], f16),
+    "df": ("sbuf", [128, 4 * R], f16), "mz": ("sbuf", [128, 4 * 144], bf), "mz4": ("sbuf", [128, 3 * 144], f16), "my": ("sbuf", [128, 9 * 144], f16),
     "mm": ("sbuf", [128, 22 * 128], f16), "mb16": ("sbuf", [128, 6 * 128], bf),
-    "dg": ("sbuf", [128, 256], f32), "kt16": ("sbuf", [128, 160], bf), "ktw": ("sbuf", [128, 64], bf), "x9": ("sbuf", [128, 4 * 64], f32),
+    "dg": ("sbuf", [128, 128], bf), "kt": ("sbuf", [128, 16], bf), "fw": ("sbuf", [128, BX], bf), "x9": ("sbuf", [128, 4 * 64], f32),
     "tc16": ("sbuf", [128, 6 * 128], f16), "jb": ("sbuf", [128, 2 * LB], bf),
     "dz": ("sbuf", [128, 8 * LB], f16), "ne": ("sbuf", [128, 8 * LB], f16), "lo": ("sbuf", [128, 3 * 8 * LB], f16), "ch": ("sbuf", [128, 48], f16),
     "g16": ("sbuf", [128, R], f16), "ti": ("sbuf", [128, 192], i32), "tau": ("sbuf", [128, 192], f32),
@@ -49,13 +53,13 @@ SCRATCH = {
     "pm": ("sbuf", [128, 272], f32), "rk": ("sbuf", [128, 240], f32), "eq": ("sbuf", [128, 192], f32), "eqw": ("sbuf", [128, 128], f32),
     "ve": ("sbuf", [128, 384], f32), "vw": ("sbuf", [128, 5 * 64], f32), "lv": ("sbuf", [128, 96], u16),
     "xg": ("sbuf", [128, R], bf), "sh": ("sbuf", [128, R], f16),
-    "ky": ("sbuf", [128, 384], f16), "xk": ("sbuf", [128, 128], f16), "la": ("sbuf", [128, 48], u16),
-    "f8": ("sbuf", [128, 16], bf), "xf": ("sbuf", [128, 128], bf), "mxi": ("sbuf", [128, 128], i32), "dm": ("sbuf", [128, 128], f32),
+    "ky": ("sbuf", [128, 384], f16), "la": ("sbuf", [128, 64], u16),
+    "f8": ("sbuf", [128, 16], bf), "mxi": ("sbuf", [128, 128], i32), "dm": ("sbuf", [128, 128], f32),
     "gv": ("sbuf", [128, 128], f16), "gi": ("sbuf", [128, 128], f16),
     "ic": ("sbuf", [128, 128], i32), "ij": ("sbuf", [128, 256], i32), "iu": ("sbuf", [128, 256], f32),
     "kf": ("sbuf", [128, 128], bf), "kk": ("sbuf", [128, 256], f16), "gs": ("sbuf", [128, 256], f16),
     "g32": ("sbuf", [128, 256], f32), "yy": ("sbuf", [128, 256], f16), "w1": ("sbuf", [128, 256], f32),
-    "t1": ("sbuf", [128, 256], f32), "md": ("sbuf", [128, 128], f32),
+    "t1": ("sbuf", [128, 256], f32), "md": ("sbuf", [128, 128], f16),
     "q1": ("sbuf", [128, 128], bf), "rr": ("sbuf", [128, 128], f16),
 }
 for _b in range(8):
@@ -67,7 +71,7 @@ for _b in range(1, len(CHUNKS)):
 NDMA = 40
 SEMAPHORES = ["cV", "cS", "cP", "cG", "snt0", "snt1", "snt2", "arr0", "arr1", "arr2"] + ["d%d" % _i for _i in range(NDMA)]
 TWO = (bf, f16, u16)
-HC = set(range(22)) | set(range(40, 48))
+HC = set(range(24)) | set(range(40, 48))
 A = AluOpType
 F = ActivationFunctionType
 al = slice(None)
@@ -80,7 +84,7 @@ def bits(lo, n, step=1):
 def build(rank_peers, cost=None):
     CY, PEC, GAM, SCA, TTG, SFIX, DFIX, DRATE, XLAT = (cost or COST)[:9]
     ops = []
-    ndma, tag = [0], ["_"]
+    ndma, tag, early = [0], ["_"], [True]
 
     def ref(name, lo, n, step=1):
         return (name, lo, lo + (n - 1) * step + 1, step)
@@ -211,6 +215,12 @@ def build(rank_peers, cost=None):
         else:
             fn = lambda g, T: g.iota(ap(T, out), pattern, base, mult, allow_small_or_imprecise_dtypes=True)
         add("G", fn, [out], [], 130 + 2 * nel(out) * CY)
+        ops[-1].update(after=early[1:], free=early[1:])
+        if early[0]:
+            early[1:] = [len(ops) - 1]
+
+    def gcopy(out, a):
+        add("G", lambda g, T: g.affine_select(ap(T, out), ap(T, a), [[0, nel(out)]], A.is_ge, 0.0, 0, 0), [out], [a], 170 + 2 * nel(out) * CY)
 
     def dma(q, pairs, out, ins, nbytes):
         sem = "d%d" % ndma[0]; ndma[0] += 1
@@ -223,16 +233,31 @@ def build(rank_peers, cost=None):
             return None
         add(q, fn, out, ins, 60.0 * n, lat=DFIX + nbytes / DRATE, sem=sem, inc=16 * n)
 
+    def Q(c, n, step=1, k=0):
+        return ref("q4", 4 * c + k, n, 4 * step)
+
+    def four(t, i, rd):
+        w = PER.get("%d%d%d" % (t, i, rd), CHUNKS[i][2 + rd][0])
+        return int(w[1:4]) if w[0] in "FG" and t < RO else 0
+
+    def pieces(lo, hi, most):
+        k = -(-(hi - lo) // most)
+        cut = [lo + (hi - lo) * i // k // 8 * 8 for i in range(k)] + [hi]
+        return [(a, b - a) for a, b in zip(cut, cut[1:])]
+
     col = lambda c: ref("col", c, 1)
     aff = lambda o, a, s, b: act(o, a, F.Identity, scale=s, bias=b)
     dma("Y", (lambda T: [(T.sti[:], T.st[:])], 1), [ref("sti", 0, 48)], [], 60000)
-    dma("S", (lambda T: [(T.qb[:], T.qr[:])], 1), [ref("qb", 0, R)], [], 250000)
-    dma("S", (lambda T: [(T.mi[2::4, :], T.bd[:]), (T.mi[3::4, :], T.bd[:])], 2), [ref("mi", 0, B // 2)], [], 1250000)
+    dma("S", (lambda T: [(T.qb[:, 0:Q0], T.qr[:, 0:Q0])], 1), [ref("qb", 0, Q0)], [], 70000 + 256 * Q0)
+    dma("S", (lambda T: [(T.mi[2::4, :], T.bd[:]), (T.mi[3::4, :], T.bd[:])], 2), [ref("mi", 0, B // 2)], [], 1090000 + 256 * Q0)
     ops[-1].update(after=[1], free=[1])
-    dma("Y", (lambda T: [(T.mi[0::4, :], T.pf[:]), (T.mi[1::4, :], T.mb[:])], 2), [ref("mi", B // 2, B // 2)], [], 1250000)
+    dma("Y", (lambda T: [(T.mi[0::4, :], T.pf[:]), (T.mi[1::4, :], T.mb[:])], 2), [ref("mi", B // 2, B // 2)], [], 1090000 + 256 * Q0)
     ops[-1].update(after=[0], free=[0])
-    dma("S", (lambda T: [(T.xt[:, OFF:OFF + B], T.xn[:])], 1), [ref("xt", OFF, B)], [], 1750000)
+    dma("S", (lambda T: [(T.xt[:, OFF:OFF + B], T.xn[:])], 1), [ref("xt", OFF, B)], [], 1600000 + 256 * Q0)
     ops[-1].update(after=[2], free=[2])
+    if Q0 < R:
+        dma("S", (lambda T: [(T.qb[:, Q0:R], T.qr[:, Q0:R])], 1), [ref("qb", Q0, R - Q0)], [], 1800000)
+        ops[-1].update(after=[4], free=[4])
     dma("Y", (lambda T: [(T.ic[:], T.ip[:])], 1), [ref("ic", 0, 128)], [], 250000)
     ops[-1]["after"] = [2, 3]
     dma("Y", (lambda T: [(T.xs[:, 0:B], T.xn[:])], 1), [ref("xs", 0, B)], [], 600000)
@@ -240,20 +265,22 @@ def build(rank_peers, cost=None):
     iota(ref("pi", 0, 1), [[0, 1]], 0, 1)
     iota(ref("ci", 0, 144), [[1, 144]], 0, 0)
     iota(ref("c4", 0, 144), [[1, 36], [0, 4]], 0, 0)
-    iota(ref("j16", 0, 128), [[0, 8], [1, 16]], 0, 0)
+    iota(ref("ei", 0, 8), [[1, 8]], 0, 0)
+    iota(ref("x9", 0, 64), [[0, 8], [1, 8]], 0, 0)
     iota(ref("c16", 0, 128), [[1, 8], [0, 16]], 0, 0)
+    iota(ref("jb", 0, 2 * LB), [[0, 2], [1, LB]], 19 - LB, 0)
     iota(ref("cp", 0, 128), [[1, 8], [0, 4], [64, 4]], 0, 0)
     iota(ref("cp", 128, 128), [[1, 8], [16, 16]], -112, 0)
-    iota(ref("ei", 0, 8), [[1, 8]], 0, 0)
-    R4 = max(c[1] for c in CHUNKS) // 4
-    iota(ref("kt16", 0, R4), [[0, R4 // 4], [1, 4]], 0, 0)
-    iota(ref("x9", 0, 64), [[0, 8], [1, 8]], 0, 0)
+    iota(ref("j16", 0, 128), [[0, 8], [1, 16]], 0, 0)
+    iota(ref("cc", 0, 192, 2), [[0, 192]], 0, 0)
     iota(ref("eqw", 0, 128), [[0, 128]], 1, 0)
+    early[0] = False
+    R4 = max(c[1] for c in CHUNKS) // 4
+    for k in range(4):
+        iota(ref("rk", 80 + k, R4 // 4, 4), [[0, R4 // 4]], -1 if k else 1000000, 0)
     iota(ref("c9", 0, 192), [[0, 192]], 0, 0)
-    iota(ref("jb", 0, 2 * LB), [[0, 2], [1, LB]], 19 - LB, 0)
     iota(ref("nt", 0, B), [[1, B]], -int(ENC), 0)
     iota(ref("nt", B, SN - B), [[1, SN - B]], B - int(ENC), 0)
-    iota(ref("cc", 0, 384), [[0, 384]], 0, 0)
     p0 = ref("pi", 0, 1)
     ts(ref("pi", 1, 1), p0, 3, A.bitwise_and)
     ts(ref("pi", 2, 1), p0, 2, A.logical_shift_right, 3, A.bitwise_and)
@@ -292,7 +319,6 @@ def build(rank_peers, cost=None):
     tt(ref("ch", 40, 3), ref("col", 8, 3), ref("col", 9, 3), A.subtract)
     for k in range(3):
         ts(ref("my", 144 * (5 + k), 140), ref("ci", 0, 140), col(12), A.is_equal, col(40 + k), A.mult)
-    ts(ref("rk", 80, R4), ref("kt16", 0, R4), 0.0, A.is_equal, 1.0e6, A.mult)
     ts(ref("my", 144 * 8, 140), ref("my", 144 * 2, 140), 0.25, A.mult)
     ts(ref("mz4", 0, 140), ref("c4", 0, 140), col(15), A.is_equal, 0.25, A.mult)
     ts(ref("mz", 0, 143), ref("ci", 0, 143), col(16), A.is_equal, 4.0, A.mult)
@@ -301,10 +327,10 @@ def build(rank_peers, cost=None):
     M = lambda i: ref("mm", 128 * i, 128)
     ci, c16 = ref("ci", 0, 128), ref("c16", 0, 128)
     ts(ref("mb16", 0, 128), ci, CP, A.is_equal)
-    IB, IBH, INQ, BOQ, LQ, BOP = [ref("mb16", 128 * i, 128) for i in range(6)]
-    INEG, IH, I16, BO, DAL, DX, IP, IPB, SH, PMS, BODP, IS, NB, IK3, IT3, IU, IM, IMD, BU, BK, BOK = [M(i) for i in range(21)]
+    IB, IBH, INQ, BOQ, LQ = [ref("mb16", 128 * i, 128) for i in range(5)]
+    INEG, IH, I16, BO, DAL, DX, IP, IPB, SH, PMS, BODP, IS, NB, IK3, IT3, IU, IM, IMD, BU, BK, BOK, DY = [M(i) for i in range(22)]
     iota(NB, [[0, 128]], -int(BIG), 0)
-    if any("R" in x for c in CHUNKS for w in c[2:] for x in w):
+    if any("R" in x or "G" in x for x in [x for c in CHUNKS[1:] for w in c[2:] for x in w] + [PER[x] for x in PER if x[1] != "0"]):
         aff(ref("mz", 288, 143), ref("mz", 0, 143), 2.0, 0.0)
         aff(ref("mz4", 144, 143), ref("mz", 0, 143), -1.0, 0.0)
     ts(BO, c16, col(17), A.is_equal)
@@ -312,19 +338,13 @@ def build(rank_peers, cost=None):
     ts(SH, ci, col(20), A.is_equal, T1, A.mult)
     ts(PMS, ci, col(20), A.is_equal, col(40), A.mult)
     ts(BODP, ref("cp", 0, 128), col(17), A.is_equal, col(21), A.mult)
-    ts(BOP, ref("cp", 0, 128), col(17), A.is_equal, BIG / 4, A.mult)
-    ts(BOK, ref("cp", 128, 128), col(17), A.is_equal)
+    tt(ref("ch", 43, 1), CA, T0, A.mult)
+    ts(BOK, ref("cp", 128, 128), col(17), A.is_equal, col(43), A.mult)
     aff(BOQ, BO, 0.25, 0.0)
     add("G", lambda g, T: g.affine_select(ap(T, LQ), ap(T, BOQ), [[1, 128]], A.is_gt, 0.0, 0, -1), [LQ], [BOQ], 170 + 256 * CY)
-    DG = ref("dg", 0, 128)
-    ts(DG, ref("j16", 0, 128), CS, A.is_equal)
-    ts(ref("eu", 0, 8), ref("ei", 0, 8), 8.0, A.mult, 7.0, A.add)
-    tc(ref("eu", 8, 8), ref("ei", 0, 8))
     aff(col(36), T0, ENC, col(22))
     aff(col(37), T0, ENC - BIG, col(22))
     aff(col(38), T1, -ENC, 0.0)
-    aff(col(48), col(21), -1.0 / BIG, 0.0)
-    aff(col(39), CU, ENC, col(48))
     aff(col(44), T3, -1.0, 1.0)
     aff(col(45), T1, BIG, 0.0)
     aff(col(46), T2, BIG, col(45))
@@ -341,22 +361,26 @@ def build(rank_peers, cost=None):
         aff(m_, BO, c, 0.0)
     aff(ref("kf", 0, 128), DAL, -BIG, 0.0)
     tt(DX, ref("kf", 0, 128), IM, A.subtract)
-    ts(ref("mz4", 288, 143), ref("ci", 0, 143), col(16), A.is_equal, CU, A.mult)
+    tt(DY, ref("kf", 0, 128), I16, A.add)
     aff(ref("mz", 432, 143), ref("mz", 0, 143), T2, 0.0)
     cw = lambda i: ref("cw", 8 * i, 8)
     ts(cw(0), ref("ei", 0, 8), 16.0, A.mult, CS, A.add)
     ts(col(31), CH, 4.0, A.mult)
     ts(col(32), CH, 4.0, A.mult, 3.0, A.add)
     x9 = lambda i: ref("x9", 64 * i, 64)
-    ts(ref("rk", 0, 64), x9(0), 0.0, A.is_equal, 1.0e6, A.mult)
     ts(x9(1), x9(0), col(32), A.is_equal, 4.0, A.mult)
-    ts(x9(2), x9(0), col(31), A.is_ge)
-    ts(x9(3), x9(0), col(32), A.is_gt)
-    tt(x9(2), x9(3), x9(2), A.subtract)
-    tt(x9(1), x9(1), x9(2), A.add)
-    ts(x9(2), x9(2), 1.0, A.add, 32768.0, A.mult)
-    ts(x9(3), x9(0), col(31), A.subtract)
-    tt(ref("ktw", 0, 64), x9(2), x9(3), A.add)
+    ts(x9(2), x9(0), col(32), A.is_le)
+    tt(x9(1), x9(1), x9(2), A.subtract)
+    ts(x9(3), x9(0), col(31), A.is_equal, 1.0e6, A.mult)
+    ts(x9(2), x9(2), 1.0e5 - 1, A.mult, -1.0e5, A.add)
+    tt(ref("rk", 0, 64), x9(2), x9(3), A.add)
+    ts(ref("dg", 0, 128), ref("j16", 0, 128), CS, A.is_equal, 17 * BIG, A.mult)
+    ts(ref("dg", 0, 128), ref("dg", 0, 128), -BIG, A.add)
+    aff(col(53), CS, -BIG, 15 * BIG)
+    aff(col(54), CS, -BIG, 15 * BIG + OFF + ENC)
+    ts(ref("kt", 0, 4), ref("ci", 0, 4), CA, A.is_equal)
+    iota(ref("fw", 0, 128), [[0, 128]], 1, 0)
+    iota(ref("fw", 128, BX - 128), [[0, BX - 128]], 0, 0)
     blk = lambda nm, i, x: ref(nm, 8 * LB * i + x, 8, LB)
     pair = lambda nm, i, a: ref(nm, 8 * LB * i + 2 * a * (LB - 16) + LB - 20, LB + 20 + 32 * a)
     for a in range(4):
@@ -382,16 +406,20 @@ def build(rank_peers, cost=None):
         aff(col(33 + t), T2, 6.0 - t - BIG, col(38))
         aff(col(50 + t), col(33 + t), 1.0, -7 * BIG)
         iota(ref("tc16", 256 * t, 256), [[1, 256]], B + 384 * t - int(BIG), 0)
-    for z in range(2):
-        aff(ref("mt", 384 * z, 384), ref("nt", 0, 384), CU, col(39))
-    iota(ref("mt", 768, 128), [[0, 128]], 0, 0)
+    iota(ref("mt", 0, OFF), [[0, OFF]], 0, 0)
+    e_ = int(ENC)
+    dma("Y", (lambda T: [(T.mt[3::16, x:x + 384], T.nt[3::16, e_:e_ + 384]) for x in (0, 384)] + [(T.mt[11::16, 0:768], T.nt[11::16, e_ + 1:e_ + 769])], 3),
+        [ref("mt", 0, 768)], [ref("nt", e_, 769)], 50000)
     iota(ref("xt", 0, OFF), [[0, OFF]], 0, 0)
     for t in range(RO):
-        iota(ref("snd", BX * t, BX), [[0, BX]], 4096, 0)
+        iota(ref("snd", BX * t, 64), [[0, 64]], 4096, 0)
         iota(ref("rcv", BX * t + 64, BX - 64), [[0, BX - 64]], 4096, 0)
     for c0, n, _, _ in CHUNKS:
         tc(ref("stu", c0 // 16, n // 16), ref("sti", c0 // 16, n // 16))
-        act(ref("qh", c0, n), ref("qb", c0, n), F.Identity, bias=QO)
+        act(Q(c0, n), ref("qb", c0, n), F.Identity, bias=QO)
+        na = four(0, [c[0] for c in CHUNKS].index(c0), 0)
+        for k in range(1, 4 * (na > 0)):
+            act(Q(c0, na, 1, k), ref("qb", c0, na), F.Identity, bias=QO)
     for i in range(8):
         aff(ref("mt", OFF + 256 * i, 256), ref("mi", 256 * i, 256), CSG, C7)
         ops[-1]["after"] = [2, 3]
@@ -433,8 +461,7 @@ def build(rank_peers, cost=None):
         pU = pS if ci_ else ref("ps2", 384, r4)
         tb = 2 * o4 + (64 if ci_ else 0)
         pc = PIECE if ci_ else 99
-        qs = "sh" if ci_ == 0 and t > 0 else "qh"
-        sums = [(ref("mz4", 12 - 4 * s, 128), ref(qs, c0 + s, r4, 4)) for s in range(4)]
+        sums = [(ref("mz4", 12 - 4 * s, 128), ref("sh", s, r4, 4) if ci_ == 0 and t > 0 else Q(c0 + s, r4, 4)) for s in range(4)]
         mm([(pU, sums)])
         ts(c4_("ti"), pU, -0.375, A.add)
         tt(c4_("tau"), c4_("ti"), pU, A.subtract)
@@ -445,7 +472,7 @@ def build(rank_peers, cost=None):
             XW = lambda off: ind("xt", OFF, OFF + base, off) if ci_ == 0 or (rd == 0 and (t == 0 or ci_ in LIVE)) else ind("xs", SN * t, SN * t + base, off)
             for h in range(H):
                 groute, lh, go = ways[rd][h][5], part(lst, h, mh), ref("g16", c0 + h * nh, nh)
-                gw = ind("mn", 0, base, lh) if ci_ and rd else ind("mt", OFF, OFF + base, lh)
+                gw = ind("mn", 0, base, lh) if ci_ and rd else ind("mt", OFF, OFF + (base if rd else B), lh)
                 if t == 0:
                     aff(go, ind("mi", 0, B, lh), CSG, CGS)
                 elif groute == "S":
@@ -469,7 +496,7 @@ def build(rank_peers, cost=None):
             if last:
                 ts(ref("t16", 65, r4, 2), pD, -1.7, A.is_gt)
             t16 = lambda cl, cnt=m: ref("t16", tb + 2 * cl + 1, cnt, 8)
-            whole = ways[rd][0][0] == "E"
+            whole = ways[rd][0][0] in "EFG"
             if whole:
                 ts(c4_("ou"), ref("t16", tb + 1, r4, 2), ENC, A.add)
             for k0, k1 in ([] if whole else KS if ci_ == 0 else [(0, 4)]):
@@ -482,20 +509,24 @@ def build(rank_peers, cost=None):
                 cnt = 16 if last else 8
                 mm([(ref("ps2", 64 + 8 * h + 2 * k, cnt, 16), [(YD(k, cl), t16(cl, cnt)) for cl in (2 * h, 2 * h + 1)]) for h in range(2) for k in range(4)]
                    + [(ref("ps2", 193, 64, 2), [(I16, ref("c9", 64 * t, 64))])] * last)
-            relu = any("R" in x for x in ways[rd])
+            relu = any("R" in x or "G" in x for x in ways[rd])
             if whole:
-                parts = 4 if ci_ else 1
-                w = n // parts
-                for h in range(parts):
-                    pd, lo = px(0, 4 * w), 4 * (c0 + h * w)
-                    cut = 1 if ci_ else int(ways[rd][0][1])
+                na = four(t, ci_, rd)
+                some = lambda nm, j, w: view(nm, slice(j, j + w), al) if ci_ else view(nm, slice(j // 8, (j + w) // 8), al, al)
+                for j, w in pieces(0, na, AW if ci_ else AWW):
+                    d = ref("df", 4 * (c0 + j), 4 * w)
+                    tt(d, XW(c4_("ou", j // 4, w // 4)), ref("q4", 4 * (c0 + j), 4 * w), A.subtract)
+                    act(some("ab%d" % ci_, j, w), d, F.Relu if relu else F.Abs, bias=QO)
+                for j, w in pieces(na, n, DW if ci_ else n):
+                    pd, lo = px(0, 4 * w), 4 * (c0 + j)
+                    cut = 1 if ci_ or na else int(ways[rd][0][1])
                     for x in range(cut):
-                        act(ref("xr", lo + x * 4 * w // cut, 4 * w // cut), XW(c4_("ou", h * w // 4 + x * w // 4 // cut, w // 4 // cut)), F.Copy)
-                    minus = [(INEG, ref("qh", c0 + h * w, w), ref(pd[0], pd[1] + k, w, 4)) for k in range(4)]
+                        act(ref("xr", lo + x * 4 * w // cut, 4 * w // cut), XW(c4_("ou", j // 4 + x * w // 4 // cut, w // 4 // cut)), F.Copy)
+                    minus = [(INEG, Q(c0 + j, w), ref(pd[0], pd[1] + k, w, 4)) for k in range(4)]
                     mm([(pd, minus + [(IB, ref("xr", lo, 4 * w))])], 4)
-                    act(view("ab%d" % ci_, slice(h * w, h * w + w), al) if ci_ else view("ab0", al, al, al), pd, F.Abs, bias=QO)
+                    act(some("ab%d" % ci_, j, w), pd, F.Abs, bias=QO)
             for h in range(0 if whole else H):
-                routes, q, js = ways[rd][h][:4], ref("qh", c0 + h * nh, nh), slice(h * nh, h * nh + nh)
+                routes, q, js = ways[rd][h][:4], Q(c0 + h * nh, nh), slice(h * nh, h * nh + nh)
                 run = lambda x: [(k, k + 1) for k in range(4) if routes[k] == x] if not (ci_ and x in JOIN and (x != "D" or H == 1)) else \
                     [(routes.index(x), routes.rindex(x) + 1)] if x in routes else []
                 ab = lambda k0, k1: view("ab%d" % ci_, js, slice(k0, k1)) if ci_ else view("ab0", al, al, k0)
@@ -517,14 +548,16 @@ def build(rank_peers, cost=None):
             lst = ref("lv", 48 * rd + c0 // 16, m)
             if ci_:
                 every = lambda nm, s: view(nm % ci_, slice(s, None, 16), al)
-                mm([(pS, [(IB, ref("kt16", 0, r4))] + [(ref("mz4", 144 + 15 - s, 128), every("dd%d" + str(rd), s)) for s in range(16 * relu)]
-                     + [(ref("mz", 288 * relu + 15 - s, 128), every("ab%d", s)) for s in range(16)])], pc)
+                na = four(t, ci_, rd) or n
+                less = [(ref("mz4", 144 + 15 - s, 128), view("dd%d%d" % (ci_, rd), slice(s, na, 16), al), ref(pS[0], pS[1], na // 4)) for s in range(16 * relu)]
+                more = [(ref("mz", 288 * relu + 15 - s, 128), every("ab%d", s)) for s in range(16)]
+                mm([(pS, less + more)], pc)
                 scan(c4_("pm", 48), ref("rk", 80, r4), pS, 0.0, A.add, A.min)
                 tt(c4_("eq"), pS, c4_("pm", 48), A.not_equal)
                 scan(ref("ve", 192 * rd + o4, r4), c4_("eq"), ref(pb2, at + 2 * r4, r4), 0.0, A.mult, A.add)
                 ts(lst, ref("ve", 192 * rd + o4 + 3, m, 4), ENC, A.add)
             else:
-                mm([(pS, [(IB, ref("ktw", 0, 64))] + [(ref("mz", 144 + 7 - s, 128), view("ab0", al, s, al)) for s in range(8)])])
+                mm([(pS, [(ref("mz", 144 + 7 - s, 128), view("ab0", al, s, al)) for s in range(8)])])
                 eq = ref("eqw", 0, 64, 2)
                 scan(ref("pm", 0, 64), ref("rk", 0, 64), pS, 0.0, A.add, A.min)
                 tt(eq, pS, ref("pm", 0, 64), A.not_equal)
@@ -538,20 +571,25 @@ def build(rank_peers, cost=None):
             hb = QO / 2 - 0.25
             for h in range(H):
                 qroute, c1, xw = ways[rd][h][4], c0 + h * nh, XW(part(lst, h, mh))
-                q, sh, xg, pq = ref("qh", c1, nh), ref("sh", c1, nh), ref("xg", c1, nh), px(h, nh)
+                q, sh, xg, pq = Q(c1, nh), ref("sh", c1, nh), ref("xg", c1, nh), px(h, nh)
+                na = four(t + rd, ci_, 1 - rd) if ci_ or not rd else 0
                 if qroute == "M":
                     tt(sh, xw, q, A.add)
                     act(q, sh, F.Identity, scale=0.5, bias=hb)
-                elif qroute == "V":
-                    tt(sh, xw, q, A.add)
-                    ts(q, sh, 0.5, A.mult, hb, A.add)
+                    for k in range(1, 4 * (na > 0)):
+                        if ci_ and 2 * t + rd >= GQ and k <= GK:
+                            gcopy(Q(c1, na, 1, k), Q(c1, na))
+                        else:
+                            act(Q(c1, na, 1, k), ref("sh", c1, na), F.Identity, scale=0.5, bias=hb)
                 else:
                     act(xg, xw, F.Copy)
                     mm([(pq, [(IH, q), (IBH, xg)])])
-                    if qroute == "S":
-                        act(q, pq, F.Identity, bias=hb)
-                    else:
+                    if na:
                         ts(q, pq, hb, A.add)
+                    else:
+                        act(q, pq, F.Identity, bias=hb)
+                    for k in range(1, 4 * (na > 0)):
+                        ts(Q(c1, na, 1, k), ref(pq[0], pq[1], na), hb, A.add)
                 if t == RO - 1 and ci_ and rd:
                     if "o" in ONS:
                         act(ref("qo", c1, nh), q, F.Identity, bias=-QO)
@@ -585,9 +623,8 @@ def build(rank_peers, cost=None):
     node = [ref("g16", 0, 128), ref("gs", 0, 128)]
 
     def step_a(z):
-        mm([(pL, [(DAL, node[z])])])
-        act(pL, pL, F.Relu, bias=1.0 if z else -6.0, scale=-1.0)
-        tt(ref("yy", 128 * z, 128), pL, node[z], A.mult)
+        mm([(pL, [(DY, node[z])])])
+        ts(ref("yy", 128 * z, 128), pL, 0.0 if z else -7 * BIG, A.add, -2048.0, A.max)
 
     def step_b(t, z, lg, la, back):
         base = B + 384 * t
@@ -597,7 +634,7 @@ def build(rank_peers, cost=None):
         mm([(pY, [(DX, node[z]), (IM, name), (IMD, h("kk"))])])
         act(h("w1"), pY, F.Relu, bias=col((33 if z else 50) + t))
         tt(ind("mt", 0, OFF + base, la), h("g32"), h("w1"), A.add)
-        off = (BODP, back) if z == 0 else (BOP, ref("xf", 0, 128))
+        off = (BODP, back) if z == 0 else (IPB, ref("md", 0, 128))
         mm([(pR, [(SH, node[z]), (PMS, h("yy")), (IT3, back), off]), (pM, [(IP, name), (IPB, h("kk"))] + [(IP, NB)] * z + [off])])
         act(h("t1"), pR, F.Relu, bias=col(37) if z else col(36))
         tt(ref("mt", OFF + base + 128 * (z + 1), 128), pM, h("t1"), A.max)
@@ -606,19 +643,17 @@ def build(rank_peers, cost=None):
 
     def writers(t):
         base = B + 384 * t
-        q = ref("qh", 0, 128)
+        q = Q(0, 128)
         lv = ref("lv", 48, 8)
         nn = OFF + base
         tag[0] = "1"
         lowest_of(t, 1, lv)
-        xk = ref("xk", 0, 128)
-        tt(xk, ind("vw", 128, 192, ref("eu", 0, 8)), DG, A.mult)
-        pk, pN, pmd = ref("ps0", 128, 128), ref("ps0", 256, 128), ref("ps0", 384, 128)
+        tc(LA(6), vw(2))
+        act(ref("kk", 0, 128), ind("kt", 0, 4, LA(6)), F.Copy)
+        pN = ref("ps0", 384, 128)
         act(ref("gv", 0, 128), ind("mt", OFF, OFF + base, lv), F.Identity, bias=CGS)
-        mm([(pN, [(IK3, ref("gv", 0, 128)), (IU, ref("ky", 0, 128)), (BOK, xk)])])
+        mm([(pN, [(IK3, ref("gv", 0, 128)), (IU, ref("ky", 0, 128)), (BOK, ref("kk", 0, 128))])])
         act(ref("mt", nn, 128), pN, F.Identity, bias=CGN)
-        mm([(pk, [(BO, xk)])])
-        ts(ref("kk", 0, 128), pk, CA, A.is_equal)
         if "x" in ONS:
             act(ref("xt", nn, 128), q, F.Identity, bias=-QO)
         else:
@@ -637,16 +672,17 @@ def build(rank_peers, cost=None):
         act(gi, ind("mt", 0, nn, LA(4)), F.Identity, bias=CGS)
         step_b(t, 0, LA(0), LA(0), gi)
         act(ref("xt", nn + 128, 128), ind("xt", 0, nn, LA(4)), F.Copy)
-        pkey, own, pk2 = ref("ps7", 384, 128), ref("ps2", 0, 8), ref("ps0", 0, 128)
+        pkey, pown, pk2, own = ref("ps7", 384, 128), ref("ps2", 64, 128), ref("ps0", 0, 128), ref("dm", 15, 8, 16)
+        mm([(pown, [(BU, gi)])])
         mm([(pkey, [(BU, gi)])])
-        mm([(own, [(ref("mz4", 288 + 15 - s, 128), ref("gi", s, 8, 16)) for s in range(16)])])
         mm([(pk2, [(BK, gi)])])
+        scan(ref("dm", 0, 128), ref("dg", 0, 128), pown, 0.0, A.add, A.min)
         act(ref("ky", 256, 128), pkey, F.Copy)
-        ts(LA(5), own, OFF + ENC, A.add)
+        ts(LA(5), own, col(54), A.add)
         ts(ref("kk", 128, 128), pk2, CA, A.is_equal)
         aff(blk("dz", 0, LB - 2), cw(0), 1.0, 128.0 * t - OFF - ENC)
         aff(blk("dz", 0, LB - 1), cw(0), -1.0, OFF + ENC - 128.0 * t)
-        tc(blk("ne", 0, LB - 2), own)
+        ts(blk("ne", 0, LB - 2), own, col(53), A.add)
         lowest(2, ref("ky", 256, 128), own)
         tt(ref("kf", 0, 128), ind("mt", 0, nn, LA(5)), ref("kk", 128, 128), A.min)
         pF, pos = ref("ps2", 448, 8), ref("ps2", 464, 8)
@@ -664,13 +700,11 @@ def build(rank_peers, cost=None):
         sent.append(len(ops) - 1)
         add("G", lambda g, T: None, [ro], [so], 1.0, lat=XLAT, sem="arr%d" % t, inc=NENG)
         ts(LA(2), blk("lo", 2, LB - 2), OFF + ENC, A.add)
-        tt(ref("xf", 0, 128), ind("f8", 0, 8, ref("eu", 8, 8)), DG, A.mult)
         tag[0] = "2"
+        act(ref("md", 0, 128), ind("fw", 0, BX, LA(3)), F.Copy)
         act(node[1], ind("mt", 0, nn, LA(5)), F.Identity, bias=CGS)
         step_a(1)
         step_b(t, 1, LA(5), LA(2), node[1])
-        mm([(pmd, [(BOQ, ref("xf", 0, 128))])])
-        act(ref("md", 0, 128), pmd, F.Copy)
         tt(ref("xt", nn + 256, 128), ind("xt", 0, nn, LA(5)), ref("md", 0, 128), A.mult)
         if t < RO - 1:
             x0 = 0 if LATE else base
@@ -688,10 +722,17 @@ def build(rank_peers, cost=None):
         elif "r" in ONS:
             act(ref("rr", 0, 128), sh, F.Sign, bias=-QO / 2)
             mm([(PC, [(I16, sh), (IS, ref("rr", 0, 128))])])
-            act(q, PC, F.Identity, bias=QO / 2)
+            ts(q, PC, QO / 2, A.add)
+            na = four(t + 1, 0, 0)
+            for k in range(1, 4 * (na > 0)):
+                ts(Q(0, na, 1, k), ref(PC[0], PC[1], na), QO / 2, A.add)
         else:
             ts(ref("rr", 0, 128), sh, QO / 2, A.is_lt, QO, A.mult)
-            tt(q, ref("rr", 0, 128), sh, A.add)
+            mm([(PC, [(I16, sh), (I16, ref("rr", 0, 128))])])
+            tc(q, PC)
+            na = four(t + 1, 0, 0)
+            for k in range(1, 4 * (na > 0)):
+                tc(Q(0, na, 1, k), ref(PC[0], PC[1], na))
 
     for t in range(RO):
         for i, c in enumerate(CHUNKS):
@@ -807,21 +848,19 @@ def one_pass(ops, succ, pred, pr, rdy, choose):
     return order, start
 
 
-def replay(s, order, lo, fin):
+def replay(s, order, lo, fin, last=()):
     eng, c, pred, ends = s
-    fin, free = fin[:], {}
-    for k in range(lo - 1, -1, -1):
-        if eng[order[k]] not in free:
-            free[eng[order[k]]] = fin[order[k]]
-            if len(free) == 5:
-                break
-    for k in range(lo, len(order)):
-        i = order[k]
-        t = free.get(eng[i], 0.0)
+    fin, free = fin[:], dict.fromkeys("VSPGY", 0.0)
+    for i in last:
+        free[eng[i]] = fin[i]
+    for i in order[lo:]:
+        e = eng[i]
+        t = free[e]
         for j, d in pred[i]:
-            if fin[j] + d > t:
-                t = fin[j] + d
-        fin[i] = free[eng[i]] = t + c[i]
+            x = fin[j] + d
+            if x > t:
+                t = x
+        fin[i] = free[e] = t + c[i]
     return max(fin[i] + d for i, d in ends), fin
 
 
@@ -833,6 +872,13 @@ def polish(ops, order):
     for i in range(n):
         for j in pred[i]:
             succ[j].add(i)
+    above, near = [], []
+    for i in range(n):
+        far = 0
+        for j in pred[i]:
+            far |= above[j]
+        near.append([j for j in pred[i] if ops[j]["lat"] or not far >> j & 1])
+        above.append(far | sum(1 << j for j in pred[i] if not far >> j & 1))
     alts = [build([(0, 0, 0)] * RO, cost) for cost in OTHER]
     sets = [(eng, [0.0] * n, [0] * n, [(i, alt[i]["lat"]) for i in range(n) if not succ[i]]) for alt in alts]
 
@@ -841,7 +887,7 @@ def polish(ops, order):
             for i in calls:
                 s[1][i] = alt[i]["alt"][eng[i]][1] if "alt" in alt[i] else alt[i]["c"]
                 s[2][i] = [(j, 0.0 if j in ops[i].get("free", ()) else alt[j]["lat"] + (cost[10] if eng[i] == eng[j] and not ops[j]["sem"] else cost[9]))
-                           for j in ops[i]["dep"]]
+                           for j in near[i]]
 
     def flip(i):
         eng[i] = "S" if eng[i] == "V" else "V"
@@ -869,7 +915,7 @@ def polish(ops, order):
                         i = p
                     else:
                         i = max([j for j, d in s[2][i] if abs(fin[j] + d - st) < 1e-6] + [-1])
-            place = {x: k for k, x in enumerate(order)}
+            place = dict(zip(order, range(n)))
         j, i = held[int(rnd() * len(held))]
         a, b, k, up = place[j], place[i], (0, 0, 1, 2, 3, 5)[int(rnd() * 6)], rnd() < 0.5
         other = (i if up else j) if "alt" in ops[i if up else j] and rnd() < FLIP else -1
@@ -889,9 +935,9 @@ def polish(ops, order):
                 continue
             new = order[:a] + [x for x in seg if (x in move) == up] + [x for x in seg if (x in move) != up] + order[b + 1:]
         room, got = -WARM * (1 - it / MOVES) * math.log(rnd()), []
-        lost = 0.0
+        lost, last = 0.0, {eng[x]: x for x in order[:a]}.values()
         for s, x, u in zip(sets, now, unit):
-            got.append(replay(s, new, a, x[1]))
+            got.append(replay(s, new, a, x[1], last))
             lost += (got[-1][0] - x[0]) / u
             if lost > room + 0.001:
                 break

import math
from concourse.bass import DstId, RemoteDMATransfer
from concourse.mybir import dt, AluOpType, AxisListType, ActivationFunctionType

B, W, R, L, RO = 2048, 3200, 768, 128, 3
OFF = 896
ENC = 1152.0
QO = 1280.0
BIG = 4096.0
LB = 132
BX = 384

SN = 2816
CHUNKS = [(0, 128, ["F064MS"], ["F064SS"]), (128, 320, ["F192MS"], ["F096MS"]), (448, 320, ["F096MS"], ["F096MS"])]
PER = {}
LIVE, LATE = (1, 2), True
BANKS = ["07", "35", "46"]
JOIN = "R"
KS = [(0, 4)]
ONS = "xvo"
SEED, JIT, LOOK, PASSES = 1, 200.0, 0.3, 6
PIECE, NV = 4, 13
Q0 = 768
GQ, GK = 1, 3
AW, AWW, DW = 96, 128, 128
AHEAD, WEIGH = 1000.0, {"S": 1.0, "V": 4.0}
ONV, ONS2 = "cb_ cw_ dz1 kf_ ky1 mb16_ ne_ q400 q410 q411 q420 qo11 ab000 ab001".split(), "dz_ g1600 g1621 md2 ne00 q421 q4_ qo21 xt1".split()
NENG = 16
COST = (1.0, 0.49, 1.55, 3.8, 0.0, 45.0, 1300.0, 280.0, 1800.0, 185.0, 220.0)
OTHER = [(0.84, 0.42, 1.55, 3.8, 0.0, 45.0, 1400.0, 300.0, 1700.0, 215.0, 225.0), (1.05, 0.50, 1.3, 5.0, 0.0, 45.0, 1800.0, 200.0, 2500.0, 150.0, 150.0),
         (1.0, 0.45, 1.9, 2.5, 2.0, 20.0, 1000.0, 350.0, 1500.0, 250.0, 250.0), (1.22, 0.55, 1.75, 4.5, 0.0, 60.0, 1500.0, 250.0, 2200.0, 200.0, 200.0)]
MOVES, WARM, FLIP = 40000, 0.0003, 0.3

f32, bf, f16, i32, u16 = "float32", "bfloat16", "float16", "int32", "uint16"
SCRATCH = {
    "xt": ("sbuf", [128, OFF + W], bf), "mt": ("sbuf", [128, OFF + W], f32),
    "xs": ("sbuf", [128, 3 * SN], bf), "mn": ("sbuf", [128, SN], f32), "nt": ("sbuf", [128, SN], f32),
    "mi": ("sbuf", [128, B], i32), "sti": ("sbuf", [128, 48], i32), "stu": ("sbuf", [128, 48], u16),
    "qb": ("sbuf", [128, R], bf), "qo": ("sbuf", [128, R], bf),
    "q4": ("sbuf", [128, 4 * R], f16),
    "snd": ("sbuf", [128, 3 * BX], bf), "rcv": ("sbuf", [128, 3 * BX], bf),
    "ci": ("sbuf", [128, 144], bf), "c4": ("sbuf", [128, 144], bf), "c16": ("sbuf", [128, 128], bf), "j16": ("sbuf", [128, 128], bf), "cp": ("sbuf", [128, 256], bf),
    "pi": ("sbuf", [128, 8], i32), "ei": ("sbuf", [128, 8], i32), "eu": ("sbuf", [128, 16], u16),
    "col": ("sbuf", [128, 64], f32), "cw": ("sbuf", [128, 128], f32), "c9": ("sbuf", [128, 192], f16), "cb": ("sbuf", [128, 8], bf),
    "df": ("sbuf", [128, 4 * R], f16), "mz": ("sbuf", [128, 4 * 144], bf), "mz4": ("sbuf", [128, 3 * 144], f16), "my": ("sbuf", [128, 9 * 144], f16),
    "mm": ("sbuf", [128, 22 * 128], f16), "mb16": ("sbuf", [128, 6 * 128], bf),
    "dg": ("sbuf", [128, 128], bf), "kt": ("sbuf", [128, 16], bf), "fw": ("sbuf", [128, BX], bf), "x9": ("sbuf", [128, 4 * 64], f32),
    "tc16": ("sbuf", [128, 6 * 128], f16), "jb": ("sbuf", [128, 2 * LB], bf),
    "dz": ("sbuf", [128, 8 * LB], f16), "ne": ("sbuf", [128, 8 * LB], f16), "lo": ("sbuf", [128, 3 * 8 * LB], f16), "ch": ("sbuf", [128, 48], f16),
    "g16": ("sbuf", [128, R], f16), "ti": ("sbuf", [128, 192], i32), "tau": ("sbuf", [128, 192], f32),
    "cc": ("sbuf", [128, 384], f32), "t16": ("sbuf", [128, 448], f16), "ou": ("sbuf", [128, 192], u16),
    "dd": ("sbuf", [128, 4 * L], f16), "xr": ("sbuf", [128, 4 * R], bf), "ab0": ("sbuf", [128, 16, 8, 4], bf),
    "pm": ("sbuf", [128, 272], f32), "rk": ("sbuf", [128, 240], f32), "eq": ("sbuf", [128, 192], f32), "eqw": ("sbuf", [128, 128], f32),
    "ve": ("sbuf", [128, 384], f32), "vw": ("sbuf", [128, 5 * 64], f32), "lv": ("sbuf", [128, 96], u16),
    "xg": ("sbuf", [128, R], bf), "sh": ("sbuf", [128, R], f16),
    "ky": ("sbuf", [128, 384], f16), "la": ("sbuf", [128, 64], u16),
    "f8": ("sbuf", [128, 16], bf), "mxi": ("sbuf", [128, 128], i32), "dm": ("sbuf", [128, 128], f32),
    "gv": ("sbuf", [128, 128], f16), "gi": ("sbuf", [128, 128], f16),
    "ic": ("sbuf", [128, 128], i32), "ij": ("sbuf", [128, 256], i32), "iu": ("sbuf", [128, 256], f32),
    "kf": ("sbuf", [128, 128], bf), "kk": ("sbuf", [128, 256], f16), "gs": ("sbuf", [128, 256], f16),
    "g32": ("sbuf", [128, 256], f32), "yy": ("sbuf", [128, 256], f16), "w1": ("sbuf", [128, 256], f32),
    "t1": ("sbuf", [128, 256], f32), "md": ("sbuf", [128, 128], f16),
    "q1": ("sbuf", [128, 128], bf), "rr": ("sbuf", [128, 128], f16),
}
for _b in range(8):
    SCRATCH["ps%d" % _b] = ("psum", [128, 512], f32)
for _b in range(1, len(CHUNKS)):
    SCRATCH["ab%d" % _b] = ("sbuf", [128, CHUNKS[_b][1], 4], bf)
    for _r in range(2):
        SCRATCH["dd%d%d" % (_b, _r)] = ("sbuf", [128, CHUNKS[_b][1], 4], f16)
NDMA = 40
SEMAPHORES = ["cV", "cS", "cP", "cG", "snt0", "snt1", "snt2", "arr0", "arr1", "arr2"] + ["d%d" % _i for _i in range(NDMA)]
TWO = (bf, f16, u16)
HC = set(range(24)) | set(range(40, 48))
A = AluOpType
F = ActivationFunctionType
al = slice(None)


def bits(lo, n, step=1):
    return ((1 << (n * step)) - 1) // ((1 << step) - 1) << lo


def build(rank_peers, cost=None):
    CY, PEC, GAM, SCA, TTG, SFIX, DFIX, DRATE, XLAT = (cost or COST)[:9]
    ops = []
    ndma, tag, early = [0], ["_"], [True]

    def ref(name, lo, n, step=1):
        return (name, lo, lo + (n - 1) * step + 1, step)

    def view(name, *idx):
        cols, n, size = 1, 1, 1
        for d, x in list(zip(SCRATCH[name][1][1:], idx))[::-1]:
            r = range(d)[x] if isinstance(x, slice) else range(x, x + 1)
            cols *= bits(r.start * size, len(r), r.step * size)
            n, size = n * len(r), size * d
        return (name, cols, None, None, n, (al,) + idx)

    def ind(name, lo, hi, off):
        return ("*", name, lo, hi, off)

    def nel(r):
        if len(r) == 6:
            return r[4]
        if r[0] == "*":
            return 16 * (r[4][2] - r[4][1])
        return (r[2] - r[1] + r[3] - 1) // r[3]

    def reg(r):
        if len(r) == 6:
            return r[:2]
        if r[0] == "*":
            return (r[1], bits(r[2], r[3] - r[2]))
        return (r[0], bits(r[1], nel(r), r[3]))

    def ap(T, r):
        if not isinstance(r, tuple):
            return r
        if len(r) == 6:
            return T[r[0]][r[5]]
        if r[0] == "*":
            return T[r[1]][:, r[2]:r[3]].indirect(ap(T, r[4]))
        if r[3] == 1:
            return T[r[0]][:, r[1]:r[2]]
        return T[r[0]][:, r[1]:r[2]:r[3]]

    def kind(r):
        return SCRATCH[r[1] if r[0] == "*" else r[0]]

    def add(eng, fn, out, ins, cost, lat=0.0, sem=None, inc=1):
        rd, wr = [], []
        for r in ins:
            if isinstance(r, tuple):
                rd.append(reg(r))
                if r[0] == "*":
                    rd.append(reg(r[4]))
        for r in out:
            wr.append(reg(r))
            if r[0] == "*":
                rd.append(reg(r[4]))
        ops.append({"e": eng, "fn": fn, "rd": rd, "wr": wr, "c": cost, "lat": lat, "sem": sem, "inc": inc})

    def vcost(out, ins, rate):
        n = nel(out)
        if out[0] == "*":
            return 50 + SCA * n * CY
        if ins[0][0] == "*":
            return 50 + max(GAM, TTG * (rate == 2)) * n * CY
        return max(64, n * rate) * CY

    def half(*rs):
        return 0.5 if all(kind(r)[2] in TWO for r in rs if isinstance(r, tuple)) else 1.0

    def tc(out, a):
        add("V", lambda g, T: g.vector.tensor_copy(ap(T, out), ap(T, a)), [out], [a], vcost(out, [a], half(out, a)))

    def fill(out, c):
        add("V", lambda g, T: g.vector.memset(ap(T, out), c), [out], [], max(64, nel(out) * half(out)) * CY)

    def tt(out, a, b, op):
        rate = 1.0 if "psum" in (kind(a)[0], kind(b)[0]) else 2.0
        add("V", lambda g, T: g.vector.tensor_tensor(ap(T, out), ap(T, a), ap(T, b), op), [out], [a, b], vcost(out, [a], rate))

    def ts(out, a, s1, op0, s2=None, op1=None):
        if nel(out) > 64 and half(out, a) < 1 and a[0] != "*":
            s1, s2 = [("ch",) + x[1:] if isinstance(x, tuple) and x[0] == "col" and x[1] in HC else x for x in (s1, s2)]
        if op1 is None:
            fn = lambda g, T: g.vector.tensor_scalar(ap(T, out), ap(T, a), ap(T, s1), None, op0)
        else:
            fn = lambda g, T: g.vector.tensor_scalar(ap(T, out), ap(T, a), ap(T, s1), ap(T, s2), op0, op1)
        add("V", fn, [out], [a, s1, s2], vcost(out, [a], half(out, a, s1, s2)))

    def scan(out, d0, d1, init, op0, op1):
        add("V", lambda g, T: g.vector.tensor_tensor_scan(ap(T, out), ap(T, d0), ap(T, d1), init, op0, op1), [out], [d0, d1],
            max(64, nel(out) * half(out, d0, d1)) * CY)

    def act(out, a, func, bias=0.0, scale=1.0):
        c = 65 + GAM * nel(out) * CY if a[0] == "*" else max(64, nel(out)) * CY + SFIX
        add("S", lambda g, T: g.scalar.activation(ap(T, out), ap(T, a), func, bias=ap(T, bias), scale=ap(T, scale)), [out], [a, bias, scale], c)
        if func == F.Copy:
            tc(out, a)
        elif func == F.Identity:
            ts(out, a, scale, A.mult, bias, A.add)
        elif func == F.Relu and scale == 1.0:
            ts(out, a, bias, A.add, 0.0, A.max)
        else:
            return
        v = ops.pop()
        ops[-1]["rd"] += [x for x in v["rd"] if x not in ops[-1]["rd"]]
        name = out[0] + tag[0]
        ops[-1]["name"] = name
        ops[-1]["alt"] = {"S": (ops[-1]["fn"], c), "V": (v["fn"], v["c"])}
        ops[-1]["pin"] = name in ONV or name in ONS2
        if name in ONV:
            ops[-1].update(e="V", fn=v["fn"], c=v["c"])

    def mm(groups, piece=99):
        calls = [(x[2] if len(x) > 2 else out, x[0], x[1], i == 0, i == len(terms) - 1) for out, terms in groups for i, x in enumerate(terms)]
        first = len(ops)
        for lo in range(0, len(calls), piece):
            def fn(g, T, part=calls[lo:lo + piece]):
                for out, l, r, st, sp in part:
                    last = g.tensor.matmul(ap(T, out), ap(T, l), ap(T, r), st, sp)
                return last
            part = calls[lo:lo + piece]
            add("P", fn, [x[0] for x in part], [x[1] for x in part] + [x[2] for x in part],
                sum(max(64, nel(x[2])) for x in part) * PEC + (60 if lo + piece >= len(calls) else 0))
            ops[-1]["free"] = list(range(first, len(ops) - 1))
            ops[-1]["after"] = ops[-1]["free"][-1:]

    def iota(out, pattern, base, mult):
        if kind(out)[2] == i32:
            fn = lambda g, T: g.iota(ap(T, out), pattern, base, mult)
        else:
            fn = lambda g, T: g.iota(ap(T, out), pattern, base, mult, allow_small_or_imprecise_dtypes=True)
        add("G", fn, [out], [], 130 + 2 * nel(out) * CY)
        ops[-1].update(after=early[1:], free=early[1:])
        if early[0]:
            early[1:] = [len(ops) - 1]

    def gcopy(out, a):
        add("G", lambda g, T: g.affine_select(ap(T, out), ap(T, a), [[0, nel(out)]], A.is_ge, 0.0, 0, 0), [out], [a], 170 + 2 * nel(out) * CY)

    def dma(q, pairs, out, ins, nbytes):
        sem = "d%d" % ndma[0]; ndma[0] += 1
        n = pairs[1]

        def fn(g, T):
            e = g.sync if q == "Y" else g.scalar
            for o, i in pairs[0](T):
                e.dma_start(o, i).then_inc(T.sem[sem], 16)
            return None
        add(q, fn, out, ins, 60.0 * n, lat=DFIX + nbytes / DRATE, sem=sem, inc=16 * n)

    def Q(c, n, step=1, k=0):
        return ref("q4", 4 * c + k, n, 4 * step)

    def four(t, i, rd):
        w = PER.get("%d%d%d" % (t, i, rd), CHUNKS[i][2 + rd][0])
        return int(w[1:4]) if w[0] in "FG" and t < RO else 0

    def pieces(lo, hi, most):
        k = -(-(hi - lo) // most)
        cut = [lo + (hi - lo) * i // k // 8 * 8 for i in range(k)] + [hi]
        return [(a, b - a) for a, b in zip(cut, cut[1:])]

    col = lambda c: ref("col", c, 1)
    aff = lambda o, a, s, b: act(o, a, F.Identity, scale=s, bias=b)
    dma("Y", (lambda T: [(T.sti[:], T.st[:])], 1), [ref("sti", 0, 48)], [], 60000)
    dma("S", (lambda T: [(T.qb[:, 0:Q0], T.qr[:, 0:Q0])], 1), [ref("qb", 0, Q0)], [], 70000 + 256 * Q0)
    dma("S", (lambda T: [(T.mi[2::4, :], T.bd[:]), (T.mi[3::4, :], T.bd[:])], 2), [ref("mi", 0, B // 2)], [], 1090000 + 256 * Q0)
    ops[-1].update(after=[1], free=[1])
    dma("Y", (lambda T: [(T.mi[0::4, :], T.pf[:]), (T.mi[1::4, :], T.mb[:])], 2), [ref("mi", B // 2, B // 2)], [], 1090000 + 256 * Q0)
    ops[-1].update(after=[0], free=[0])
    dma("S", (lambda T: [(T.xt[:, OFF:OFF + B], T.xn[:])], 1), [ref("xt", OFF, B)], [], 1600000 + 256 * Q0)
    ops[-1].update(after=[2], free=[2])
    if Q0 < R:
        dma("S", (lambda T: [(T.qb[:, Q0:R], T.qr[:, Q0:R])], 1), [ref("qb", Q0, R - Q0)], [], 1800000)
        ops[-1].update(after=[4], free=[4])
    dma("Y", (lambda T: [(T.ic[:], T.ip[:])], 1), [ref("ic", 0, 128)], [], 250000)
    ops[-1]["after"] = [2, 3]
    dma("Y", (lambda T: [(T.xs[:, 0:B], T.xn[:])], 1), [ref("xs", 0, B)], [], 600000)
    ops[-1]["after"] = [4]
    iota(ref("pi", 0, 1), [[0, 1]], 0, 1)
    iota(ref("ci", 0, 144), [[1, 144]], 0, 0)
    iota(ref("c4", 0, 144), [[1, 36], [0, 4]], 0, 0)
    iota(ref("ei", 0, 8), [[1, 8]], 0, 0)
    iota(ref("x9", 0, 64), [[0, 8], [1, 8]], 0, 0)
    iota(ref("c16", 0, 128), [[1, 8], [0, 16]], 0, 0)
    iota(ref("jb", 0, 2 * LB), [[0, 2], [1, LB]], 19 - LB, 0)
    iota(ref("cp", 0, 128), [[1, 8], [0, 4], [64, 4]], 0, 0)
    iota(ref("cp", 128, 128), [[1, 8], [16, 16]], -112, 0)
    iota(ref("j16", 0, 128), [[0, 8], [1, 16]], 0, 0)
    iota(ref("cc", 0, 192, 2), [[0, 192]], 0, 0)
    iota(ref("eqw", 0, 128), [[0, 128]], 1, 0)
    early[0] = False
    R4 = max(c[1] for c in CHUNKS) // 4
    for k in range(4):
        iota(ref("rk", 80 + k, R4 // 4, 4), [[0, R4 // 4]], -1 if k else 1000000, 0)
    iota(ref("c9", 0, 192), [[0, 192]], 0, 0)
    iota(ref("nt", 0, B), [[1, B]], -int(ENC), 0)
    iota(ref("nt", B, SN - B), [[1, SN - B]], B - int(ENC), 0)
    p0 = ref("pi", 0, 1)
    ts(ref("pi", 1, 1), p0, 3, A.bitwise_and)
    ts(ref("pi", 2, 1), p0, 2, A.logical_shift_right, 3, A.bitwise_and)
    ts(ref("pi", 3, 1), p0, 112, A.bitwise_and)
    ts(ref("pi", 4, 1), p0, 15, A.bitwise_and)
    ts(ref("pi", 5, 1), p0, 2, A.logical_shift_right)
    ts(ref("pi", 6, 1), p0, 3, A.logical_shift_right, 1, A.bitwise_and)
    tc(ref("col", 0, 7), ref("pi", 0, 7))
    CP, CTY, CA, CG16, CS, CP4, CH = [col(i) for i in range(7)]
    ts(ref("col", 8, 4), ref("ci", 0, 4), CTY, A.is_equal)
    T0, T1, T2, T3 = [col(8 + i) for i in range(4)]
    ts(col(12), CG16, CA, A.add, 12.0, A.add)
    tt(col(13), T1, T0, A.subtract)
    CPM, CGS, CG, CSG, C7, CGN, CAD = [col(14)] + [col(24 + i) for i in range(6)]
    CU, CK = col(18), col(19)
    ts(CPM, CTY, 1.5, A.is_lt)
    ts(CU, CS, 3.0, A.is_equal)
    ts(CK, CS, 7.0, A.is_equal)
    ts(col(22), CU, OFF + ENC, A.mult)
    ts(CGN, CPM, ENC, A.mult, col(22), A.add)
    ts(CGS, CGN, -1.0, A.mult)
    ts(C7, T2, 7.0, A.mult)
    tt(CG, CGS, C7, A.subtract)
    tt(CSG, CPM, T2, A.subtract)
    ts(col(15), CG16, 0.25, A.mult, 3.0, A.add)
    ts(col(16), CG16, 15.0, A.add)
    ts(col(17), CG16, 0.0625, A.mult)
    tt(col(20), CP, T1, A.subtract)
    ts(col(21), CS, 11.0, A.is_equal, -BIG, A.mult)
    tc(ref("ch", 0, 7), ref("pi", 0, 7))
    tc(ref("ch", 8, 6), ref("col", 8, 6))
    tc(ref("ch", 14, 8), ref("col", 14, 8))
    for k in range(4):
        ts(ref("my", 144 * k, 140), ref("ci", 0, 140), col(12), A.is_equal, col(8 + k), A.mult)
    ts(ref("my", 144 * 4, 140), ref("ci", 0, 140), col(12), A.is_equal, col(13), A.mult)
    tt(ref("ch", 40, 3), ref("col", 8, 3), ref("col", 9, 3), A.subtract)
    for k in range(3):
        ts(ref("my", 144 * (5 + k), 140), ref("ci", 0, 140), col(12), A.is_equal, col(40 + k), A.mult)
    ts(ref("my", 144 * 8, 140), ref("my", 144 * 2, 140), 0.25, A.mult)
    ts(ref("mz4", 0, 140), ref("c4", 0, 140), col(15), A.is_equal, 0.25, A.mult)
    ts(ref("mz", 0, 143), ref("ci", 0, 143), col(16), A.is_equal, 4.0, A.mult)
    tt(ref("mz", 144, 135), ref("mz", 0, 135), ref("mz", 8, 135), A.add)
    Y = lambda k, sh: ref("my", 144 * k + 12 - 4 * sh, 128)
    M = lambda i: ref("mm", 128 * i, 128)
    ci, c16 = ref("ci", 0, 128), ref("c16", 0, 128)
    ts(ref("mb16", 0, 128), ci, CP, A.is_equal)
    IB, IBH, INQ, BOQ, LQ = [ref("mb16", 128 * i, 128) for i in range(5)]
    INEG, IH, I16, BO, DAL, DX, IP, IPB, SH, PMS, BODP, IS, NB, IK3, IT3, IU, IM, IMD, BU, BK, BOK, DY = [M(i) for i in range(22)]
    iota(NB, [[0, 128]], -int(BIG), 0)
    if any("R" in x or "G" in x for x in [x for c in CHUNKS[1:] for w in c[2:] for x in w] + [PER[x] for x in PER if x[1] != "0"]):
        aff(ref("mz", 288, 143), ref("mz", 0, 143), 2.0, 0.0)
        aff(ref("mz4", 144, 143), ref("mz", 0, 143), -1.0, 0.0)
    ts(BO, c16, col(17), A.is_equal)
    ts(DAL, ref("c4", 0, 128), CP4, A.is_equal, T2, A.mult)
    ts(SH, ci, col(20), A.is_equal, T1, A.mult)
    ts(PMS, ci, col(20), A.is_equal, col(40), A.mult)
    ts(BODP, ref("cp", 0, 128), col(17), A.is_equal, col(21), A.mult)
    tt(ref("ch", 43, 1), CA, T0, A.mult)
    ts(BOK, ref("cp", 128, 128), col(17), A.is_equal, col(43), A.mult)
    aff(BOQ, BO, 0.25, 0.0)
    add("G", lambda g, T: g.affine_select(ap(T, LQ), ap(T, BOQ), [[1, 128]], A.is_gt, 0.0, 0, -1), [LQ], [BOQ], 170 + 256 * CY)
    aff(col(36), T0, ENC, col(22))
    aff(col(37), T0, ENC - BIG, col(22))
    aff(col(38), T1, -ENC, 0.0)
    aff(col(44), T3, -1.0, 1.0)
    aff(col(45), T1, BIG, 0.0)
    aff(col(46), T2, BIG, col(45))
    aff(col(47), T0, BIG, 0.0)
    tc(ref("ch", 44, 4), ref("col", 44, 4))
    rows = [(INEG, -1.0), (IH, 0.5), (IBH, 0.5), (I16, 1.0), (IP, T0), (IM, T1), (IPB, col(47)), (IMD, col(46)), (IK3, col(44)), (IT3, T3), (IU, CU),
            (INQ, -0.25), (IS, -QO / 2)]
    for i, (m_, c) in enumerate(rows):
        if i < NV:
            ts(m_, ci, CP, A.is_equal, c, A.mult)
        else:
            aff(m_, IB, c, 0.0)
    for m_, c in ((BU, CU), (BK, CK)):
        aff(m_, BO, c, 0.0)
    aff(ref("kf", 0, 128), DAL, -BIG, 0.0)
    tt(DX, ref("kf", 0, 128), IM, A.subtract)
    tt(DY, ref("kf", 0, 128), I16, A.add)
    aff(ref("mz", 432, 143), ref("mz", 0, 143), T2, 0.0)
    cw = lambda i: ref("cw", 8 * i, 8)
    ts(cw(0), ref("ei", 0, 8), 16.0, A.mult, CS, A.add)
    ts(col(31), CH, 4.0, A.mult)
    ts(col(32), CH, 4.0, A.mult, 3.0, A.add)
    x9 = lambda i: ref("x9", 64 * i, 64)
    ts(x9(1), x9(0), col(32), A.is_equal, 4.0, A.mult)
    ts(x9(2), x9(0), col(32), A.is_le)
    tt(x9(1), x9(1), x9(2), A.subtract)
    ts(x9(3), x9(0), col(31), A.is_equal, 1.0e6, A.mult)
    ts(x9(2), x9(2), 1.0e5 - 1, A.mult, -1.0e5, A.add)
    tt(ref("rk", 0, 64), x9(2), x9(3), A.add)
    ts(ref("dg", 0, 128), ref("j16", 0, 128), CS, A.is_equal, 17 * BIG, A.mult)
    ts(ref("dg", 0, 128), ref("dg", 0, 128), -BIG, A.add)
    aff(col(53), CS, -BIG, 15 * BIG)
    aff(col(54), CS, -BIG, 15 * BIG + OFF + ENC)
    ts(ref("kt", 0, 4), ref("ci", 0, 4), CA, A.is_equal)
    iota(ref("fw", 0, 128), [[0, 128]], 1, 0)
    iota(ref("fw", 128, BX - 128), [[0, BX - 128]], 0, 0)
    blk = lambda nm, i, x: ref(nm, 8 * LB * i + x, 8, LB)
    pair = lambda nm, i, a: ref(nm, 8 * LB * i + 2 * a * (LB - 16) + LB - 20, LB + 20 + 32 * a)
    for a in range(4):
        ts(pair("dz", 0, a), ref("jb", LB - 20 - 32 * a, LB + 20 + 32 * a), CS, A.is_equal, -BIG, A.mult)
        iota(ref("ne", LB * (2 * a + 1), LB - 35 - 32 * a), [[0, LB - 35 - 32 * a]], int(BIG), 0)
    iota(ref("ne", LB - 20, 4, 2 * LB - 32), [[0, 4]], int(BIG), 0)
    iota(blk("ne", 0, LB - 3), [[0, 8]], int(BIG), 0)
    iota(ref("dz", LB - 20, 8, LB - 16), [[0, 8]], 4 * int(BIG), 0)
    iota(blk("dz", 0, LB - 3), [[0, 8]], int(BIG), 0)
    aff(blk("ne", 0, LB - 1), cw(0), 1.0, 128.0)
    aff(ref("cb", 0, 8), cw(0), 1.0, 128.0)
    for i in range(1, len(CHUNKS)):
        for rd in range(2):
            w = CHUNKS[i][2 + rd]
            nh = CHUNKS[i][1] // len(w)
            for h in range(len(w)):
                for k in range(4):
                    if any("R" in x for x in w) and w[h][k] == "D":
                        iota(view("dd%d%d" % (i, rd), slice(h * nh, h * nh + nh), k), [[0, nh]], -int(QO), 0)
    for t in range(RO):
        aff(ref("c9", 64 * t + 7, 8, 8), cw(0), 1.0, 128.0 * t)
        aff(cw(1 + t), cw(0), -1.0, ENC + OFF - 128.0 * t)
        aff(col(33 + t), T2, 6.0 - t - BIG, col(38))
        aff(col(50 + t), col(33 + t), 1.0, -7 * BIG)
        iota(ref("tc16", 256 * t, 256), [[1, 256]], B + 384 * t - int(BIG), 0)
    iota(ref("mt", 0, OFF), [[0, OFF]], 0, 0)
    e_ = int(ENC)
    dma("Y", (lambda T: [(T.mt[3::16, x:x + 384], T.nt[3::16, e_:e_ + 384]) for x in (0, 384)] + [(T.mt[11::16, 0:768], T.nt[11::16, e_ + 1:e_ + 769])], 3),
        [ref("mt", 0, 768)], [ref("nt", e_, 769)], 50000)
    iota(ref("xt", 0, OFF), [[0, OFF]], 0, 0)
    for t in range(RO):
        iota(ref("snd", BX * t, 64), [[0, 64]], 4096, 0)
        iota(ref("rcv", BX * t + 64, BX - 64), [[0, BX - 64]], 4096, 0)
    for c0, n, _, _ in CHUNKS:
        tc(ref("stu", c0 // 16, n // 16), ref("sti", c0 // 16, n // 16))
        act(Q(c0, n), ref("qb", c0, n), F.Identity, bias=QO)
        na = four(0, [c[0] for c in CHUNKS].index(c0), 0)
        for k in range(1, 4 * (na > 0)):
            act(Q(c0, na, 1, k), ref("qb", c0, na), F.Identity, bias=QO)
    for i in range(8):
        aff(ref("mt", OFF + 256 * i, 256), ref("mi", 256 * i, 256), CSG, C7)
        ops[-1]["after"] = [2, 3]
    conv = list(range(len(ops) - 8, len(ops)))
    ts(ref("ij", 0, 128), ref("ic", 0, 128), 2, A.logical_shift_right)
    ts(ref("ij", 128, 128), ref("ic", 0, 128), 3, A.bitwise_and)
    aff(ref("iu", 0, 128), ref("ij", 0, 128), 1.0, float(OFF))
    act(ref("iu", 128, 128), ref("ij", 128, 128), F.Copy)
    dma("Y", (lambda T: [(T.mt[3 + 4 * r::16, OFF:OFF + B], T.iu[:, 128 * r:128 * r + 128]) for r in range(2)], 2), [ref("mt", OFF, B)],
        [ref("iu", 0, 256)], 1 << 17)
    back = len(ops) - 1
    dma("Y", (lambda T: [(T.mn[3::4, 0:B], T.nt[3::4, 0:B])], 1), [ref("mn", 0, B // 2)], [ref("nt", 0, B)], 1 << 18)
    dma("Y", (lambda T: [(T.mn[0::4, 0:B], T.mt[0::4, OFF:OFF + B])], 1), [ref("mn", B // 2, B // 2)], [ref("mt", OFF, B)], 1 << 18)
    dma("Y", (lambda T: [(T.yp[:, 0:B], T.mt[0::4, OFF:OFF + B])], 1), [], [ref("mt", OFF, B)], 262144)
    for o in ops[-2:]:
        o["after"], o["skip"] = conv, back

    LA = lambda i: ref("la", 8 * i, 8)
    vw = lambda i: ref("vw", 64 * i + 7, 8, 8)

    def reads(t, ci_, c0, n, ways):
        base = B + 384 * t
        m, r4 = n // 16, n // 4
        ways = [[PER["%d%d%d" % (t, ci_, rd)]] if "%d%d%d" % (t, ci_, rd) in PER else ways[rd] for rd in range(2)]
        H = len(ways[0])
        nh, mh = n // H, m // H
        pb = pb2 = "ps" + BANKS[ci_][0]
        at = 0 if pb[2] in BANKS[ci_][1:] else 3 * r4
        turn = [0]

        def px(h, w):
            turn[0] += 1
            b = BANKS[ci_][1 + turn[0] % (len(BANKS[ci_]) - 1)]
            return ref("ps" + b, 3 * r4 if b == pb[2] else 0, w)
        o4 = c0 // 4
        c4_ = lambda nm, lo=0, cnt=r4: ref(nm, o4 + lo, cnt)
        pD, pE, pP = ref(pb, 0, r4), ref(pb, r4, r4, 2), ref(pb, r4 + 1, r4, 2)
        pS = ref(pb2, at + r4, r4) if ci_ else ref("ps2", 320, 64)
        pU = pS if ci_ else ref("ps2", 384, r4)
        tb = 2 * o4 + (64 if ci_ else 0)
        pc = PIECE if ci_ else 99
        sums = [(ref("mz4", 12 - 4 * s, 128), ref("sh", s, r4, 4) if ci_ == 0 and t > 0 else Q(c0 + s, r4, 4)) for s in range(4)]
        mm([(pU, sums)])
        ts(c4_("ti"), pU, -0.375, A.add)
        tt(c4_("tau"), c4_("ti"), pU, A.subtract)
        lst = ref("stu", c0 // 16, m)
        part = lambda r, h, w: ref(r[0], r[1] + h * w, w)
        for rd in range(2):
            tag[0] = "%d%d" % (ci_, rd)
            XW = lambda off: ind("xt", OFF, OFF + base, off) if ci_ == 0 or (rd == 0 and (t == 0 or ci_ in LIVE)) else ind("xs", SN * t, SN * t + base, off)
            for h in range(H):
                groute, lh, go = ways[rd][h][5], part(lst, h, mh), ref("g16", c0 + h * nh, nh)
                gw = ind("mn", 0, base, lh) if ci_ and rd else ind("mt", OFF, OFF + (base if rd else B), lh)
                if t == 0:
                    aff(go, ind("mi", 0, B, lh), CSG, CGS)
                elif groute == "S":
                    act(go, gw, F.Identity, bias=CG)
                else:
                    ts(go, gw, CG, A.add)
            gs = lambda s: ref("g16", c0 + s, r4, 4)
            if rd == 0 and ci_ == 0:
                mm([(pE, [(Y(4, s), gs(s)) for s in range(4)]), (pP, [(Y(0, s), gs(s)) for s in range(4)])], pc)
                mm([(pD, [(Y(8, s), gs(s)) for s in range(4)] + sums)], 4)
                ops[-2]["after"] = [len(ops) - 3]
                ops[-2]["free"] = [len(ops) - 3]
                tt(ref("cc", 2 * o4 + 1, r4, 2), pD, c4_("ti"), A.is_ge)
            else:
                pD = ref("ps" + BANKS[ci_][1], n, r4) if ci_ else ref("ps2", 416, r4)
                mm([(pD, [(Y(8, s), gs(s)) for s in range(4)])])
                mm([(pE, [(Y(4, s), gs(s)) for s in range(4)]), (pP, [(Y(0, s), gs(s)) for s in range(4)])], pc)
                tt(ref("cc", 2 * o4 + 1, r4, 2), pD, c4_("tau"), A.is_ge)
            scan(ref("t16", tb, 2 * r4), ref("cc", 2 * o4, 2 * r4), ref(pb, r4, 2 * r4), 0.0, A.mult, A.add)
            last = ci_ == 0 and rd == 1
            if last:
                ts(ref("t16", 65, r4, 2), pD, -1.7, A.is_gt)
            t16 = lambda cl, cnt=m: ref("t16", tb + 2 * cl + 1, cnt, 8)
            whole = ways[rd][0][0] in "EFG"
            if whole:
                ts(c4_("ou"), ref("t16", tb + 1, r4, 2), ENC, A.add)
            for k0, k1 in ([] if whole else KS if ci_ == 0 else [(0, 4)]):
                mm([(ref(pb2, at + k * m, m), [(Y(k, cl), t16(cl)) for cl in range(4)]) for k in range(k0, k1)], pc)
                ts(c4_("ou", k0 * m, (k1 - k0) * m), ref(pb2, at + k0 * m, (k1 - k0) * m), ENC, A.add)
            YD = lambda k, cl: Y(5 + k if k < 3 else 3, cl)
            if ci_:
                mm([(ref(pb2, at + 2 * r4 + k, m, 4), [(YD(k, cl), t16(cl)) for cl in range(4)]) for k in range(4)], pc)
            else:
                cnt = 16 if last else 8
                mm([(ref("ps2", 64 + 8 * h + 2 * k, cnt, 16), [(YD(k, cl), t16(cl, cnt)) for cl in (2 * h, 2 * h + 1)]) for h in range(2) for k in range(4)]
                   + [(ref("ps2", 193, 64, 2), [(I16, ref("c9", 64 * t, 64))])] * last)
            relu = any("R" in x or "G" in x for x in ways[rd])
            if whole:
                na = four(t, ci_, rd)
                some = lambda nm, j, w: view(nm, slice(j, j + w), al) if ci_ else view(nm, slice(j // 8, (j + w) // 8), al, al)
                for j, w in pieces(0, na, AW if ci_ else AWW):
                    d = ref("df", 4 * (c0 + j), 4 * w)
                    tt(d, XW(c4_("ou", j // 4, w // 4)), ref("q4", 4 * (c0 + j), 4 * w), A.subtract)
                    act(some("ab%d" % ci_, j, w), d, F.Relu if relu else F.Abs, bias=QO)
                for j, w in pieces(na, n, DW if ci_ else n):
                    pd, lo = px(0, 4 * w), 4 * (c0 + j)
                    cut = 1 if ci_ or na else int(ways[rd][0][1])
                    for x in range(cut):
                        act(ref("xr", lo + x * 4 * w // cut, 4 * w // cut), XW(c4_("ou", j // 4 + x * w // 4 // cut, w // 4 // cut)), F.Copy)
                    minus = [(INEG, Q(c0 + j, w), ref(pd[0], pd[1] + k, w, 4)) for k in range(4)]
                    mm([(pd, minus + [(IB, ref("xr", lo, 4 * w))])], 4)
                    act(some("ab%d" % ci_, j, w), pd, F.Abs, bias=QO)
            for h in range(0 if whole else H):
                routes, q, js = ways[rd][h][:4], Q(c0 + h * nh, nh), slice(h * nh, h * nh + nh)
                run = lambda x: [(k, k + 1) for k in range(4) if routes[k] == x] if not (ci_ and x in JOIN and (x != "D" or H == 1)) else \
                    [(routes.index(x), routes.rindex(x) + 1)] if x in routes else []
                ab = lambda k0, k1: view("ab%d" % ci_, js, slice(k0, k1)) if ci_ else view("ab0", al, al, k0)
                dd = lambda k0, k1: view("dd%d%d" % (ci_, rd), js, slice(k0, k1) if k1 > k0 + 1 else k0) if ci_ else ref("dd", k0 * n, n)
                for k0, k1 in run("D"):
                    act(ref("xr", 4 * c0 + k0 * n + h * nh, (k1 - k0) * nh), XW(c4_("ou", k0 * m + h * mh, (k1 - k0) * mh)), F.Copy)
                    for k in range(k0, k1):
                        pd = px(h, nh)
                        mm([(pd, [(INEG, q), (IB, ref("xr", 4 * c0 + k * n + h * nh, nh))])])
                        act(ab(k, k + 1), pd, F.Abs, bias=QO / (1 + relu), scale=1.0 / (1 + relu))
                for x in "AR":
                    for k0, k1 in run(x):
                        for k in range(k0, k1):
                            tt(dd(k, k + 1), XW(c4_("ou", k * m + h * mh, mh)), q, A.subtract)
                        if x == "A":
                            act(ab(k0, k1), dd(k0, k1), F.Relu if relu else F.Abs, bias=QO)
                        else:
                            ts(ab(k0, k1), dd(k0, k1), QO, A.add, 0.0, A.max)
            lst = ref("lv", 48 * rd + c0 // 16, m)
            if ci_:
                every = lambda nm, s: view(nm % ci_, slice(s, None, 16), al)
                na = four(t, ci_, rd) or n
                less = [(ref("mz4", 144 + 15 - s, 128), view("dd%d%d" % (ci_, rd), slice(s, na, 16), al), ref(pS[0], pS[1], na // 4)) for s in range(16 * relu)]
                more = [(ref("mz", 288 * relu + 15 - s, 128), every("ab%d", s)) for s in range(16)]
                mm([(pS, less + more)], pc)
                scan(c4_("pm", 48), ref("rk", 80, r4), pS, 0.0, A.add, A.min)
                tt(c4_("eq"), pS, c4_("pm", 48), A.not_equal)
                scan(ref("ve", 192 * rd + o4, r4), c4_("eq"), ref(pb2, at + 2 * r4, r4), 0.0, A.mult, A.add)
                ts(lst, ref("ve", 192 * rd + o4 + 3, m, 4), ENC, A.add)
            else:
                mm([(pS, [(ref("mz", 144 + 7 - s, 128), view("ab0", al, s, al)) for s in range(8)])])
                eq = ref("eqw", 0, 64, 2)
                scan(ref("pm", 0, 64), ref("rk", 0, 64), pS, 0.0, A.add, A.min)
                tt(eq, pS, ref("pm", 0, 64), A.not_equal)
                scan(ref("vw", 64 * rd, 64), eq, ref("ps2", 64, 64, 2), 0.0, A.mult, A.add)
                ts(lst, vw(rd), ENC, A.add)
                if last:
                    scan(ref("vw", 128, 64), eq, x9(1), 0.0, A.mult, A.add)
                    tt(ref("eqw", 15, 8, 16), blk("lo", 0, LB - 2), cw(1 + t), A.add)
                    scan(ref("vw", 192, 128), ref("eqw", 0, 128), ref("ps2", 192, 128), 0.0, A.mult, A.add)
                    tc(LA(4), ref("vw", 192 + 15, 8, 16))
            hb = QO / 2 - 0.25
            for h in range(H):
                qroute, c1, xw = ways[rd][h][4], c0 + h * nh, XW(part(lst, h, mh))
                q, sh, xg, pq = Q(c1, nh), ref("sh", c1, nh), ref("xg", c1, nh), px(h, nh)
                na = four(t + rd, ci_, 1 - rd) if ci_ or not rd else 0
                if qroute == "M":
                    tt(sh, xw, q, A.add)
                    act(q, sh, F.Identity, scale=0.5, bias=hb)
                    for k in range(1, 4 * (na > 0)):
                        if ci_ and 2 * t + rd >= GQ and k <= GK:
                            gcopy(Q(c1, na, 1, k), Q(c1, na))
                        else:
                            act(Q(c1, na, 1, k), ref("sh", c1, na), F.Identity, scale=0.5, bias=hb)
                else:
                    act(xg, xw, F.Copy)
                    mm([(pq, [(IH, q), (IBH, xg)])])
                    if na:
                        ts(q, pq, hb, A.add)
                    else:
                        act(q, pq, F.Identity, bias=hb)
                    for k in range(1, 4 * (na > 0)):
                        ts(Q(c1, na, 1, k), ref(pq[0], pq[1], na), hb, A.add)
                if t == RO - 1 and ci_ and rd:
                    if "o" in ONS:
                        act(ref("qo", c1, nh), q, F.Identity, bias=-QO)
                    else:
                        ts(ref("qo", c1, nh), q, -QO, A.add)
                    dma("Y", (lambda T, c1=c1: [(T.yq[:, c1:c1 + nh], T.qo[:, c1:c1 + nh])], 1), [], [ref("qo", c1, nh)], 256 * nh)
            if ci_ == 0 and rd == 0:
                lowest_of(t, 0, lst)
            elif ci_ == 0:
                step_a(0)

    def lowest(i, key, own):
        for c in range(7, -1, -1):
            ts(ref("ne", (LB - 16) * c + LB - 19, 16 * c + 16), ref(key[0], key[1], 16 * c + 16), ref("ne", LB * c + LB - 2, 1), A.not_equal, BIG, A.mult)
        for a in range(3, -1, -1):
            scan(pair("lo", i, a), pair("dz", 0, a), pair("ne", 0, a), 0.0, A.add, A.min)

    def lowest_of(t, i, lst):
        key = ref("ky", 128 * i, 128)
        act(key, ind("nt", 0, B + 384 * t, lst), F.Copy)
        aff(blk("dz", 0, LB - 2), cw(0), 1.0, (768.0 if i else 384.0 + 128 * t) - OFF - ENC)
        if "v" in ONS:
            act(blk("ne", 0, LB - 2), vw(i), F.Copy)
        else:
            tc(blk("ne", 0, LB - 2), vw(i))
        lowest(i, key, vw(i))
        ts(LA(i), blk("lo", i, LB - 2), OFF + ENC, A.add)

    pL, pY, pR, pM = [ref("ps1", 128 * i, 128) for i in range(4)]

    node = [ref("g16", 0, 128), ref("gs", 0, 128)]

    def step_a(z):
        mm([(pL, [(DY, node[z])])])
        ts(ref("yy", 128 * z, 128), pL, 0.0 if z else -7 * BIG, A.add, -2048.0, A.max)

    def step_b(t, z, lg, la, back):
        base = B + 384 * t
        h = lambda nm: ref(nm, 128 * z, 128)
        name = ref("tc16", 128 * (2 * t + z), 128)
        act(h("g32"), ind("mt", 0, OFF + base, lg), F.Copy)
        mm([(pY, [(DX, node[z]), (IM, name), (IMD, h("kk"))])])
        act(h("w1"), pY, F.Relu, bias=col((33 if z else 50) + t))
        tt(ind("mt", 0, OFF + base, la), h("g32"), h("w1"), A.add)
        off = (BODP, back) if z == 0 else (IPB, ref("md", 0, 128))
        mm([(pR, [(SH, node[z]), (PMS, h("yy")), (IT3, back), off]), (pM, [(IP, name), (IPB, h("kk"))] + [(IP, NB)] * z + [off])])
        act(h("t1"), pR, F.Relu, bias=col(37) if z else col(36))
        tt(ref("mt", OFF + base + 128 * (z + 1), 128), pM, h("t1"), A.max)

    sent = []

    def writers(t):
        base = B + 384 * t
        q = Q(0, 128)
        lv = ref("lv", 48, 8)
        nn = OFF + base
        tag[0] = "1"
        lowest_of(t, 1, lv)
        tc(LA(6), vw(2))
        act(ref("kk", 0, 128), ind("kt", 0, 4, LA(6)), F.Copy)
        pN = ref("ps0", 384, 128)
        act(ref("gv", 0, 128), ind("mt", OFF, OFF + base, lv), F.Identity, bias=CGS)
        mm([(pN, [(IK3, ref("gv", 0, 128)), (IU, ref("ky", 0, 128)), (BOK, ref("kk", 0, 128))])])
        act(ref("mt", nn, 128), pN, F.Identity, bias=CGN)
        if "x" in ONS:
            act(ref("xt", nn, 128), q, F.Identity, bias=-QO)
        else:
            ts(ref("xt", nn, 128), q, -QO, A.add)
        if t == RO - 1:
            act(ref("q1", 0, 128), q, F.Identity, scale=-1.0, bias=QO)
        PC = ref("ps7", 128, 128)
        mm([(PC, [(IH, q), (IBH, ref("xg", 0, 128))])])
        ts(ref("mxi", 0, 128), PC, -QO / 2 - 0.25, A.add)
        tc(ind("mt", 0, nn, LA(1)), ref("mt", nn, 128))
        tc(ind("xt", 0, nn, LA(1)), ref("mxi", 0, 128))
        sn = SN * (t + 1)
        if t < RO - 1 and not LATE:
            dma("Y", (lambda T: [(T.xs[:, sn:sn + base], T.xt[:, OFF:nn])], 1), [ref("xs", sn, base)], [ref("xt", OFF, base)], 256 * base)
        gi = ref("gi", 0, 128)
        act(gi, ind("mt", 0, nn, LA(4)), F.Identity, bias=CGS)
        step_b(t, 0, LA(0), LA(0), gi)
        act(ref("xt", nn + 128, 128), ind("xt", 0, nn, LA(4)), F.Copy)
        pkey, pown, pk2, own = ref("ps7", 384, 128), ref("ps2", 64, 128), ref("ps0", 0, 128), ref("dm", 15, 8, 16)
        mm([(pown, [(BU, gi)])])
        mm([(pkey, [(BU, gi)])])
        mm([(pk2, [(BK, gi)])])
        scan(ref("dm", 0, 128), ref("dg", 0, 128), pown, 0.0, A.add, A.min)
        act(ref("ky", 256, 128), pkey, F.Copy)
        ts(LA(5), own, col(54), A.add)
        ts(ref("kk", 128, 128), pk2, CA, A.is_equal)
        aff(blk("dz", 0, LB - 2), cw(0), 1.0, 128.0 * t - OFF - ENC)
        aff(blk("dz", 0, LB - 1), cw(0), -1.0, OFF + ENC - 128.0 * t)
        ts(blk("ne", 0, LB - 2), own, col(53), A.add)
        lowest(2, ref("ky", 256, 128), own)
        tt(ref("kf", 0, 128), ind("mt", 0, nn, LA(5)), ref("kk", 128, 128), A.min)
        pF, pos = ref("ps2", 448, 8), ref("ps2", 464, 8)
        mm([(pF, [(ref("mz", 432 + 15 - s, 128), ref("kf", s, 8, 16)) for s in range(16)])])
        f, f2 = ref("f8", 0, 8), ref("f8", 8, 8)
        tt(f, pF, blk("lo", 2, LB - 3), A.min)
        tt(f2, pF, blk("lo", 2, LB - 1), A.mult)
        mm([(pos, [(IB, ref("cb", 0, 8)), (LQ, f)] + [(BOQ, ref("f8", 0, 8 - d), ref("ps2", 464 + d, 8 - d)) for d in range(1, 8)] + [(INQ, f2)])])
        tc(LA(3), pos)
        tc(ind("snd", BX * t, BX * t + BX, LA(3)), ref("xt", nn, 128) if t < RO - 1 else ref("q1", 0, 128))
        rid, pid, mask = rank_peers[t]
        so, ro = ref("snd", BX * t, 64), ref("rcv", BX * t, 64)
        add("G", lambda g, T: g.remote_dma(ap(T, ro), ap(T, so), T.sem["arr%d" % t], T.sem["snt%d" % t], pid, rid, mask),
            [], [so], 200.0, lat=XLAT - 500, sem="snt%d" % t, inc=NENG)
        sent.append(len(ops) - 1)
        add("G", lambda g, T: None, [ro], [so], 1.0, lat=XLAT, sem="arr%d" % t, inc=NENG)
        ts(LA(2), blk("lo", 2, LB - 2), OFF + ENC, A.add)
        tag[0] = "2"
        act(ref("md", 0, 128), ind("fw", 0, BX, LA(3)), F.Copy)
        act(node[1], ind("mt", 0, nn, LA(5)), F.Identity, bias=CGS)
        step_a(1)
        step_b(t, 1, LA(5), LA(2), node[1])
        tt(ref("xt", nn + 256, 128), ind("xt", 0, nn, LA(5)), ref("md", 0, 128), A.mult)
        if t < RO - 1:
            x0 = 0 if LATE else base
            dma("Y", (lambda T: [(T.xs[:, sn + x0:sn + base + 384], T.xt[:, OFF + x0:nn + 384])], 1), [ref("xs", sn + x0, base + 384 - x0)],
                [ref("xt", OFF + x0, base + 384 - x0)], 256 * (base + 384 - x0) * (1 + LATE))
            ops[-1]["after"] = [sent[t]] * LATE
            dma("Y", (lambda T: [(T.mn[r::4, 0:base], T.mt[r::4, OFF:nn]) for r in (1, 2)] + [(T.mn[:, base:base + 384], T.mt[:, nn:nn + 384])], 3),
                [ref("mn", 0, base + 384)], [ref("mt", OFF, base + 384)], 256 * base + 200000)
            ops[-1]["after"] = [sent[t]]
        sh = ref("sh", 0, 128)
        tt(sh, ind("rcv", BX * t, BX * t + BX, LA(3)), q if t < RO - 1 else ref("xt", nn, 128), A.min)
        if t == RO - 1:
            act(ref("qo", 0, 128), sh, F.Abs)
            dma("S", (lambda T: [(T.yq[:, 0:128], T.qo[:, 0:128])], 1), [], [ref("qo", 0, 128)], 32768)
        elif "r" in ONS:
            act(ref("rr", 0, 128), sh, F.Sign, bias=-QO / 2)
            mm([(PC, [(I16, sh), (IS, ref("rr", 0, 128))])])
            ts(q, PC, QO / 2, A.add)
            na = four(t + 1, 0, 0)
            for k in range(1, 4 * (na > 0)):
                ts(Q(0, na, 1, k), ref(PC[0], PC[1], na), QO / 2, A.add)
        else:
            ts(ref("rr", 0, 128), sh, QO / 2, A.is_lt, QO, A.mult)
            mm([(PC, [(I16, sh), (I16, ref("rr", 0, 128))])])
            tc(q, PC)
            na = four(t + 1, 0, 0)
            for k in range(1, 4 * (na > 0)):
                tc(Q(0, na, 1, k), ref(PC[0], PC[1], na))

    for t in range(RO):
        for i, c in enumerate(CHUNKS):
            reads(t, i, c[0], c[1], c[2:])
        writers(t)
    e0 = W - 256
    dma("Y", (lambda T: [(T.yx[:, 0:e0], T.xt[:, OFF:OFF + e0])], 1), [], [ref("xt", OFF, e0)], 256 * e0)
    dma("Y", (lambda T: [(T.yp[:, B:e0], T.mt[0::4, OFF + B:OFF + e0])], 1), [], [ref("mt", OFF + B, e0 - B)], 128 * (e0 - B))
    dma("Y", (lambda T: [(T.ym[:], T.mt[1::4, OFF:OFF + W])], 1), [], [ref("mt", OFF, W)], 128 * W)
    dma("S", (lambda T: [(T.yx[:, e0:W], T.xt[:, OFF + e0:OFF + W]), (T.yp[:, e0:W], T.mt[0::4, OFF + e0:OFF + W])], 2), [],
        [ref("xt", OFF + e0, 256), ref("mt", OFF + e0, 256)], 98304)
    return ops


def depends(ops):
    hist, bank = {}, {}
    for i, o in enumerate(ops):
        dep = set(o.get("after", ()))
        for acc, regs in ((0, o["rd"]), (1, o["wr"])):
            for nm, cols in regs:
                ps = SCRATCH[nm][0] == "psum"
                for j, w, c2 in hist.get(nm, ()):
                    if j != i and ((cols & c2 and (w or acc)) or (ps and (ops[j]["e"] != o["e"] or "alt" in o or "alt" in ops[j]))):
                        dep.add(j)
        if o["e"] == "P":
            for nm, _ in o["wr"]:
                j = bank.get(nm, i)
                if j != i and j not in dep:
                    dep.add(j); o["free"] = o["free"] + [j]
                bank[nm] = i
        for acc, regs in ((0, o["rd"]), (1, o["wr"])):
            for nm, cols in regs:
                h = hist.setdefault(nm, [])
                if acc:
                    h[:] = [x for x in h if x[2] & ~cols]
                h.append((i, acc, cols))
        o["dep"] = sorted(dep - {o.get("skip")})


def schedule(ops):
    n = len(ops)
    HOP, SELF = COST[9:]
    succ, pred = [[] for _ in ops], [[] for _ in ops]
    for i, o in enumerate(ops):
        for j in o["dep"]:
            p = ops[j]
            either = "alt" in p or "alt" in o
            d = 0.0 if j in o.get("free", ()) else p["lat"] + ((HOP + SELF) / 2 if either else SELF if p["e"] == o["e"] and not p["sem"] else HOP)
            succ[j].append((i, d)); pred[i].append((j, d))
    pr = [0.0] * n
    for i in range(n - 1, -1, -1):
        pr[i] = ops[i]["c"] + max([pr[j] + d for j, d in succ[i]] + [ops[i]["lat"]])
    x = SEED
    best = None
    for it in range(PASSES):
        for i in range(n):
            x = (x * 1103515245 + 12345) % 2147483648
            pr[i] += JIT * (x / 2147483648.0)
        order, st = one_pass(ops, succ, pred, pr, [0.0] * n, True)
        end = max(st[i] + ops[i]["c"] + ops[i]["lat"] for i in range(n))
        if best is None or end < best[1]:
            best = (order, end, st, [o["e"] for o in ops])
        if it + 1 < PASSES:
            _, sb = one_pass(ops, pred, succ, [st[i] + ops[i]["c"] for i in range(n)], [o["lat"] for o in ops], False)
            pr = [sb[i] + ops[i]["c"] for i in range(n)]
    for i, o in enumerate(ops):
        o["t"], o["e"] = best[2][i], best[3][i]
        if "alt" in o:
            o["fn"], o["c"] = o["alt"][o["e"]]
    return best[0], best[1]


def one_pass(ops, succ, pred, pr, rdy, choose):
    n = len(ops)
    left = [len(p) for p in pred]
    free = {e: 0.0 for e in "VSPGY"}
    pool = {e: [] for e in free}

    def enter(i):
        o = ops[i]
        if choose and "alt" in o and not o["pin"]:
            end = {e: max(rdy[i], free[e] + sum(ops[j]["c"] for j in pool[e] if pr[j] > pr[i] - AHEAD)) + o["alt"][e][1] * WEIGH[e] for e in "SV"}
            o["e"] = min("SV", key=lambda e: end[e])
            o["c"] = o["alt"][o["e"]][1]
        pool[o["e"]].append(i)
    for i in range(n):
        if not left[i]:
            enter(i)
    order, start = [], [0.0] * n
    while len(order) < n:
        best = None
        for e in pool:
            if pool[e]:
                t0 = max(free[e], min(rdy[i] for i in pool[e]))
                if best is None or t0 < best[0]:
                    best = (t0, e)
        t0, e = best
        i = max((i for i in pool[e] if rdy[i] <= t0 + 40.0), key=lambda i: pr[i])
        late = [j for j in pool[e] if t0 + 40.0 < rdy[j] < t0 + LOOK * ops[i]["c"] and pr[j] > pr[i] + ops[i]["c"]]
        if late:
            j = max(late, key=lambda j: pr[j])
            fit = [k for k in pool[e] if rdy[k] <= t0 + 40.0 and t0 + ops[k]["c"] <= rdy[j] + 30.0]
            i = max(fit, key=lambda k: pr[k]) if fit else j
        pool[e].remove(i)
        start[i] = max(t0, rdy[i])
        free[e] = start[i] + ops[i]["c"]
        order.append(i)
        for j, d in succ[i]:
            rdy[j] = max(rdy[j], free[e] + d)
            left[j] -= 1
            if not left[j]:
                enter(j)
    return order, start


def replay(s, order, lo, fin, last=()):
    eng, c, pred, ends = s
    fin, free = fin[:], dict.fromkeys("VSPGY", 0.0)
    for i in last:
        free[eng[i]] = fin[i]
    for i in order[lo:]:
        e = eng[i]
        t = free[e]
        for j, d in pred[i]:
            x = fin[j] + d
            if x > t:
                t = x
        fin[i] = free[e] = t + c[i]
    return max(fin[i] + d for i, d in ends), fin


def polish(ops, order):
    n = len(ops)
    eng = [o["e"] for o in ops]
    pred = [set(o["dep"]) for o in ops]
    succ = [set() for _ in ops]
    for i in range(n):
        for j in pred[i]:
            succ[j].add(i)
    above, near = [], []
    for i in range(n):
        far = 0
        for j in pred[i]:
            far |= above[j]
        near.append([j for j in pred[i] if ops[j]["lat"] or not far >> j & 1])
        above.append(far | sum(1 << j for j in pred[i] if not far >> j & 1))
    alts = [build([(0, 0, 0)] * RO, cost) for cost in OTHER]
    sets = [(eng, [0.0] * n, [0] * n, [(i, alt[i]["lat"]) for i in range(n) if not succ[i]]) for alt in alts]

    def price(calls):
        for s, alt, cost in zip(sets, alts, OTHER):
            for i in calls:
                s[1][i] = alt[i]["alt"][eng[i]][1] if "alt" in alt[i] else alt[i]["c"]
                s[2][i] = [(j, 0.0 if j in ops[i].get("free", ()) else alt[j]["lat"] + (cost[10] if eng[i] == eng[j] and not ops[j]["sem"] else cost[9]))
                           for j in near[i]]

    def flip(i):
        eng[i] = "S" if eng[i] == "V" else "V"
        price([i] + sorted(succ[i]))
    price(range(n))
    now = [replay(s, order, 0, [0.0] * n) for s in sets]
    unit = [len(sets) * x[0] for x in now]
    seed, val, best, held = [SEED], 1.0, (1.0, order, eng[:]), None

    def rnd():
        seed[0] = (seed[0] * 1103515245 + 12345) % 2147483648
        return (seed[0] + 1) / 2147483650.0
    for it in range(MOVES):
        if held is None:
            held, last, prev = [], {}, {}
            for i in order:
                prev[i], last[eng[i]] = last.get(eng[i], -1), i
            for s, (_, fin) in zip(sets, now):
                i = max(s[3], key=lambda x: fin[x[0]] + x[1])[0]
                while i >= 0:
                    st, p = fin[i] - s[1][i], prev[i]
                    if p >= 0 and abs(fin[p] - st) < 1e-6:
                        if p not in pred[i]:
                            held.append((p, i))
                        i = p
                    else:
                        i = max([j for j, d in s[2][i] if abs(fin[j] + d - st) < 1e-6] + [-1])
            place = dict(zip(order, range(n)))
        j, i = held[int(rnd() * len(held))]
        a, b, k, up = place[j], place[i], (0, 0, 1, 2, 3, 5)[int(rnd() * 6)], rnd() < 0.5
        other = (i if up else j) if "alt" in ops[i if up else j] and rnd() < FLIP else -1
        if other >= 0:
            flip(other)
            a, new = place[other], order
        else:
            while k and 0 < a and b < n - 1:
                a, b = (a - 1, b) if up else (a, b + 1)
                k -= eng[order[a if up else b]] == eng[i]
            seg = order[a:b + 1]
            move = {i if up else j}
            for x in (seg[::-1] if up else seg):
                if (succ if up else pred)[x] & move:
                    move.add(x)
            if seg[0 if up else -1] in move:
                continue
            new = order[:a] + [x for x in seg if (x in move) == up] + [x for x in seg if (x in move) != up] + order[b + 1:]
        room, got = -WARM * (1 - it / MOVES) * math.log(rnd()), []
        lost, last = 0.0, {eng[x]: x for x in order[:a]}.values()
        for s, x, u in zip(sets, now, unit):
            got.append(replay(s, new, a, x[1], last))
            lost += (got[-1][0] - x[0]) / u
            if lost > room + 0.001:
                break
        if lost < room:
            order, val, now, held = new, val + lost, got, None
            if val < best[0]:
                best = (val, new, eng[:])
        elif other >= 0:
            flip(other)
    eng[:] = best[2]
    price(range(n))
    fin = replay(sets[0], best[1], 0, [0.0] * n)[1]
    for i, o in enumerate(ops):
        o["t"], o["e"] = fin[i] - sets[0][1][i], eng[i]
    return best[1]


PLAN = []


def rank_program(g, core, T, topo):
    rank = T.rank_of(core)
    if rank is None:
        return
    n = len(T.cores)
    peers = []
    for t in range(RO):
        dst = T.cores[(rank + 1 + t % (n - 1)) % n]
        rid, pid, _ = topo.addr(dst)
        peers.append((rid, pid, sum(1 << e for e in topo.engines(core, dst)[:NENG])))
    ops = build(peers)
    if not PLAN:
        depends(ops)
        PLAN.extend([polish(ops, schedule(ops)[0]), ops])
    order = PLAN[0]
    for o, p in zip(ops, PLAN[1]):
        o.update(e=p["e"], dep=p["dep"], free=p.get("free", ()), t=p["t"])
        if "alt" in o:
            o["fn"] = o["alt"][o["e"]][0]
    queue = {"V": g.vector, "S": g.scalar, "P": g.tensor, "G": g, "Y": g.sync}
    count = {}
    known = {e: {} for e in queue}
    for i in order:
        o = ops[i]
        e = o["e"]
        kn = known[e]
        need = {}
        for j in o["dep"]:
            if j in o.get("free", ()):
                continue
            s, v = ops[j]["sig"]
            if kn.get(s, 0) < v and need.get(s, (0, 0))[0] < v:
                need[s] = (v, j)
        for s, (v, j) in sorted(need.items(), key=lambda x: -ops[x[1][1]]["t"]):
            if kn.get(s, 0) < v:
                queue[e].wait_ge(T.sem[s], v)
                kn[s] = v
                for s2, v2 in ops[j]["kn"].items():
                    if kn.get(s2, 0) < v2:
                        kn[s2] = v2
        o["kn"] = dict(kn)
        ins = o["fn"](g, T)
        if o["sem"]:
            o["sig"] = (o["sem"], o["inc"])
            count[o["sem"]] = o["inc"]
        else:
            s = "c" + e
            count[s] = count.get(s, 0) + 1
            o["sig"] = (s, count[s])
            ins.then_inc(T.sem[s], 1)
    for s in sorted(count):
        if known["G"].get(s, 0) < count[s]:
            g.wait_ge(T.sem[s], count[s])
